import numpy as np
import ml_dtypes


def mxq(x, axis, fmt="e4m3"):
    dtype, down = {"e4m3": (ml_dtypes.float8_e4m3fn, 7), "e5m2": (ml_dtypes.float8_e5m2, 14)}[fmt]
    v = np.moveaxis(np.asarray(x, np.float32).astype(ml_dtypes.bfloat16).astype(np.float64), axis, -1)
    blocks = v.reshape(v.shape[:-1] + (-1, 32))
    amax = np.abs(blocks).max(-1, keepdims=True)
    byte = np.maximum(np.where(amax > 0, np.frexp(amax)[1] - 1 + 127, 0) - down, 1)
    scale = np.exp2(byte - 127.0)
    codes = (blocks / scale).astype(np.float32).astype(dtype).astype(np.float64)
    return np.moveaxis((codes * scale).reshape(v.shape), -1, axis)


WIDE = False


def mx_kscale(k):
    if not WIDE:
        return np.ones(k)
    levels = np.array([10, -10, 5, -5, 0])
    if k % 512:
        return np.exp2(np.random.permutation(np.resize(levels, k // 32))).repeat(32)
    a = np.empty((k // 512, 16))
    for p in range(k // 512):
        a[p, :8] = np.random.permutation(np.resize(levels, 8))
        for g in range(8):
            far = levels[np.abs(levels - a[p, g]) >= 10]
            a[p, g + 8] = far[np.random.randint(len(far))]
    return np.exp2(a.ravel()).repeat(32)


def f64(x):
    return np.asarray(x).astype(np.float64)


def striped(idx):
    return np.tile(idx.reshape(-1, 16).T, (8, 1)).astype(np.uint16)


def unstriped(offs):
    return offs[:16].T.reshape(-1).astype(np.int64)


E2M1 = np.array([0.0, 0.5, 1.0, 1.5, 2.0, 3.0, 4.0, 6.0, -0.0, -0.5, -1.0, -1.5, -2.0, -3.0, -4.0, -6.0])


def pack_weight(w, fmt):
    k, n = w.shape
    w = f64(np.asarray(w, np.float32).astype(ml_dtypes.bfloat16)).reshape(k // 32, 32, n)
    amax = np.abs(w).max(1)
    if fmt == "e4m3":
        byte = np.frexp(amax)[1] - 1 + 127 - 7
    else:
        mant, ex = np.frexp(amax / 6.0)
        byte = np.where(mant > 0.5, ex, ex - 1) + 127
    byte = np.clip(np.where(amax > 0, byte, 1), 1, 254)
    scaled = (w * np.exp2(127.0 - byte)[:, None, :]).reshape(k, n).astype(np.float32)
    by_word = np.ascontiguousarray(scaled.reshape(k // 512, 128, 4, n).transpose(0, 1, 3, 2))
    if fmt == "e4m3":
        words = by_word.astype(ml_dtypes.float8_e4m3fn).view(np.uint8)
    else:
        c = by_word.astype(ml_dtypes.float4_e2m1fn).view(np.uint8) & 0xF
        words = (c[..., 0::2] | (c[..., 1::2] << 4)).reshape(k // 512, 128, 2 * n)
    return np.ascontiguousarray(words), np.ascontiguousarray(byte.astype(np.uint8).reshape(k // 512, 16, n))


def unpack_weight(words, scales, fmt):
    g, _, n = scales.shape
    words = np.ascontiguousarray(words).reshape(g, 128, n, -1)
    if fmt == "e4m3":
        vals = words.view(ml_dtypes.float8_e4m3fn).astype(np.float64)
    else:
        nib = np.empty((g, 128, n, 4), np.uint8)
        nib[..., 0::2] = words & 0xF
        nib[..., 1::2] = words >> 4
        vals = E2M1[nib]
    vals = vals * np.repeat(np.exp2(scales.astype(np.float64) - 127.0), 8, axis=1)[..., None]
    return vals.transpose(0, 1, 3, 2).reshape(g * 512, n)


def gelu(v):
    return 0.5 * v * (1.0 + np.tanh(np.sqrt(2.0 / np.pi) * (v + 0.044715 * v**3)))


K, H, N, T, S, T2 = 512, 1024, 384, 4096, 1024, 2048

def setup_inputs():
    n = np.random.standard_normal
    s = mx_kscale(K)[:, None]
    u = mx_kscale(H)[:, None]
    tab_words, tab_scales = pack_weight(n((K, T)) * s, "e4m3")
    w2_words, w2_scales = pack_weight(0.25 * n((K, H)) / np.sqrt(K) / s / u.T, "e2m1")
    return {
        "tab_words": tab_words, "tab_scales": tab_scales,
        "offs": striped(np.random.permutation(T)[:S]),
        "offs2": striped(np.random.permutation(T2)[:S]),
        "offs3": striped(np.random.permutation(T2)[:S]),
        "w1": (0.8 * n((K, H)) / np.sqrt(K) / s * u.T).astype(np.float32),
        "w2_words": w2_words, "w2_scales": w2_scales,
        "eq": (0.5 * n((H, S)) * u).astype(np.float32),
        "wg1": np.exp(0.3 * n((128, S))).astype(np.float32),
        "wg2": np.exp(0.3 * n((128, S))).astype(np.float32),
        "wall": (0.6 * n((H, T2)) * u).astype(np.float32),
        "w3": (n((H, N)) / np.sqrt(H) / u).astype(np.float32),
    }

def reference(tab_words, tab_scales, offs, offs2, offs3, w1, w2_words, w2_scales, eq, wg1, wg2, wall, w3):
    v = unpack_weight(tab_words, tab_scales, "e4m3")[:, unstriped(offs)]
    w2 = unpack_weight(w2_words, w2_scales, "e2m1")
    h1 = mxq(f64(w1), 0, "e4m3").T @ v
    rate = w2.T @ v
    h2 = (h1 - f64(eq)) * rate
    pageA = np.zeros((H, T2))
    pageA[:, unstriped(offs2)] = np.tile(f64(wg1), (H // 128, 1)) * h1
    pageB = np.zeros((H, T2))
    pageB[:, unstriped(offs3)] = np.tile(f64(wg2), (H // 128, 1)) * h2
    z = pageA * np.exp(pageB) + f64(wall)
    out = mxq(f64(w3), 0, "e4m3").T @ mxq(z, 0, "e4m3")
    return out

@@ -1,0 +1,306 @@
+from contextlib import ExitStack
+
+import concourse.mybir as mybir
+from concourse.masks import make_identity
+
+K, H, N, T, S, T2 = 512, 1024, 384, 4096, 1024, 2048
+FLOPS = 2 * K * H * S * 2 + 2 * H * N * T2
+
+F32 = mybir.dt.float32
+BF16 = mybir.dt.bfloat16
+I32 = mybir.dt.int32
+U32 = mybir.dt.uint32
+U16 = mybir.dt.uint16
+U8 = mybir.dt.uint8
+FP8X4 = mybir.dt.float8_e4m3fn_x4
+FP4X4 = mybir.dt.float4_e2m1fn_x4
+MULT = mybir.AluOpType.mult
+SUB = mybir.AluOpType.subtract
+EXP = mybir.ActivationFunctionType.Exp
+
+P = 128
+BANK = 512
+SLICES = H // P
+PASSES = H // 512
+CHUNKS = T2 // BANK
+W1_CHUNKS = ((0, 128), (128, 256), (256, 512), (512, 1024))
+
+
+def tile_list_cave_wall_growth_kernel(
+    tc, tab_words, tab_scales, offs, offs2, offs3, w1, w2_words, w2_scales, eq, wg1, wg2, wall, w3, out
+):
+    nc = tc.nc
+    with ExitStack() as ctx:
+        keep = ctx.enter_context(tc.tile_pool(name="keep", bufs=1))
+        two = ctx.enter_context(tc.tile_pool(name="two", bufs=2))
+        three = ctx.enter_context(tc.tile_pool(name="three", bufs=3))
+        psum = ctx.enter_context(tc.psum_pool(name="psum", bufs=4))
+        psum2 = ctx.enter_context(tc.psum_pool(name="psum2", bufs=2))
+
+        idx = keep.tile([P, S // 16], U16, name="idx")
+        idx2 = keep.tile([P, S // 16], U16, name="idx2")
+        idx3 = keep.tile([P, S // 16], U16, name="idx3")
+        tabw = keep.tile([P, T], U32, name="tabw")
+        tabs = keep.tile([P, T], U8, name="tabs")
+        w2w = keep.tile([P, 2 * H], U8, name="w2w", align_bytes=64)
+        w2s = keep.tile([P, H], U8, name="w2s", align_bytes=64)
+        wg1s = keep.tile([P, S], F32, name="wg1s")
+        wg2s = keep.tile([P, S], F32, name="wg2s")
+        ident = keep.tile([P, P], F32, name="ident")
+        page_a = keep.tile([P, T2], F32, name="page_a")
+        page_b = [keep.tile([P, T2], F32, name="page_b%d" % i) for i in range(2)]
+
+        def load_scale_rows(queue, plane, rows):
+            for q in range(4):
+                queue.dma_start(
+                    out=plane[32 * q : 32 * q + 4, :].bitcast(I32), in_=rows[4 * q : 4 * q + 4, :].bitcast(I32)
+                )
+
+        def interleave(grouped, raw):
+            nc.scalar.copy(
+                out=grouped.rearrange("p (c i t) -> p c t i", i=4, t=4),
+                in_=raw.rearrange("p t (c i) -> p c t i", i=4),
+            )
+
+        w1q = []
+
+        def w1_chunk(lo, hi):
+            width = hi - lo
+            raw = keep.tile([P, 4, width], F32, name="w1raw%d" % lo)
+            nc.sync.dma_start(out=raw[:], in_=w1[:, lo:hi].rearrange("(p t) c -> p t c", t=4))
+            grouped = keep.tile([P, 4 * width], BF16, name="w1bf%d" % lo, align_bytes=64)
+            interleave(grouped[:], raw[:])
+            codes = keep.tile([P, width], U32, name="w1c%d" % lo, align_bytes=64)
+            scales = keep.tile([P, width], U8, name="w1s%d" % lo, align_bytes=64)
+            nc.vector.quantize_mx(out=codes[:].bitcast(FP8X4), scales=scales[:], in_=grouped[:])
+            for c0 in range(0, width, P):
+                w1q.append((codes[:, c0 : c0 + P].bitcast(FP8X4), scales[:, c0 : c0 + P]))
+
+        nc.vector.memset(tabs[:].bitcast(I32), 0)
+        nc.vector.memset(w2s[:].bitcast(I32), 0)
+        nc.sync.dma_start(idx[:], offs)
+        nc.sync.dma_start(out=tabw[:].bitcast(I32), in_=tab_words[0].rearrange("p t i -> p (t i)").bitcast(I32))
+        load_scale_rows(nc.gpsimd, tabs, tab_scales[0])
+        nc.vector.memset(page_a[:], 0.0)
+        for page in page_b:
+            nc.vector.memset(page[:], 0.0)
+        make_identity(nc, ident[:])
+
+        vw = [keep.tile([P, BANK], U32, name="vw%d" % h, align_bytes=64) for h in range(2)]
+        vs = [keep.tile([P, BANK], U8, name="vs%d" % h, align_bytes=64) for h in range(2)]
+        w1_chunk(*W1_CHUNKS[0])
+        for h in range(2):
+            nc.vector.tensor_copy(vw[h][:], tabw[:].indirect(idx[:, 32 * h : 32 * h + 32]))
+            nc.vector.tensor_copy(vs[h][:], tabs[:].indirect(idx[:, 32 * h : 32 * h + 32]))
+
+        h1_banks = {}
+        sinks = {}
+        staged = {}
+        products = {}
+
+        def load_eq(s):
+            sink = three.tile([P, S], F32, name="sink", align_bytes=64)
+            nc.sync.dma_start(out=sink[:], in_=eq[P * s : P * s + P, :])
+            sinks[s] = sink
+
+        def scores(s):
+            both = three.tile([P, 2 * S], F32, name="both")
+            h1s, rates = both[:, :S], both[:, S:]
+            staged[s] = both
+            h1_banks[s] = []
+            for h in range(2):
+                cols = slice(BANK * h, BANK * h + BANK)
+                bank = psum2.tile([P, BANK], F32, name="source_bank")
+                nc.tensor.matmul_mx(
+                    out=bank[:], lhsT=w1q[s][0], lhsT_scale=w1q[s][1],
+                    rhs=vw[h][:].bitcast(FP8X4), rhs_scale=vs[h][:], start=True, stop=True,
+                )
+                h1_banks[s].append(bank)
+                if s == 0:
+                    weigh_source(s, h)
+                nc.scalar.copy(out=h1s[:, cols], in_=bank[:])
+            for h in range(2):
+                cols = slice(BANK * h, BANK * h + BANK)
+                bank = psum2.tile([P, BANK], F32, name="rate_bank")
+                nc.tensor.matmul_mx(
+                    out=bank[:], lhsT=w2w[:, 2 * P * s : 2 * P * s + 2 * P].bitcast(FP4X4),
+                    lhsT_scale=w2s[:, P * s : P * s + P],
+                    rhs=vw[h][:].bitcast(FP8X4), rhs_scale=vs[h][:], start=True, stop=True,
+                )
+                nc.scalar.copy(out=rates[:, cols], in_=bank[:])
+
+        def weigh_sink(s):
+            sink = sinks[s]
+            h1s, rates = staged[s][:, :S], staged[s][:, S:]
+            halves = [slice(BANK * h, BANK * h + BANK) for h in range(2)]
+            for cols in halves:
+                nc.gpsimd.tensor_tensor(sink[:, cols], h1s[:, cols], sink[:, cols], SUB)
+            for cols in halves:
+                nc.gpsimd.tensor_tensor(sink[:, cols], sink[:, cols], rates[:, cols], MULT)
+            for cols in halves:
+                nc.gpsimd.tensor_tensor(sink[:, cols], sink[:, cols], wg2s[:, cols], MULT)
+
+        sources = {}
+
+        def weigh_source(s, h):
+            if h == 0:
+                sources[s] = keep.tile([P, S], F32, name="source")
+            cols = slice(BANK * h, BANK * h + BANK)
+            nc.vector.tensor_tensor(sources[s][:, cols], h1_banks[s][h][:], wg1s[:, cols], MULT)
+
+        def scatter_source(s):
+            nc.vector.tensor_copy(page_a[:].indirect(idx2[:]), sources[s][:])
+
+        def scatter_sink(s):
+            nc.vector.tensor_copy(page_b[s % 2][:].indirect(idx3[:]), sinks[s][:])
+
+        def exponentiate(s, width):
+            tile = products[s]
+            for c0 in range(0, T2, width):
+                nc.scalar.activation(out=tile[:, c0 : c0 + width], in_=page_b[s % 2][:, c0 : c0 + width], func=EXP)
+
+        def grow(s, engine, width):
+            tile = products[s]
+            for c0 in range(0, T2, width):
+                cols = slice(c0, c0 + width)
+                engine.tensor_tensor(tile[:, cols], tile[:, cols], page_a[:, cols], MULT)
+
+        walls = {}
+
+        def load_wall(s):
+            rows = two.tile([P, T2], F32, name="wall_rows")
+            nc.sync.dma_start(out=rows[:], in_=wall[P * s : P * s + P, :])
+            walls[s] = rows
+
+        z_t = {}
+        zq = {}
+
+        def add_wall(s, c):
+            b, sl = divmod(s, 4)
+            if sl == 0:
+                z_t[c] = keep.tile([P, 4 * BANK], BF16, name="z_t%d" % c)
+            bank = psum.tile([P, BANK], F32, name="brief")
+            for i, rows in enumerate((walls[s], products[s])):
+                for g in range(4):
+                    nc.tensor.matmul(
+                        bank[:, P * g : P * g + P], lhsT=rows[:, BANK * c + P * g : BANK * c + P * g + P], rhs=ident[:],
+                        start=(i == 0 and g == 0), stop=(i == 1 and g == 3), is_transpose=True,
+                    )
+            nc.scalar.copy(
+                out=z_t[c][:].rearrange("m (u g q e) -> m u g q e", u=2, g=4, e=2)[:, :, :, 32 * sl : 32 * sl + 32, :],
+                in_=bank[:].rearrange("m (g q u e) -> m u g q e", g=4, u=2, e=2),
+            )
+
+        def regroup_z(c, grouped):
+            words = z_t[c][:].bitcast(F32)
+            for h in range(2):
+                bank = psum.tile([P, BANK], F32, name="brief")
+                for u in range(2):
+                    for g2 in range(2):
+                        w0 = P * (4 * u + 2 * h + g2)
+                        o0 = P * (2 * u + g2)
+                        nc.tensor.transpose(bank[:, o0 : o0 + P], words[:, w0 : w0 + P], ident[:])
+                nc.scalar.copy(
+                    out=grouped.bitcast(F32)[:, BANK * h : BANK * h + BANK].rearrange("p (m u) -> p m u", u=2),
+                    in_=bank[:].rearrange("p (u m) -> p m u", u=2),
+                )
+
+        def regroup_chunks(chunks):
+            grouped = two.tile([P, 8 * BANK], BF16, name="grouped", align_bytes=64)
+            for i, c in enumerate(chunks):
+                regroup_z(c, grouped[:, 4 * BANK * i : 4 * BANK * (i + 1)])
+            return grouped
+
+        def quantize_z(b, chunks, grouped, codes):
+            n = len(chunks)
+            scales = keep.tile([P, n * BANK], U8, name="zs%d_%d" % (b, chunks[0]), align_bytes=64)
+            nc.vector.quantize_mx(out=codes.bitcast(FP8X4), scales=scales[:], in_=grouped[:, : 4 * BANK * n])
+            for i, c in enumerate(chunks):
+                zq[b, c] = (codes[:, BANK * i : BANK * (i + 1)], scales[:, BANK * i : BANK * (i + 1)])
+
+        w3c = keep.tile([P, PASSES * N], U32, name="w3c", align_bytes=64)
+        w3s = keep.tile([P, PASSES * N], U8, name="w3s", align_bytes=64)
+
+        def quantize_w3():
+            grouped = keep.tile([P, 4 * PASSES * N], BF16, name="w3bf", align_bytes=64)
+            for b in range(PASSES):
+                raw = keep.tile([P, 4, N], F32, name="w3raw%d" % b)
+                nc.sync.dma_start(out=raw[:], in_=w3[512 * b : 512 * b + 512, :].rearrange("(p t) n -> p t n", t=4))
+                interleave(grouped[:, 4 * N * b : 4 * N * b + 4 * N], raw[:])
+            for lo, hi in ((0, 512), (512, PASSES * N)):
+                nc.vector.quantize_mx(
+                    out=w3c[:, lo:hi].bitcast(FP8X4), scales=w3s[:, lo:hi], in_=grouped[:, 4 * lo : 4 * hi]
+                )
+
+        def project(c):
+            for nb in range(N // P):
+                bank = psum2.tile([P, BANK], F32, name=("source_bank", "rate_bank")[(3 * c + nb) % 2])
+                for b in range(PASSES):
+                    cols = slice(N * b + P * nb, N * b + P * nb + P)
+                    nc.tensor.matmul_mx(
+                        out=bank[:], lhsT=w3c[:, cols].bitcast(FP8X4), lhsT_scale=w3s[:, cols],
+                        rhs=zq[b, c][0].bitcast(FP8X4), rhs_scale=zq[b, c][1],
+                        start=(b == 0), stop=(b == PASSES - 1),
+                    )
+                result = three.tile([P, BANK], F32, name="result%d" % (nb % 2))
+                copy = nc.scalar.copy if nb == 0 else nc.vector.tensor_copy
+                copy(out=result[:], in_=bank[:])
+                nc.sync.dma_start(out=out[P * nb : P * nb + P, BANK * c : BANK * c + BANK], in_=result[:])
+
+        load_eq(0)
+        nc.sync.dma_start(out=wg1s[:], in_=wg1)
+        nc.sync.dma_start(out=w2w[:].bitcast(I32), in_=w2_words[0].bitcast(I32))
+        nc.sync.dma_start(idx2[:], offs2)
+        load_scale_rows(nc.sync, w2s, w2_scales[0])
+        nc.sync.dma_start(out=wg2s[:], in_=wg2)
+        scores(0)
+        weigh_sink(0)
+        scatter_source(0)
+        nc.sync.dma_start(idx3[:], offs3)
+        w1_chunk(*W1_CHUNKS[1])
+        load_eq(1)
+        scores(1)
+        weigh_sink(1)
+        scatter_sink(0)
+        w1_chunk(*W1_CHUNKS[2])
+        products[0] = staged[1]
+        exponentiate(0, S)
+        last = SLICES - 1
+        for s in range(1, SLICES):
+            for h in range(2):
+                weigh_source(s, h)
+            if s < last:
+                load_eq(s + 1)
+                scores(s + 1)
+            scatter_sink(s)
+            load_wall(s - 1)
+            grow(s - 1, nc.gpsimd, S)
+            scatter_source(s)
+            for c in range(CHUNKS):
+                add_wall(s - 1, c)
+            if s < last:
+                weigh_sink(s + 1)
+                products[s] = staged[s + 1]
+                exponentiate(s, S)
+            if s == 1:
+                w1_chunk(*W1_CHUNKS[3])
+            if s == 2:
+                quantize_w3()
+            if s == 4:
+                first_pass = [(pair, regroup_chunks(pair)) for pair in ((0, 1), (2, 3))]
+            if s == 6:
+                for pair, grouped in first_pass:
+                    codes = three.tile([P, 2 * BANK], U32, name="sink", align_bytes=64)
+                    quantize_z(0, pair, grouped, codes[:])
+        load_wall(last)
+        products[last] = three.tile([P, T2], F32, name="both")
+        exponentiate(last, BANK)
+        grow(last, nc.vector, BANK)
+        for step in range(CHUNKS + 2):
+            if step < CHUNKS:
+                add_wall(last, step)
+            if 1 <= step <= CHUNKS:
+                codes = keep.tile([P, BANK], U32, name="zc%d" % step, align_bytes=64)
+                quantize_z(1, (step - 1,), regroup_chunks((step - 1,)), codes[:])
+            if step >= 2:
+                project(step - 2)

@@ -16,6 +16,7 @@ FP8X4 = mybir.dt.float8_e4m3fn_x4
 FP4X4 = mybir.dt.float4_e2m1fn_x4
 MULT = mybir.AluOpType.mult
 SUB = mybir.AluOpType.subtract
+COPY = mybir.ActivationFunctionType.Copy
 EXP = mybir.ActivationFunctionType.Exp
 
 P = 128
@@ -34,8 +35,8 @@ def tile_list_cave_wall_growth_kernel(
         keep = ctx.enter_context(tc.tile_pool(name="keep", bufs=1))
         two = ctx.enter_context(tc.tile_pool(name="two", bufs=2))
         three = ctx.enter_context(tc.tile_pool(name="three", bufs=3))
-        psum = ctx.enter_context(tc.psum_pool(name="psum", bufs=4))
-        psum2 = ctx.enter_context(tc.psum_pool(name="psum2", bufs=2))
+        psum = ctx.enter_context(tc.psum_pool(name="psum", bufs=2))
+        psum6 = ctx.enter_context(tc.psum_pool(name="psum6", bufs=6))
 
         idx = keep.tile([P, S // 16], U16, name="idx")
         idx2 = keep.tile([P, S // 16], U16, name="idx2")
@@ -78,8 +79,10 @@ def tile_list_cave_wall_growth_kernel(
 
         nc.vector.memset(tabs[:].bitcast(I32), 0)
         nc.vector.memset(w2s[:].bitcast(I32), 0)
+        table = tab_words[0].rearrange("p t i -> p (t i)").bitcast(I32)
+        for half in (slice(0, T // 2), slice(T // 2, T)):
+            nc.sync.dma_start(out=tabw[:].bitcast(I32)[:, half], in_=table[:, half])
         nc.sync.dma_start(idx[:], offs)
-        nc.sync.dma_start(out=tabw[:].bitcast(I32), in_=tab_words[0].rearrange("p t i -> p (t i)").bitcast(I32))
         load_scale_rows(nc.gpsimd, tabs, tab_scales[0])
         nc.vector.memset(page_a[:], 0.0)
         for page in page_b:
@@ -103,40 +106,74 @@ def tile_list_cave_wall_growth_kernel(
             nc.sync.dma_start(out=sink[:], in_=eq[P * s : P * s + P, :])
             sinks[s] = sink
 
+        def source_scores(s, h):
+            bank = psum6.tile([P, BANK], F32, name="held")
+            nc.tensor.matmul_mx(
+                out=bank[:], lhsT=w1q[s][0], lhsT_scale=w1q[s][1],
+                rhs=vw[h][:].bitcast(FP8X4), rhs_scale=vs[h][:], start=True, stop=True,
+            )
+            h1_banks[s, h] = bank
+            return bank
+
+        def rate_scores(s, h):
+            bank = psum.tile([P, BANK], F32, name="brief")
+            nc.tensor.matmul_mx(
+                out=bank[:], lhsT=w2w[:, 2 * P * s : 2 * P * s + 2 * P].bitcast(FP4X4),
+                lhsT_scale=w2s[:, P * s : P * s + P],
+                rhs=vw[h][:].bitcast(FP8X4), rhs_scale=vs[h][:], start=True, stop=True,
+            )
+            return bank
+
         def scores(s):
             both = three.tile([P, 2 * S], F32, name="both")
-            h1s, rates = both[:, :S], both[:, S:]
             staged[s] = both
-            h1_banks[s] = []
+            for h in range(2):
+                nc.scalar.activation(
+                    out=both[:, BANK * h : BANK * h + BANK], in_=source_scores(s, h)[:], func=COPY, scale=-1.0
+                )
+            for h in range(2):
+                nc.scalar.copy(out=both[:, S + BANK * h : S + BANK * h + BANK], in_=rate_scores(s, h)[:])
+
+        def first_sink():
+            sink = sinks[0]
             for h in range(2):
                 cols = slice(BANK * h, BANK * h + BANK)
-                bank = psum2.tile([P, BANK], F32, name="source_bank")
-                nc.tensor.matmul_mx(
-                    out=bank[:], lhsT=w1q[s][0], lhsT_scale=w1q[s][1],
-                    rhs=vw[h][:].bitcast(FP8X4), rhs_scale=vs[h][:], start=True, stop=True,
-                )
-                h1_banks[s].append(bank)
-                if s == 0:
-                    weigh_source(s, h)
-                nc.scalar.copy(out=h1s[:, cols], in_=bank[:])
+                nc.vector.tensor_tensor(sink[:, cols], source_scores(0, h)[:], sink[:, cols], SUB)
             for h in range(2):
                 cols = slice(BANK * h, BANK * h + BANK)
-                bank = psum2.tile([P, BANK], F32, name="rate_bank")
-                nc.tensor.matmul_mx(
-                    out=bank[:], lhsT=w2w[:, 2 * P * s : 2 * P * s + 2 * P].bitcast(FP4X4),
-                    lhsT_scale=w2s[:, P * s : P * s + P],
-                    rhs=vw[h][:].bitcast(FP8X4), rhs_scale=vs[h][:], start=True, stop=True,
+                nc.vector.tensor_tensor(sink[:, cols], rate_scores(0, h)[:], sink[:, cols], MULT)
+            nc.vector.tensor_tensor(page_b[0][:].indirect(idx3[:]), sink[:], wg2s[:], MULT)
+
+        def add_transposed(bank, rows, opens):
+            for g in range(4):
+                nc.tensor.matmul(
+                    bank[:, P * g : P * g + P], lhsT=rows[:, P * g : P * g + P], rhs=ident[:],
+                    start=(opens and g == 0), stop=(not opens and g == 3), is_transpose=True,
                 )
-                nc.scalar.copy(out=rates[:, cols], in_=bank[:])
+
+        def subtract_eq(s):
+            turned = []
+            for h in range(2):
+                cols = slice(BANK * h, BANK * h + BANK)
+                bank = psum.tile([P, BANK], F32, name="brief")
+                add_transposed(bank, sinks[s][:, cols], True)
+                add_transposed(bank, staged[s][:, cols], False)
+                gap_t = two.tile([P, BANK], F32, name="gap_t")
+                nc.scalar.copy(out=gap_t[:], in_=bank[:])
+                turned.append(gap_t)
+            for h in range(2):
+                cols = slice(BANK * h, BANK * h + BANK)
+                bank = psum6.tile([P, BANK], F32, name="held")
+                for g in range(4):
+                    nc.tensor.transpose(bank[:, P * g : P * g + P], turned[h][:, P * g : P * g + P], ident[:])
+                nc.scalar.activation(out=staged[s][:, cols], in_=bank[:], func=COPY, scale=-1.0)
 
         def weigh_sink(s):
             sink = sinks[s]
             h1s, rates = staged[s][:, :S], staged[s][:, S:]
             halves = [slice(BANK * h, BANK * h + BANK) for h in range(2)]
             for cols in halves:
-                nc.gpsimd.tensor_tensor(sink[:, cols], h1s[:, cols], sink[:, cols], SUB)
-            for cols in halves:
-                nc.gpsimd.tensor_tensor(sink[:, cols], sink[:, cols], rates[:, cols], MULT)
+                nc.gpsimd.tensor_tensor(sink[:, cols], h1s[:, cols], rates[:, cols], MULT)
             for cols in halves:
                 nc.gpsimd.tensor_tensor(sink[:, cols], sink[:, cols], wg2s[:, cols], MULT)
 
@@ -146,7 +183,7 @@ def tile_list_cave_wall_growth_kernel(
             if h == 0:
                 sources[s] = keep.tile([P, S], F32, name="source")
             cols = slice(BANK * h, BANK * h + BANK)
-            nc.vector.tensor_tensor(sources[s][:, cols], h1_banks[s][h][:], wg1s[:, cols], MULT)
+            nc.vector.tensor_tensor(sources[s][:, cols], h1_banks[s, h][:], wg1s[:, cols], MULT)
 
         def scatter_source(s):
             nc.vector.tensor_copy(page_a[:].indirect(idx2[:]), sources[s][:])
@@ -175,40 +212,38 @@ def tile_list_cave_wall_growth_kernel(
         z_t = {}
         zq = {}
 
-        def add_wall(s, c):
-            b, sl = divmod(s, 4)
+        def open_with_wall(s, c, bank):
+            add_transposed(bank, walls[s][:, BANK * c : BANK * c + BANK], True)
+            return bank
+
+        def add_product(s, c, bank):
+            sl = s % 4
             if sl == 0:
                 z_t[c] = keep.tile([P, 4 * BANK], BF16, name="z_t%d" % c)
-            bank = psum.tile([P, BANK], F32, name="brief")
-            for i, rows in enumerate((walls[s], products[s])):
-                for g in range(4):
-                    nc.tensor.matmul(
-                        bank[:, P * g : P * g + P], lhsT=rows[:, BANK * c + P * g : BANK * c + P * g + P], rhs=ident[:],
-                        start=(i == 0 and g == 0), stop=(i == 1 and g == 3), is_transpose=True,
-                    )
+            add_transposed(bank, products[s][:, BANK * c : BANK * c + BANK], False)
             nc.scalar.copy(
                 out=z_t[c][:].rearrange("m (u g q e) -> m u g q e", u=2, g=4, e=2)[:, :, :, 32 * sl : 32 * sl + 32, :],
                 in_=bank[:].rearrange("m (g q u e) -> m u g q e", g=4, u=2, e=2),
             )
 
-        def regroup_z(c, grouped):
+        def regroup_z(b, c, grouped):
             words = z_t[c][:].bitcast(F32)
-            for h in range(2):
+            for h, copy in enumerate((nc.scalar.copy, nc.vector.tensor_copy if b == PASSES - 1 else nc.scalar.copy)):
                 bank = psum.tile([P, BANK], F32, name="brief")
                 for u in range(2):
                     for g2 in range(2):
                         w0 = P * (4 * u + 2 * h + g2)
                         o0 = P * (2 * u + g2)
                         nc.tensor.transpose(bank[:, o0 : o0 + P], words[:, w0 : w0 + P], ident[:])
-                nc.scalar.copy(
+                copy(
                     out=grouped.bitcast(F32)[:, BANK * h : BANK * h + BANK].rearrange("p (m u) -> p m u", u=2),
                     in_=bank[:].rearrange("p (u m) -> p m u", u=2),
                 )
 
-        def regroup_chunks(chunks):
+        def regroup_chunks(b, chunks):
             grouped = two.tile([P, 8 * BANK], BF16, name="grouped", align_bytes=64)
             for i, c in enumerate(chunks):
-                regroup_z(c, grouped[:, 4 * BANK * i : 4 * BANK * (i + 1)])
+                regroup_z(b, c, grouped[:, 4 * BANK * i : 4 * BANK * (i + 1)])
             return grouped
 
         def quantize_z(b, chunks, grouped, codes):
@@ -234,7 +269,7 @@ def tile_list_cave_wall_growth_kernel(
 
         def project(c):
             for nb in range(N // P):
-                bank = psum2.tile([P, BANK], F32, name=("source_bank", "rate_bank")[(3 * c + nb) % 2])
+                bank = psum6.tile([P, BANK], F32, name="held")
                 for b in range(PASSES):
                     cols = slice(N * b + P * nb, N * b + P * nb + P)
                     nc.tensor.matmul_mx(
@@ -243,64 +278,70 @@ def tile_list_cave_wall_growth_kernel(
                         start=(b == 0), stop=(b == PASSES - 1),
                     )
                 result = three.tile([P, BANK], F32, name="result%d" % (nb % 2))
-                copy = nc.scalar.copy if nb == 0 else nc.vector.tensor_copy
+                copy = nc.vector.tensor_copy if nb == 1 else nc.scalar.copy
                 copy(out=result[:], in_=bank[:])
                 nc.sync.dma_start(out=out[P * nb : P * nb + P, BANK * c : BANK * c + BANK], in_=result[:])
 
-        load_eq(0)
-        nc.sync.dma_start(out=wg1s[:], in_=wg1)
         nc.sync.dma_start(out=w2w[:].bitcast(I32), in_=w2_words[0].bitcast(I32))
-        nc.sync.dma_start(idx2[:], offs2)
-        load_scale_rows(nc.sync, w2s, w2_scales[0])
-        nc.sync.dma_start(out=wg2s[:], in_=wg2)
-        scores(0)
-        weigh_sink(0)
-        scatter_source(0)
         nc.sync.dma_start(idx3[:], offs3)
         w1_chunk(*W1_CHUNKS[1])
-        load_eq(1)
-        scores(1)
-        weigh_sink(1)
-        scatter_sink(0)
         w1_chunk(*W1_CHUNKS[2])
+        load_scale_rows(nc.sync, w2s, w2_scales[0])
+        load_eq(0)
+        nc.sync.dma_start(out=wg2s[:], in_=wg2)
+        first_sink()
+        load_eq(1)
+        nc.sync.dma_start(out=wg1s[:], in_=wg1)
+        nc.sync.dma_start(idx2[:], offs2)
+        scores(1)
+        subtract_eq(1)
+        w1_chunk(*W1_CHUNKS[3])
+        load_eq(2)
+        for h in range(2):
+            weigh_source(0, h)
+        scatter_source(0)
+        weigh_sink(1)
         products[0] = staged[1]
-        exponentiate(0, S)
+        exponentiate(0, BANK)
+        scores(2)
+        subtract_eq(2)
         last = SLICES - 1
         for s in range(1, SLICES):
             for h in range(2):
                 weigh_source(s, h)
-            if s < last:
-                load_eq(s + 1)
-                scores(s + 1)
+            if s + 2 <= last:
+                load_eq(s + 2)
             scatter_sink(s)
             load_wall(s - 1)
             grow(s - 1, nc.gpsimd, S)
             scatter_source(s)
             for c in range(CHUNKS):
-                add_wall(s - 1, c)
+                add_product(s - 1, c, open_with_wall(s - 1, c, psum.tile([P, BANK], F32, name="brief")))
             if s < last:
                 weigh_sink(s + 1)
                 products[s] = staged[s + 1]
-                exponentiate(s, S)
-            if s == 1:
-                w1_chunk(*W1_CHUNKS[3])
+                exponentiate(s, BANK)
+            if s + 2 <= last:
+                scores(s + 2)
+                subtract_eq(s + 2)
             if s == 2:
                 quantize_w3()
             if s == 4:
-                first_pass = [(pair, regroup_chunks(pair)) for pair in ((0, 1), (2, 3))]
+                first_pass = [(pair, regroup_chunks(0, pair)) for pair in ((0, 1), (2, 3))]
             if s == 6:
                 for pair, grouped in first_pass:
                     codes = three.tile([P, 2 * BANK], U32, name="sink", align_bytes=64)
                     quantize_z(0, pair, grouped, codes[:])
         load_wall(last)
+        last_banks = [open_with_wall(last, c, psum6.tile([P, BANK], F32, name="held")) for c in range(CHUNKS)]
         products[last] = three.tile([P, T2], F32, name="both")
         exponentiate(last, BANK)
         grow(last, nc.vector, BANK)
         for step in range(CHUNKS + 2):
             if step < CHUNKS:
-                add_wall(last, step)
+                add_product(last, step, last_banks[step])
             if 1 <= step <= CHUNKS:
                 codes = keep.tile([P, BANK], U32, name="zc%d" % step, align_bytes=64)
-                quantize_z(1, (step - 1,), regroup_chunks((step - 1,)), codes[:])
+                quantize_z(1, (step - 1,), regroup_chunks(1, (step - 1,)), codes[:])
             if step >= 2:
                 project(step - 2)

@@ -24,7 +24,8 @@ BANK = 512
 SLICES = H // P
 PASSES = H // 512
 CHUNKS = T2 // BANK
-W1_CHUNKS = ((0, 128), (128, 256), (256, 512), (512, 1024))
+W1_CHUNKS = ((0, 256), (256, 512), (512, 1024))
+Z_T_TAGS = (("z_t0", "z_t1", "z_t2", "z_t3"), ("w1raw0", "w1raw256", "w1raw512", "w3raw0"))
 
 
 def tile_list_cave_wall_growth_kernel(
@@ -79,11 +80,13 @@ def tile_list_cave_wall_growth_kernel(
 
         nc.vector.memset(tabs[:].bitcast(I32), 0)
         nc.vector.memset(w2s[:].bitcast(I32), 0)
+        nc.sync.dma_start(idx[:], offs)
+        nc.sync.dma_start(idx3[:], offs3)
+        nc.sync.dma_start(idx2[:], offs2)
         table = tab_words[0].rearrange("p t i -> p (t i)").bitcast(I32)
         for half in (slice(0, T // 2), slice(T // 2, T)):
             nc.sync.dma_start(out=tabw[:].bitcast(I32)[:, half], in_=table[:, half])
-        nc.sync.dma_start(idx[:], offs)
-        load_scale_rows(nc.gpsimd, tabs, tab_scales[0])
+        load_scale_rows(nc.sync, tabs, tab_scales[0])
         nc.vector.memset(page_a[:], 0.0)
         for page in page_b:
             nc.vector.memset(page[:], 0.0)
@@ -219,15 +222,15 @@ def tile_list_cave_wall_growth_kernel(
         def add_product(s, c, bank):
             sl = s % 4
             if sl == 0:
-                z_t[c] = keep.tile([P, 4 * BANK], BF16, name="z_t%d" % c)
+                z_t[s // 4, c] = keep.tile([P, 4 * BANK], BF16, name=Z_T_TAGS[s // 4][c])
             add_transposed(bank, products[s][:, BANK * c : BANK * c + BANK], False)
             nc.scalar.copy(
-                out=z_t[c][:].rearrange("m (u g q e) -> m u g q e", u=2, g=4, e=2)[:, :, :, 32 * sl : 32 * sl + 32, :],
+                out=z_t[s // 4, c][:].rearrange("m (u g q e) -> m u g q e", u=2, g=4, e=2)[:, :, :, 32 * sl : 32 * sl + 32, :],
                 in_=bank[:].rearrange("m (g q u e) -> m u g q e", g=4, u=2, e=2),
             )
 
         def regroup_z(b, c, grouped):
-            words = z_t[c][:].bitcast(F32)
+            words = z_t[b, c][:].bitcast(F32)
             for h, copy in enumerate((nc.scalar.copy, nc.vector.tensor_copy if b == PASSES - 1 else nc.scalar.copy)):
                 bank = psum.tile([P, BANK], F32, name="brief")
                 for u in range(2):
@@ -277,35 +280,33 @@ def tile_list_cave_wall_growth_kernel(
                         rhs=zq[b, c][0].bitcast(FP8X4), rhs_scale=zq[b, c][1],
                         start=(b == 0), stop=(b == PASSES - 1),
                     )
-                result = three.tile([P, BANK], F32, name="result%d" % (nb % 2))
+                result = three.tile([P, BANK], F32, name="result%d" % nb)
                 copy = nc.vector.tensor_copy if nb == 1 else nc.scalar.copy
                 copy(out=result[:], in_=bank[:])
                 nc.sync.dma_start(out=out[P * nb : P * nb + P, BANK * c : BANK * c + BANK], in_=result[:])
 
         nc.sync.dma_start(out=w2w[:].bitcast(I32), in_=w2_words[0].bitcast(I32))
-        nc.sync.dma_start(idx3[:], offs3)
-        w1_chunk(*W1_CHUNKS[1])
-        w1_chunk(*W1_CHUNKS[2])
-        load_scale_rows(nc.sync, w2s, w2_scales[0])
+        load_scale_rows(nc.gpsimd, w2s, w2_scales[0])
         load_eq(0)
+        w1_chunk(*W1_CHUNKS[1])
         nc.sync.dma_start(out=wg2s[:], in_=wg2)
         first_sink()
         load_eq(1)
         nc.sync.dma_start(out=wg1s[:], in_=wg1)
-        nc.sync.dma_start(idx2[:], offs2)
         scores(1)
         subtract_eq(1)
-        w1_chunk(*W1_CHUNKS[3])
+        w1_chunk(*W1_CHUNKS[2])
         load_eq(2)
         for h in range(2):
             weigh_source(0, h)
         scatter_source(0)
         weigh_sink(1)
         products[0] = staged[1]
-        exponentiate(0, BANK)
+        exponentiate(0, S)
         scores(2)
         subtract_eq(2)
         last = SLICES - 1
+        first_pass = {}
         for s in range(1, SLICES):
             for h in range(2):
                 weigh_source(s, h)
@@ -313,25 +314,26 @@ def tile_list_cave_wall_growth_kernel(
                 load_eq(s + 2)
             scatter_sink(s)
             load_wall(s - 1)
-            grow(s - 1, nc.gpsimd, S)
+            grow(s - 1, nc.gpsimd, BANK)
             scatter_source(s)
             for c in range(CHUNKS):
                 add_product(s - 1, c, open_with_wall(s - 1, c, psum.tile([P, BANK], F32, name="brief")))
             if s < last:
                 weigh_sink(s + 1)
                 products[s] = staged[s + 1]
-                exponentiate(s, BANK)
+                exponentiate(s, S)
             if s + 2 <= last:
                 scores(s + 2)
                 subtract_eq(s + 2)
             if s == 2:
                 quantize_w3()
-            if s == 4:
-                first_pass = [(pair, regroup_chunks(0, pair)) for pair in ((0, 1), (2, 3))]
-            if s == 6:
-                for pair, grouped in first_pass:
+            for pair, at in (((0, 1), 4), ((2, 3), 5)):
+                if s == at:
+                    first_pass[pair] = regroup_chunks(0, pair)
+            for pair, at in (((0, 1), 6), ((2, 3), 6)):
+                if s == at:
                     codes = three.tile([P, 2 * BANK], U32, name="sink", align_bytes=64)
-                    quantize_z(0, pair, grouped, codes[:])
+                    quantize_z(0, pair, first_pass[pair], codes[:])
         load_wall(last)
         last_banks = [open_with_wall(last, c, psum6.tile([P, BANK], F32, name="held")) for c in range(CHUNKS)]
         products[last] = three.tile([P, T2], F32, name="both")

@@ -15,7 +15,7 @@ U8 = mybir.dt.uint8
 FP8X4 = mybir.dt.float8_e4m3fn_x4
 FP4X4 = mybir.dt.float4_e2m1fn_x4
 MULT = mybir.AluOpType.mult
-SUB = mybir.AluOpType.subtract
+ADD = mybir.AluOpType.add
 COPY = mybir.ActivationFunctionType.Copy
 EXP = mybir.ActivationFunctionType.Exp
 
@@ -36,8 +36,10 @@ def tile_list_cave_wall_growth_kernel(
         keep = ctx.enter_context(tc.tile_pool(name="keep", bufs=1))
         two = ctx.enter_context(tc.tile_pool(name="two", bufs=2))
         three = ctx.enter_context(tc.tile_pool(name="three", bufs=3))
-        psum = ctx.enter_context(tc.psum_pool(name="psum", bufs=2))
-        psum6 = ctx.enter_context(tc.psum_pool(name="psum6", bufs=6))
+        psum = ctx.enter_context(tc.psum_pool(name="psum", bufs=8))
+
+        def next_bank():
+            return psum.tile([P, BANK], F32, name="bank")
 
         idx = keep.tile([P, S // 16], U16, name="idx")
         idx2 = keep.tile([P, S // 16], U16, name="idx2")
@@ -46,10 +48,10 @@ def tile_list_cave_wall_growth_kernel(
         tabs = keep.tile([P, T], U8, name="tabs")
         w2w = keep.tile([P, 2 * H], U8, name="w2w", align_bytes=64)
         w2s = keep.tile([P, H], U8, name="w2s", align_bytes=64)
-        wg1s = keep.tile([P, S], F32, name="wg1s")
-        wg2s = keep.tile([P, S], F32, name="wg2s")
+        wg = keep.tile([P, 2 * S], F32, name="wg")
         ident = keep.tile([P, P], F32, name="ident")
-        page_a = keep.tile([P, T2], F32, name="page_a")
+        page_a = [keep.tile([P, T2], F32, name="page_a%d" % i) for i in range(2)]
+        growth = [keep.tile([P, T2], F32, name="growth%d" % i) for i in range(2)]
         page_b = [keep.tile([P, T2], F32, name="page_b%d" % i) for i in range(2)]
 
         def load_scale_rows(queue, plane, rows):
@@ -66,10 +68,13 @@ def tile_list_cave_wall_growth_kernel(
 
         w1q = []
 
-        def w1_chunk(lo, hi):
+        def w1_chunk(lo, hi, parts=1):
             width = hi - lo
             raw = keep.tile([P, 4, width], F32, name="w1raw%d" % lo)
-            nc.sync.dma_start(out=raw[:], in_=w1[:, lo:hi].rearrange("(p t) c -> p t c", t=4))
+            rows = w1[:, lo:hi].rearrange("(p t) c -> p t c", t=4)
+            for part in range(parts):
+                planes = slice(4 // parts * part, 4 // parts * (part + 1))
+                nc.sync.dma_start(out=raw[:, planes, :], in_=rows[:, planes, :])
             grouped = keep.tile([P, 4 * width], BF16, name="w1bf%d" % lo, align_bytes=64)
             interleave(grouped[:], raw[:])
             codes = keep.tile([P, width], U32, name="w1c%d" % lo, align_bytes=64)
@@ -78,74 +83,39 @@ def tile_list_cave_wall_growth_kernel(
             for c0 in range(0, width, P):
                 w1q.append((codes[:, c0 : c0 + P].bitcast(FP8X4), scales[:, c0 : c0 + P]))
 
-        nc.vector.memset(tabs[:].bitcast(I32), 0)
-        nc.vector.memset(w2s[:].bitcast(I32), 0)
-        nc.sync.dma_start(idx[:], offs)
-        nc.sync.dma_start(idx3[:], offs3)
-        nc.sync.dma_start(idx2[:], offs2)
-        table = tab_words[0].rearrange("p t i -> p (t i)").bitcast(I32)
-        for half in (slice(0, T // 2), slice(T // 2, T)):
-            nc.sync.dma_start(out=tabw[:].bitcast(I32)[:, half], in_=table[:, half])
-        load_scale_rows(nc.sync, tabs, tab_scales[0])
-        nc.vector.memset(page_a[:], 0.0)
-        for page in page_b:
-            nc.vector.memset(page[:], 0.0)
-        make_identity(nc, ident[:])
-
         vw = [keep.tile([P, BANK], U32, name="vw%d" % h, align_bytes=64) for h in range(2)]
         vs = [keep.tile([P, BANK], U8, name="vs%d" % h, align_bytes=64) for h in range(2)]
-        w1_chunk(*W1_CHUNKS[0])
-        for h in range(2):
-            nc.vector.tensor_copy(vw[h][:], tabw[:].indirect(idx[:, 32 * h : 32 * h + 32]))
-            nc.vector.tensor_copy(vs[h][:], tabs[:].indirect(idx[:, 32 * h : 32 * h + 32]))
-
-        h1_banks = {}
+        halves = [slice(BANK * h, BANK * h + BANK) for h in range(2)]
         sinks = {}
         staged = {}
-        products = {}
+        sources = {}
 
         def load_eq(s):
             sink = three.tile([P, S], F32, name="sink", align_bytes=64)
             nc.sync.dma_start(out=sink[:], in_=eq[P * s : P * s + P, :])
             sinks[s] = sink
 
-        def source_scores(s, h):
-            bank = psum6.tile([P, BANK], F32, name="held")
-            nc.tensor.matmul_mx(
-                out=bank[:], lhsT=w1q[s][0], lhsT_scale=w1q[s][1],
-                rhs=vw[h][:].bitcast(FP8X4), rhs_scale=vs[h][:], start=True, stop=True,
-            )
-            h1_banks[s, h] = bank
-            return bank
-
-        def rate_scores(s, h):
-            bank = psum.tile([P, BANK], F32, name="brief")
-            nc.tensor.matmul_mx(
-                out=bank[:], lhsT=w2w[:, 2 * P * s : 2 * P * s + 2 * P].bitcast(FP4X4),
-                lhsT_scale=w2s[:, P * s : P * s + P],
-                rhs=vw[h][:].bitcast(FP8X4), rhs_scale=vs[h][:], start=True, stop=True,
-            )
-            return bank
-
-        def scores(s):
-            both = three.tile([P, 2 * S], F32, name="both")
+        def source_scores(s):
+            both = three.tile([P, 2 * S], F32, name="both", align_bytes=64)
             staged[s] = both
+            sources[s] = both[:, :S]
             for h in range(2):
-                nc.scalar.activation(
-                    out=both[:, BANK * h : BANK * h + BANK], in_=source_scores(s, h)[:], func=COPY, scale=-1.0
+                bank = next_bank()
+                nc.tensor.matmul_mx(
+                    out=bank[:], lhsT=w1q[s][0], lhsT_scale=w1q[s][1],
+                    rhs=vw[h][:].bitcast(FP8X4), rhs_scale=vs[h][:], start=True, stop=True,
                 )
-            for h in range(2):
-                nc.scalar.copy(out=both[:, S + BANK * h : S + BANK * h + BANK], in_=rate_scores(s, h)[:])
+                nc.scalar.activation(out=both[:, halves[h]], in_=bank[:], func=COPY, scale=-1.0)
 
-        def first_sink():
-            sink = sinks[0]
+        def rate_scores(s):
             for h in range(2):
-                cols = slice(BANK * h, BANK * h + BANK)
-                nc.vector.tensor_tensor(sink[:, cols], source_scores(0, h)[:], sink[:, cols], SUB)
-            for h in range(2):
-                cols = slice(BANK * h, BANK * h + BANK)
-                nc.vector.tensor_tensor(sink[:, cols], rate_scores(0, h)[:], sink[:, cols], MULT)
-            nc.vector.tensor_tensor(page_b[0][:].indirect(idx3[:]), sink[:], wg2s[:], MULT)
+                bank = next_bank()
+                nc.tensor.matmul_mx(
+                    out=bank[:], lhsT=w2w[:, 2 * P * s : 2 * P * s + 2 * P].bitcast(FP4X4),
+                    lhsT_scale=w2s[:, P * s : P * s + P],
+                    rhs=vw[h][:].bitcast(FP8X4), rhs_scale=vs[h][:], start=True, stop=True,
+                )
+                nc.scalar.copy(out=staged[s][:, S + BANK * h : S + BANK * h + BANK], in_=bank[:])
 
         def add_transposed(bank, rows, opens):
             for g in range(4):
@@ -156,54 +126,50 @@ def tile_list_cave_wall_growth_kernel(
 
         def subtract_eq(s):
             turned = []
-            for h in range(2):
-                cols = slice(BANK * h, BANK * h + BANK)
-                bank = psum.tile([P, BANK], F32, name="brief")
+            for cols in halves:
+                bank = next_bank()
                 add_transposed(bank, sinks[s][:, cols], True)
                 add_transposed(bank, staged[s][:, cols], False)
                 gap_t = two.tile([P, BANK], F32, name="gap_t")
                 nc.scalar.copy(out=gap_t[:], in_=bank[:])
                 turned.append(gap_t)
             for h in range(2):
-                cols = slice(BANK * h, BANK * h + BANK)
-                bank = psum6.tile([P, BANK], F32, name="held")
+                bank = next_bank()
                 for g in range(4):
                     nc.tensor.transpose(bank[:, P * g : P * g + P], turned[h][:, P * g : P * g + P], ident[:])
-                nc.scalar.activation(out=staged[s][:, cols], in_=bank[:], func=COPY, scale=-1.0)
+                nc.scalar.activation(out=sinks[s][:, halves[h]], in_=bank[:], func=COPY, scale=-1.0)
+
+        def weigh_both(s):
+            nc.gpsimd.tensor_tensor(staged[s][:], staged[s][:], wg[:], MULT)
+
+        def weigh_source(s, tile, pieces):
+            sources[s] = tile
+            for cols in pieces:
+                nc.gpsimd.tensor_tensor(tile[:, cols], staged[s][:, cols], wg[:, cols], MULT)
+
+        def weigh_rate(s):
+            nc.gpsimd.tensor_tensor(staged[s][:, S:], staged[s][:, S:], wg[:, S:], MULT)
 
         def weigh_sink(s):
-            sink = sinks[s]
-            h1s, rates = staged[s][:, :S], staged[s][:, S:]
-            halves = [slice(BANK * h, BANK * h + BANK) for h in range(2)]
-            for cols in halves:
-                nc.gpsimd.tensor_tensor(sink[:, cols], h1s[:, cols], rates[:, cols], MULT)
-            for cols in halves:
-                nc.gpsimd.tensor_tensor(sink[:, cols], sink[:, cols], wg2s[:, cols], MULT)
+            nc.gpsimd.tensor_tensor(sinks[s][:], sinks[s][:], staged[s][:, S:], MULT)
 
-        sources = {}
-
-        def weigh_source(s, h):
-            if h == 0:
-                sources[s] = keep.tile([P, S], F32, name="source")
-            cols = slice(BANK * h, BANK * h + BANK)
-            nc.vector.tensor_tensor(sources[s][:, cols], h1_banks[s, h][:], wg1s[:, cols], MULT)
-
-        def scatter_source(s):
-            nc.vector.tensor_copy(page_a[:].indirect(idx2[:]), sources[s][:])
+        def scatter_source(s, pieces):
+            for cols in pieces:
+                nc.vector.tensor_copy(
+                    page_a[s % 2][:].indirect(idx2[:, cols.start // 16 : cols.stop // 16]), sources[s][:, cols]
+                )
 
         def scatter_sink(s):
             nc.vector.tensor_copy(page_b[s % 2][:].indirect(idx3[:]), sinks[s][:])
 
         def exponentiate(s, width):
-            tile = products[s]
             for c0 in range(0, T2, width):
-                nc.scalar.activation(out=tile[:, c0 : c0 + width], in_=page_b[s % 2][:, c0 : c0 + width], func=EXP)
+                nc.scalar.activation(out=growth[s % 2][:, c0 : c0 + width], in_=page_b[s % 2][:, c0 : c0 + width], func=EXP)
 
         def grow(s, engine, width):
-            tile = products[s]
             for c0 in range(0, T2, width):
                 cols = slice(c0, c0 + width)
-                engine.tensor_tensor(tile[:, cols], tile[:, cols], page_a[:, cols], MULT)
+                engine.tensor_tensor(growth[s % 2][:, cols], growth[s % 2][:, cols], page_a[s % 2][:, cols], MULT)
 
         walls = {}
 
@@ -223,7 +189,7 @@ def tile_list_cave_wall_growth_kernel(
             sl = s % 4
             if sl == 0:
                 z_t[s // 4, c] = keep.tile([P, 4 * BANK], BF16, name=Z_T_TAGS[s // 4][c])
-            add_transposed(bank, products[s][:, BANK * c : BANK * c + BANK], False)
+            add_transposed(bank, growth[s % 2][:, BANK * c : BANK * c + BANK], False)
             nc.scalar.copy(
                 out=z_t[s // 4, c][:].rearrange("m (u g q e) -> m u g q e", u=2, g=4, e=2)[:, :, :, 32 * sl : 32 * sl + 32, :],
                 in_=bank[:].rearrange("m (g q u e) -> m u g q e", g=4, u=2, e=2),
@@ -232,7 +198,7 @@ def tile_list_cave_wall_growth_kernel(
         def regroup_z(b, c, grouped):
             words = z_t[b, c][:].bitcast(F32)
             for h, copy in enumerate((nc.scalar.copy, nc.vector.tensor_copy if b == PASSES - 1 else nc.scalar.copy)):
-                bank = psum.tile([P, BANK], F32, name="brief")
+                bank = next_bank()
                 for u in range(2):
                     for g2 in range(2):
                         w0 = P * (4 * u + 2 * h + g2)
@@ -259,20 +225,32 @@ def tile_list_cave_wall_growth_kernel(
         w3c = keep.tile([P, PASSES * N], U32, name="w3c", align_bytes=64)
         w3s = keep.tile([P, PASSES * N], U8, name="w3s", align_bytes=64)
 
-        def quantize_w3():
-            grouped = keep.tile([P, 4 * PASSES * N], BF16, name="w3bf", align_bytes=64)
+        w3bf = keep.tile([P, 4 * PASSES * N], BF16, name="w3bf", align_bytes=64)
+        w3raw = []
+
+        def load_w3():
             for b in range(PASSES):
                 raw = keep.tile([P, 4, N], F32, name="w3raw%d" % b)
                 nc.sync.dma_start(out=raw[:], in_=w3[512 * b : 512 * b + 512, :].rearrange("(p t) n -> p t n", t=4))
-                interleave(grouped[:, 4 * N * b : 4 * N * b + 4 * N], raw[:])
-            for lo, hi in ((0, 512), (512, PASSES * N)):
-                nc.vector.quantize_mx(
-                    out=w3c[:, lo:hi].bitcast(FP8X4), scales=w3s[:, lo:hi], in_=grouped[:, 4 * lo : 4 * hi]
-                )
+                w3raw.append(raw)
+
+        def quantize_w3(lo, hi):
+            for b in range(PASSES):
+                first, stop = max(lo, N * b), min(hi, N * b + N)
+                if first < stop:
+                    interleave(w3bf[:, 4 * first : 4 * stop], w3raw[b][:, :, first - N * b : stop - N * b])
+            nc.vector.quantize_mx(out=w3c[:, lo:hi].bitcast(FP8X4), scales=w3s[:, lo:hi], in_=w3bf[:, 4 * lo : 4 * hi])
+
+        results = {}
 
         def project(c):
+            if c < 2:
+                results[c] = keep.tile([P, N // P * BANK], F32, name=("w3raw1", "wg")[c])[:]
+            elif c == 2:
+                pair = keep.tile([P, 2 * N // P * BANK], F32, name="tabw")
+                results[2], results[3] = pair[:, : N // P * BANK], pair[:, N // P * BANK :]
             for nb in range(N // P):
-                bank = psum6.tile([P, BANK], F32, name="held")
+                bank = next_bank()
                 for b in range(PASSES):
                     cols = slice(N * b + P * nb, N * b + P * nb + P)
                     nc.tensor.matmul_mx(
@@ -280,64 +258,99 @@ def tile_list_cave_wall_growth_kernel(
                         rhs=zq[b, c][0].bitcast(FP8X4), rhs_scale=zq[b, c][1],
                         start=(b == 0), stop=(b == PASSES - 1),
                     )
-                result = three.tile([P, BANK], F32, name="result%d" % nb)
+                result = results[c][:, BANK * nb : BANK * nb + BANK]
                 copy = nc.vector.tensor_copy if nb == 1 else nc.scalar.copy
-                copy(out=result[:], in_=bank[:])
-                nc.sync.dma_start(out=out[P * nb : P * nb + P, BANK * c : BANK * c + BANK], in_=result[:])
+                copy(out=result, in_=bank[:])
+                nc.sync.dma_start(out=out[P * nb : P * nb + P, BANK * c : BANK * c + BANK], in_=result)
 
+        whole = [slice(0, S)]
+        last = SLICES - 1
+
+        nc.vector.memset(tabs[:].bitcast(I32), 0)
+        nc.vector.memset(w2s[:].bitcast(I32), 0)
+        nc.sync.dma_start(idx[:], offs)
+        nc.sync.dma_start(idx2[:], offs2)
+        nc.sync.dma_start(idx3[:], offs3)
+        table = tab_words[0].rearrange("p t i -> p (t i)").bitcast(I32)
+        w1_chunk(*W1_CHUNKS[0], parts=2)
+        for c0 in range(0, T, T // 4):
+            nc.sync.dma_start(out=tabw[:].bitcast(I32)[:, c0 : c0 + T // 4], in_=table[:, c0 : c0 + T // 4])
+        load_scale_rows(nc.sync, tabs, tab_scales[0])
+        for page in page_a + page_b:
+            nc.vector.memset(page[:], 0.0)
+        make_identity(nc, ident[:])
+        nc.sync.dma_start(out=wg[:, :S], in_=wg1)
+        nc.gpsimd.tensor_scalar(wg[:, :S], wg[:, :S], -1.0, 0.0, MULT, ADD)
+        for h in range(2):
+            nc.vector.tensor_copy(vw[h][:], tabw[:].indirect(idx[:, 32 * h : 32 * h + 32]))
+            nc.vector.tensor_copy(vs[h][:], tabs[:].indirect(idx[:, 32 * h : 32 * h + 32]))
+        source_scores(0)
+        early = two.tile([P, 2 * S], F32, name="grouped", align_bytes=64)
+        weigh_source(0, early[:, :S], halves)
+        scatter_source(0, halves)
+        source_scores(1)
+        weigh_source(1, early[:, S:], whole)
+        w1_chunk(*W1_CHUNKS[1])
         nc.sync.dma_start(out=w2w[:].bitcast(I32), in_=w2_words[0].bitcast(I32))
         load_scale_rows(nc.gpsimd, w2s, w2_scales[0])
-        load_eq(0)
-        w1_chunk(*W1_CHUNKS[1])
-        nc.sync.dma_start(out=wg2s[:], in_=wg2)
-        first_sink()
-        load_eq(1)
-        nc.sync.dma_start(out=wg1s[:], in_=wg1)
-        scores(1)
-        subtract_eq(1)
-        w1_chunk(*W1_CHUNKS[2])
+        nc.sync.dma_start(out=wg[:, S:], in_=wg2)
+        scatter_source(1, whole)
+        for s in range(2):
+            load_eq(s)
+            rate_scores(s)
+            weigh_rate(s)
+            subtract_eq(s)
+            weigh_sink(s)
+        scatter_sink(0)
         load_eq(2)
-        for h in range(2):
-            weigh_source(0, h)
-        scatter_source(0)
-        weigh_sink(1)
-        products[0] = staged[1]
-        exponentiate(0, S)
-        scores(2)
-        subtract_eq(2)
-        last = SLICES - 1
+        w1_chunk(*W1_CHUNKS[2])
         first_pass = {}
-        for s in range(1, SLICES):
-            for h in range(2):
-                weigh_source(s, h)
+
+        def prepare(s):
+            source_scores(s)
+            rate_scores(s)
+            subtract_eq(s)
+
+        def form_z(s):
+            for c in range(CHUNKS):
+                add_product(s, c, open_with_wall(s, c, next_bank()))
+
+        prepare(2)
+        weigh_both(2)
+        weigh_sink(2)
+        load_wall(0)
+        exponentiate(0, S)
+        scatter_sink(1)
+        grow(0, nc.gpsimd, T2)
+        load_eq(3)
+        prepare(3)
+        weigh_both(3)
+        form_z(0)
+        load_wall(1)
+        exponentiate(1, S)
+        load_w3()
+        for s in range(2, SLICES):
+            scatter_sink(s)
+            grow(s - 1, nc.gpsimd, T2)
             if s + 2 <= last:
                 load_eq(s + 2)
-            scatter_sink(s)
-            load_wall(s - 1)
-            grow(s - 1, nc.gpsimd, BANK)
-            scatter_source(s)
-            for c in range(CHUNKS):
-                add_product(s - 1, c, open_with_wall(s - 1, c, psum.tile([P, BANK], F32, name="brief")))
-            if s < last:
+                prepare(s + 2)
+            if s + 1 <= last:
                 weigh_sink(s + 1)
-                products[s] = staged[s + 1]
-                exponentiate(s, S)
             if s + 2 <= last:
-                scores(s + 2)
-                subtract_eq(s + 2)
-            if s == 2:
-                quantize_w3()
-            for pair, at in (((0, 1), 4), ((2, 3), 5)):
-                if s == at:
-                    first_pass[pair] = regroup_chunks(0, pair)
-            for pair, at in (((0, 1), 6), ((2, 3), 6)):
-                if s == at:
-                    codes = three.tile([P, 2 * BANK], U32, name="sink", align_bytes=64)
-                    quantize_z(0, pair, first_pass[pair], codes[:])
-        load_wall(last)
-        last_banks = [open_with_wall(last, c, psum6.tile([P, BANK], F32, name="held")) for c in range(CHUNKS)]
-        products[last] = three.tile([P, T2], F32, name="both")
-        exponentiate(last, BANK)
+                weigh_both(s + 2)
+            form_z(s - 1)
+            load_wall(s)
+            exponentiate(s, S if s < last else BANK)
+            scatter_source(s, whole)
+            if s in (2, 3):
+                quantize_w3(*((0, 512), (512, PASSES * N))[s - 2])
+            if s in (5, 6):
+                pair = (2 * s - 10, 2 * s - 9)
+                grouped = regroup_chunks(0, pair)
+                codes = three.tile([P, 2 * BANK], U32, name="both", align_bytes=64)
+                quantize_z(0, pair, grouped, codes[:])
+        last_banks = [open_with_wall(last, c, next_bank()) for c in range(CHUNKS)]
         grow(last, nc.vector, BANK)
         for step in range(CHUNKS + 2):
             if step < CHUNKS:

@@ -24,8 +24,9 @@ BANK = 512
 SLICES = H // P
 PASSES = H // 512
 CHUNKS = T2 // BANK
+W3_SLICE = 3
 W1_CHUNKS = ((0, 256), (256, 512), (512, 1024))
-Z_T_TAGS = (("z_t0", "z_t1", "z_t2", "z_t3"), ("w1raw0", "w1raw256", "w1raw512", "w3raw0"))
+Z_T_TAGS = (("z_t0", "z_t1", "z_t2", "z_t3"), ("w1raw0", "w1raw256", "w1raw512", "w1bf512"))
 
 
 def tile_list_cave_wall_growth_kernel(
@@ -36,7 +37,11 @@ def tile_list_cave_wall_growth_kernel(
         keep = ctx.enter_context(tc.tile_pool(name="keep", bufs=1))
         two = ctx.enter_context(tc.tile_pool(name="two", bufs=2))
         three = ctx.enter_context(tc.tile_pool(name="three", bufs=3))
-        psum = ctx.enter_context(tc.psum_pool(name="psum", bufs=8))
+        psum = ctx.enter_context(tc.psum_pool(name="psum", bufs=4))
+        held = ctx.enter_context(tc.psum_pool(name="held", bufs=2))
+
+        def spare_bank(i):
+            return held.tile([P, BANK], F32, name=("wide", "gap")[i % 4 // 2])
 
         def next_bank():
             return psum.tile([P, BANK], F32, name="bank")
@@ -44,14 +49,14 @@ def tile_list_cave_wall_growth_kernel(
         idx = keep.tile([P, S // 16], U16, name="idx")
         idx2 = keep.tile([P, S // 16], U16, name="idx2")
         idx3 = keep.tile([P, S // 16], U16, name="idx3")
-        tabw = keep.tile([P, T], U32, name="tabw")
+        tabw = keep.tile([P, T], U32, name="tabw", align_bytes=64)
         tabs = keep.tile([P, T], U8, name="tabs")
         w2w = keep.tile([P, 2 * H], U8, name="w2w", align_bytes=64)
         w2s = keep.tile([P, H], U8, name="w2s", align_bytes=64)
         wg = keep.tile([P, 2 * S], F32, name="wg")
         ident = keep.tile([P, P], F32, name="ident")
-        page_a = [keep.tile([P, T2], F32, name="page_a%d" % i) for i in range(2)]
-        growth = [keep.tile([P, T2], F32, name="growth%d" % i) for i in range(2)]
+        page_a = keep.tile([P, T2], F32, name="page_a")
+        growth = keep.tile([P, T2], F32, name="growth")
         page_b = [keep.tile([P, T2], F32, name="page_b%d" % i) for i in range(2)]
 
         def load_scale_rows(queue, plane, rows):
@@ -68,20 +73,32 @@ def tile_list_cave_wall_growth_kernel(
 
         w1q = []
 
-        def w1_chunk(lo, hi, parts=1):
-            width = hi - lo
-            raw = keep.tile([P, 4, width], F32, name="w1raw%d" % lo)
+        w1s = keep.tile([P, H], U8, name="w1s", align_bytes=64)
+
+        def w1_columns(lo, hi, parts):
+            raw = keep.tile([P, 4, hi - lo], F32, name="w1raw%d" % lo, align_bytes=64)
             rows = w1[:, lo:hi].rearrange("(p t) c -> p t c", t=4)
             for part in range(parts):
                 planes = slice(4 // parts * part, 4 // parts * (part + 1))
                 nc.sync.dma_start(out=raw[:, planes, :], in_=rows[:, planes, :])
-            grouped = keep.tile([P, 4 * width], BF16, name="w1bf%d" % lo, align_bytes=64)
+            grouped = keep.tile([P, 4 * (hi - lo)], BF16, name="w1bf%d" % lo, align_bytes=64)
             interleave(grouped[:], raw[:])
-            codes = keep.tile([P, width], U32, name="w1c%d" % lo, align_bytes=64)
-            scales = keep.tile([P, width], U8, name="w1s%d" % lo, align_bytes=64)
-            nc.vector.quantize_mx(out=codes[:].bitcast(FP8X4), scales=scales[:], in_=grouped[:])
-            for c0 in range(0, width, P):
-                w1q.append((codes[:, c0 : c0 + P].bitcast(FP8X4), scales[:, c0 : c0 + P]))
+            return grouped
+
+        def quantize_w1(lo, hi, grouped, codes):
+            nc.vector.quantize_mx(out=codes.bitcast(FP8X4), scales=w1s[:, lo:hi], in_=grouped[:])
+            for c0 in range(0, hi - lo, P):
+                w1q.append((codes[:, c0 : c0 + P].bitcast(FP8X4), w1s[:, lo + c0 : lo + c0 + P]))
+
+        def w1_first():
+            lo, hi = W1_CHUNKS[0]
+            codes = keep.tile([P, hi - lo], U32, name="w1c", align_bytes=64)
+            quantize_w1(lo, hi, w1_columns(lo, hi, 2), codes[:])
+
+        def w1_later(s, grouped):
+            lo, hi = W1_CHUNKS[s + 1]
+            codes = keep.tile([P, hi - lo], U32, name="early%d" % s, align_bytes=64)
+            quantize_w1(lo, hi, grouped, codes[:])
 
         vw = [keep.tile([P, BANK], U32, name="vw%d" % h, align_bytes=64) for h in range(2)]
         vs = [keep.tile([P, BANK], U8, name="vs%d" % h, align_bytes=64) for h in range(2)]
@@ -95,27 +112,28 @@ def tile_list_cave_wall_growth_kernel(
             nc.sync.dma_start(out=sink[:], in_=eq[P * s : P * s + P, :])
             sinks[s] = sink
 
-        def source_scores(s):
-            both = three.tile([P, 2 * S], F32, name="both", align_bytes=64)
-            staged[s] = both
-            sources[s] = both[:, :S]
-            for h in range(2):
-                bank = next_bank()
-                nc.tensor.matmul_mx(
-                    out=bank[:], lhsT=w1q[s][0], lhsT_scale=w1q[s][1],
-                    rhs=vw[h][:].bitcast(FP8X4), rhs_scale=vs[h][:], start=True, stop=True,
-                )
-                nc.scalar.activation(out=both[:, halves[h]], in_=bank[:], func=COPY, scale=-1.0)
+        def stage(s):
+            staged[s] = two.tile([P, 2 * S], F32, name="both", align_bytes=64)
+            sources[s] = staged[s][:, :S]
 
-        def rate_scores(s):
-            for h in range(2):
-                bank = next_bank()
-                nc.tensor.matmul_mx(
-                    out=bank[:], lhsT=w2w[:, 2 * P * s : 2 * P * s + 2 * P].bitcast(FP4X4),
-                    lhsT_scale=w2s[:, P * s : P * s + P],
-                    rhs=vw[h][:].bitcast(FP8X4), rhs_scale=vs[h][:], start=True, stop=True,
-                )
-                nc.scalar.copy(out=staged[s][:, S + BANK * h : S + BANK * h + BANK], in_=bank[:])
+        def source_scores(s, h, bank):
+            nc.tensor.matmul_mx(
+                out=bank[:], lhsT=w1q[s][0], lhsT_scale=w1q[s][1],
+                rhs=vw[h][:].bitcast(FP8X4), rhs_scale=vs[h][:], start=True, stop=True,
+            )
+            return bank
+
+        def stage_source(s, h, bank):
+            nc.scalar.activation(out=staged[s][:, halves[h]], in_=bank[:], func=COPY, scale=-1.0)
+
+        def rate_scores(s, h):
+            bank = next_bank()
+            nc.tensor.matmul_mx(
+                out=bank[:], lhsT=w2w[:, 2 * P * s : 2 * P * s + 2 * P].bitcast(FP4X4),
+                lhsT_scale=w2s[:, P * s : P * s + P],
+                rhs=vw[h][:].bitcast(FP8X4), rhs_scale=vs[h][:], start=True, stop=True,
+            )
+            nc.scalar.copy(out=staged[s][:, S + BANK * h : S + BANK * h + BANK], in_=bank[:])
 
         def add_transposed(bank, rows, opens):
             for g in range(4):
@@ -124,39 +142,37 @@ def tile_list_cave_wall_growth_kernel(
                     start=(opens and g == 0), stop=(not opens and g == 3), is_transpose=True,
                 )
 
-        def subtract_eq(s):
+        gaps = {}
+
+        def rates_and_gaps(s):
             turned = []
-            for cols in halves:
+            for h in range(2):
+                rate_scores(s, h)
                 bank = next_bank()
-                add_transposed(bank, sinks[s][:, cols], True)
-                add_transposed(bank, staged[s][:, cols], False)
+                add_transposed(bank, sinks[s][:, halves[h]], True)
+                add_transposed(bank, staged[s][:, halves[h]], False)
                 gap_t = two.tile([P, BANK], F32, name="gap_t")
                 nc.scalar.copy(out=gap_t[:], in_=bank[:])
                 turned.append(gap_t)
             for h in range(2):
-                bank = next_bank()
+                gaps[s, h] = held.tile([P, BANK], F32, name="gap")
                 for g in range(4):
-                    nc.tensor.transpose(bank[:, P * g : P * g + P], turned[h][:, P * g : P * g + P], ident[:])
-                nc.scalar.activation(out=sinks[s][:, halves[h]], in_=bank[:], func=COPY, scale=-1.0)
+                    nc.tensor.transpose(gaps[s, h][:, P * g : P * g + P], turned[h][:, P * g : P * g + P], ident[:])
 
-        def weigh_both(s):
-            nc.gpsimd.tensor_tensor(staged[s][:], staged[s][:], wg[:], MULT)
-
-        def weigh_source(s, tile, pieces):
-            sources[s] = tile
-            for cols in pieces:
-                nc.gpsimd.tensor_tensor(tile[:, cols], staged[s][:, cols], wg[:, cols], MULT)
-
-        def weigh_rate(s):
-            nc.gpsimd.tensor_tensor(staged[s][:, S:], staged[s][:, S:], wg[:, S:], MULT)
+        def weigh(s, out, cols):
+            nc.gpsimd.tensor_tensor(out, staged[s][:, cols], wg[:, cols], MULT)
 
         def weigh_sink(s):
-            nc.gpsimd.tensor_tensor(sinks[s][:], sinks[s][:], staged[s][:, S:], MULT)
+            for h in range(2):
+                nc.vector.scalar_tensor_tensor(
+                    sinks[s][:, halves[h]], gaps[s, h][:], -1.0,
+                    staged[s][:, S + BANK * h : S + BANK * h + BANK], MULT, MULT,
+                )
 
         def scatter_source(s, pieces):
             for cols in pieces:
                 nc.vector.tensor_copy(
-                    page_a[s % 2][:].indirect(idx2[:, cols.start // 16 : cols.stop // 16]), sources[s][:, cols]
+                    page_a[:].indirect(idx2[:, cols.start // 16 : cols.stop // 16]), sources[s][:, cols]
                 )
 
         def scatter_sink(s):
@@ -164,19 +180,21 @@ def tile_list_cave_wall_growth_kernel(
 
         def exponentiate(s, width):
             for c0 in range(0, T2, width):
-                nc.scalar.activation(out=growth[s % 2][:, c0 : c0 + width], in_=page_b[s % 2][:, c0 : c0 + width], func=EXP)
+                nc.scalar.activation(out=growth[:, c0 : c0 + width], in_=page_b[s % 2][:, c0 : c0 + width], func=EXP)
 
         def grow(s, engine, width):
             for c0 in range(0, T2, width):
                 cols = slice(c0, c0 + width)
-                engine.tensor_tensor(growth[s % 2][:, cols], growth[s % 2][:, cols], page_a[s % 2][:, cols], MULT)
+                engine.tensor_tensor(growth[:, cols], growth[:, cols], page_a[:, cols], MULT)
 
         walls = {}
 
         def load_wall(s):
-            rows = two.tile([P, T2], F32, name="wall_rows")
-            nc.sync.dma_start(out=rows[:], in_=wall[P * s : P * s + P, :])
-            walls[s] = rows
+            if s == W3_SLICE:
+                walls[s] = keep.tile([P, T2], F32, name="w3bf", align_bytes=64)
+            else:
+                walls[s] = two.tile([P, T2], F32, name="wall_rows")
+            nc.sync.dma_start(out=walls[s][:], in_=wall[P * s : P * s + P, :])
 
         z_t = {}
         zq = {}
@@ -188,8 +206,8 @@ def tile_list_cave_wall_growth_kernel(
         def add_product(s, c, bank):
             sl = s % 4
             if sl == 0:
-                z_t[s // 4, c] = keep.tile([P, 4 * BANK], BF16, name=Z_T_TAGS[s // 4][c])
-            add_transposed(bank, growth[s % 2][:, BANK * c : BANK * c + BANK], False)
+                z_t[s // 4, c] = keep.tile([P, 4 * BANK], BF16, name=Z_T_TAGS[s // 4][c], align_bytes=64)
+            add_transposed(bank, growth[:, BANK * c : BANK * c + BANK], False)
             nc.scalar.copy(
                 out=z_t[s // 4, c][:].rearrange("m (u g q e) -> m u g q e", u=2, g=4, e=2)[:, :, :, 32 * sl : 32 * sl + 32, :],
                 in_=bank[:].rearrange("m (g q u e) -> m u g q e", g=4, u=2, e=2),
@@ -197,7 +215,7 @@ def tile_list_cave_wall_growth_kernel(
 
         def regroup_z(b, c, grouped):
             words = z_t[b, c][:].bitcast(F32)
-            for h, copy in enumerate((nc.scalar.copy, nc.vector.tensor_copy if b == PASSES - 1 else nc.scalar.copy)):
+            for h, copy in enumerate((nc.scalar.copy, nc.vector.tensor_copy if b == PASSES - 1 and c % 2 == 0 else nc.scalar.copy)):
                 bank = next_bank()
                 for u in range(2):
                     for g2 in range(2):
@@ -215,148 +233,178 @@ def tile_list_cave_wall_growth_kernel(
                 regroup_z(b, c, grouped[:, 4 * BANK * i : 4 * BANK * (i + 1)])
             return grouped
 
-        def quantize_z(b, chunks, grouped, codes):
+        def quantize_z(b, chunks, grouped, codes, pool, tag):
             n = len(chunks)
-            scales = keep.tile([P, n * BANK], U8, name="zs%d_%d" % (b, chunks[0]), align_bytes=64)
+            scales = pool.tile([P, n * BANK], U8, name=tag, align_bytes=64)
             nc.vector.quantize_mx(out=codes.bitcast(FP8X4), scales=scales[:], in_=grouped[:, : 4 * BANK * n])
             for i, c in enumerate(chunks):
                 zq[b, c] = (codes[:, BANK * i : BANK * (i + 1)], scales[:, BANK * i : BANK * (i + 1)])
 
-        w3c = keep.tile([P, PASSES * N], U32, name="w3c", align_bytes=64)
-        w3s = keep.tile([P, PASSES * N], U8, name="w3s", align_bytes=64)
 
-        w3bf = keep.tile([P, 4 * PASSES * N], BF16, name="w3bf", align_bytes=64)
+        w3bf = []
         w3raw = []
 
         def load_w3():
+            both_passes = keep.tile([P, PASSES * 4 * N], F32, name="w3raw", align_bytes=64)
             for b in range(PASSES):
-                raw = keep.tile([P, 4, N], F32, name="w3raw%d" % b)
-                nc.sync.dma_start(out=raw[:], in_=w3[512 * b : 512 * b + 512, :].rearrange("(p t) n -> p t n", t=4))
+                raw = both_passes[:, 4 * N * b : 4 * N * b + 4 * N].rearrange("p (t n) -> p t n", t=4)
+                nc.sync.dma_start(out=raw, in_=w3[512 * b : 512 * b + 512, :].rearrange("(p t) n -> p t n", t=4))
                 w3raw.append(raw)
 
-        def quantize_w3(lo, hi):
+        def interleave_w3():
+            w3bf.append(keep.tile([P, 4 * PASSES * N], BF16, name="w3bf", align_bytes=64))
             for b in range(PASSES):
-                first, stop = max(lo, N * b), min(hi, N * b + N)
-                if first < stop:
-                    interleave(w3bf[:, 4 * first : 4 * stop], w3raw[b][:, :, first - N * b : stop - N * b])
-            nc.vector.quantize_mx(out=w3c[:, lo:hi].bitcast(FP8X4), scales=w3s[:, lo:hi], in_=w3bf[:, 4 * lo : 4 * hi])
+                interleave(w3bf[0][:, 4 * N * b : 4 * N * b + 4 * N], w3raw[b])
+
+        w3q = []
+
+        def quantize_w3(codes):
+            w3s = three.tile([P, PASSES * N], U8, name="sink", align_bytes=64)
+            w3q.extend((codes, w3s))
+            for lo, hi in ((0, 512), (512, PASSES * N)):
+                nc.vector.quantize_mx(
+                    out=codes[:, lo:hi].bitcast(FP8X4), scales=w3s[:, lo:hi], in_=w3bf[0][:, 4 * lo : 4 * hi]
+                )
 
         results = {}
 
+        def summed_early(c, nb):
+            return nb == 1 or (nb == 0 and c % 2 == 0)
+
+        def multiply(bank, b, c, nb, start, stop):
+            cols = slice(N * b + P * nb, N * b + P * nb + P)
+            nc.tensor.matmul_mx(
+                out=bank[:], lhsT=w3q[0][:, cols].bitcast(FP8X4), lhsT_scale=w3q[1][:, cols],
+                rhs=zq[b, c][0].bitcast(FP8X4), rhs_scale=zq[b, c][1], start=start, stop=stop,
+            )
+
+        def project_early(chunks, tag):
+            rows = keep.tile([P, len(chunks) * N // P * BANK], F32, name=tag, align_bytes=64)
+            for i, c in enumerate(chunks):
+                for nb in range(N // P):
+                    c0 = BANK * (N // P * i + nb)
+                    results[c, nb] = rows[:, c0 : c0 + BANK]
+                    if summed_early(c, nb):
+                        bank = next_bank()
+                        multiply(bank, 0, c, nb, True, True)
+                        nc.scalar.copy(out=results[c, nb], in_=bank[:])
+
         def project(c):
-            if c < 2:
-                results[c] = keep.tile([P, N // P * BANK], F32, name=("w3raw1", "wg")[c])[:]
-            elif c == 2:
-                pair = keep.tile([P, 2 * N // P * BANK], F32, name="tabw")
-                results[2], results[3] = pair[:, : N // P * BANK], pair[:, N // P * BANK :]
             for nb in range(N // P):
-                bank = next_bank()
-                for b in range(PASSES):
-                    cols = slice(N * b + P * nb, N * b + P * nb + P)
-                    nc.tensor.matmul_mx(
-                        out=bank[:], lhsT=w3c[:, cols].bitcast(FP8X4), lhsT_scale=w3s[:, cols],
-                        rhs=zq[b, c][0].bitcast(FP8X4), rhs_scale=zq[b, c][1],
-                        start=(b == 0), stop=(b == PASSES - 1),
-                    )
-                result = results[c][:, BANK * nb : BANK * nb + BANK]
-                copy = nc.vector.tensor_copy if nb == 1 else nc.scalar.copy
-                copy(out=result, in_=bank[:])
-                nc.sync.dma_start(out=out[P * nb : P * nb + P, BANK * c : BANK * c + BANK], in_=result)
+                bank = spare_bank(N // P * c + nb)
+                if summed_early(c, nb):
+                    multiply(bank, 1, c, nb, True, True)
+                    nc.vector.tensor_tensor(results[c, nb], bank[:], results[c, nb], ADD)
+                else:
+                    for b in range(PASSES):
+                        multiply(bank, b, c, nb, b == 0, b == PASSES - 1)
+                    nc.scalar.copy(out=results[c, nb], in_=bank[:])
+                nc.sync.dma_start(out=out[P * nb : P * nb + P, BANK * c : BANK * c + BANK], in_=results[c, nb])
 
         whole = [slice(0, S)]
+        first_pass = {}
         last = SLICES - 1
 
         nc.vector.memset(tabs[:].bitcast(I32), 0)
-        nc.vector.memset(w2s[:].bitcast(I32), 0)
+        nc.gpsimd.memset(w2s[:].bitcast(I32), 0)
+        load_scale_rows(nc.gpsimd, w2s, w2_scales[0])
         nc.sync.dma_start(idx[:], offs)
         nc.sync.dma_start(idx2[:], offs2)
         nc.sync.dma_start(idx3[:], offs3)
         table = tab_words[0].rearrange("p t i -> p (t i)").bitcast(I32)
-        w1_chunk(*W1_CHUNKS[0], parts=2)
+        w1_first()
         for c0 in range(0, T, T // 4):
             nc.sync.dma_start(out=tabw[:].bitcast(I32)[:, c0 : c0 + T // 4], in_=table[:, c0 : c0 + T // 4])
         load_scale_rows(nc.sync, tabs, tab_scales[0])
-        for page in page_a + page_b:
-            nc.vector.memset(page[:], 0.0)
+        nc.vector.memset(page_a[:], 0.0)
         make_identity(nc, ident[:])
-        nc.sync.dma_start(out=wg[:, :S], in_=wg1)
-        nc.gpsimd.tensor_scalar(wg[:, :S], wg[:, :S], -1.0, 0.0, MULT, ADD)
+        wg1s = keep.tile([P, S], F32, name="early1", align_bytes=64)
+        nc.sync.dma_start(out=wg1s[:], in_=wg1)
+        nc.gpsimd.tensor_scalar(wg[:, :S], wg1s[:], -1.0, 0.0, MULT, ADD)
+        for page in page_b:
+            nc.gpsimd.memset(page[:], 0.0)
         for h in range(2):
             nc.vector.tensor_copy(vw[h][:], tabw[:].indirect(idx[:, 32 * h : 32 * h + 32]))
             nc.vector.tensor_copy(vs[h][:], tabs[:].indirect(idx[:, 32 * h : 32 * h + 32]))
-        source_scores(0)
-        early = two.tile([P, 2 * S], F32, name="grouped", align_bytes=64)
-        weigh_source(0, early[:, :S], halves)
+        early = keep.tile([P, S], F32, name="early0", align_bytes=64)
+        stage(0)
+        sources[0] = early[:]
+        bank = source_scores(0, 0, next_bank())
+        nc.vector.tensor_tensor(early[:, halves[0]], bank[:], wg1s[:, halves[0]], MULT)
+        stage_source(0, 0, bank)
+        stage_source(0, 1, source_scores(0, 1, next_bank()))
+        weigh(0, early[:, halves[1]], halves[1])
         scatter_source(0, halves)
-        source_scores(1)
-        weigh_source(1, early[:, S:], whole)
-        w1_chunk(*W1_CHUNKS[1])
+        w1_later(0, w1_columns(*W1_CHUNKS[1], 1))
         nc.sync.dma_start(out=w2w[:].bitcast(I32), in_=w2_words[0].bitcast(I32))
-        load_scale_rows(nc.gpsimd, w2s, w2_scales[0])
         nc.sync.dma_start(out=wg[:, S:], in_=wg2)
-        scatter_source(1, whole)
-        for s in range(2):
-            load_eq(s)
-            rate_scores(s)
-            weigh_rate(s)
-            subtract_eq(s)
-            weigh_sink(s)
-        scatter_sink(0)
-        load_eq(2)
-        w1_chunk(*W1_CHUNKS[2])
-        first_pass = {}
+        load_eq(0)
+        load_eq(1)
+        rates_and_gaps(0)
+        for h in range(2):
+            cols = slice(S + BANK * h, S + BANK * h + BANK)
+            weigh(0, staged[0][:, cols], cols)
 
         def prepare(s):
-            source_scores(s)
-            rate_scores(s)
-            subtract_eq(s)
+            stage(s)
+            for h in range(2):
+                stage_source(s, h, source_scores(s, h, next_bank()))
+            rates_and_gaps(s)
+            if s == 1:
+                weigh(s, staged[s][:, S:], slice(S, 2 * S))
+                sources[s] = keep.tile([P, S], F32, name="early1", align_bytes=64)[:]
+                weigh(s, sources[s], slice(0, S))
+            else:
+                weigh(s, staged[s][:], slice(0, 2 * S))
 
         def form_z(s):
             for c in range(CHUNKS):
                 add_product(s, c, open_with_wall(s, c, next_bank()))
 
-        prepare(2)
-        weigh_both(2)
-        weigh_sink(2)
+        weigh_sink(0)
+        scatter_sink(0)
+        prepare(1)
+        load_eq(2)
+        w1_last = w1_columns(*W1_CHUNKS[2], 1)
         load_wall(0)
         exponentiate(0, S)
-        scatter_sink(1)
-        grow(0, nc.gpsimd, T2)
-        load_eq(3)
-        prepare(3)
-        weigh_both(3)
-        form_z(0)
-        load_wall(1)
-        exponentiate(1, S)
-        load_w3()
-        for s in range(2, SLICES):
+        for s in range(1, SLICES):
+            weigh_sink(s)
             scatter_sink(s)
-            grow(s - 1, nc.gpsimd, T2)
+            grow(s - 1, nc.gpsimd, S if s == 1 else T2)
             if s + 2 <= last:
                 load_eq(s + 2)
-                prepare(s + 2)
             if s + 1 <= last:
-                weigh_sink(s + 1)
-            if s + 2 <= last:
-                weigh_both(s + 2)
-            form_z(s - 1)
+                prepare(s + 1)
             load_wall(s)
-            exponentiate(s, S if s < last else BANK)
-            scatter_source(s, whole)
-            if s in (2, 3):
-                quantize_w3(*((0, 512), (512, PASSES * N))[s - 2])
+            if s == last:
+                project_early((0, 1), "tabw")
+            form_z(s - 1)
+            if s == W3_SLICE:
+                load_w3()
             if s in (5, 6):
-                pair = (2 * s - 10, 2 * s - 9)
-                grouped = regroup_chunks(0, pair)
-                codes = three.tile([P, 2 * BANK], U32, name="both", align_bytes=64)
-                quantize_z(0, pair, grouped, codes[:])
-        last_banks = [open_with_wall(last, c, next_bank()) for c in range(CHUNKS)]
+                first_pass[s - 5] = regroup_chunks(0, (2 * s - 10, 2 * s - 9))
+            exponentiate(s, S if s < last else BANK)
+            if s == W3_SLICE + 1:
+                interleave_w3()
+            if s == last:
+                codes = three.tile([P, 2 * BANK], U32, name="sink", align_bytes=64)
+                quantize_z(0, (2, 3), first_pass[1], codes[:], keep, "zs0")
+                project_early((2, 3), "late")
+            scatter_source(s, whole)
+            if s == 1:
+                w1_later(1, w1_last)
+            if s == last - 1:
+                codes = two.tile([P, 4 * BANK], U32, name="both", align_bytes=64)
+                quantize_z(0, (0, 1), first_pass[0], codes[:, : 2 * BANK], three, "sink")
+                quantize_w3(codes[:, 2 * BANK : 2 * BANK + PASSES * N])
+        last_banks = [open_with_wall(last, c, spare_bank(c)) for c in range(CHUNKS)]
         grow(last, nc.vector, BANK)
         for step in range(CHUNKS + 2):
             if step < CHUNKS:
                 add_product(last, step, last_banks[step])
             if 1 <= step <= CHUNKS:
                 codes = keep.tile([P, BANK], U32, name="zc%d" % step, align_bytes=64)
-                quantize_z(1, (step - 1,), regroup_chunks(1, (step - 1,)), codes[:])
+                quantize_z(1, (step - 1,), regroup_chunks(1, (step - 1,)), codes[:], keep, "zs%d" % step)
             if step >= 2:
                 project(step - 2)

@@ -16,7 +16,7 @@ FP8X4 = mybir.dt.float8_e4m3fn_x4
 FP4X4 = mybir.dt.float4_e2m1fn_x4
 MULT = mybir.AluOpType.mult
 ADD = mybir.AluOpType.add
-COPY = mybir.ActivationFunctionType.Copy
+SUB = mybir.AluOpType.subtract
 EXP = mybir.ActivationFunctionType.Exp
 
 P = 128
@@ -24,9 +24,9 @@ BANK = 512
 SLICES = H // P
 PASSES = H // 512
 CHUNKS = T2 // BANK
-W3_SLICE = 3
 W1_CHUNKS = ((0, 256), (256, 512), (512, 1024))
-Z_T_TAGS = (("z_t0", "z_t1", "z_t2", "z_t3"), ("w1raw0", "w1raw256", "w1raw512", "w1bf512"))
+W3_CHUNKS = ((), ((0, 0, 256),), ((0, 256, 384), (1, 0, 384)))
+Z_T_TAGS = (("z_t0", "z_t1", "z_t2", "z_t3"), ("w1raw0", "w1raw256", "w1raw512", "w3raw0_0"))
 
 
 def tile_list_cave_wall_growth_kernel(
@@ -36,7 +36,6 @@ def tile_list_cave_wall_growth_kernel(
     with ExitStack() as ctx:
         keep = ctx.enter_context(tc.tile_pool(name="keep", bufs=1))
         two = ctx.enter_context(tc.tile_pool(name="two", bufs=2))
-        three = ctx.enter_context(tc.tile_pool(name="three", bufs=3))
         psum = ctx.enter_context(tc.psum_pool(name="psum", bufs=4))
         held = ctx.enter_context(tc.psum_pool(name="held", bufs=2))
 
@@ -56,7 +55,6 @@ def tile_list_cave_wall_growth_kernel(
         wg = keep.tile([P, 2 * S], F32, name="wg")
         ident = keep.tile([P, P], F32, name="ident")
         page_a = keep.tile([P, T2], F32, name="page_a")
-        growth = keep.tile([P, T2], F32, name="growth")
         page_b = [keep.tile([P, T2], F32, name="page_b%d" % i) for i in range(2)]
 
         def load_scale_rows(queue, plane, rows):
@@ -73,48 +71,56 @@ def tile_list_cave_wall_growth_kernel(
 
         w1q = []
 
-        w1s = keep.tile([P, H], U8, name="w1s", align_bytes=64)
+        w3q = []
 
-        def w1_columns(lo, hi, parts):
-            raw = keep.tile([P, 4, hi - lo], F32, name="w1raw%d" % lo, align_bytes=64)
-            rows = w1[:, lo:hi].rearrange("(p t) c -> p t c", t=4)
+        def load_rows(rows, name, parts=1):
+            raw = keep.tile([P, 4, rows.shape[1]], F32, name=name, align_bytes=64)
+            dealt = rows.rearrange("(p t) c -> p t c", t=4)
             for part in range(parts):
                 planes = slice(4 // parts * part, 4 // parts * (part + 1))
-                nc.sync.dma_start(out=raw[:, planes, :], in_=rows[:, planes, :])
-            grouped = keep.tile([P, 4 * (hi - lo)], BF16, name="w1bf%d" % lo, align_bytes=64)
-            interleave(grouped[:], raw[:])
+                nc.sync.dma_start(out=raw[:, planes, :], in_=dealt[:, planes, :])
+            return raw
+
+        def group_weights(i):
+            lo, hi = W1_CHUNKS[i]
+            pieces = [load_rows(w1[:, lo:hi], "w1raw%d" % lo, 2 if i == 0 else 1)]
+            for b, first, stop in W3_CHUNKS[i]:
+                pieces.append(load_rows(w3[512 * b : 512 * b + 512, first:stop], "w3raw%d_%d" % (b, first)))
+            grouped = keep.tile([P, 4 * sum(x.shape[2] for x in pieces)], BF16, name="wbf%d" % i, align_bytes=64)
+            c0 = 0
+            for raw in pieces:
+                interleave(grouped[:, 4 * c0 : 4 * (c0 + raw.shape[2])], raw[:])
+                c0 = c0 + raw.shape[2]
             return grouped
 
-        def quantize_w1(lo, hi, grouped, codes):
-            nc.vector.quantize_mx(out=codes.bitcast(FP8X4), scales=w1s[:, lo:hi], in_=grouped[:])
-            for c0 in range(0, hi - lo, P):
-                w1q.append((codes[:, c0 : c0 + P].bitcast(FP8X4), w1s[:, lo + c0 : lo + c0 + P]))
-
-        def w1_first():
-            lo, hi = W1_CHUNKS[0]
-            codes = keep.tile([P, hi - lo], U32, name="w1c", align_bytes=64)
-            quantize_w1(lo, hi, w1_columns(lo, hi, 2), codes[:])
-
-        def w1_later(s, grouped):
-            lo, hi = W1_CHUNKS[s + 1]
-            codes = keep.tile([P, hi - lo], U32, name="early%d" % s, align_bytes=64)
-            quantize_w1(lo, hi, grouped, codes[:])
+        def quantize_weights(i, grouped, tag):
+            width = grouped.shape[1] // 4
+            codes = keep.tile([P, width], U32, name=tag, align_bytes=64)
+            scales = keep.tile([P, width], U8, name="ws%d" % i, align_bytes=64)
+            nc.vector.quantize_mx(out=codes[:].bitcast(FP8X4), scales=scales[:], in_=grouped[:])
+            lo, hi = W1_CHUNKS[i]
+            for c0 in range(0, width, P):
+                (w1q if c0 < hi - lo else w3q).append((codes[:, c0 : c0 + P].bitcast(FP8X4), scales[:, c0 : c0 + P]))
 
         vw = [keep.tile([P, BANK], U32, name="vw%d" % h, align_bytes=64) for h in range(2)]
         vs = [keep.tile([P, BANK], U8, name="vs%d" % h, align_bytes=64) for h in range(2)]
         halves = [slice(BANK * h, BANK * h + BANK) for h in range(2)]
-        sinks = {}
+        last = SLICES - 1
         staged = {}
-        sources = {}
+        rates = {}
 
-        def load_eq(s):
-            sink = three.tile([P, S], F32, name="sink", align_bytes=64)
-            nc.sync.dma_start(out=sink[:], in_=eq[P * s : P * s + P, :])
-            sinks[s] = sink
+        sources = {}
+        gaps = {}
 
         def stage(s):
-            staged[s] = two.tile([P, 2 * S], F32, name="both", align_bytes=64)
-            sources[s] = staged[s][:, :S]
+            tag = "early%d" % s if s < 2 else "wbf%d" % (1 + s % 2)
+            if s < last:
+                staged[s] = keep.tile([P, 2 * S], F32, name=tag, align_bytes=64)
+                sources[s], gaps[s] = staged[s][:, :S], staged[s][:, S:]
+            else:
+                sources[s] = keep.tile([P, S], F32, name="last_source")[:]
+                gaps[s] = keep.tile([P, S], F32, name=tag, align_bytes=64)[:]
+            nc.sync.dma_start(out=gaps[s], in_=eq[P * s : P * s + P, :])
 
         def source_scores(s, h, bank):
             nc.tensor.matmul_mx(
@@ -123,17 +129,14 @@ def tile_list_cave_wall_growth_kernel(
             )
             return bank
 
-        def stage_source(s, h, bank):
-            nc.scalar.activation(out=staged[s][:, halves[h]], in_=bank[:], func=COPY, scale=-1.0)
-
-        def rate_scores(s, h):
-            bank = next_bank()
-            nc.tensor.matmul_mx(
-                out=bank[:], lhsT=w2w[:, 2 * P * s : 2 * P * s + 2 * P].bitcast(FP4X4),
-                lhsT_scale=w2s[:, P * s : P * s + P],
-                rhs=vw[h][:].bitcast(FP8X4), rhs_scale=vs[h][:], start=True, stop=True,
-            )
-            nc.scalar.copy(out=staged[s][:, S + BANK * h : S + BANK * h + BANK], in_=bank[:])
+        def rate_scores(s):
+            for h in range(2):
+                rates[s, h] = held.tile([P, BANK], F32, name="gap")
+                nc.tensor.matmul_mx(
+                    out=rates[s, h][:], lhsT=w2w[:, 2 * P * s : 2 * P * s + 2 * P].bitcast(FP4X4),
+                    lhsT_scale=w2s[:, P * s : P * s + P],
+                    rhs=vw[h][:].bitcast(FP8X4), rhs_scale=vs[h][:], start=True, stop=True,
+                )
 
         def add_transposed(bank, rows, opens):
             for g in range(4):
@@ -142,41 +145,27 @@ def tile_list_cave_wall_growth_kernel(
                     start=(opens and g == 0), stop=(not opens and g == 3), is_transpose=True,
                 )
 
-        gaps = {}
+        def weigh(s, cols):
+            nc.gpsimd.tensor_tensor(staged[s][:, cols], staged[s][:, cols], wg[:, cols], MULT)
 
-        def rates_and_gaps(s):
-            turned = []
+        def prepare(s):
+            stage(s)
             for h in range(2):
-                rate_scores(s, h)
-                bank = next_bank()
-                add_transposed(bank, sinks[s][:, halves[h]], True)
-                add_transposed(bank, staged[s][:, halves[h]], False)
-                gap_t = two.tile([P, BANK], F32, name="gap_t")
-                nc.scalar.copy(out=gap_t[:], in_=bank[:])
-                turned.append(gap_t)
-            for h in range(2):
-                gaps[s, h] = held.tile([P, BANK], F32, name="gap")
-                for g in range(4):
-                    nc.tensor.transpose(gaps[s, h][:, P * g : P * g + P], turned[h][:, P * g : P * g + P], ident[:])
+                nc.scalar.copy(out=sources[s][:, halves[h]], in_=source_scores(s, h, held.tile([P, BANK], F32, name="wide"))[:])
+            nc.gpsimd.tensor_tensor(gaps[s], sources[s], gaps[s], SUB)
+            if s < last:
+                weigh(s, slice(0, 2 * S))
+            else:
+                nc.gpsimd.tensor_tensor(gaps[s], gaps[s], wg[:, S:], MULT)
 
-        def weigh(s, out, cols):
-            nc.gpsimd.tensor_tensor(out, staged[s][:, cols], wg[:, cols], MULT)
-
-        def weigh_sink(s):
-            for h in range(2):
-                nc.vector.scalar_tensor_tensor(
-                    sinks[s][:, halves[h]], gaps[s, h][:], -1.0,
-                    staged[s][:, S + BANK * h : S + BANK * h + BANK], MULT, MULT,
-                )
-
-        def scatter_source(s, pieces):
-            for cols in pieces:
-                nc.vector.tensor_copy(
-                    page_a[:].indirect(idx2[:, cols.start // 16 : cols.stop // 16]), sources[s][:, cols]
-                )
+        def scatter_source(s, cols):
+            nc.vector.tensor_copy(page_a[:].indirect(idx2[:, cols.start // 16 : cols.stop // 16]), sources[s][:, cols])
 
         def scatter_sink(s):
-            nc.vector.tensor_copy(page_b[s % 2][:].indirect(idx3[:]), sinks[s][:])
+            for h in range(2):
+                gap = gaps[s][:, halves[h]]
+                nc.vector.tensor_tensor(gap, rates[s, h][:], gap, MULT)
+            nc.vector.tensor_copy(page_b[s % 2][:].indirect(idx3[:]), gaps[s])
 
         def exponentiate(s, width):
             for c0 in range(0, T2, width):
@@ -190,10 +179,7 @@ def tile_list_cave_wall_growth_kernel(
         walls = {}
 
         def load_wall(s):
-            if s == W3_SLICE:
-                walls[s] = keep.tile([P, T2], F32, name="w3bf", align_bytes=64)
-            else:
-                walls[s] = two.tile([P, T2], F32, name="wall_rows")
+            walls[s] = two.tile([P, T2], F32, name="wall_rows")
             nc.sync.dma_start(out=walls[s][:], in_=wall[P * s : P * s + P, :])
 
         z_t = {}
@@ -204,10 +190,13 @@ def tile_list_cave_wall_growth_kernel(
             return bank
 
         def add_product(s, c, bank):
+            add_transposed(bank, growth[:, BANK * c : BANK * c + BANK], False)
+            round_z(s, c, bank)
+
+        def round_z(s, c, bank):
             sl = s % 4
             if sl == 0:
                 z_t[s // 4, c] = keep.tile([P, 4 * BANK], BF16, name=Z_T_TAGS[s // 4][c], align_bytes=64)
-            add_transposed(bank, growth[:, BANK * c : BANK * c + BANK], False)
             nc.scalar.copy(
                 out=z_t[s // 4, c][:].rearrange("m (u g q e) -> m u g q e", u=2, g=4, e=2)[:, :, :, 32 * sl : 32 * sl + 32, :],
                 in_=bank[:].rearrange("m (g q u e) -> m u g q e", g=4, u=2, e=2),
@@ -241,40 +230,15 @@ def tile_list_cave_wall_growth_kernel(
                 zq[b, c] = (codes[:, BANK * i : BANK * (i + 1)], scales[:, BANK * i : BANK * (i + 1)])
 
 
-        w3bf = []
-        w3raw = []
-
-        def load_w3():
-            both_passes = keep.tile([P, PASSES * 4 * N], F32, name="w3raw", align_bytes=64)
-            for b in range(PASSES):
-                raw = both_passes[:, 4 * N * b : 4 * N * b + 4 * N].rearrange("p (t n) -> p t n", t=4)
-                nc.sync.dma_start(out=raw, in_=w3[512 * b : 512 * b + 512, :].rearrange("(p t) n -> p t n", t=4))
-                w3raw.append(raw)
-
-        def interleave_w3():
-            w3bf.append(keep.tile([P, 4 * PASSES * N], BF16, name="w3bf", align_bytes=64))
-            for b in range(PASSES):
-                interleave(w3bf[0][:, 4 * N * b : 4 * N * b + 4 * N], w3raw[b])
-
-        w3q = []
-
-        def quantize_w3(codes):
-            w3s = three.tile([P, PASSES * N], U8, name="sink", align_bytes=64)
-            w3q.extend((codes, w3s))
-            for lo, hi in ((0, 512), (512, PASSES * N)):
-                nc.vector.quantize_mx(
-                    out=codes[:, lo:hi].bitcast(FP8X4), scales=w3s[:, lo:hi], in_=w3bf[0][:, 4 * lo : 4 * hi]
-                )
-
         results = {}
 
         def summed_early(c, nb):
             return nb == 1 or (nb == 0 and c % 2 == 0)
 
         def multiply(bank, b, c, nb, start, stop):
-            cols = slice(N * b + P * nb, N * b + P * nb + P)
+            codes, scales = w3q[N // P * b + nb]
             nc.tensor.matmul_mx(
-                out=bank[:], lhsT=w3q[0][:, cols].bitcast(FP8X4), lhsT_scale=w3q[1][:, cols],
+                out=bank[:], lhsT=codes, lhsT_scale=scales,
                 rhs=zq[b, c][0].bitcast(FP8X4), rhs_scale=zq[b, c][1], start=start, stop=stop,
             )
 
@@ -285,7 +249,7 @@ def tile_list_cave_wall_growth_kernel(
                     c0 = BANK * (N // P * i + nb)
                     results[c, nb] = rows[:, c0 : c0 + BANK]
                     if summed_early(c, nb):
-                        bank = next_bank()
+                        bank = held.tile([P, BANK], F32, name="gap")
                         multiply(bank, 0, c, nb, True, True)
                         nc.scalar.copy(out=results[c, nb], in_=bank[:])
 
@@ -301,9 +265,7 @@ def tile_list_cave_wall_growth_kernel(
                     nc.scalar.copy(out=results[c, nb], in_=bank[:])
                 nc.sync.dma_start(out=out[P * nb : P * nb + P, BANK * c : BANK * c + BANK], in_=results[c, nb])
 
-        whole = [slice(0, S)]
         first_pass = {}
-        last = SLICES - 1
 
         nc.vector.memset(tabs[:].bitcast(I32), 0)
         nc.gpsimd.memset(w2s[:].bitcast(I32), 0)
@@ -312,92 +274,82 @@ def tile_list_cave_wall_growth_kernel(
         nc.sync.dma_start(idx2[:], offs2)
         nc.sync.dma_start(idx3[:], offs3)
         table = tab_words[0].rearrange("p t i -> p (t i)").bitcast(I32)
-        w1_first()
+        quantize_weights(0, group_weights(0), "w1c")
         for c0 in range(0, T, T // 4):
             nc.sync.dma_start(out=tabw[:].bitcast(I32)[:, c0 : c0 + T // 4], in_=table[:, c0 : c0 + T // 4])
         load_scale_rows(nc.sync, tabs, tab_scales[0])
         nc.vector.memset(page_a[:], 0.0)
         make_identity(nc, ident[:])
-        wg1s = keep.tile([P, S], F32, name="early1", align_bytes=64)
-        nc.sync.dma_start(out=wg1s[:], in_=wg1)
-        nc.gpsimd.tensor_scalar(wg[:, :S], wg1s[:], -1.0, 0.0, MULT, ADD)
+        nc.sync.dma_start(out=wg[:, halves[0]], in_=wg1[:, halves[0]])
         for page in page_b:
             nc.gpsimd.memset(page[:], 0.0)
         for h in range(2):
             nc.vector.tensor_copy(vw[h][:], tabw[:].indirect(idx[:, 32 * h : 32 * h + 32]))
             nc.vector.tensor_copy(vs[h][:], tabs[:].indirect(idx[:, 32 * h : 32 * h + 32]))
-        early = keep.tile([P, S], F32, name="early0", align_bytes=64)
         stage(0)
-        sources[0] = early[:]
-        bank = source_scores(0, 0, next_bank())
-        nc.vector.tensor_tensor(early[:, halves[0]], bank[:], wg1s[:, halves[0]], MULT)
-        stage_source(0, 0, bank)
-        stage_source(0, 1, source_scores(0, 1, next_bank()))
-        weigh(0, early[:, halves[1]], halves[1])
-        scatter_source(0, halves)
-        w1_later(0, w1_columns(*W1_CHUNKS[1], 1))
-        nc.sync.dma_start(out=w2w[:].bitcast(I32), in_=w2_words[0].bitcast(I32))
+        nc.sync.dma_start(out=wg[:, halves[1]], in_=wg1[:, halves[1]])
         nc.sync.dma_start(out=wg[:, S:], in_=wg2)
-        load_eq(0)
-        load_eq(1)
-        rates_and_gaps(0)
+        nc.sync.dma_start(out=w2w[:].bitcast(I32), in_=w2_words[0].bitcast(I32))
+        first = [source_scores(0, h, next_bank()) for h in range(2)]
+        nc.vector.tensor_tensor(staged[0][:, halves[0]], first[0][:], wg[:, halves[0]], MULT)
+        scatter_source(0, halves[0])
+        nc.scalar.copy(out=staged[0][:, halves[1]], in_=first[1][:])
         for h in range(2):
-            cols = slice(S + BANK * h, S + BANK * h + BANK)
-            weigh(0, staged[0][:, cols], cols)
-
-        def prepare(s):
-            stage(s)
-            for h in range(2):
-                stage_source(s, h, source_scores(s, h, next_bank()))
-            rates_and_gaps(s)
-            if s == 1:
-                weigh(s, staged[s][:, S:], slice(S, 2 * S))
-                sources[s] = keep.tile([P, S], F32, name="early1", align_bytes=64)[:]
-                weigh(s, sources[s], slice(0, S))
-            else:
-                weigh(s, staged[s][:], slice(0, 2 * S))
+            gap = staged[0][:, S + BANK * h : S + BANK * h + BANK]
+            nc.vector.tensor_tensor(gap, first[h][:], gap, SUB)
+        weigh(0, halves[1])
+        scatter_source(0, halves[1])
+        weigh(0, slice(S, 2 * S))
+        rate_scores(0)
+        prepare(1)
 
         def form_z(s):
             for c in range(CHUNKS):
-                add_product(s, c, open_with_wall(s, c, next_bank()))
+                if s == last - 1:
+                    add_product(s, c, open_with_wall(s, c, next_bank()))
+                elif c >= 2:
+                    add_product(s, c, open_with_wall(s, c, held.tile([P, BANK], F32, name="wide")))
+                else:
+                    bank = held.tile([P, BANK], F32, name="gap")
+                    add_transposed(bank, growth[:, BANK * c : BANK * c + BANK], True)
+                    add_transposed(bank, walls[s][:, BANK * c : BANK * c + BANK], False)
+                    round_z(s, c, bank)
 
-        weigh_sink(0)
+        second = group_weights(1)
         scatter_sink(0)
-        prepare(1)
-        load_eq(2)
-        w1_last = w1_columns(*W1_CHUNKS[2], 1)
+        quantize_weights(1, second, "early0")
+        rate_scores(1)
+        third = group_weights(2)
+        growth = keep.tile([P, T2], F32, name="w3raw1_0", align_bytes=64)
         load_wall(0)
         exponentiate(0, S)
         for s in range(1, SLICES):
-            weigh_sink(s)
             scatter_sink(s)
             grow(s - 1, nc.gpsimd, S if s == 1 else T2)
-            if s + 2 <= last:
-                load_eq(s + 2)
             if s + 1 <= last:
                 prepare(s + 1)
             load_wall(s)
             if s == last:
                 project_early((0, 1), "tabw")
             form_z(s - 1)
-            if s == W3_SLICE:
-                load_w3()
+            if s + 1 <= last:
+                rate_scores(s + 1)
+            exponentiate(s, S if s < last else BANK)
             if s in (5, 6):
                 first_pass[s - 5] = regroup_chunks(0, (2 * s - 10, 2 * s - 9))
-            exponentiate(s, S if s < last else BANK)
-            if s == W3_SLICE + 1:
-                interleave_w3()
             if s == last:
-                codes = three.tile([P, 2 * BANK], U32, name="sink", align_bytes=64)
+                codes = keep.tile([P, 2 * BANK], U32, name="wbf2", align_bytes=64)
                 quantize_z(0, (2, 3), first_pass[1], codes[:], keep, "zs0")
                 project_early((2, 3), "late")
-            scatter_source(s, whole)
+            if s < last:
+                scatter_source(s, slice(0, S))
+            else:
+                nc.vector.tensor_tensor(page_a[:].indirect(idx2[:]), sources[s], wg[:, :S], MULT)
             if s == 1:
-                w1_later(1, w1_last)
+                quantize_weights(2, third, "early1")
             if s == last - 1:
-                codes = two.tile([P, 4 * BANK], U32, name="both", align_bytes=64)
-                quantize_z(0, (0, 1), first_pass[0], codes[:, : 2 * BANK], three, "sink")
-                quantize_w3(codes[:, 2 * BANK : 2 * BANK + PASSES * N])
+                codes = keep.tile([P, 2 * BANK], U32, name="wbf1", align_bytes=64)
+                quantize_z(0, (0, 1), first_pass[0], codes[:], keep, "zs5")
         last_banks = [open_with_wall(last, c, spare_bank(c)) for c in range(CHUNKS)]
         grow(last, nc.vector, BANK)
         for step in range(CHUNKS + 2):

@@ -24,9 +24,10 @@ BANK = 512
 SLICES = H // P
 PASSES = H // 512
 CHUNKS = T2 // BANK
+EVEN_AT = BANK + 8 * T2
 W1_CHUNKS = ((0, 256), (256, 512), (512, 1024))
 W3_CHUNKS = ((), ((0, 0, 256),), ((0, 256, 384), (1, 0, 384)))
-Z_T_TAGS = (("z_t0", "z_t1", "z_t2", "z_t3"), ("w1raw0", "w1raw256", "w1raw512", "w3raw0_0"))
+PAIR_TAGS = ("raw0", "wbf0", "pairs2", "pairs3")
 
 
 def tile_list_cave_wall_growth_kernel(
@@ -36,11 +37,20 @@ def tile_list_cave_wall_growth_kernel(
     with ExitStack() as ctx:
         keep = ctx.enter_context(tc.tile_pool(name="keep", bufs=1))
         two = ctx.enter_context(tc.tile_pool(name="two", bufs=2))
+        placed = ctx.enter_context(tc.tile_pool(name="placed", bufs=1))
         psum = ctx.enter_context(tc.psum_pool(name="psum", bufs=4))
         held = ctx.enter_context(tc.psum_pool(name="held", bufs=2))
 
         def spare_bank(i):
-            return held.tile([P, BANK], F32, name=("wide", "gap")[i % 4 // 2])
+            if i % 8 >= 4:
+                return next_bank()
+            return held.tile([P, BANK], F32, name=("gap", "wide")[i % 8 // 2])
+
+        def lane_rows(rows, t):
+            return rows.rearrange("(q t i) n -> t q i n", t=4, i=8)[t]
+
+        def slice_rows(matrix, s):
+            return matrix[P * s : P * s + P, :] if s < 4 else lane_rows(matrix[512:, :], s - 4)
 
         def next_bank():
             return psum.tile([P, BANK], F32, name="bank")
@@ -52,7 +62,7 @@ def tile_list_cave_wall_growth_kernel(
         tabs = keep.tile([P, T], U8, name="tabs")
         w2w = keep.tile([P, 2 * H], U8, name="w2w", align_bytes=64)
         w2s = keep.tile([P, H], U8, name="w2s", align_bytes=64)
-        wg = keep.tile([P, 2 * S], F32, name="wg")
+        wg = keep.tile([P, 2 * S], F32, name="wg", align_bytes=64)
         ident = keep.tile([P, P], F32, name="ident")
         page_a = keep.tile([P, T2], F32, name="page_a")
         page_b = [keep.tile([P, T2], F32, name="page_b%d" % i) for i in range(2)]
@@ -73,30 +83,54 @@ def tile_list_cave_wall_growth_kernel(
 
         w3q = []
 
-        def load_rows(rows, name, parts=1):
-            raw = keep.tile([P, 4, rows.shape[1]], F32, name=name, align_bytes=64)
-            dealt = rows.rearrange("(p t) c -> p t c", t=4)
-            for part in range(parts):
-                planes = slice(4 // parts * part, 4 // parts * (part + 1))
-                nc.sync.dma_start(out=raw[:, planes, :], in_=dealt[:, planes, :])
-            return raw
-
-        def group_weights(i):
+        def group_weights(i, staging):
             lo, hi = W1_CHUNKS[i]
-            pieces = [load_rows(w1[:, lo:hi], "w1raw%d" % lo, 2 if i == 0 else 1)]
-            for b, first, stop in W3_CHUNKS[i]:
-                pieces.append(load_rows(w3[512 * b : 512 * b + 512, first:stop], "w3raw%d_%d" % (b, first)))
-            grouped = keep.tile([P, 4 * sum(x.shape[2] for x in pieces)], BF16, name="wbf%d" % i, align_bytes=64)
+            pieces = [(w1[:, lo:hi], False)]
+            pieces.extend((w3[512 * b : 512 * b + 512, first:stop], b == 1) for b, first, stop in W3_CHUNKS[i])
+            if i == 1:
+                grouped = placed.tile([P, staging.shape[1]], BF16, name="wbf1", align_bytes=64, offset=EVEN_AT + 6 * S)
+            else:
+                grouped = keep.tile([P, staging.shape[1]], BF16, name="wbf%d" % i, align_bytes=64)
             c0 = 0
-            for raw in pieces:
-                interleave(grouped[:, 4 * c0 : 4 * (c0 + raw.shape[2])], raw[:])
-                c0 = c0 + raw.shape[2]
+            for rows, by_lanes in pieces:
+                cols = slice(4 * c0, 4 * (c0 + rows.shape[1]))
+                raw = staging[:, cols].rearrange("p (t c) -> p t c", t=4)
+                if by_lanes:
+                    for t in range(4):
+                        nc.sync.dma_start(out=raw[:, t, :], in_=lane_rows(rows, t))
+                else:
+                    dealt = rows.rearrange("(p t) c -> p t c", t=4)
+                    for planes in (slice(0, 2), slice(2, 4)) if i == 0 else (slice(0, 4),):
+                        nc.sync.dma_start(out=raw[:, planes, :], in_=dealt[:, planes, :])
+                if lo == 512 and c0 == 0:
+                    dealt = raw.rearrange("p j (q t h i) -> p t q h j i", t=4, h=2, i=4)
+                    for t in range(4):
+                        nc.scalar.copy(
+                            out=grouped[:, 512 * t : 512 * t + 512].rearrange("p (q h i j) -> p q h j i", h=2, i=4, j=4),
+                            in_=dealt[:, t],
+                        )
+                else:
+                    interleave(grouped[:, cols], raw)
+                c0 = c0 + rows.shape[1]
             return grouped
+
+        w2_lanes = keep.tile([P, H], U8, name="w2_lanes", align_bytes=64)
+        w2s_lanes = keep.tile([P, H // 2], U8, name="w2s_lanes", align_bytes=64)
+
+        def deal_w2():
+            for dealt, packed in ((w2_lanes[:], w2w[:, H:]), (w2s_lanes[:], w2s[:, H // 2 :])):
+                nc.gpsimd.tensor_copy(
+                    dealt.bitcast(I32).rearrange("p (t q w) -> p t q w", t=4, q=16),
+                    packed.bitcast(I32).rearrange("p (q t w) -> p t q w", t=4, q=16),
+                )
 
         def quantize_weights(i, grouped, tag):
             width = grouped.shape[1] // 4
             codes = keep.tile([P, width], U32, name=tag, align_bytes=64)
-            scales = keep.tile([P, width], U8, name="ws%d" % i, align_bytes=64)
+            if i == 1:
+                scales = placed.tile([P, width], U8, name="ws1", align_bytes=64, offset=0)
+            else:
+                scales = keep.tile([P, width], U8, name="ws%d" % i, align_bytes=64)
             nc.vector.quantize_mx(out=codes[:].bitcast(FP8X4), scales=scales[:], in_=grouped[:])
             lo, hi = W1_CHUNKS[i]
             for c0 in range(0, width, P):
@@ -112,15 +146,33 @@ def tile_list_cave_wall_growth_kernel(
         sources = {}
         gaps = {}
 
+        weights = {}
+        eqs = {}
+        weighted = {}
+
+        def load_given(s):
+            given = two.tile([P, (1 if s < 4 else 3) * S], F32, name="given")
+            eqs[s] = given[:, :S]
+            nc.sync.dma_start(out=eqs[s], in_=slice_rows(eq, s))
+            weights[s] = wg[:] if s < 4 else given[:, S:]
+            if s >= 4:
+                for i, matrix in enumerate((wg1, wg2)):
+                    for p0 in range(0, P, 32):
+                        nc.sync.dma_start(
+                            out=weights[s][p0 : p0 + 32, S * i : S * i + S], in_=lane_rows(matrix, s - 4)
+                        )
+
         def stage(s):
-            tag = "early%d" % s if s < 2 else "wbf%d" % (1 + s % 2)
-            if s < last:
+            tag = "early%d" % s if s < 2 else "wbf2"
+            if s >= 2 and s % 2 == 0:
+                staged[s] = placed.tile([P, 2 * S], F32, name="even", align_bytes=64, offset=EVEN_AT)
+                sources[s], gaps[s] = staged[s][:, :S], staged[s][:, S:]
+            elif s < last:
                 staged[s] = keep.tile([P, 2 * S], F32, name=tag, align_bytes=64)
                 sources[s], gaps[s] = staged[s][:, :S], staged[s][:, S:]
             else:
                 sources[s] = keep.tile([P, S], F32, name="last_source")[:]
                 gaps[s] = keep.tile([P, S], F32, name=tag, align_bytes=64)[:]
-            nc.sync.dma_start(out=gaps[s], in_=eq[P * s : P * s + P, :])
 
         def source_scores(s, h, bank):
             nc.tensor.matmul_mx(
@@ -130,11 +182,13 @@ def tile_list_cave_wall_growth_kernel(
             return bank
 
         def rate_scores(s):
+            words, scales = (w2w, w2s) if s < 4 else (w2_lanes, w2s_lanes)
+            c0 = P * (s % 4)
             for h in range(2):
                 rates[s, h] = held.tile([P, BANK], F32, name="gap")
                 nc.tensor.matmul_mx(
-                    out=rates[s, h][:], lhsT=w2w[:, 2 * P * s : 2 * P * s + 2 * P].bitcast(FP4X4),
-                    lhsT_scale=w2s[:, P * s : P * s + P],
+                    out=rates[s, h][:], lhsT=words[:, 2 * c0 : 2 * c0 + 2 * P].bitcast(FP4X4),
+                    lhsT_scale=scales[:, c0 : c0 + P],
                     rhs=vw[h][:].bitcast(FP8X4), rhs_scale=vs[h][:], start=True, stop=True,
                 )
 
@@ -146,41 +200,46 @@ def tile_list_cave_wall_growth_kernel(
                 )
 
         def weigh(s, cols):
-            nc.gpsimd.tensor_tensor(staged[s][:, cols], staged[s][:, cols], wg[:, cols], MULT)
+            nc.gpsimd.tensor_tensor(staged[s][:, cols], staged[s][:, cols], weights[s][:, cols], MULT)
 
-        def prepare(s):
+        def score_sources(s):
             stage(s)
             for h in range(2):
                 nc.scalar.copy(out=sources[s][:, halves[h]], in_=source_scores(s, h, held.tile([P, BANK], F32, name="wide"))[:])
-            nc.gpsimd.tensor_tensor(gaps[s], sources[s], gaps[s], SUB)
+            gap = gaps[s] if s == 1 else growth[:, :S]
+            nc.gpsimd.tensor_tensor(gap, sources[s], eqs[s], SUB)
+            return gap
+
+        def weigh_slice(s, gap):
+            weighted[s] = gaps[s] if s == 1 else product[:, S:]
+            nc.gpsimd.tensor_tensor(weighted[s], gap, weights[s][:, S:], MULT)
             if s < last:
-                weigh(s, slice(0, 2 * S))
-            else:
-                nc.gpsimd.tensor_tensor(gaps[s], gaps[s], wg[:, S:], MULT)
+                nc.gpsimd.tensor_tensor(sources[s], sources[s], weights[s][:, :S], MULT)
 
         def scatter_source(s, cols):
             nc.vector.tensor_copy(page_a[:].indirect(idx2[:, cols.start // 16 : cols.stop // 16]), sources[s][:, cols])
 
         def scatter_sink(s):
+            sink = gaps[s]
+            if s == 1:
+                sink = placed.tile([P, S], F32, name="sink1", align_bytes=64, offset=EVEN_AT + 8 * S)[:]
             for h in range(2):
-                gap = gaps[s][:, halves[h]]
-                nc.vector.tensor_tensor(gap, rates[s, h][:], gap, MULT)
-            nc.vector.tensor_copy(page_b[s % 2][:].indirect(idx3[:]), gaps[s])
+                nc.vector.tensor_tensor(sink[:, halves[h]], rates[s, h][:], weighted[s][:, halves[h]], MULT)
+            nc.vector.tensor_copy(page_b[s % 2][:].indirect(idx3[:]), sink)
 
         def exponentiate(s, width):
-            for c0 in range(0, T2, width):
+            for c0 in range(0, T2, width) if s in (0, last) else (S, 0):
                 nc.scalar.activation(out=growth[:, c0 : c0 + width], in_=page_b[s % 2][:, c0 : c0 + width], func=EXP)
 
-        def grow(s, engine, width):
-            for c0 in range(0, T2, width):
-                cols = slice(c0, c0 + width)
-                engine.tensor_tensor(growth[:, cols], growth[:, cols], page_a[:, cols], MULT)
+        def grow():
+            for cols in (slice(0, S), slice(S, T2)):
+                nc.gpsimd.tensor_tensor(product[:, cols], growth[:, cols], page_a[:, cols], MULT)
 
         walls = {}
 
         def load_wall(s):
             walls[s] = two.tile([P, T2], F32, name="wall_rows")
-            nc.sync.dma_start(out=walls[s][:], in_=wall[P * s : P * s + P, :])
+            nc.sync.dma_start(out=walls[s][:], in_=slice_rows(wall, s))
 
         z_t = {}
         zq = {}
@@ -190,37 +249,52 @@ def tile_list_cave_wall_growth_kernel(
             return bank
 
         def add_product(s, c, bank):
-            add_transposed(bank, growth[:, BANK * c : BANK * c + BANK], False)
+            add_transposed(bank, product[:, BANK * c : BANK * c + BANK], False)
             round_z(s, c, bank)
 
         def round_z(s, c, bank):
-            sl = s % 4
-            if sl == 0:
-                z_t[s // 4, c] = keep.tile([P, 4 * BANK], BF16, name=Z_T_TAGS[s // 4][c], align_bytes=64)
-            nc.scalar.copy(
-                out=z_t[s // 4, c][:].rearrange("m (u g q e) -> m u g q e", u=2, g=4, e=2)[:, :, :, 32 * sl : 32 * sl + 32, :],
-                in_=bank[:].rearrange("m (g q u e) -> m u g q e", g=4, u=2, e=2),
-            )
-
-        def regroup_z(b, c, grouped):
-            words = z_t[b, c][:].bitcast(F32)
-            for h, copy in enumerate((nc.scalar.copy, nc.vector.tensor_copy if b == PASSES - 1 and c % 2 == 0 else nc.scalar.copy)):
-                bank = next_bank()
-                for u in range(2):
-                    for g2 in range(2):
-                        w0 = P * (4 * u + 2 * h + g2)
-                        o0 = P * (2 * u + g2)
-                        nc.tensor.transpose(bank[:, o0 : o0 + P], words[:, w0 : w0 + P], ident[:])
-                copy(
-                    out=grouped.bitcast(F32)[:, BANK * h : BANK * h + BANK].rearrange("p (m u) -> p m u", u=2),
-                    in_=bank[:].rearrange("p (u m) -> p m u", u=2),
+            if s < 4:
+                if s == 0:
+                    z_t[0, c] = keep.tile([P, 4 * BANK], BF16, name="z_t%d" % c, align_bytes=64)
+                nc.scalar.copy(
+                    out=z_t[0, c][:].rearrange("m (u g q e) -> m u g q e", u=2, g=4, e=2)[:, :, :, 32 * s : 32 * s + 32, :],
+                    in_=bank[:].rearrange("m (g q u e) -> m u g q e", g=4, u=2, e=2),
                 )
+            else:
+                if s == 4:
+                    z_t[1, c] = keep.tile([P, 2 * BANK], BF16, name=PAIR_TAGS[c], align_bytes=64)
+                nc.scalar.copy(out=z_t[1, c][:].rearrange("m (x e) -> m x e", e=2)[:, :, s % 2], in_=bank[:])
 
-        def regroup_chunks(b, chunks):
+        def regroup_chunks(chunks):
             grouped = two.tile([P, 8 * BANK], BF16, name="grouped", align_bytes=64)
             for i, c in enumerate(chunks):
-                regroup_z(b, c, grouped[:, 4 * BANK * i : 4 * BANK * (i + 1)])
+                words = z_t[0, c][:].bitcast(F32)
+                for h in range(2):
+                    bank = next_bank()
+                    for u in range(2):
+                        for g2 in range(2):
+                            w0 = P * (4 * u + 2 * h + g2)
+                            o0 = P * (2 * u + g2)
+                            nc.tensor.transpose(bank[:, o0 : o0 + P], words[:, w0 : w0 + P], ident[:])
+                    c0 = BANK * (2 * i + h)
+                    nc.scalar.copy(
+                        out=grouped[:].bitcast(F32)[:, c0 : c0 + BANK].rearrange("p (m u) -> p m u", u=2),
+                        in_=bank[:].rearrange("p (u m) -> p m u", u=2),
+                    )
             return grouped
+
+        planes = {}
+
+        def turn_pairs(u):
+            for c in range(CHUNKS):
+                if u == 0 and c % 2 == 0:
+                    both = keep.tile([P, 4 * BANK], F32, name=("raw1", "wg")[c // 2], align_bytes=64)
+                    planes[c], planes[c + 1] = both[:, : 2 * BANK], both[:, 2 * BANK :]
+                words = z_t[1, c][:].bitcast(F32)
+                bank = next_bank()
+                for g in range(4):
+                    nc.tensor.transpose(bank[:, P * g : P * g + P], words[:, P * g : P * g + P], ident[:])
+                nc.scalar.copy(out=planes[c][:, BANK * u : BANK * u + BANK], in_=bank[:])
 
         def quantize_z(b, chunks, grouped, codes, pool, tag):
             n = len(chunks)
@@ -230,40 +304,19 @@ def tile_list_cave_wall_growth_kernel(
                 zq[b, c] = (codes[:, BANK * i : BANK * (i + 1)], scales[:, BANK * i : BANK * (i + 1)])
 
 
-        results = {}
-
-        def summed_early(c, nb):
-            return nb == 1 or (nb == 0 and c % 2 == 0)
-
-        def multiply(bank, b, c, nb, start, stop):
-            codes, scales = w3q[N // P * b + nb]
-            nc.tensor.matmul_mx(
-                out=bank[:], lhsT=codes, lhsT_scale=scales,
-                rhs=zq[b, c][0].bitcast(FP8X4), rhs_scale=zq[b, c][1], start=start, stop=stop,
-            )
-
-        def project_early(chunks, tag):
-            rows = keep.tile([P, len(chunks) * N // P * BANK], F32, name=tag, align_bytes=64)
-            for i, c in enumerate(chunks):
-                for nb in range(N // P):
-                    c0 = BANK * (N // P * i + nb)
-                    results[c, nb] = rows[:, c0 : c0 + BANK]
-                    if summed_early(c, nb):
-                        bank = held.tile([P, BANK], F32, name="gap")
-                        multiply(bank, 0, c, nb, True, True)
-                        nc.scalar.copy(out=results[c, nb], in_=bank[:])
-
-        def project(c):
+        def project(c, rows):
             for nb in range(N // P):
                 bank = spare_bank(N // P * c + nb)
-                if summed_early(c, nb):
-                    multiply(bank, 1, c, nb, True, True)
-                    nc.vector.tensor_tensor(results[c, nb], bank[:], results[c, nb], ADD)
-                else:
-                    for b in range(PASSES):
-                        multiply(bank, b, c, nb, b == 0, b == PASSES - 1)
-                    nc.scalar.copy(out=results[c, nb], in_=bank[:])
-                nc.sync.dma_start(out=out[P * nb : P * nb + P, BANK * c : BANK * c + BANK], in_=results[c, nb])
+                for b in range(PASSES):
+                    codes, scales = w3q[N // P * b + nb]
+                    nc.tensor.matmul_mx(
+                        out=bank[:], lhsT=codes, lhsT_scale=scales,
+                        rhs=zq[b, c][0].bitcast(FP8X4), rhs_scale=zq[b, c][1], start=(b == 0), stop=(b == PASSES - 1),
+                    )
+                result = rows[nb]
+                copy = nc.vector.tensor_copy if nb == 1 and c >= 1 or nb == 0 and c == CHUNKS - 1 else nc.scalar.copy
+                copy(out=result, in_=bank[:])
+                nc.sync.dma_start(out=out[P * nb : P * nb + P, BANK * c : BANK * c + BANK], in_=result)
 
         first_pass = {}
 
@@ -274,7 +327,7 @@ def tile_list_cave_wall_growth_kernel(
         nc.sync.dma_start(idx2[:], offs2)
         nc.sync.dma_start(idx3[:], offs3)
         table = tab_words[0].rearrange("p t i -> p (t i)").bitcast(I32)
-        quantize_weights(0, group_weights(0), "w1c")
+        quantize_weights(0, group_weights(0, keep.tile([P, 4 * 256], F32, name="raw0", align_bytes=64)), "w1c")
         for c0 in range(0, T, T // 4):
             nc.sync.dma_start(out=tabw[:].bitcast(I32)[:, c0 : c0 + T // 4], in_=table[:, c0 : c0 + T // 4])
         load_scale_rows(nc.sync, tabs, tab_scales[0])
@@ -287,6 +340,7 @@ def tile_list_cave_wall_growth_kernel(
             nc.vector.tensor_copy(vw[h][:], tabw[:].indirect(idx[:, 32 * h : 32 * h + 32]))
             nc.vector.tensor_copy(vs[h][:], tabs[:].indirect(idx[:, 32 * h : 32 * h + 32]))
         stage(0)
+        load_given(0)
         nc.sync.dma_start(out=wg[:, halves[1]], in_=wg1[:, halves[1]])
         nc.sync.dma_start(out=wg[:, S:], in_=wg2)
         nc.sync.dma_start(out=w2w[:].bitcast(I32), in_=w2_words[0].bitcast(I32))
@@ -295,68 +349,94 @@ def tile_list_cave_wall_growth_kernel(
         scatter_source(0, halves[0])
         nc.scalar.copy(out=staged[0][:, halves[1]], in_=first[1][:])
         for h in range(2):
-            gap = staged[0][:, S + BANK * h : S + BANK * h + BANK]
-            nc.vector.tensor_tensor(gap, first[h][:], gap, SUB)
+            nc.vector.tensor_tensor(gaps[0][:, halves[h]], first[h][:], eqs[0][:, halves[h]], SUB)
         weigh(0, halves[1])
         scatter_source(0, halves[1])
         weigh(0, slice(S, 2 * S))
+        weighted[0] = gaps[0]
         rate_scores(0)
-        prepare(1)
+        load_given(1)
+        weigh_slice(1, score_sources(1))
+        deal_w2()
 
         def form_z(s):
             for c in range(CHUNKS):
-                if s == last - 1:
-                    add_product(s, c, open_with_wall(s, c, next_bank()))
-                elif c >= 2:
+                if c >= 2:
                     add_product(s, c, open_with_wall(s, c, held.tile([P, BANK], F32, name="wide")))
                 else:
                     bank = held.tile([P, BANK], F32, name="gap")
-                    add_transposed(bank, growth[:, BANK * c : BANK * c + BANK], True)
+                    add_transposed(bank, product[:, BANK * c : BANK * c + BANK], True)
                     add_transposed(bank, walls[s][:, BANK * c : BANK * c + BANK], False)
                     round_z(s, c, bank)
 
-        second = group_weights(1)
+        second = group_weights(1, keep.tile([P, 4 * 512], F32, name="raw1", align_bytes=64))
+        third = group_weights(2, placed.tile([P, 4 * 1024], F32, name="raw2", offset=0))
         scatter_sink(0)
         quantize_weights(1, second, "early0")
         rate_scores(1)
-        third = group_weights(2)
-        growth = keep.tile([P, T2], F32, name="w3raw1_0", align_bytes=64)
+        pair = placed.tile([P, 2 * T2], F32, name="pair", offset=BANK)
+        growth, product = pair[:, :T2], pair[:, T2:]
+        load_given(2)
         load_wall(0)
         exponentiate(0, S)
         for s in range(1, SLICES):
             scatter_sink(s)
-            grow(s - 1, nc.gpsimd, S if s == 1 else T2)
+            grow()
             if s + 1 <= last:
-                prepare(s + 1)
+                gap = score_sources(s + 1)
+            if s + 2 <= last:
+                load_given(s + 2)
             load_wall(s)
             if s == last:
-                project_early((0, 1), "tabw")
+                turn_pairs(0)
             form_z(s - 1)
             if s + 1 <= last:
                 rate_scores(s + 1)
+                weigh_slice(s + 1, gap)
             exponentiate(s, S if s < last else BANK)
-            if s in (5, 6):
-                first_pass[s - 5] = regroup_chunks(0, (2 * s - 10, 2 * s - 9))
+            if s in (4, 5):
+                first_pass[s - 4] = regroup_chunks((2 * s - 8, 2 * s - 7))
             if s == last:
                 codes = keep.tile([P, 2 * BANK], U32, name="wbf2", align_bytes=64)
                 quantize_z(0, (2, 3), first_pass[1], codes[:], keep, "zs0")
-                project_early((2, 3), "late")
+                turn_pairs(1)
             if s < last:
                 scatter_source(s, slice(0, S))
             else:
-                nc.vector.tensor_tensor(page_a[:].indirect(idx2[:]), sources[s], wg[:, :S], MULT)
+                nc.vector.tensor_tensor(page_a[:].indirect(idx2[:]), sources[s], weights[s][:, :S], MULT)
             if s == 1:
                 quantize_weights(2, third, "early1")
             if s == last - 1:
-                codes = keep.tile([P, 2 * BANK], U32, name="wbf1", align_bytes=64)
+                codes = placed.tile([P, 2 * BANK], U32, name="even", align_bytes=64, offset=EVEN_AT)
                 quantize_z(0, (0, 1), first_pass[0], codes[:], keep, "zs5")
-        last_banks = [open_with_wall(last, c, spare_bank(c)) for c in range(CHUNKS)]
-        grow(last, nc.vector, BANK)
-        for step in range(CHUNKS + 2):
+        rows = keep.tile([P, 8 * BANK], F32, name="tabw", align_bytes=64)
+        results = [rows[:, BANK * i : BANK * i + BANK] for i in range(8)]
+        for i in range(2):
+            rows = keep.tile([P, 2 * BANK], F32, name="z_t%d" % i, align_bytes=64)
+            results.extend((rows[:, :BANK], rows[:, BANK:]))
+        products = []
+        for step in range(CHUNKS + 3):
             if step < CHUNKS:
-                add_product(last, step, last_banks[step])
+                cols = slice(BANK * step, BANK * step + BANK)
+                products.append(two.tile([P, BANK], F32, name="product"))
+                nc.vector.tensor_tensor(products[step][:], growth[:, cols], page_a[:, cols], MULT)
             if 1 <= step <= CHUNKS:
-                codes = keep.tile([P, BANK], U32, name="zc%d" % step, align_bytes=64)
-                quantize_z(1, (step - 1,), regroup_chunks(1, (step - 1,)), codes[:], keep, "zs%d" % step)
-            if step >= 2:
-                project(step - 2)
+                c = step - 1
+                cols = slice(BANK * c, BANK * c + BANK)
+                high = planes[c][:, BANK:].bitcast(BF16).rearrange("p (m e) -> p m e", e=2)[:, :, 1]
+                nc.vector.tensor_tensor(high, products[c][:], walls[last][:, cols], ADD)
+                if c % 2 == 0:
+                    grouped = two.tile([P, 8 * BANK], BF16, name="grouped", align_bytes=64)
+                woven = grouped[:, 4 * BANK * (c % 2) : 4 * BANK * (c % 2 + 1)]
+                nc.scalar.copy(
+                    out=woven.bitcast(F32).rearrange("p (m u) -> p m u", u=2),
+                    in_=planes[c].rearrange("p (u m) -> p m u", u=2),
+                )
+                first_pass[2 + c] = woven
+            if 2 <= step <= CHUNKS + 1:
+                c = step - 2
+                codes = keep.tile([P, BANK], U32, name="zc%d" % c, align_bytes=64)
+                quantize_z(1, (c,), first_pass[2 + c], codes[:], keep, "zs%d" % (c + 1))
+            if step >= 3:
+                c = step - 3
+                project(c, results[N // P * c : N // P * (c + 1)])

@@ -25,9 +25,9 @@ SLICES = H // P
 PASSES = H // 512
 CHUNKS = T2 // BANK
 EVEN_AT = BANK + 8 * T2
+SCALAR_WEAVES = (192, 256, 128, 0)
 W1_CHUNKS = ((0, 256), (256, 512), (512, 1024))
 W3_CHUNKS = ((), ((0, 0, 256),), ((0, 256, 384), (1, 0, 384)))
-PAIR_TAGS = ("raw0", "wbf0", "pairs2", "pairs3")
 
 
 def tile_list_cave_wall_growth_kernel(
@@ -47,7 +47,7 @@ def tile_list_cave_wall_growth_kernel(
             return held.tile([P, BANK], F32, name=("gap", "wide")[i % 8 // 2])
 
         def lane_rows(rows, t):
-            return rows.rearrange("(q t i) n -> t q i n", t=4, i=8)[t]
+            return rows.rearrange("(b t i) n -> t b i n", t=4, i=2)[t]
 
         def slice_rows(matrix, s):
             return matrix[P * s : P * s + P, :] if s < 4 else lane_rows(matrix[512:, :], s - 4)
@@ -64,6 +64,7 @@ def tile_list_cave_wall_growth_kernel(
         w2s = keep.tile([P, H], U8, name="w2s", align_bytes=64)
         wg = keep.tile([P, 2 * S], F32, name="wg", align_bytes=64)
         ident = keep.tile([P, P], F32, name="ident")
+        ident_bf = keep.tile([P, P], BF16, name="ident_bf")
         page_a = keep.tile([P, T2], F32, name="page_a")
         page_b = [keep.tile([P, T2], F32, name="page_b%d" % i) for i in range(2)]
 
@@ -103,10 +104,10 @@ def tile_list_cave_wall_growth_kernel(
                     for planes in (slice(0, 2), slice(2, 4)) if i == 0 else (slice(0, 4),):
                         nc.sync.dma_start(out=raw[:, planes, :], in_=dealt[:, planes, :])
                 if lo == 512 and c0 == 0:
-                    dealt = raw.rearrange("p j (q t h i) -> p t q h j i", t=4, h=2, i=4)
+                    dealt = raw.rearrange("p j (b t i) -> p t b j i", t=4, i=2)
                     for t in range(4):
                         nc.scalar.copy(
-                            out=grouped[:, 512 * t : 512 * t + 512].rearrange("p (q h i j) -> p q h j i", h=2, i=4, j=4),
+                            out=grouped[:, 512 * t : 512 * t + 512].rearrange("p (b i j) -> p b j i", i=2, j=4),
                             in_=dealt[:, t],
                         )
                 else:
@@ -118,10 +119,14 @@ def tile_list_cave_wall_growth_kernel(
         w2s_lanes = keep.tile([P, H // 2], U8, name="w2s_lanes", align_bytes=64)
 
         def deal_w2():
-            for dealt, packed in ((w2_lanes[:], w2w[:, H:]), (w2s_lanes[:], w2s[:, H // 2 :])):
+            nc.gpsimd.tensor_copy(
+                w2_lanes[:].bitcast(I32).rearrange("p (t b) -> p t b", t=4),
+                w2w[:, H:].bitcast(I32).rearrange("p (b t) -> p t b", t=4),
+            )
+            for t in range(4):
                 nc.gpsimd.tensor_copy(
-                    dealt.bitcast(I32).rearrange("p (t q w) -> p t q w", t=4, q=16),
-                    packed.bitcast(I32).rearrange("p (q t w) -> p t q w", t=4, q=16),
+                    w2s_lanes[:, P * t : P * t + P].rearrange("p (b i) -> p b i", i=2),
+                    w2s[:, H // 2 :].rearrange("p (b t i) -> p t b i", t=4, i=2)[:, t],
                 )
 
         def quantize_weights(i, grouped, tag):
@@ -261,9 +266,8 @@ def tile_list_cave_wall_growth_kernel(
                     in_=bank[:].rearrange("m (g q u e) -> m u g q e", g=4, u=2, e=2),
                 )
             else:
-                if s == 4:
-                    z_t[1, c] = keep.tile([P, 2 * BANK], BF16, name=PAIR_TAGS[c], align_bytes=64)
-                nc.scalar.copy(out=z_t[1, c][:].rearrange("m (x e) -> m x e", e=2)[:, :, s % 2], in_=bank[:])
+                z_t[1, c] = keep.tile([P, BANK], BF16, name="lane_t%d" % c, align_bytes=64)
+                nc.scalar.copy(out=z_t[1, c][:], in_=bank[:])
 
         def regroup_chunks(chunks):
             grouped = two.tile([P, 8 * BANK], BF16, name="grouped", align_bytes=64)
@@ -285,16 +289,15 @@ def tile_list_cave_wall_growth_kernel(
 
         planes = {}
 
-        def turn_pairs(u):
+        def turn_lane(t):
             for c in range(CHUNKS):
-                if u == 0 and c % 2 == 0:
-                    both = keep.tile([P, 4 * BANK], F32, name=("raw1", "wg")[c // 2], align_bytes=64)
-                    planes[c], planes[c + 1] = both[:, : 2 * BANK], both[:, 2 * BANK :]
-                words = z_t[1, c][:].bitcast(F32)
-                bank = next_bank()
+                if t == 0 and c % 2 == 0:
+                    both = keep.tile([P, 8 * BANK], BF16, name=("raw1", "wg")[c // 2], align_bytes=64)
+                    planes[c], planes[c + 1] = both[:, : 4 * BANK], both[:, 4 * BANK :]
+                bank = psum.tile([P, BANK], BF16, name="bank")
                 for g in range(4):
-                    nc.tensor.transpose(bank[:, P * g : P * g + P], words[:, P * g : P * g + P], ident[:])
-                nc.scalar.copy(out=planes[c][:, BANK * u : BANK * u + BANK], in_=bank[:])
+                    nc.tensor.transpose(bank[:, P * g : P * g + P], z_t[1, c][:, P * g : P * g + P], ident_bf[:])
+                nc.scalar.copy(out=planes[c][:, BANK * t : BANK * t + BANK], in_=bank[:])
 
         def quantize_z(b, chunks, grouped, codes, pool, tag):
             n = len(chunks)
@@ -314,7 +317,7 @@ def tile_list_cave_wall_growth_kernel(
                         rhs=zq[b, c][0].bitcast(FP8X4), rhs_scale=zq[b, c][1], start=(b == 0), stop=(b == PASSES - 1),
                     )
                 result = rows[nb]
-                copy = nc.vector.tensor_copy if nb == 1 and c >= 1 or nb == 0 and c == CHUNKS - 1 else nc.scalar.copy
+                copy = nc.vector.tensor_copy if nb == 1 and c == CHUNKS - 1 else nc.scalar.copy
                 copy(out=result, in_=bank[:])
                 nc.sync.dma_start(out=out[P * nb : P * nb + P, BANK * c : BANK * c + BANK], in_=result)
 
@@ -333,6 +336,7 @@ def tile_list_cave_wall_growth_kernel(
         load_scale_rows(nc.sync, tabs, tab_scales[0])
         nc.vector.memset(page_a[:], 0.0)
         make_identity(nc, ident[:])
+        make_identity(nc, ident_bf[:])
         nc.sync.dma_start(out=wg[:, halves[0]], in_=wg1[:, halves[0]])
         for page in page_b:
             nc.gpsimd.memset(page[:], 0.0)
@@ -387,19 +391,18 @@ def tile_list_cave_wall_growth_kernel(
             if s + 2 <= last:
                 load_given(s + 2)
             load_wall(s)
-            if s == last:
-                turn_pairs(0)
             form_z(s - 1)
             if s + 1 <= last:
                 rate_scores(s + 1)
                 weigh_slice(s + 1, gap)
             exponentiate(s, S if s < last else BANK)
+            if s >= 5:
+                turn_lane(s - 5)
             if s in (4, 5):
                 first_pass[s - 4] = regroup_chunks((2 * s - 8, 2 * s - 7))
             if s == last:
                 codes = keep.tile([P, 2 * BANK], U32, name="wbf2", align_bytes=64)
                 quantize_z(0, (2, 3), first_pass[1], codes[:], keep, "zs0")
-                turn_pairs(1)
             if s < last:
                 scatter_source(s, slice(0, S))
             else:
@@ -414,29 +417,31 @@ def tile_list_cave_wall_growth_kernel(
         for i in range(2):
             rows = keep.tile([P, 2 * BANK], F32, name="z_t%d" % i, align_bytes=64)
             results.extend((rows[:, :BANK], rows[:, BANK:]))
-        products = []
-        for step in range(CHUNKS + 3):
+        def weave(copy, c, woven, lo, hi):
+            copy(
+                out=woven[:, 4 * lo : 4 * hi].rearrange("p (c i t) -> p c t i", i=4, t=4),
+                in_=planes[c].rearrange("p (t c i) -> p c t i", t=4, i=4)[:, lo // 4 : hi // 4],
+            )
+
+        woven = {}
+        for step in range(CHUNKS + 2):
             if step < CHUNKS:
-                cols = slice(BANK * step, BANK * step + BANK)
-                products.append(two.tile([P, BANK], F32, name="product"))
-                nc.vector.tensor_tensor(products[step][:], growth[:, cols], page_a[:, cols], MULT)
-            if 1 <= step <= CHUNKS:
-                c = step - 1
+                c = step
                 cols = slice(BANK * c, BANK * c + BANK)
-                high = planes[c][:, BANK:].bitcast(BF16).rearrange("p (m e) -> p m e", e=2)[:, :, 1]
-                nc.vector.tensor_tensor(high, products[c][:], walls[last][:, cols], ADD)
+                part = keep.tile([P, BANK], F32, name="lane_t3", align_bytes=64)
+                nc.vector.tensor_tensor(part[:], growth[:, cols], page_a[:, cols], MULT)
+            if 1 <= step <= CHUNKS:
+                codes = keep.tile([P, BANK], U32, name="zc%d" % (step - 1), align_bytes=64)
+                quantize_z(1, (step - 1,), woven[step - 1], codes[:], keep, "zs%d" % step)
+            if step < CHUNKS:
+                nc.vector.tensor_tensor(planes[c][:, 3 * BANK :], part[:], walls[last][:, cols], ADD)
                 if c % 2 == 0:
                     grouped = two.tile([P, 8 * BANK], BF16, name="grouped", align_bytes=64)
-                woven = grouped[:, 4 * BANK * (c % 2) : 4 * BANK * (c % 2 + 1)]
-                nc.scalar.copy(
-                    out=woven.bitcast(F32).rearrange("p (m u) -> p m u", u=2),
-                    in_=planes[c].rearrange("p (u m) -> p m u", u=2),
-                )
-                first_pass[2 + c] = woven
-            if 2 <= step <= CHUNKS + 1:
-                c = step - 2
-                codes = keep.tile([P, BANK], U32, name="zc%d" % c, align_bytes=64)
-                quantize_z(1, (c,), first_pass[2 + c], codes[:], keep, "zs%d" % (c + 1))
-            if step >= 3:
-                c = step - 3
-                project(c, results[N // P * c : N // P * (c + 1)])
+                woven[c] = grouped[:, 4 * BANK * (c % 2) : 4 * BANK * (c % 2 + 1)]
+                split = SCALAR_WEAVES[c]
+                if split > 0:
+                    weave(nc.scalar.copy, c, woven[c], 0, split)
+                if split < BANK:
+                    weave(nc.vector.tensor_copy, c, woven[c], split, BANK)
+            if step >= 1 and step <= CHUNKS:
+                project(step - 1, results[N // P * (step - 1) : N // P * step])

@@ -25,7 +25,8 @@ SLICES = H // P
 PASSES = H // 512
 CHUNKS = T2 // BANK
 EVEN_AT = BANK + 8 * T2
-SCALAR_WEAVES = (192, 256, 128, 0)
+PIECES = ((0, 256, 128, 0), (256, 512, 256, 0), (512, 1024, 320, 0), (1024, 1536, 128, 1), (1536, 1792, 0, 1), (1792, 2048, 0, 2))
+PART_TAGS = ("lane_t3", "lane_t2")
 W1_CHUNKS = ((0, 256), (256, 512), (512, 1024))
 W3_CHUNKS = ((), ((0, 0, 256),), ((0, 256, 384), (1, 0, 384)))
 
@@ -152,6 +153,7 @@ def tile_list_cave_wall_growth_kernel(
         gaps = {}
 
         weights = {}
+        early_gap = keep.tile([P, S], F32, name="last_source")
         eqs = {}
         weighted = {}
 
@@ -204,14 +206,11 @@ def tile_list_cave_wall_growth_kernel(
                     start=(opens and g == 0), stop=(not opens and g == 3), is_transpose=True,
                 )
 
-        def weigh(s, cols):
-            nc.gpsimd.tensor_tensor(staged[s][:, cols], staged[s][:, cols], weights[s][:, cols], MULT)
-
         def score_sources(s):
             stage(s)
             for h in range(2):
                 nc.scalar.copy(out=sources[s][:, halves[h]], in_=source_scores(s, h, held.tile([P, BANK], F32, name="wide"))[:])
-            gap = gaps[s] if s == 1 else growth[:, :S]
+            gap = early_gap[:] if s == 1 else growth[:, :S]
             nc.gpsimd.tensor_tensor(gap, sources[s], eqs[s], SUB)
             return gap
 
@@ -220,6 +219,10 @@ def tile_list_cave_wall_growth_kernel(
             nc.gpsimd.tensor_tensor(weighted[s], gap, weights[s][:, S:], MULT)
             if s < last:
                 nc.gpsimd.tensor_tensor(sources[s], sources[s], weights[s][:, :S], MULT)
+            else:
+                for h in range(2):
+                    nc.scalar.copy(out=gaps[s][:, halves[h]], in_=rates[s, h][:])
+                nc.gpsimd.tensor_tensor(gaps[s], gaps[s], weighted[s], MULT)
 
         def scatter_source(s, cols):
             nc.vector.tensor_copy(page_a[:].indirect(idx2[:, cols.start // 16 : cols.stop // 16]), sources[s][:, cols])
@@ -228,7 +231,7 @@ def tile_list_cave_wall_growth_kernel(
             sink = gaps[s]
             if s == 1:
                 sink = placed.tile([P, S], F32, name="sink1", align_bytes=64, offset=EVEN_AT + 8 * S)[:]
-            for h in range(2):
+            for h in range(2 if s < last else 0):
                 nc.vector.tensor_tensor(sink[:, halves[h]], rates[s, h][:], weighted[s][:, halves[h]], MULT)
             nc.vector.tensor_copy(page_b[s % 2][:].indirect(idx3[:]), sink)
 
@@ -307,19 +310,21 @@ def tile_list_cave_wall_growth_kernel(
                 zq[b, c] = (codes[:, BANK * i : BANK * (i + 1)], scales[:, BANK * i : BANK * (i + 1)])
 
 
-        def project(c, rows):
+        def project(turn, lo, hi, second, rows):
+            c, c0 = divmod(lo, BANK)
+            first = [x[:, c0 : c0 + hi - lo] for x in zq[0, c]]
             for nb in range(N // P):
-                bank = spare_bank(N // P * c + nb)
-                for b in range(PASSES):
+                bank = spare_bank(N // P * turn + nb)
+                for b, (z_codes, z_scales) in enumerate((first, second)):
                     codes, scales = w3q[N // P * b + nb]
                     nc.tensor.matmul_mx(
-                        out=bank[:], lhsT=codes, lhsT_scale=scales,
-                        rhs=zq[b, c][0].bitcast(FP8X4), rhs_scale=zq[b, c][1], start=(b == 0), stop=(b == PASSES - 1),
+                        out=bank[:, : hi - lo], lhsT=codes, lhsT_scale=scales,
+                        rhs=z_codes.bitcast(FP8X4), rhs_scale=z_scales, start=(b == 0), stop=(b == PASSES - 1),
                     )
-                result = rows[nb]
-                copy = nc.vector.tensor_copy if nb == 1 and c == CHUNKS - 1 else nc.scalar.copy
-                copy(out=result, in_=bank[:])
-                nc.sync.dma_start(out=out[P * nb : P * nb + P, BANK * c : BANK * c + BANK], in_=result)
+                result = rows[nb][:, c0 : c0 + hi - lo]
+                copy = nc.vector.tensor_copy if nb < PIECES[turn][3] else nc.scalar.copy
+                copy(out=result, in_=bank[:, : hi - lo])
+                nc.sync.dma_start(out=out[P * nb : P * nb + P, lo:hi], in_=result)
 
         first_pass = {}
 
@@ -333,7 +338,7 @@ def tile_list_cave_wall_growth_kernel(
         quantize_weights(0, group_weights(0, keep.tile([P, 4 * 256], F32, name="raw0", align_bytes=64)), "w1c")
         for c0 in range(0, T, T // 4):
             nc.sync.dma_start(out=tabw[:].bitcast(I32)[:, c0 : c0 + T // 4], in_=table[:, c0 : c0 + T // 4])
-        load_scale_rows(nc.sync, tabs, tab_scales[0])
+        load_scale_rows(nc.scalar, tabs, tab_scales[0])
         nc.vector.memset(page_a[:], 0.0)
         make_identity(nc, ident[:])
         make_identity(nc, ident_bf[:])
@@ -349,14 +354,17 @@ def tile_list_cave_wall_growth_kernel(
         nc.sync.dma_start(out=wg[:, S:], in_=wg2)
         nc.sync.dma_start(out=w2w[:].bitcast(I32), in_=w2_words[0].bitcast(I32))
         first = [source_scores(0, h, next_bank()) for h in range(2)]
-        nc.vector.tensor_tensor(staged[0][:, halves[0]], first[0][:], wg[:, halves[0]], MULT)
+        scores = sources[0]
+        sources[0] = keep.tile([P, S], F32, name="first_source")[:]
+        nc.vector.tensor_tensor(sources[0][:, halves[0]], first[0][:], wg[:, halves[0]], MULT)
         scatter_source(0, halves[0])
-        nc.scalar.copy(out=staged[0][:, halves[1]], in_=first[1][:])
-        for h in range(2):
-            nc.vector.tensor_tensor(gaps[0][:, halves[h]], first[h][:], eqs[0][:, halves[h]], SUB)
-        weigh(0, halves[1])
+        for h in (1, 0):
+            nc.scalar.copy(out=scores[:, halves[h]], in_=first[h][:])
+        nc.gpsimd.tensor_tensor(sources[0][:, halves[1]], scores[:, halves[1]], wg[:, halves[1]], MULT)
         scatter_source(0, halves[1])
-        weigh(0, slice(S, 2 * S))
+        nc.gpsimd.tensor_tensor(early_gap[:], scores, eqs[0], SUB)
+        for h in range(2):
+            nc.gpsimd.tensor_tensor(gaps[0][:, halves[h]], early_gap[:, halves[h]], wg[:, S + BANK * h : S + BANK * h + BANK], MULT)
         weighted[0] = gaps[0]
         rate_scores(0)
         load_given(1)
@@ -417,31 +425,38 @@ def tile_list_cave_wall_growth_kernel(
         for i in range(2):
             rows = keep.tile([P, 2 * BANK], F32, name="z_t%d" % i, align_bytes=64)
             results.extend((rows[:, :BANK], rows[:, BANK:]))
-        def weave(copy, c, woven, lo, hi):
+
+        def weave(copy, woven, lo, hi):
+            c, c0 = divmod(lo, BANK)
             copy(
-                out=woven[:, 4 * lo : 4 * hi].rearrange("p (c i t) -> p c t i", i=4, t=4),
-                in_=planes[c].rearrange("p (t c i) -> p c t i", t=4, i=4)[:, lo // 4 : hi // 4],
+                out=woven.rearrange("p (c i t) -> p c t i", i=4, t=4),
+                in_=planes[c].rearrange("p (t c i) -> p c t i", t=4, i=4)[:, c0 // 4 : (c0 + hi - lo) // 4],
             )
 
+        last_codes = keep.tile([P, T2], U32, name="last_codes", align_bytes=64)
+        last_scales = keep.tile([P, T2], U8, name="last_scales", align_bytes=64)
         woven = {}
-        for step in range(CHUNKS + 2):
-            if step < CHUNKS:
-                c = step
-                cols = slice(BANK * c, BANK * c + BANK)
-                part = keep.tile([P, BANK], F32, name="lane_t3", align_bytes=64)
-                nc.vector.tensor_tensor(part[:], growth[:, cols], page_a[:, cols], MULT)
-            if 1 <= step <= CHUNKS:
-                codes = keep.tile([P, BANK], U32, name="zc%d" % (step - 1), align_bytes=64)
-                quantize_z(1, (step - 1,), woven[step - 1], codes[:], keep, "zs%d" % step)
-            if step < CHUNKS:
-                nc.vector.tensor_tensor(planes[c][:, 3 * BANK :], part[:], walls[last][:, cols], ADD)
-                if c % 2 == 0:
+        for step in range(len(PIECES) + 1):
+            if step < len(PIECES):
+                lo, hi, split = PIECES[step][:3]
+                c, c0 = divmod(lo, BANK)
+                part = keep.tile([P, hi - lo], F32, name=PART_TAGS[step % len(PART_TAGS)], align_bytes=64)
+                nc.vector.tensor_tensor(part[:], growth[:, lo:hi], page_a[:, lo:hi], MULT)
+            if step >= 1:
+                done = slice(*PIECES[step - 1][:2])
+                nc.vector.quantize_mx(
+                    out=last_codes[:, done].bitcast(FP8X4), scales=last_scales[:, done], in_=woven[step - 1]
+                )
+            if step < len(PIECES):
+                lane = planes[c][:, 3 * BANK + c0 : 3 * BANK + c0 + hi - lo]
+                nc.vector.tensor_tensor(lane, part[:], walls[last][:, lo:hi], ADD)
+                if lo % S == 0:
                     grouped = two.tile([P, 8 * BANK], BF16, name="grouped", align_bytes=64)
-                woven[c] = grouped[:, 4 * BANK * (c % 2) : 4 * BANK * (c % 2 + 1)]
-                split = SCALAR_WEAVES[c]
+                woven[step] = grouped[:, 4 * (lo % S) : 4 * (lo % S + hi - lo)]
                 if split > 0:
-                    weave(nc.scalar.copy, c, woven[c], 0, split)
-                if split < BANK:
-                    weave(nc.vector.tensor_copy, c, woven[c], split, BANK)
-            if step >= 1 and step <= CHUNKS:
-                project(step - 1, results[N // P * (step - 1) : N // P * step])
+                    weave(nc.scalar.copy, woven[step][:, : 4 * split], lo, lo + split)
+                if split < hi - lo:
+                    weave(nc.vector.tensor_copy, woven[step][:, 4 * split :], lo + split, hi)
+            if step >= 1:
+                first = N // P * (done.start // BANK)
+                project(step - 1, done.start, done.stop, (last_codes[:, done], last_scales[:, done]), results[first : first + N // P])

@@ -25,7 +25,7 @@ SLICES = H // P
 PASSES = H // 512
 CHUNKS = T2 // BANK
 EVEN_AT = BANK + 8 * T2
-PIECES = ((0, 256, 128, 0), (256, 512, 256, 0), (512, 1024, 320, 0), (1024, 1536, 128, 1), (1536, 1792, 0, 1), (1792, 2048, 0, 2))
+PIECES = ((0, 256), (256, 512), (512, 1024), (1024, 1536), (1536, 1792), (1792, 2048))
 PART_TAGS = ("lane_t3", "lane_t2")
 W1_CHUNKS = ((0, 256), (256, 512), (512, 1024))
 W3_CHUNKS = ((), ((0, 0, 256),), ((0, 256, 384), (1, 0, 384)))
@@ -142,7 +142,8 @@ def tile_list_cave_wall_growth_kernel(
             for c0 in range(0, width, P):
                 (w1q if c0 < hi - lo else w3q).append((codes[:, c0 : c0 + P].bitcast(FP8X4), scales[:, c0 : c0 + P]))
 
-        vw = [keep.tile([P, BANK], U32, name="vw%d" % h, align_bytes=64) for h in range(2)]
+        words = keep.tile([P, S], U32, name="words", align_bytes=64)
+        vw = [words[:, BANK * h : BANK * h + BANK] for h in range(2)]
         vs = [keep.tile([P, BANK], U8, name="vs%d" % h, align_bytes=64) for h in range(2)]
         halves = [slice(BANK * h, BANK * h + BANK) for h in range(2)]
         last = SLICES - 1
@@ -184,7 +185,7 @@ def tile_list_cave_wall_growth_kernel(
         def source_scores(s, h, bank):
             nc.tensor.matmul_mx(
                 out=bank[:], lhsT=w1q[s][0], lhsT_scale=w1q[s][1],
-                rhs=vw[h][:].bitcast(FP8X4), rhs_scale=vs[h][:], start=True, stop=True,
+                rhs=vw[h].bitcast(FP8X4), rhs_scale=vs[h][:], start=True, stop=True,
             )
             return bank
 
@@ -196,7 +197,7 @@ def tile_list_cave_wall_growth_kernel(
                 nc.tensor.matmul_mx(
                     out=rates[s, h][:], lhsT=words[:, 2 * c0 : 2 * c0 + 2 * P].bitcast(FP4X4),
                     lhsT_scale=scales[:, c0 : c0 + P],
-                    rhs=vw[h][:].bitcast(FP8X4), rhs_scale=vs[h][:], start=True, stop=True,
+                    rhs=vw[h].bitcast(FP8X4), rhs_scale=vs[h][:], start=True, stop=True,
                 )
 
         def add_transposed(bank, rows, opens):
@@ -322,7 +323,7 @@ def tile_list_cave_wall_growth_kernel(
                         rhs=z_codes.bitcast(FP8X4), rhs_scale=z_scales, start=(b == 0), stop=(b == PASSES - 1),
                     )
                 result = rows[nb][:, c0 : c0 + hi - lo]
-                copy = nc.vector.tensor_copy if nb < PIECES[turn][3] else nc.scalar.copy
+                copy = nc.vector.tensor_copy if nb < turn - 3 else nc.scalar.copy
                 copy(out=result, in_=bank[:, : hi - lo])
                 nc.sync.dma_start(out=out[P * nb : P * nb + P, lo:hi], in_=result)
 
@@ -345,8 +346,8 @@ def tile_list_cave_wall_growth_kernel(
         nc.sync.dma_start(out=wg[:, halves[0]], in_=wg1[:, halves[0]])
         for page in page_b:
             nc.gpsimd.memset(page[:], 0.0)
+        nc.vector.tensor_copy(words[:], tabw[:].indirect(idx[:]))
         for h in range(2):
-            nc.vector.tensor_copy(vw[h][:], tabw[:].indirect(idx[:, 32 * h : 32 * h + 32]))
             nc.vector.tensor_copy(vs[h][:], tabs[:].indirect(idx[:, 32 * h : 32 * h + 32]))
         stage(0)
         load_given(0)
@@ -438,12 +439,13 @@ def tile_list_cave_wall_growth_kernel(
         woven = {}
         for step in range(len(PIECES) + 1):
             if step < len(PIECES):
-                lo, hi, split = PIECES[step][:3]
+                lo, hi = PIECES[step]
+                split = (hi - lo) // 2 if hi <= 3 * BANK else 0
                 c, c0 = divmod(lo, BANK)
                 part = keep.tile([P, hi - lo], F32, name=PART_TAGS[step % len(PART_TAGS)], align_bytes=64)
                 nc.vector.tensor_tensor(part[:], growth[:, lo:hi], page_a[:, lo:hi], MULT)
             if step >= 1:
-                done = slice(*PIECES[step - 1][:2])
+                done = slice(*PIECES[step - 1])
                 nc.vector.quantize_mx(
                     out=last_codes[:, done].bitcast(FP8X4), scales=last_scales[:, done], in_=woven[step - 1]
                 )

@@ -154,7 +154,6 @@ def tile_list_cave_wall_growth_kernel(
         gaps = {}
 
         weights = {}
-        early_gap = keep.tile([P, S], F32, name="last_source")
         eqs = {}
         weighted = {}
 
@@ -211,7 +210,7 @@ def tile_list_cave_wall_growth_kernel(
             stage(s)
             for h in range(2):
                 nc.scalar.copy(out=sources[s][:, halves[h]], in_=source_scores(s, h, held.tile([P, BANK], F32, name="wide"))[:])
-            gap = early_gap[:] if s == 1 else growth[:, :S]
+            gap = gaps[s] if s == 1 else growth[:, :S]
             nc.gpsimd.tensor_tensor(gap, sources[s], eqs[s], SUB)
             return gap
 
@@ -339,7 +338,7 @@ def tile_list_cave_wall_growth_kernel(
         quantize_weights(0, group_weights(0, keep.tile([P, 4 * 256], F32, name="raw0", align_bytes=64)), "w1c")
         for c0 in range(0, T, T // 4):
             nc.sync.dma_start(out=tabw[:].bitcast(I32)[:, c0 : c0 + T // 4], in_=table[:, c0 : c0 + T // 4])
-        load_scale_rows(nc.scalar, tabs, tab_scales[0])
+        load_scale_rows(nc.sync, tabs, tab_scales[0])
         nc.vector.memset(page_a[:], 0.0)
         make_identity(nc, ident[:])
         make_identity(nc, ident_bf[:])
@@ -355,17 +354,14 @@ def tile_list_cave_wall_growth_kernel(
         nc.sync.dma_start(out=wg[:, S:], in_=wg2)
         nc.sync.dma_start(out=w2w[:].bitcast(I32), in_=w2_words[0].bitcast(I32))
         first = [source_scores(0, h, next_bank()) for h in range(2)]
-        scores = sources[0]
-        sources[0] = keep.tile([P, S], F32, name="first_source")[:]
         nc.vector.tensor_tensor(sources[0][:, halves[0]], first[0][:], wg[:, halves[0]], MULT)
         scatter_source(0, halves[0])
-        for h in (1, 0):
-            nc.scalar.copy(out=scores[:, halves[h]], in_=first[h][:])
-        nc.gpsimd.tensor_tensor(sources[0][:, halves[1]], scores[:, halves[1]], wg[:, halves[1]], MULT)
-        scatter_source(0, halves[1])
-        nc.gpsimd.tensor_tensor(early_gap[:], scores, eqs[0], SUB)
+        nc.scalar.copy(out=sources[0][:, halves[1]], in_=first[1][:])
         for h in range(2):
-            nc.gpsimd.tensor_tensor(gaps[0][:, halves[h]], early_gap[:, halves[h]], wg[:, S + BANK * h : S + BANK * h + BANK], MULT)
+            nc.vector.tensor_tensor(gaps[0][:, halves[h]], first[h][:], eqs[0][:, halves[h]], SUB)
+        nc.gpsimd.tensor_tensor(sources[0][:, halves[1]], sources[0][:, halves[1]], wg[:, halves[1]], MULT)
+        scatter_source(0, halves[1])
+        nc.gpsimd.tensor_tensor(gaps[0], gaps[0], wg[:, S:], MULT)
         weighted[0] = gaps[0]
         rate_scores(0)
         load_given(1)

@@ -25,6 +25,7 @@ SLICES = H // P
 PASSES = H // 512
 CHUNKS = T2 // BANK
 EVEN_AT = BANK + 8 * T2
+ODD_AT = EVEN_AT + 12 * S
 PIECES = ((0, 256), (256, 512), (512, 1024), (1024, 1536), (1536, 1792), (1792, 2048))
 PART_TAGS = ("lane_t3", "lane_t2")
 W1_CHUNKS = ((0, 256), (256, 512), (512, 1024))
@@ -89,8 +90,9 @@ def tile_list_cave_wall_growth_kernel(
             lo, hi = W1_CHUNKS[i]
             pieces = [(w1[:, lo:hi], False)]
             pieces.extend((w3[512 * b : 512 * b + 512, first:stop], b == 1) for b, first, stop in W3_CHUNKS[i])
-            if i == 1:
-                grouped = placed.tile([P, staging.shape[1]], BF16, name="wbf1", align_bytes=64, offset=EVEN_AT + 6 * S)
+            if i >= 1:
+                at = (EVEN_AT + 6 * S, ODD_AT + 4 * S)[i - 1]
+                grouped = placed.tile([P, staging.shape[1]], BF16, name="wbf%d" % i, align_bytes=64, offset=at)
             else:
                 grouped = keep.tile([P, staging.shape[1]], BF16, name="wbf%d" % i, align_bytes=64)
             c0 = 0
@@ -170,16 +172,16 @@ def tile_list_cave_wall_growth_kernel(
                         )
 
         def stage(s):
-            tag = "early%d" % s if s < 2 else "wbf2"
-            if s >= 2 and s % 2 == 0:
-                staged[s] = placed.tile([P, 2 * S], F32, name="even", align_bytes=64, offset=EVEN_AT)
-                sources[s], gaps[s] = staged[s][:, :S], staged[s][:, S:]
-            elif s < last:
-                staged[s] = keep.tile([P, 2 * S], F32, name=tag, align_bytes=64)
-                sources[s], gaps[s] = staged[s][:, :S], staged[s][:, S:]
-            else:
+            if s == last:
                 sources[s] = keep.tile([P, S], F32, name="last_source")[:]
-                gaps[s] = keep.tile([P, S], F32, name=tag, align_bytes=64)[:]
+                gaps[s] = placed.tile([P, S], F32, name="odd", align_bytes=64, offset=ODD_AT)[:]
+                return
+            if s < 2:
+                staged[s] = keep.tile([P, 2 * S], F32, name="early%d" % s, align_bytes=64)
+            else:
+                name, at = (("even", EVEN_AT), ("odd", ODD_AT))[s % 2]
+                staged[s] = placed.tile([P, 2 * S], F32, name=name, align_bytes=64, offset=at)
+            sources[s], gaps[s] = staged[s][:, :S], staged[s][:, S:]
 
         def source_scores(s, h, bank):
             nc.tensor.matmul_mx(
@@ -239,9 +241,18 @@ def tile_list_cave_wall_growth_kernel(
             for c0 in range(0, T2, width) if s in (0, last) else (S, 0):
                 nc.scalar.activation(out=growth[:, c0 : c0 + width], in_=page_b[s % 2][:, c0 : c0 + width], func=EXP)
 
-        def grow():
-            for cols in (slice(0, S), slice(S, T2)):
-                nc.gpsimd.tensor_tensor(product[:, cols], growth[:, cols], page_a[:, cols], MULT)
+        products = {}
+
+        def grow(s):
+            front = product[:, :S]
+            if s == 1:
+                front = placed.tile([P, S], F32, name="front1", offset=ODD_AT + 8 * S)[:]
+            if s == last - 1:
+                front = two.tile([P, S], F32, name="grouped", align_bytes=64)[:]
+            for i, half in enumerate((front, product[:, S:])):
+                cols = slice(S * i, S * i + S)
+                nc.gpsimd.tensor_tensor(half, growth[:, cols], page_a[:, cols], MULT)
+                products[s, 2 * i], products[s, 2 * i + 1] = half[:, :BANK], half[:, BANK:]
 
         walls = {}
 
@@ -257,7 +268,7 @@ def tile_list_cave_wall_growth_kernel(
             return bank
 
         def add_product(s, c, bank):
-            add_transposed(bank, product[:, BANK * c : BANK * c + BANK], False)
+            add_transposed(bank, products[s, c], False)
             round_z(s, c, bank)
 
         def round_z(s, c, bank):
@@ -374,7 +385,7 @@ def tile_list_cave_wall_growth_kernel(
                     add_product(s, c, open_with_wall(s, c, held.tile([P, BANK], F32, name="wide")))
                 else:
                     bank = held.tile([P, BANK], F32, name="gap")
-                    add_transposed(bank, product[:, BANK * c : BANK * c + BANK], True)
+                    add_transposed(bank, products[s, c], True)
                     add_transposed(bank, walls[s][:, BANK * c : BANK * c + BANK], False)
                     round_z(s, c, bank)
 
@@ -390,7 +401,7 @@ def tile_list_cave_wall_growth_kernel(
         exponentiate(0, S)
         for s in range(1, SLICES):
             scatter_sink(s)
-            grow()
+            grow(s - 1)
             if s + 1 <= last:
                 gap = score_sources(s + 1)
             if s + 2 <= last:
@@ -406,7 +417,7 @@ def tile_list_cave_wall_growth_kernel(
             if s in (4, 5):
                 first_pass[s - 4] = regroup_chunks((2 * s - 8, 2 * s - 7))
             if s == last:
-                codes = keep.tile([P, 2 * BANK], U32, name="wbf2", align_bytes=64)
+                codes = placed.tile([P, 2 * BANK], U32, name="odd", align_bytes=64, offset=ODD_AT)
                 quantize_z(0, (2, 3), first_pass[1], codes[:], keep, "zs0")
             if s < last:
                 scatter_source(s, slice(0, S))

@@ -22,14 +22,38 @@ EXP = mybir.ActivationFunctionType.Exp
 P = 128
 BANK = 512
 SLICES = H // P
-PASSES = H // 512
+LAST = SLICES - 1
 CHUNKS = T2 // BANK
-EVEN_AT = BANK + 8 * T2
-ODD_AT = EVEN_AT + 12 * S
+OUT_TILES = N // P
 PIECES = ((0, 256), (256, 512), (512, 1024), (1024, 1536), (1536, 1792), (1792, 2048))
-PART_TAGS = ("lane_t3", "lane_t2")
-W1_CHUNKS = ((0, 256), (256, 512), (512, 1024))
-W3_CHUNKS = ((), ((0, 0, 256),), ((0, 256, 384), (1, 0, 384)))
+VECTOR_WEAVES = (3, 4, 5)
+AHEAD = 3
+VECTOR_EMPTIES_FROM = 3
+
+
+def lay_out(areas):
+    starts, at = {}, 0
+    for name, size in areas:
+        starts[name] = at
+        at = at + size
+    return starts
+
+
+AT = lay_out(
+    (
+        ("words", 4 * S), ("bytes", S), ("w2w", 2 * H), ("w2s", H),
+        ("ident", 4 * P), ("page_a", 4 * T2), ("page_b", 8 * T2), ("growth", 4 * T2), ("product", 4 * T2),
+        ("scores", 4 * S), ("source", 8 * S), ("gain", 4 * S), ("sink", 8 * S), ("eq", 12 * S),
+        ("wall", 8 * T2), ("wg", 16 * S),
+        ("codes_a", 4 * 128), ("scales_a", 128), ("codes_b", 4 * 256), ("scales_b", 256), ("scales_c", 640),
+        ("scales_w3", 768),
+        ("table", 4 * T),
+        ("table_bytes", T), ("raw_a", 16 * 128), ("raw_b", 16 * 256), ("grouped_a", 8 * 128), ("grouped_b", 8 * 256),
+        ("dealt", 512), ("first_gain", 4 * S),
+        ("raw_w3", 16 * 768), ("raw_c", 16 * 640), ("grouped_c", 4 * T2), ("grouped_w3", 4 * T2),
+        ("turned", 8 * T2), ("codes_z", 4 * T2), ("scales_z", T2),
+    )
+)
 
 
 def tile_list_cave_wall_growth_kernel(
@@ -37,38 +61,43 @@ def tile_list_cave_wall_growth_kernel(
 ):
     nc = tc.nc
     with ExitStack() as ctx:
-        keep = ctx.enter_context(tc.tile_pool(name="keep", bufs=1))
-        two = ctx.enter_context(tc.tile_pool(name="two", bufs=2))
-        placed = ctx.enter_context(tc.tile_pool(name="placed", bufs=1))
-        psum = ctx.enter_context(tc.psum_pool(name="psum", bufs=4))
-        held = ctx.enter_context(tc.psum_pool(name="held", bufs=2))
+        lists = ctx.enter_context(tc.tile_pool(name="lists", bufs=1))
+        sbuf = ctx.enter_context(tc.tile_pool(name="sbuf", bufs=1))
+        psum = ctx.enter_context(tc.psum_pool(name="psum", bufs=2))
 
-        def spare_bank(i):
-            if i % 8 >= 4:
-                return next_bank()
-            return held.tile([P, BANK], F32, name=("gap", "wide")[i % 8 // 2])
+        def place(name, columns, dtype, area, skip=0):
+            return sbuf.tile([P, columns], dtype, name=name, align_bytes=64, offset=AT[area] + skip)
 
-        def lane_rows(rows, t):
-            return rows.rearrange("(b t i) n -> t b i n", t=4, i=2)[t]
+        def bank_of(ring):
+            return psum.tile([P, BANK], F32, name=ring)
+
+        def by_eights(rows):
+            return rows.rearrange("(b e) n -> b e n", e=8)
 
         def slice_rows(matrix, s):
-            return matrix[P * s : P * s + P, :] if s < 4 else lane_rows(matrix[512:, :], s - 4)
+            if s < 4:
+                return matrix[P * s : P * s + P, :]
+            dealt = by_eights(matrix[512:, :])
+            if s < 6:
+                return dealt[32 * (s - 4) : 32 * (s - 3), 0:4]
+            return dealt[:, 2 * s - 8 : 2 * s - 6]
 
-        def next_bank():
-            return psum.tile([P, BANK], F32, name="bank")
-
-        idx = keep.tile([P, S // 16], U16, name="idx")
-        idx2 = keep.tile([P, S // 16], U16, name="idx2")
-        idx3 = keep.tile([P, S // 16], U16, name="idx3")
-        tabw = keep.tile([P, T], U32, name="tabw", align_bytes=64)
-        tabs = keep.tile([P, T], U8, name="tabs")
-        w2w = keep.tile([P, 2 * H], U8, name="w2w", align_bytes=64)
-        w2s = keep.tile([P, H], U8, name="w2s", align_bytes=64)
-        wg = keep.tile([P, 2 * S], F32, name="wg", align_bytes=64)
-        ident = keep.tile([P, P], F32, name="ident")
-        ident_bf = keep.tile([P, P], BF16, name="ident_bf")
-        page_a = keep.tile([P, T2], F32, name="page_a")
-        page_b = [keep.tile([P, T2], F32, name="page_b%d" % i) for i in range(2)]
+        idx = lists.tile([P, S // 16], U16, name="idx")
+        idx2 = lists.tile([P, S // 16], U16, name="idx2")
+        idx3 = lists.tile([P, S // 16], U16, name="idx3")
+        tabw = place("tabw", T, U32, "table")
+        tabs = place("tabs", T, U8, "table_bytes")
+        w2w = place("w2w", 2 * H, U8, "w2w")
+        w2s = place("w2s", H, U8, "w2s")
+        ident = place("ident", P, F32, "ident")
+        page_a = place("page_a", T2, F32, "page_a")
+        page_b = [place("page_b%d" % i, T2, F32, "page_b", 4 * T2 * i) for i in range(2)]
+        scores = place("scores", S, F32, "scores")
+        source = [place("source%d" % i, S, F32, "source", 4 * S * i) for i in range(2)]
+        sink = [place("sink%d" % i, S, F32, "sink", 4 * S * i) for i in range(2)]
+        halves = [slice(BANK * h, BANK * h + BANK) for h in range(2)]
+        vw = [place("vw%d" % h, BANK, U32, "words", 4 * BANK * h) for h in range(2)]
+        vs = [place("vs%d" % h, BANK, U8, "bytes", BANK * h) for h in range(2)]
 
         def load_scale_rows(queue, plane, rows):
             for q in range(4):
@@ -76,130 +105,177 @@ def tile_list_cave_wall_growth_kernel(
                     out=plane[32 * q : 32 * q + 4, :].bitcast(I32), in_=rows[4 * q : 4 * q + 4, :].bitcast(I32)
                 )
 
-        def interleave(grouped, raw):
-            nc.scalar.copy(
-                out=grouped.rearrange("p (c i t) -> p c t i", i=4, t=4),
-                in_=raw.rearrange("p t (c i) -> p c t i", i=4),
-            )
+        def by_fours(rows):
+            return rows.rearrange("(p t) c -> p t c", t=4)
+
+        def interleave(grouped, raw, run):
+            nc.scalar.copy(out=grouped.rearrange("p (b c t) -> p b t c", c=run, t=4), in_=raw)
+
+        def plain_runs(raw):
+            return raw.rearrange("p (t b c) -> p b t c", t=4, c=4)
+
+        def group_w1(part, lo, hi):
+            raw = place("raw_" + part, 4 * (hi - lo), F32, "raw_" + part)
+            nc.sync.dma_start(out=raw[:].rearrange("p (t c) -> p t c", t=4), in_=by_fours(w1[:, lo:hi]))
+            grouped = place("grouped_" + part, 4 * (hi - lo), BF16, "grouped_" + part)
+            plain = min(hi, 512) - lo
+            planes = raw[:].rearrange("p (t c) -> p t c", t=4)
+            interleave(grouped[:, : 4 * plain], planes[:, :, :plain].rearrange("p t (b c) -> p b t c", c=4), 4)
+            if hi > 512:
+                dealt = planes[:, :, plain:].rearrange("p t (b e) -> p b t e", e=8)
+                c0 = 4 * plain
+                interleave(grouped[:, c0 : c0 + 1024], dealt[:, :, :, 0:4], 4)
+                interleave(grouped[:, c0 + 1024 : c0 + 1536], dealt[:, :, :, 4:6], 2)
+                interleave(grouped[:, c0 + 1536 :], dealt[:, :, :, 6:8], 2)
+            return grouped
+
+        def load_w3():
+            raw = place("raw_w3", 8 * N, F32, "raw_w3")
+            nc.sync.dma_start(out=raw[:, : 4 * N].rearrange("p (t c) -> p t c", t=4), in_=by_fours(w3[:512, :]))
+            dealt = by_eights(w3[512:, :])
+            nc.sync.dma_start(out=raw[:, 4 * N : 6 * N], in_=dealt[:, 0:4].rearrange("b (i t) n -> b i (t n)", i=2))
+            for t in (2, 3):
+                nc.sync.dma_start(out=raw[:, (4 + t) * N : (5 + t) * N], in_=dealt[:, 2 * t : 2 * t + 2])
+            return raw
+
+        def group_w3(raw):
+            grouped = place("grouped_w3", 8 * N, BF16, "grouped_w3")
+            for b in range(2):
+                cols = slice(4 * N * b, 4 * N * (b + 1))
+                interleave(grouped[:, cols], plain_runs(raw[:, cols]), 4)
+            return grouped
+
+        def quantize(name, grouped, cut, codes_at, scales_at):
+            width = grouped.shape[1] // 4
+            codes = place(name + "_codes", width, U32, *codes_at)
+            scales = place(name + "_scales", width, U8, *scales_at)
+            for c0 in range(0, width, cut):
+                cols = slice(c0, min(c0 + cut, width))
+                nc.vector.quantize_mx(
+                    out=codes[:, cols].bitcast(FP8X4), scales=scales[:, cols], in_=grouped[:, 4 * cols.start : 4 * cols.stop]
+                )
+            return codes, scales
+
+        def stationary(codes, scales):
+            return [(codes[:, c0 : c0 + P].bitcast(FP8X4), scales[:, c0 : c0 + P]) for c0 in range(0, codes.shape[1], P)]
 
         w1q = []
 
-        w3q = []
+        def quantize_w1(part, grouped):
+            w1q.extend(stationary(*quantize("w1" + part, grouped, 512, ("raw_c" if part == "c" else "codes_" + part,), ("scales_" + part,))))
 
-        def group_weights(i, staging):
-            lo, hi = W1_CHUNKS[i]
-            pieces = [(w1[:, lo:hi], False)]
-            pieces.extend((w3[512 * b : 512 * b + 512, first:stop], b == 1) for b, first, stop in W3_CHUNKS[i])
-            if i >= 1:
-                at = (EVEN_AT + 6 * S, ODD_AT + 4 * S)[i - 1]
-                grouped = placed.tile([P, staging.shape[1]], BF16, name="wbf%d" % i, align_bytes=64, offset=at)
-            else:
-                grouped = keep.tile([P, staging.shape[1]], BF16, name="wbf%d" % i, align_bytes=64)
-            c0 = 0
-            for rows, by_lanes in pieces:
-                cols = slice(4 * c0, 4 * (c0 + rows.shape[1]))
-                raw = staging[:, cols].rearrange("p (t c) -> p t c", t=4)
-                if by_lanes:
-                    for t in range(4):
-                        nc.sync.dma_start(out=raw[:, t, :], in_=lane_rows(rows, t))
-                else:
-                    dealt = rows.rearrange("(p t) c -> p t c", t=4)
-                    for planes in (slice(0, 2), slice(2, 4)) if i == 0 else (slice(0, 4),):
-                        nc.sync.dma_start(out=raw[:, planes, :], in_=dealt[:, planes, :])
-                if lo == 512 and c0 == 0:
-                    dealt = raw.rearrange("p j (b t i) -> p t b j i", t=4, i=2)
-                    for t in range(4):
-                        nc.scalar.copy(
-                            out=grouped[:, 512 * t : 512 * t + 512].rearrange("p (b i j) -> p b j i", i=2, j=4),
-                            in_=dealt[:, t],
-                        )
-                else:
-                    interleave(grouped[:, cols], raw)
-                c0 = c0 + rows.shape[1]
-            return grouped
+        w2q = [(w2w[:, 2 * c0 : 2 * c0 + 2 * P], w2s[:, c0 : c0 + P]) for c0 in range(0, H // 2, P)]
 
-        w2_lanes = keep.tile([P, H], U8, name="w2_lanes", align_bytes=64)
-        w2s_lanes = keep.tile([P, H // 2], U8, name="w2s_lanes", align_bytes=64)
-
-        def deal_w2():
-            nc.gpsimd.tensor_copy(
-                w2_lanes[:].bitcast(I32).rearrange("p (t b) -> p t b", t=4),
-                w2w[:, H:].bitcast(I32).rearrange("p (b t) -> p t b", t=4),
-            )
-            for t in range(4):
+        def deal_w2(i):
+            words = place("w2w_dealt%d" % i, H // 2, U8, "grouped_b", S + 768 * i)
+            scales = place("w2s_dealt%d" % i, H // 4, U8, "grouped_b", S + 768 * i + H // 2)
+            pairs = w2w[:, H:].bitcast(I32).rearrange("p (b e) -> p b e", e=4)
+            if i == 0:
+                nc.gpsimd.tensor_copy(words[:].bitcast(I32).rearrange("p (b e) -> p b e", e=2), pairs[:, :, 0:2])
                 nc.gpsimd.tensor_copy(
-                    w2s_lanes[:, P * t : P * t + P].rearrange("p (b i) -> p b i", i=2),
-                    w2s[:, H // 2 :].rearrange("p (b t i) -> p t b i", t=4, i=2)[:, t],
+                    scales[:].bitcast(I32), w2s[:, H // 2 :].bitcast(I32).rearrange("p (b e) -> p b e", e=2)[:, :, 0]
                 )
-
-        def quantize_weights(i, grouped, tag):
-            width = grouped.shape[1] // 4
-            codes = keep.tile([P, width], U32, name=tag, align_bytes=64)
-            if i == 1:
-                scales = placed.tile([P, width], U8, name="ws1", align_bytes=64, offset=0)
             else:
-                scales = keep.tile([P, width], U8, name="ws%d" % i, align_bytes=64)
-            nc.vector.quantize_mx(out=codes[:].bitcast(FP8X4), scales=scales[:], in_=grouped[:])
-            lo, hi = W1_CHUNKS[i]
-            for c0 in range(0, width, P):
-                (w1q if c0 < hi - lo else w3q).append((codes[:, c0 : c0 + P].bitcast(FP8X4), scales[:, c0 : c0 + P]))
-
-        words = keep.tile([P, S], U32, name="words", align_bytes=64)
-        vw = [words[:, BANK * h : BANK * h + BANK] for h in range(2)]
-        vs = [keep.tile([P, BANK], U8, name="vs%d" % h, align_bytes=64) for h in range(2)]
-        halves = [slice(BANK * h, BANK * h + BANK) for h in range(2)]
-        last = SLICES - 1
-        staged = {}
-        rates = {}
-
-        sources = {}
-        gaps = {}
+                nc.gpsimd.tensor_copy(
+                    words[:].bitcast(I32).rearrange("p (e b) -> p e b", e=2),
+                    pairs[:, :, 2:4].rearrange("p b e -> p e b"),
+                )
+                nc.gpsimd.tensor_copy(
+                    scales[:].rearrange("p (t b i) -> p t b i", t=2, i=2),
+                    w2s[:, H // 2 :].rearrange("p (b t i) -> p t b i", t=4, i=2)[:, 2:4],
+                )
+            w2q.extend((words[:, 2 * c0 : 2 * c0 + 2 * P], scales[:, c0 : c0 + P]) for c0 in (0, P))
 
         weights = {}
+
+        def load_weights(s):
+            both = place("wg%d" % s, 2 * S, F32, "wg", 8 * S * (0, 0, 0, 0, 1, 1, 0, 1)[s])
+            rows = {4: slice(0, 4), 6: slice(4, 6), 7: slice(6, 8)}[s]
+            span = 16 * (rows.stop - rows.start)
+            for i, matrix in enumerate((wg1, wg2)):
+                for p0 in range(0, P, span):
+                    nc.sync.dma_start(out=both[p0 : p0 + span, S * i : S * i + S], in_=by_eights(matrix)[:, rows])
+            weights[s] = both
+            if s == 4:
+                weights[5] = both
+
         eqs = {}
-        weighted = {}
 
-        def load_given(s):
-            given = two.tile([P, (1 if s < 4 else 3) * S], F32, name="given")
-            eqs[s] = given[:, :S]
-            nc.sync.dma_start(out=eqs[s], in_=slice_rows(eq, s))
-            weights[s] = wg[:] if s < 4 else given[:, S:]
-            if s >= 4:
-                for i, matrix in enumerate((wg1, wg2)):
-                    for p0 in range(0, P, 32):
-                        nc.sync.dma_start(
-                            out=weights[s][p0 : p0 + 32, S * i : S * i + S], in_=lane_rows(matrix, s - 4)
-                        )
+        def load_eq(s):
+            eqs[s] = place("eq%d" % s, S, F32, "eq", 4 * S * (s % 3))
+            nc.sync.dma_start(out=eqs[s][:], in_=slice_rows(eq, s))
 
-        def stage(s):
-            if s == last:
-                sources[s] = keep.tile([P, S], F32, name="last_source")[:]
-                gaps[s] = placed.tile([P, S], F32, name="odd", align_bytes=64, offset=ODD_AT)[:]
-                return
-            if s < 2:
-                staged[s] = keep.tile([P, 2 * S], F32, name="early%d" % s, align_bytes=64)
-            else:
-                name, at = (("even", EVEN_AT), ("odd", ODD_AT))[s % 2]
-                staged[s] = placed.tile([P, 2 * S], F32, name=name, align_bytes=64, offset=at)
-            sources[s], gaps[s] = staged[s][:, :S], staged[s][:, S:]
+        walls = {}
 
-        def source_scores(s, h, bank):
+        def load_wall(s):
+            walls[s] = place("wall%d" % s, T2, F32, "wall", 4 * T2 * (s % 2))
+            nc.sync.dma_start(out=walls[s][:], in_=slice_rows(wall, s))
+
+        def score_half(s, h, weighted=None):
+            bank = bank_of("score")
             nc.tensor.matmul_mx(
                 out=bank[:], lhsT=w1q[s][0], lhsT_scale=w1q[s][1],
-                rhs=vw[h].bitcast(FP8X4), rhs_scale=vs[h][:], start=True, stop=True,
+                rhs=vw[h][:].bitcast(FP8X4), rhs_scale=vs[h][:], start=True, stop=True,
             )
-            return bank
+            if weighted is not None:
+                nc.vector.tensor_tensor(weighted, bank[:], weights[s][:, halves[h]], MULT)
+            nc.scalar.copy(out=scores[:, halves[h]], in_=bank[:])
 
-        def rate_scores(s):
-            words, scales = (w2w, w2s) if s < 4 else (w2_lanes, w2s_lanes)
-            c0 = P * (s % 4)
+        def score(s):
             for h in range(2):
-                rates[s, h] = held.tile([P, BANK], F32, name="gap")
+                score_half(s, h)
+
+        rates = {}
+
+        def rate(s):
+            for h in range(2):
+                rates[s, h] = bank_of("rate")
                 nc.tensor.matmul_mx(
-                    out=rates[s, h][:], lhsT=words[:, 2 * c0 : 2 * c0 + 2 * P].bitcast(FP4X4),
-                    lhsT_scale=scales[:, c0 : c0 + P],
-                    rhs=vw[h].bitcast(FP8X4), rhs_scale=vs[h][:], start=True, stop=True,
+                    out=rates[s, h][:], lhsT=w2q[s][0].bitcast(FP4X4), lhsT_scale=w2q[s][1],
+                    rhs=vw[h][:].bitcast(FP8X4), rhs_scale=vs[h][:], start=True, stop=True,
                 )
+
+        gains = {}
+
+        def weigh_rate(s):
+            at = (("first_gain", 0), ("gain", 0))[s] if s < 2 else ("eq", 4 * S * ((s - 1) % 3))
+            gains[s] = place("gain%d" % s, S, F32, *at)
+            for h in range(2):
+                nc.vector.tensor_tensor(gains[s][:, halves[h]], rates[s, h][:], weights[s][:, S + BANK * h : S + BANK * (h + 1)], MULT)
+
+        GAP_AT = {1: ("growth", 0), 2: ("raw_c", 0), 4: ("raw_w3", 0), 6: ("grouped_w3", 0), 7: ("codes_z", 2 * S)}
+        gaps = {}
+
+        def subtract(s):
+            gaps[s] = place("gap%d" % s, S, F32, *GAP_AT.get(s, ("product", 0)))
+            nc.gpsimd.tensor_tensor(gaps[s][:], scores[:], eqs[s][:], SUB)
+
+        def form_sink(s):
+            if s == LAST:
+                sink[s % 2] = place("last_sink", S, F32, "turned", 12 * S)
+            nc.gpsimd.tensor_tensor(sink[s % 2][:], gaps[s][:], gains[s][:], MULT)
+
+        def form_source(s):
+            nc.gpsimd.tensor_tensor(source[s % 2][:], scores[:], weights[s][:, :S], MULT)
+
+        def scatter_sink(s):
+            nc.vector.tensor_copy(page_b[s % 2][:].indirect(idx3[:]), sink[s % 2][:])
+
+        PRODUCT_AT = {1: ("grouped_c", 0), 3: ("grouped_w3", 0), 5: ("grouped_w3", 0), 6: ("table", 4 * T2)}
+        growths = {}
+
+        def exponentiate(s):
+            at = {0: ("growth", 0), LAST: ("raw_w3", 4 * S)}.get(s, PRODUCT_AT.get(s - 1, ("product", 0)))
+            growths[s] = place("growth%d" % s, T2, F32, *at)
+            for c0 in range(0, T2, S):
+                nc.scalar.activation(out=growths[s][:, c0 : c0 + S], in_=page_b[s % 2][:, c0 : c0 + S], func=EXP)
+
+        def grow(s):
+            product = place("product%d" % s, T2, F32, *PRODUCT_AT.get(s, ("product", 0)))
+            for c0 in range(0, T2, S):
+                cols = slice(c0, c0 + S)
+                nc.gpsimd.tensor_tensor(product[:, cols], growths[s][:, cols], page_a[:, cols], MULT)
+            return product
 
         def add_transposed(bank, rows, opens):
             for g in range(4):
@@ -208,136 +284,71 @@ def tile_list_cave_wall_growth_kernel(
                     start=(opens and g == 0), stop=(not opens and g == 3), is_transpose=True,
                 )
 
-        def score_sources(s):
-            stage(s)
-            for h in range(2):
-                nc.scalar.copy(out=sources[s][:, halves[h]], in_=source_scores(s, h, held.tile([P, BANK], F32, name="wide"))[:])
-            gap = gaps[s] if s == 1 else growth[:, :S]
-            nc.gpsimd.tensor_tensor(gap, sources[s], eqs[s], SUB)
-            return gap
+        turned = {}
 
-        def weigh_slice(s, gap):
-            weighted[s] = gaps[s] if s == 1 else product[:, S:]
-            nc.gpsimd.tensor_tensor(weighted[s], gap, weights[s][:, S:], MULT)
-            if s < last:
-                nc.gpsimd.tensor_tensor(sources[s], sources[s], weights[s][:, :S], MULT)
-            else:
-                for h in range(2):
-                    nc.scalar.copy(out=gaps[s][:, halves[h]], in_=rates[s, h][:])
-                nc.gpsimd.tensor_tensor(gaps[s], gaps[s], weighted[s], MULT)
-
-        def scatter_source(s, cols):
-            nc.vector.tensor_copy(page_a[:].indirect(idx2[:, cols.start // 16 : cols.stop // 16]), sources[s][:, cols])
-
-        def scatter_sink(s):
-            sink = gaps[s]
-            if s == 1:
-                sink = placed.tile([P, S], F32, name="sink1", align_bytes=64, offset=EVEN_AT + 8 * S)[:]
-            for h in range(2 if s < last else 0):
-                nc.vector.tensor_tensor(sink[:, halves[h]], rates[s, h][:], weighted[s][:, halves[h]], MULT)
-            nc.vector.tensor_copy(page_b[s % 2][:].indirect(idx3[:]), sink)
-
-        def exponentiate(s, width):
-            for c0 in range(0, T2, width) if s in (0, last) else (S, 0):
-                nc.scalar.activation(out=growth[:, c0 : c0 + width], in_=page_b[s % 2][:, c0 : c0 + width], func=EXP)
-
-        products = {}
-
-        def grow(s):
-            front = product[:, :S]
-            if s == 1:
-                front = placed.tile([P, S], F32, name="front1", offset=ODD_AT + 8 * S)[:]
-            if s == last - 1:
-                front = two.tile([P, S], F32, name="grouped", align_bytes=64)[:]
-            for i, half in enumerate((front, product[:, S:])):
-                cols = slice(S * i, S * i + S)
-                nc.gpsimd.tensor_tensor(half, growth[:, cols], page_a[:, cols], MULT)
-                products[s, 2 * i], products[s, 2 * i + 1] = half[:, :BANK], half[:, BANK:]
-
-        walls = {}
-
-        def load_wall(s):
-            walls[s] = two.tile([P, T2], F32, name="wall_rows")
-            nc.sync.dma_start(out=walls[s][:], in_=slice_rows(wall, s))
-
-        z_t = {}
-        zq = {}
-
-        def open_with_wall(s, c, bank):
-            add_transposed(bank, walls[s][:, BANK * c : BANK * c + BANK], True)
-            return bank
-
-        def add_product(s, c, bank):
-            add_transposed(bank, products[s, c], False)
-            round_z(s, c, bank)
-
-        def round_z(s, c, bank):
-            if s < 4:
+        def form_z(s, product):
+            for c in range(CHUNKS):
+                cols = slice(BANK * c, BANK * c + BANK)
+                bank = bank_of("sum" if c < 2 else "score")
+                add_transposed(bank, walls[s][:, cols], True)
+                add_transposed(bank, product[:, cols], False)
                 if s == 0:
-                    z_t[0, c] = keep.tile([P, 4 * BANK], BF16, name="z_t%d" % c, align_bytes=64)
-                nc.scalar.copy(
-                    out=z_t[0, c][:].rearrange("m (u g q e) -> m u g q e", u=2, g=4, e=2)[:, :, :, 32 * s : 32 * s + 32, :],
-                    in_=bank[:].rearrange("m (g q u e) -> m u g q e", g=4, u=2, e=2),
-                )
-            else:
-                z_t[1, c] = keep.tile([P, BANK], BF16, name="lane_t%d" % c, align_bytes=64)
-                nc.scalar.copy(out=z_t[1, c][:], in_=bank[:])
+                    turned[0, c] = place("turned0%d" % c, 4 * BANK, BF16, "turned", 8 * BANK * c)
+                if s == 4:
+                    turned[1, c] = place("turned1%d" % c, 2 * BANK, BF16, "raw_w3", 4 * S + 4 * BANK * c)
+                if s < 4:
+                    nc.scalar.copy(
+                        out=turned[0, c][:].rearrange("m (u g q e) -> m u g q e", u=2, g=4, e=2)[:, :, :, 32 * s : 32 * s + 32, :],
+                        in_=bank[:].rearrange("m (g q u e) -> m u g q e", g=4, u=2, e=2),
+                    )
+                else:
+                    nc.scalar.copy(
+                        out=turned[1, c][:].rearrange("m (g q) -> m g q", g=4)[:, :, P * (s - 4) : P * (s - 3)],
+                        in_=bank[:].rearrange("m (g q) -> m g q", g=4),
+                    )
 
-        def regroup_chunks(chunks):
-            grouped = two.tile([P, 8 * BANK], BF16, name="grouped", align_bytes=64)
-            for i, c in enumerate(chunks):
-                words = z_t[0, c][:].bitcast(F32)
+        def regroup(i):
+            grouped = place("grouped_z%d" % i, 8 * BANK, BF16, "table", 4 * T2 * i)
+            for j in range(2):
+                words = turned[0, 2 * i + j][:].bitcast(F32)
                 for h in range(2):
-                    bank = next_bank()
+                    bank = bank_of("turn")
                     for u in range(2):
                         for g2 in range(2):
                             w0 = P * (4 * u + 2 * h + g2)
                             o0 = P * (2 * u + g2)
                             nc.tensor.transpose(bank[:, o0 : o0 + P], words[:, w0 : w0 + P], ident[:])
-                    c0 = BANK * (2 * i + h)
+                    c0 = BANK * (2 * j + h)
                     nc.scalar.copy(
                         out=grouped[:].bitcast(F32)[:, c0 : c0 + BANK].rearrange("p (m u) -> p m u", u=2),
                         in_=bank[:].rearrange("p (u m) -> p m u", u=2),
                     )
             return grouped
 
-        planes = {}
+        pairs = {}
 
-        def turn_lane(t):
+        def turn_first_lanes():
             for c in range(CHUNKS):
-                if t == 0 and c % 2 == 0:
-                    both = keep.tile([P, 8 * BANK], BF16, name=("raw1", "wg")[c // 2], align_bytes=64)
-                    planes[c], planes[c + 1] = both[:, : 4 * BANK], both[:, 4 * BANK :]
-                bank = psum.tile([P, BANK], BF16, name="bank")
+                words = turned[1, c][:].bitcast(F32)
+                bank = bank_of("turn")
                 for g in range(4):
-                    nc.tensor.transpose(bank[:, P * g : P * g + P], z_t[1, c][:, P * g : P * g + P], ident_bf[:])
-                nc.scalar.copy(out=planes[c][:, BANK * t : BANK * t + BANK], in_=bank[:])
+                    nc.tensor.transpose(bank[:, P * g : P * g + P], words[:, P * g : P * g + P], ident[:])
+                for j, (lo, hi) in enumerate(PIECES):
+                    if lo // BANK == c:
+                        pairs[j] = place("pairs%d" % j, 2 * (hi - lo), F32, "table_bytes", 8 * lo)
+                        nc.scalar.copy(out=pairs[j][:, : hi - lo], in_=bank[:, lo - BANK * c : hi - BANK * c])
 
-        def quantize_z(b, chunks, grouped, codes, pool, tag):
-            n = len(chunks)
-            scales = pool.tile([P, n * BANK], U8, name=tag, align_bytes=64)
-            nc.vector.quantize_mx(out=codes.bitcast(FP8X4), scales=scales[:], in_=grouped[:, : 4 * BANK * n])
-            for i, c in enumerate(chunks):
-                zq[b, c] = (codes[:, BANK * i : BANK * (i + 1)], scales[:, BANK * i : BANK * (i + 1)])
+        def last_lanes(j):
+            lo, hi = PIECES[j]
+            return pairs[j][:, hi - lo :].bitcast(BF16).rearrange("p (m e) -> p m e", e=2)
 
-
-        def project(turn, lo, hi, second, rows):
-            c, c0 = divmod(lo, BANK)
-            first = [x[:, c0 : c0 + hi - lo] for x in zq[0, c]]
-            for nb in range(N // P):
-                bank = spare_bank(N // P * turn + nb)
-                for b, (z_codes, z_scales) in enumerate((first, second)):
-                    codes, scales = w3q[N // P * b + nb]
-                    nc.tensor.matmul_mx(
-                        out=bank[:, : hi - lo], lhsT=codes, lhsT_scale=scales,
-                        rhs=z_codes.bitcast(FP8X4), rhs_scale=z_scales, start=(b == 0), stop=(b == PASSES - 1),
-                    )
-                result = rows[nb][:, c0 : c0 + hi - lo]
-                copy = nc.vector.tensor_copy if nb < turn - 3 else nc.scalar.copy
-                copy(out=result, in_=bank[:, : hi - lo])
-                nc.sync.dma_start(out=out[P * nb : P * nb + P, lo:hi], in_=result)
-
-        first_pass = {}
+        def form_third_lane(product):
+            lane = place("lane", T2, BF16, "grouped_c")
+            for c0 in range(0, T2, S):
+                cols = slice(c0, c0 + S)
+                nc.gpsimd.tensor_tensor(lane[:, cols], product[:, cols], walls[LAST - 1][:, cols], ADD)
+            for j, (lo, hi) in enumerate(PIECES):
+                nc.scalar.copy(out=last_lanes(j), in_=lane[:, lo:hi].unsqueeze(2).to_broadcast([P, hi - lo, 2]))
 
         nc.vector.memset(tabs[:].bitcast(I32), 0)
         nc.gpsimd.memset(w2s[:].bitcast(I32), 0)
@@ -345,127 +356,142 @@ def tile_list_cave_wall_growth_kernel(
         nc.sync.dma_start(idx[:], offs)
         nc.sync.dma_start(idx2[:], offs2)
         nc.sync.dma_start(idx3[:], offs3)
+        quantize_w1("a", group_w1("a", 0, 128))
         table = tab_words[0].rearrange("p t i -> p (t i)").bitcast(I32)
-        quantize_weights(0, group_weights(0, keep.tile([P, 4 * 256], F32, name="raw0", align_bytes=64)), "w1c")
         for c0 in range(0, T, T // 4):
             nc.sync.dma_start(out=tabw[:].bitcast(I32)[:, c0 : c0 + T // 4], in_=table[:, c0 : c0 + T // 4])
         load_scale_rows(nc.sync, tabs, tab_scales[0])
         nc.vector.memset(page_a[:], 0.0)
         make_identity(nc, ident[:])
-        make_identity(nc, ident_bf[:])
-        nc.sync.dma_start(out=wg[:, halves[0]], in_=wg1[:, halves[0]])
         for page in page_b:
             nc.gpsimd.memset(page[:], 0.0)
-        nc.vector.tensor_copy(words[:], tabw[:].indirect(idx[:]))
-        for h in range(2):
-            nc.vector.tensor_copy(vs[h][:], tabs[:].indirect(idx[:, 32 * h : 32 * h + 32]))
-        stage(0)
-        load_given(0)
-        nc.sync.dma_start(out=wg[:, halves[1]], in_=wg1[:, halves[1]])
-        nc.sync.dma_start(out=wg[:, S:], in_=wg2)
+        wg = place("wg0", 2 * S, F32, "wg")
+        for s in range(4):
+            weights[s] = wg
+        second = group_w1("b", 128, 384)
+        nc.sync.dma_start(out=wg[:, halves[0]], in_=wg1[:, halves[0]])
         nc.sync.dma_start(out=w2w[:].bitcast(I32), in_=w2_words[0].bitcast(I32))
-        first = [source_scores(0, h, next_bank()) for h in range(2)]
-        nc.vector.tensor_tensor(sources[0][:, halves[0]], first[0][:], wg[:, halves[0]], MULT)
-        scatter_source(0, halves[0])
-        nc.scalar.copy(out=sources[0][:, halves[1]], in_=first[1][:])
+        nc.sync.dma_start(out=wg[:, S:], in_=wg2)
+        nc.sync.dma_start(out=wg[:, halves[1]], in_=wg1[:, halves[1]])
+        load_eq(0)
+        load_eq(1)
         for h in range(2):
-            nc.vector.tensor_tensor(gaps[0][:, halves[h]], first[h][:], eqs[0][:, halves[h]], SUB)
-        nc.gpsimd.tensor_tensor(sources[0][:, halves[1]], sources[0][:, halves[1]], wg[:, halves[1]], MULT)
-        scatter_source(0, halves[1])
-        nc.gpsimd.tensor_tensor(gaps[0], gaps[0], wg[:, S:], MULT)
-        weighted[0] = gaps[0]
-        rate_scores(0)
-        load_given(1)
-        weigh_slice(1, score_sources(1))
-        deal_w2()
-
-        def form_z(s):
-            for c in range(CHUNKS):
-                if c >= 2:
-                    add_product(s, c, open_with_wall(s, c, held.tile([P, BANK], F32, name="wide")))
-                else:
-                    bank = held.tile([P, BANK], F32, name="gap")
-                    add_transposed(bank, products[s, c], True)
-                    add_transposed(bank, walls[s][:, BANK * c : BANK * c + BANK], False)
-                    round_z(s, c, bank)
-
-        second = group_weights(1, keep.tile([P, 4 * 512], F32, name="raw1", align_bytes=64))
-        third = group_weights(2, placed.tile([P, 4 * 1024], F32, name="raw2", offset=0))
-        scatter_sink(0)
-        quantize_weights(1, second, "early0")
-        rate_scores(1)
-        pair = placed.tile([P, 2 * T2], F32, name="pair", offset=BANK)
-        growth, product = pair[:, :T2], pair[:, T2:]
-        load_given(2)
-        load_wall(0)
-        exponentiate(0, S)
-        for s in range(1, SLICES):
-            scatter_sink(s)
-            grow(s - 1)
-            if s + 1 <= last:
-                gap = score_sources(s + 1)
-            if s + 2 <= last:
-                load_given(s + 2)
-            load_wall(s)
-            form_z(s - 1)
-            if s + 1 <= last:
-                rate_scores(s + 1)
-                weigh_slice(s + 1, gap)
-            exponentiate(s, S if s < last else BANK)
-            if s >= 5:
-                turn_lane(s - 5)
-            if s in (4, 5):
-                first_pass[s - 4] = regroup_chunks((2 * s - 8, 2 * s - 7))
-            if s == last:
-                codes = placed.tile([P, 2 * BANK], U32, name="odd", align_bytes=64, offset=ODD_AT)
-                quantize_z(0, (2, 3), first_pass[1], codes[:], keep, "zs0")
-            if s < last:
-                scatter_source(s, slice(0, S))
-            else:
-                nc.vector.tensor_tensor(page_a[:].indirect(idx2[:]), sources[s], weights[s][:, :S], MULT)
-            if s == 1:
-                quantize_weights(2, third, "early1")
-            if s == last - 1:
-                codes = placed.tile([P, 2 * BANK], U32, name="even", align_bytes=64, offset=EVEN_AT)
-                quantize_z(0, (0, 1), first_pass[0], codes[:], keep, "zs5")
-        rows = keep.tile([P, 8 * BANK], F32, name="tabw", align_bytes=64)
-        results = [rows[:, BANK * i : BANK * i + BANK] for i in range(8)]
+            nc.vector.tensor_copy(vw[h][:], tabw[:].indirect(idx[:, 32 * h : 32 * h + 32]))
+            nc.vector.tensor_copy(vs[h][:], tabs[:].indirect(idx[:, 32 * h : 32 * h + 32]))
+        quantize_w1("b", second)
+        first_source = place("first_source", BANK, F32, "grouped_a")
+        score_half(0, 0, first_source[:])
+        nc.vector.tensor_copy(page_a[:].indirect(idx2[:, :32]), first_source[:])
+        score_half(0, 1)
+        nc.gpsimd.tensor_tensor(source[0][:, halves[1]], scores[:, halves[1]], wg[:, halves[1]], MULT)
+        rate(0)
+        weigh_rate(0)
+        nc.vector.tensor_copy(page_a[:].indirect(idx2[:, 32:]), source[0][:, halves[1]])
+        rate(1)
+        weigh_rate(1)
+        subtract(0)
+        form_sink(0)
         for i in range(2):
-            rows = keep.tile([P, 2 * BANK], F32, name="z_t%d" % i, align_bytes=64)
-            results.extend((rows[:, :BANK], rows[:, BANK:]))
+            deal_w2(i)
+        score(1)
+        scatter_sink(0)
+        rate(2)
+        subtract(1)
+        form_sink(1)
+        form_source(1)
+        score(2)
+        exponentiate(0)
+        load_eq(2)
+        third = group_w1("c", 384, 1024)
+        load_wall(0)
+        load_wall(1)
+        load_eq(3)
+        raw_w3 = load_w3()
+        load_weights(4)
 
-        def weave(copy, woven, lo, hi):
-            c, c0 = divmod(lo, BANK)
-            copy(
-                out=woven.rearrange("p (c i t) -> p c t i", i=4, t=4),
-                in_=planes[c].rearrange("p (t c i) -> p c t i", t=4, i=4)[:, c0 // 4 : (c0 + hi - lo) // 4],
-            )
+        first_pass = []
+        grouped = {}
+        for s in range(1, SLICES):
+            if s == 2:
+                quantize_w1("c", third)
+                score(3)
+            if s == 4:
+                w3q = stationary(*quantize("w3", grouped["w3"], N, ("raw_w3",), ("scales_w3",)))
+            for i in range(2 if s == LAST else 0):
+                first_pass.append(quantize("z%d" % i, grouped[i], S, ("codes_z", 4 * S * i), ("scales_z", S * i)))
+            if s < LAST:
+                weigh_rate(s + 1)
+            scatter_sink(s)
+            if s + 2 <= LAST:
+                rate(s + 2)
+            product = grow(s - 1)
+            if s < LAST:
+                form_z(s - 1, product)
+                subtract(s + 1)
+                form_sink(s + 1)
+            exponentiate(s)
+            if s < LAST:
+                form_source(s + 1)
+            nc.vector.tensor_copy(page_a[:].indirect(idx2[:]), source[s % 2][:])
+            if 2 <= s <= LAST - 2:
+                score(s + 2)
+            if s + 3 <= LAST:
+                load_eq(s + 3)
+            if s + 1 <= LAST:
+                load_wall(s + 1)
+            if s == 2:
+                load_weights(6)
+                grouped["w3"] = group_w3(raw_w3)
+            if s == 4:
+                load_weights(7)
+                grouped[0] = regroup(0)
+            if s == 5:
+                grouped[1] = regroup(1)
+            if s == LAST - 1:
+                turn_first_lanes()
+            if s == LAST:
+                form_third_lane(product)
 
-        last_codes = keep.tile([P, T2], U32, name="last_codes", align_bytes=64)
-        last_scales = keep.tile([P, T2], U8, name="last_scales", align_bytes=64)
+        last_codes = place("last_codes", T2, U32, "sink")
+        last_scales = place("last_scales", T2, U8, "gain")
         woven = {}
-        for step in range(len(PIECES) + 1):
+
+        def project(j):
+            lo, hi = PIECES[j]
+            i, c0 = divmod(lo, S)
+            first = [x[:, c0 : c0 + hi - lo] for x in first_pass[i]]
+            for nb in range(OUT_TILES):
+                bank = bank_of(("rate", "sum", "score", "turn")[(OUT_TILES * j + nb) // 2 % 4])
+                for b, (codes, scales) in enumerate((first, (last_codes[:, lo:hi], last_scales[:, lo:hi]))):
+                    nc.tensor.matmul_mx(
+                        out=bank[:, : hi - lo], lhsT=w3q[OUT_TILES * b + nb][0], lhsT_scale=w3q[OUT_TILES * b + nb][1],
+                        rhs=codes.bitcast(FP8X4), rhs_scale=scales, start=(b == 0), stop=(b == 1),
+                    )
+                at = 4 * (OUT_TILES * lo + nb * (hi - lo))
+                result = place("result%d_%d" % (j, nb), hi - lo, F32, *(("turned", at) if at < 8 * T2 else ("growth", at - 8 * T2)))
+                copy = nc.vector.tensor_copy if nb == 0 and j >= VECTOR_EMPTIES_FROM else nc.scalar.copy
+                copy(out=result[:], in_=bank[:, : hi - lo])
+                nc.sync.dma_start(out=out[P * nb : P * nb + P, lo:hi], in_=result[:])
+
+        parts = {}
+        for step in range(len(PIECES) + 2):
+            j = step - 2
+            if j >= 0:
+                done = slice(*PIECES[j])
+                nc.vector.quantize_mx(out=last_codes[:, done].bitcast(FP8X4), scales=last_scales[:, done], in_=woven[j][:])
+                project(j)
             if step < len(PIECES):
                 lo, hi = PIECES[step]
-                split = (hi - lo) // 2 if hi <= 3 * BANK else 0
-                c, c0 = divmod(lo, BANK)
-                part = keep.tile([P, hi - lo], F32, name=PART_TAGS[step % len(PART_TAGS)], align_bytes=64)
-                nc.vector.tensor_tensor(part[:], growth[:, lo:hi], page_a[:, lo:hi], MULT)
-            if step >= 1:
-                done = slice(*PIECES[step - 1])
-                nc.vector.quantize_mx(
-                    out=last_codes[:, done].bitcast(FP8X4), scales=last_scales[:, done], in_=woven[step - 1]
+                at = ("scores", 4 * lo) if step < AHEAD else ("table", 8 * PIECES[step - AHEAD][0])
+                parts[step] = place("part%d" % step, hi - lo, F32, *at)
+                nc.vector.tensor_tensor(parts[step][:], growths[LAST][:, lo:hi], page_a[:, lo:hi], MULT)
+            j = step - 1
+            if 0 <= j < len(PIECES):
+                lo, hi = PIECES[j]
+                nc.vector.tensor_tensor(last_lanes(j)[:, :, 1], parts[j][:], walls[LAST][:, lo:hi], ADD)
+                woven[j] = place("woven%d" % j, 4 * (hi - lo), BF16, "table", 8 * lo)
+                weave = nc.vector.tensor_copy if j in VECTOR_WEAVES else nc.scalar.copy
+                weave(
+                    out=woven[j][:].bitcast(F32).rearrange("p (m u) -> p m u", u=2),
+                    in_=pairs[j][:].rearrange("p (u m) -> p m u", u=2),
                 )
-            if step < len(PIECES):
-                lane = planes[c][:, 3 * BANK + c0 : 3 * BANK + c0 + hi - lo]
-                nc.vector.tensor_tensor(lane, part[:], walls[last][:, lo:hi], ADD)
-                if lo % S == 0:
-                    grouped = two.tile([P, 8 * BANK], BF16, name="grouped", align_bytes=64)
-                woven[step] = grouped[:, 4 * (lo % S) : 4 * (lo % S + hi - lo)]
-                if split > 0:
-                    weave(nc.scalar.copy, woven[step][:, : 4 * split], lo, lo + split)
-                if split < hi - lo:
-                    weave(nc.vector.tensor_copy, woven[step][:, 4 * split :], lo + split, hi)
-            if step >= 1:
-                first = N // P * (done.start // BANK)
-                project(step - 1, done.start, done.stop, (last_codes[:, done], last_scales[:, done]), results[first : first + N // P])

@@ -42,15 +42,14 @@ def lay_out(areas):
 AT = lay_out(
     (
         ("words", 4 * S), ("bytes", S), ("w2w", 2 * H), ("w2s", H),
-        ("ident", 4 * P), ("page_a", 4 * T2), ("page_b", 8 * T2), ("growth", 4 * T2), ("product", 4 * T2),
+        ("ident", 4 * P), ("page_a", 4 * T2), ("page_b", 8 * T2), ("product", 4 * T2),
         ("scores", 4 * S), ("source", 8 * S), ("gain", 4 * S), ("sink", 8 * S), ("eq", 12 * S),
-        ("wall", 8 * T2), ("wg", 16 * S),
-        ("codes_a", 4 * 128), ("scales_a", 128), ("codes_b", 4 * 256), ("scales_b", 256), ("scales_c", 640),
+        ("wall", 8 * T2), ("wg", 16 * S), ("results", 4 * T2),
+        ("codes_a", 4 * 256), ("scales_a", 256), ("scales_c", 768),
         ("scales_w3", 768),
         ("table", 4 * T),
-        ("table_bytes", T), ("raw_a", 16 * 128), ("raw_b", 16 * 256), ("grouped_a", 8 * 128), ("grouped_b", 8 * 256),
-        ("dealt", 512), ("first_gain", 4 * S),
-        ("raw_w3", 16 * 768), ("raw_c", 16 * 640), ("grouped_c", 4 * T2), ("grouped_w3", 4 * T2),
+        ("table_bytes", T), ("raw_a", 16 * 256), ("grouped_a", 8 * 256), ("dealt", 2048), ("first_gain", 4 * S),
+        ("raw_w3", 16 * 768), ("growth", 4 * T2), ("raw_c", 16 * 768), ("grouped_c", 4 * T2), ("grouped_w3", 4 * T2),
         ("turned", 8 * T2), ("codes_z", 4 * T2), ("scales_z", T2),
     )
 )
@@ -96,8 +95,10 @@ def tile_list_cave_wall_growth_kernel(
         source = [place("source%d" % i, S, F32, "source", 4 * S * i) for i in range(2)]
         sink = [place("sink%d" % i, S, F32, "sink", 4 * S * i) for i in range(2)]
         halves = [slice(BANK * h, BANK * h + BANK) for h in range(2)]
-        vw = [place("vw%d" % h, BANK, U32, "words", 4 * BANK * h) for h in range(2)]
-        vs = [place("vs%d" % h, BANK, U8, "bytes", BANK * h) for h in range(2)]
+        words = place("words", S, U32, "words")
+        scale_bytes = place("scale_bytes", S, U8, "bytes")
+        vw = [words[:, half].bitcast(FP8X4) for half in halves]
+        vs = [scale_bytes[:, half] for half in halves]
 
         def load_scale_rows(queue, plane, rows):
             for q in range(4):
@@ -162,13 +163,13 @@ def tile_list_cave_wall_growth_kernel(
         w1q = []
 
         def quantize_w1(part, grouped):
-            w1q.extend(stationary(*quantize("w1" + part, grouped, 512, ("raw_c" if part == "c" else "codes_" + part,), ("scales_" + part,))))
+            w1q.extend(stationary(*quantize("w1" + part, grouped, 384, ("raw_c" if part == "c" else "codes_" + part,), ("scales_" + part,))))
 
         w2q = [(w2w[:, 2 * c0 : 2 * c0 + 2 * P], w2s[:, c0 : c0 + P]) for c0 in range(0, H // 2, P)]
 
         def deal_w2(i):
-            words = place("w2w_dealt%d" % i, H // 2, U8, "grouped_b", S + 768 * i)
-            scales = place("w2s_dealt%d" % i, H // 4, U8, "grouped_b", S + 768 * i + H // 2)
+            words = place("w2w_dealt%d" % i, H // 2, U8, "grouped_a", S + 768 * i)
+            scales = place("w2s_dealt%d" % i, H // 4, U8, "grouped_a", S + 768 * i + H // 2)
             pairs = w2w[:, H:].bitcast(I32).rearrange("p (b e) -> p b e", e=4)
             if i == 0:
                 nc.gpsimd.tensor_copy(words[:].bitcast(I32).rearrange("p (b e) -> p b e", e=2), pairs[:, :, 0:2])
@@ -215,7 +216,7 @@ def tile_list_cave_wall_growth_kernel(
             bank = bank_of("score")
             nc.tensor.matmul_mx(
                 out=bank[:], lhsT=w1q[s][0], lhsT_scale=w1q[s][1],
-                rhs=vw[h][:].bitcast(FP8X4), rhs_scale=vs[h][:], start=True, stop=True,
+                rhs=vw[h], rhs_scale=vs[h], start=True, stop=True,
             )
             if weighted is not None:
                 nc.vector.tensor_tensor(weighted, bank[:], weights[s][:, halves[h]], MULT)
@@ -232,7 +233,7 @@ def tile_list_cave_wall_growth_kernel(
                 rates[s, h] = bank_of("rate")
                 nc.tensor.matmul_mx(
                     out=rates[s, h][:], lhsT=w2q[s][0].bitcast(FP4X4), lhsT_scale=w2q[s][1],
-                    rhs=vw[h][:].bitcast(FP8X4), rhs_scale=vs[h][:], start=True, stop=True,
+                    rhs=vw[h], rhs_scale=vs[h], start=True, stop=True,
                 )
 
         gains = {}
@@ -243,11 +244,12 @@ def tile_list_cave_wall_growth_kernel(
             for h in range(2):
                 nc.vector.tensor_tensor(gains[s][:, halves[h]], rates[s, h][:], weights[s][:, S + BANK * h : S + BANK * (h + 1)], MULT)
 
-        GAP_AT = {1: ("growth", 0), 2: ("raw_c", 0), 4: ("raw_w3", 0), 6: ("grouped_w3", 0), 7: ("codes_z", 2 * S)}
+        PRODUCT_AT = {1: ("growth", 0), 3: ("grouped_w3", 0), 5: ("grouped_w3", 0), 6: ("table", 4 * T2)}
+        GAP_AT = {1: ("raw_c", -S), 4: ("raw_w3", 0), 7: ("codes_z", 2 * S)}
         gaps = {}
 
         def subtract(s):
-            gaps[s] = place("gap%d" % s, S, F32, *GAP_AT.get(s, ("product", 0)))
+            gaps[s] = place("gap%d" % s, S, F32, *GAP_AT.get(s, PRODUCT_AT.get(s - 1, ("product", 0))))
             nc.gpsimd.tensor_tensor(gaps[s][:], scores[:], eqs[s][:], SUB)
 
         def form_sink(s):
@@ -261,7 +263,6 @@ def tile_list_cave_wall_growth_kernel(
         def scatter_sink(s):
             nc.vector.tensor_copy(page_b[s % 2][:].indirect(idx3[:]), sink[s % 2][:])
 
-        PRODUCT_AT = {1: ("grouped_c", 0), 3: ("grouped_w3", 0), 5: ("grouped_w3", 0), 6: ("table", 4 * T2)}
         growths = {}
 
         def exponentiate(s):
@@ -348,19 +349,19 @@ def tile_list_cave_wall_growth_kernel(
                 cols = slice(c0, c0 + S)
                 nc.gpsimd.tensor_tensor(lane[:, cols], product[:, cols], walls[LAST - 1][:, cols], ADD)
             for j, (lo, hi) in enumerate(PIECES):
-                nc.scalar.copy(out=last_lanes(j), in_=lane[:, lo:hi].unsqueeze(2).to_broadcast([P, hi - lo, 2]))
+                nc.scalar.copy(out=last_lanes(j)[:, :, 0], in_=lane[:, lo:hi])
 
         nc.vector.memset(tabs[:].bitcast(I32), 0)
         nc.gpsimd.memset(w2s[:].bitcast(I32), 0)
-        load_scale_rows(nc.gpsimd, w2s, w2_scales[0])
         nc.sync.dma_start(idx[:], offs)
         nc.sync.dma_start(idx2[:], offs2)
         nc.sync.dma_start(idx3[:], offs3)
-        quantize_w1("a", group_w1("a", 0, 128))
-        table = tab_words[0].rearrange("p t i -> p (t i)").bitcast(I32)
-        for c0 in range(0, T, T // 4):
-            nc.sync.dma_start(out=tabw[:].bitcast(I32)[:, c0 : c0 + T // 4], in_=table[:, c0 : c0 + T // 4])
+        load_scale_rows(nc.sync, w2s, w2_scales[0])
         load_scale_rows(nc.sync, tabs, tab_scales[0])
+        table = tab_words[0].rearrange("p t i -> p (t i)").bitcast(I32)
+        for c0 in range(0, T, T // 2):
+            nc.sync.dma_start(out=tabw[:].bitcast(I32)[:, c0 : c0 + T // 2], in_=table[:, c0 : c0 + T // 2])
+        first = group_w1("a", 0, 256)
         nc.vector.memset(page_a[:], 0.0)
         make_identity(nc, ident[:])
         for page in page_b:
@@ -368,27 +369,26 @@ def tile_list_cave_wall_growth_kernel(
         wg = place("wg0", 2 * S, F32, "wg")
         for s in range(4):
             weights[s] = wg
-        second = group_w1("b", 128, 384)
-        nc.sync.dma_start(out=wg[:, halves[0]], in_=wg1[:, halves[0]])
         nc.sync.dma_start(out=w2w[:].bitcast(I32), in_=w2_words[0].bitcast(I32))
         nc.sync.dma_start(out=wg[:, S:], in_=wg2)
-        nc.sync.dma_start(out=wg[:, halves[1]], in_=wg1[:, halves[1]])
+        for h in range(2):
+            nc.sync.dma_start(out=wg[:, halves[h]], in_=wg1[:, halves[h]])
         load_eq(0)
         load_eq(1)
+        third = group_w1("c", 256, 1024)
+        nc.vector.tensor_copy(scale_bytes[:], tabs[:].indirect(idx[:]))
         for h in range(2):
-            nc.vector.tensor_copy(vw[h][:], tabw[:].indirect(idx[:, 32 * h : 32 * h + 32]))
-            nc.vector.tensor_copy(vs[h][:], tabs[:].indirect(idx[:, 32 * h : 32 * h + 32]))
-        quantize_w1("b", second)
-        first_source = place("first_source", BANK, F32, "grouped_a")
-        score_half(0, 0, first_source[:])
-        nc.vector.tensor_copy(page_a[:].indirect(idx2[:, :32]), first_source[:])
-        score_half(0, 1)
-        nc.gpsimd.tensor_tensor(source[0][:, halves[1]], scores[:, halves[1]], wg[:, halves[1]], MULT)
+            nc.vector.tensor_copy(words[:, halves[h]], tabw[:].indirect(idx[:, 32 * h : 32 * h + 32]))
+        quantize_w1("a", first)
         rate(0)
         weigh_rate(0)
-        nc.vector.tensor_copy(page_a[:].indirect(idx2[:, 32:]), source[0][:, halves[1]])
+        score_half(0, 0, source[0][:, halves[0]])
+        nc.vector.tensor_copy(page_a[:].indirect(idx2[:, :32]), source[0][:, halves[0]])
+        score_half(0, 1)
+        nc.gpsimd.tensor_tensor(source[0][:, halves[1]], scores[:, halves[1]], wg[:, halves[1]], MULT)
         rate(1)
         weigh_rate(1)
+        nc.vector.tensor_copy(page_a[:].indirect(idx2[:, 32:]), source[0][:, halves[1]])
         subtract(0)
         form_sink(0)
         for i in range(2):
@@ -399,10 +399,10 @@ def tile_list_cave_wall_growth_kernel(
         subtract(1)
         form_sink(1)
         form_source(1)
-        score(2)
+        quantize_w1("c", third)
         exponentiate(0)
+        score(2)
         load_eq(2)
-        third = group_w1("c", 384, 1024)
         load_wall(0)
         load_wall(1)
         load_eq(3)
@@ -412,9 +412,6 @@ def tile_list_cave_wall_growth_kernel(
         first_pass = []
         grouped = {}
         for s in range(1, SLICES):
-            if s == 2:
-                quantize_w1("c", third)
-                score(3)
             if s == 4:
                 w3q = stationary(*quantize("w3", grouped["w3"], N, ("raw_w3",), ("scales_w3",)))
             for i in range(2 if s == LAST else 0):
@@ -433,7 +430,7 @@ def tile_list_cave_wall_growth_kernel(
             if s < LAST:
                 form_source(s + 1)
             nc.vector.tensor_copy(page_a[:].indirect(idx2[:]), source[s % 2][:])
-            if 2 <= s <= LAST - 2:
+            if s <= LAST - 2:
                 score(s + 2)
             if s + 3 <= LAST:
                 load_eq(s + 3)
@@ -460,6 +457,8 @@ def tile_list_cave_wall_growth_kernel(
             lo, hi = PIECES[j]
             i, c0 = divmod(lo, S)
             first = [x[:, c0 : c0 + hi - lo] for x in first_pass[i]]
+            at = 4 * OUT_TILES * lo
+            results = place("results%d" % j, OUT_TILES * (hi - lo), F32, "wg", at)
             for nb in range(OUT_TILES):
                 bank = bank_of(("rate", "sum", "score", "turn")[(OUT_TILES * j + nb) // 2 % 4])
                 for b, (codes, scales) in enumerate((first, (last_codes[:, lo:hi], last_scales[:, lo:hi]))):
@@ -467,11 +466,15 @@ def tile_list_cave_wall_growth_kernel(
                         out=bank[:, : hi - lo], lhsT=w3q[OUT_TILES * b + nb][0], lhsT_scale=w3q[OUT_TILES * b + nb][1],
                         rhs=codes.bitcast(FP8X4), rhs_scale=scales, start=(b == 0), stop=(b == 1),
                     )
-                at = 4 * (OUT_TILES * lo + nb * (hi - lo))
-                result = place("result%d_%d" % (j, nb), hi - lo, F32, *(("turned", at) if at < 8 * T2 else ("growth", at - 8 * T2)))
-                copy = nc.vector.tensor_copy if nb == 0 and j >= VECTOR_EMPTIES_FROM else nc.scalar.copy
-                copy(out=result[:], in_=bank[:, : hi - lo])
-                nc.sync.dma_start(out=out[P * nb : P * nb + P, lo:hi], in_=result[:])
+                result = results[:, nb * (hi - lo) : (nb + 1) * (hi - lo)]
+                copy = nc.vector.tensor_copy if nb == OUT_TILES - 1 and j >= VECTOR_EMPTIES_FROM else nc.scalar.copy
+                copy(out=result, in_=bank[:, : hi - lo])
+                if hi - lo == BANK:
+                    nc.sync.dma_start(out=out[P * nb : P * nb + P, lo:hi], in_=result)
+            if hi - lo < BANK:
+                nc.sync.dma_start(
+                    out=out[:, lo:hi].rearrange("(b p) m -> p b m", p=P), in_=results[:].rearrange("p (b m) -> p b m", b=OUT_TILES)
+                )
 
         parts = {}
         for step in range(len(PIECES) + 2):
@@ -482,7 +485,7 @@ def tile_list_cave_wall_growth_kernel(
                 project(j)
             if step < len(PIECES):
                 lo, hi = PIECES[step]
-                at = ("scores", 4 * lo) if step < AHEAD else ("table", 8 * PIECES[step - AHEAD][0])
+                at = ("grouped_c", 4 * lo) if step < AHEAD else ("table", 8 * PIECES[step - AHEAD][0])
                 parts[step] = place("part%d" % step, hi - lo, F32, *at)
                 nc.vector.tensor_tensor(parts[step][:], growths[LAST][:, lo:hi], page_a[:, lo:hi], MULT)
             j = step - 1

@@ -28,6 +28,7 @@ OUT_TILES = N // P
 PIECES = ((0, 256), (256, 512), (512, 1024), (1024, 1536), (1536, 1792), (1792, 2048))
 VECTOR_WEAVES = (3, 4, 5)
 AHEAD = 3
+TURNED_FROM = 1
 VECTOR_EMPTIES_FROM = 3
 
 
@@ -43,13 +44,13 @@ AT = lay_out(
     (
         ("words", 4 * S), ("bytes", S), ("w2w", 2 * H), ("w2s", H),
         ("ident", 4 * P), ("page_a", 4 * T2), ("page_b", 8 * T2), ("product", 4 * T2),
-        ("scores", 4 * S), ("source", 8 * S), ("gain", 4 * S), ("sink", 8 * S), ("eq", 12 * S),
+        ("scores", 4 * S), ("source", 8 * S), ("gain", 4 * S), ("crossed", 4 * S), ("sink", 8 * S), ("eq", 12 * S),
         ("wall", 8 * T2), ("wg", 16 * S), ("results", 4 * T2),
-        ("codes_a", 4 * 256), ("scales_a", 256), ("scales_c", 768),
+        ("codes_a", 4 * 256), ("scales_a", 256), ("scales_b", 256), ("scales_c", 512),
         ("scales_w3", 768),
         ("table", 4 * T),
         ("table_bytes", T), ("raw_a", 16 * 256), ("grouped_a", 8 * 256), ("dealt", 2048), ("first_gain", 4 * S),
-        ("raw_w3", 16 * 768), ("growth", 4 * T2), ("raw_c", 16 * 768), ("grouped_c", 4 * T2), ("grouped_w3", 4 * T2),
+        ("raw_w3", 16 * 768), ("growth", 4 * T2), ("raw_b", 16 * 256), ("grouped_b", 8 * 256), ("raw_c", 16 * 512), ("grouped_c", 4 * T2), ("grouped_w3", 4 * T2),
         ("turned", 8 * T2), ("codes_z", 4 * T2), ("scales_z", T2),
     )
 )
@@ -121,8 +122,9 @@ def tile_list_cave_wall_growth_kernel(
             grouped = place("grouped_" + part, 4 * (hi - lo), BF16, "grouped_" + part)
             plain = min(hi, 512) - lo
             planes = raw[:].rearrange("p (t c) -> p t c", t=4)
-            interleave(grouped[:, : 4 * plain], planes[:, :, :plain].rearrange("p t (b c) -> p b t c", c=4), 4)
-            if hi > 512:
+            if plain > 0:
+                interleave(grouped[:], planes.rearrange("p t (b c) -> p b t c", c=4), 4)
+            else:
                 dealt = planes[:, :, plain:].rearrange("p t (b e) -> p b t e", e=8)
                 c0 = 4 * plain
                 interleave(grouped[:, c0 : c0 + 1024], dealt[:, :, :, 0:4], 4)
@@ -163,7 +165,7 @@ def tile_list_cave_wall_growth_kernel(
         w1q = []
 
         def quantize_w1(part, grouped):
-            w1q.extend(stationary(*quantize("w1" + part, grouped, 384, ("raw_c" if part == "c" else "codes_" + part,), ("scales_" + part,))))
+            w1q.extend(stationary(*quantize("w1" + part, grouped, 512, ("codes_a" if part == "a" else "raw_" + part,), ("scales_" + part,))))
 
         w2q = [(w2w[:, 2 * c0 : 2 * c0 + 2 * P], w2s[:, c0 : c0 + P]) for c0 in range(0, H // 2, P)]
 
@@ -196,6 +198,10 @@ def tile_list_cave_wall_growth_kernel(
             for i, matrix in enumerate((wg1, wg2)):
                 for p0 in range(0, P, span):
                     nc.sync.dma_start(out=both[p0 : p0 + span, S * i : S * i + S], in_=by_eights(matrix)[:, rows])
+            if s == LAST:
+                nc.gpsimd.tensor_scalar(both[:, :S], both[:, :S], -1.0, 0.0, MULT, ADD)
+            else:
+                nc.scalar.mul(both[:, :S], both[:, :S], -1.0)
             weights[s] = both
             if s == 4:
                 weights[5] = both
@@ -220,7 +226,10 @@ def tile_list_cave_wall_growth_kernel(
             )
             if weighted is not None:
                 nc.vector.tensor_tensor(weighted, bank[:], weights[s][:, halves[h]], MULT)
-            nc.scalar.copy(out=scores[:, halves[h]], in_=bank[:])
+            if s < TURNED_FROM:
+                nc.scalar.copy(out=scores[:, halves[h]], in_=bank[:])
+            else:
+                nc.scalar.mul(scores[:, halves[h]], bank[:], -1.0)
 
         def score(s):
             for h in range(2):
@@ -239,18 +248,34 @@ def tile_list_cave_wall_growth_kernel(
         gains = {}
 
         def weigh_rate(s):
-            at = (("first_gain", 0), ("gain", 0))[s] if s < 2 else ("eq", 4 * S * ((s - 1) % 3))
+            at = ("first_gain", 0) if s == 0 else ("gain", 0)
             gains[s] = place("gain%d" % s, S, F32, *at)
             for h in range(2):
                 nc.vector.tensor_tensor(gains[s][:, halves[h]], rates[s, h][:], weights[s][:, S + BANK * h : S + BANK * (h + 1)], MULT)
 
-        PRODUCT_AT = {1: ("growth", 0), 3: ("grouped_w3", 0), 5: ("grouped_w3", 0), 6: ("table", 4 * T2)}
-        GAP_AT = {1: ("raw_c", -S), 4: ("raw_w3", 0), 7: ("codes_z", 2 * S)}
+        PRODUCT_AT = {1: ("grouped_c", 0), 3: ("grouped_w3", 0), 5: ("grouped_w3", 0), 6: ("table", 4 * T2)}
+        GAP_AT = {1: ("raw_b", -S), 2: ("raw_c", 0), 4: ("raw_w3", 0), 7: ("codes_z", 2 * S)}
         gaps = {}
 
         def subtract(s):
             gaps[s] = place("gap%d" % s, S, F32, *GAP_AT.get(s, PRODUCT_AT.get(s - 1, ("product", 0))))
-            nc.gpsimd.tensor_tensor(gaps[s][:], scores[:], eqs[s][:], SUB)
+            if s < TURNED_FROM:
+                nc.gpsimd.tensor_tensor(gaps[s][:], scores[:], eqs[s][:], SUB)
+                return
+            for half in halves:
+                bank = bank_of("rate")
+                for c0 in range(0, BANK, P):
+                    nc.tensor.transpose(bank[:, c0 : c0 + P], crossed[:, half][:, c0 : c0 + P], ident[:])
+                nc.scalar.copy(out=gaps[s][:, half], in_=bank[:])
+
+        crossed = place("crossed", S, F32, "crossed")
+
+        def subtract_turned(s):
+            for half in halves:
+                bank = bank_of("turn")
+                add_transposed(bank, eqs[s][:, half], True)
+                add_transposed(bank, scores[:, half], False)
+                nc.scalar.mul(crossed[:, half], bank[:], -1.0)
 
         def form_sink(s):
             if s == LAST:
@@ -313,7 +338,7 @@ def tile_list_cave_wall_growth_kernel(
             for j in range(2):
                 words = turned[0, 2 * i + j][:].bitcast(F32)
                 for h in range(2):
-                    bank = bank_of("turn")
+                    bank = bank_of("sum")
                     for u in range(2):
                         for g2 in range(2):
                             w0 = P * (4 * u + 2 * h + g2)
@@ -344,12 +369,13 @@ def tile_list_cave_wall_growth_kernel(
             return pairs[j][:, hi - lo :].bitcast(BF16).rearrange("p (m e) -> p m e", e=2)
 
         def form_third_lane(product):
-            lane = place("lane", T2, BF16, "grouped_c")
             for c0 in range(0, T2, S):
                 cols = slice(c0, c0 + S)
-                nc.gpsimd.tensor_tensor(lane[:, cols], product[:, cols], walls[LAST - 1][:, cols], ADD)
-            for j, (lo, hi) in enumerate(PIECES):
-                nc.scalar.copy(out=last_lanes(j)[:, :, 0], in_=lane[:, lo:hi])
+                lane = place("lane%d" % c0, S, BF16, "grouped_c", BANK + 6 * c0)
+                nc.gpsimd.tensor_tensor(lane[:], product[:, cols], walls[LAST - 1][:, cols], ADD)
+                for j, (lo, hi) in enumerate(PIECES):
+                    if c0 <= lo < c0 + S:
+                        nc.scalar.copy(out=last_lanes(j)[:, :, 0], in_=lane[:, lo - c0 : hi - c0])
 
         nc.vector.memset(tabs[:].bitcast(I32), 0)
         nc.gpsimd.memset(w2s[:].bitcast(I32), 0)
@@ -371,47 +397,49 @@ def tile_list_cave_wall_growth_kernel(
             weights[s] = wg
         nc.sync.dma_start(out=w2w[:].bitcast(I32), in_=w2_words[0].bitcast(I32))
         nc.sync.dma_start(out=wg[:, S:], in_=wg2)
-        for h in range(2):
-            nc.sync.dma_start(out=wg[:, halves[h]], in_=wg1[:, halves[h]])
+        nc.sync.dma_start(out=wg[:, :S], in_=wg1)
         load_eq(0)
+        second = group_w1("b", 256, 512)
         load_eq(1)
-        third = group_w1("c", 256, 1024)
         nc.vector.tensor_copy(scale_bytes[:], tabs[:].indirect(idx[:]))
         for h in range(2):
             nc.vector.tensor_copy(words[:, halves[h]], tabw[:].indirect(idx[:, 32 * h : 32 * h + 32]))
         quantize_w1("a", first)
         rate(0)
         weigh_rate(0)
-        score_half(0, 0, source[0][:, halves[0]])
-        nc.vector.tensor_copy(page_a[:].indirect(idx2[:, :32]), source[0][:, halves[0]])
-        score_half(0, 1)
-        nc.gpsimd.tensor_tensor(source[0][:, halves[1]], scores[:, halves[1]], wg[:, halves[1]], MULT)
+        for h in range(2):
+            score_half(0, h, source[0][:, halves[h]])
         rate(1)
         weigh_rate(1)
-        nc.vector.tensor_copy(page_a[:].indirect(idx2[:, 32:]), source[0][:, halves[1]])
+        nc.vector.tensor_copy(page_a[:].indirect(idx2[:]), source[0][:])
         subtract(0)
         form_sink(0)
         for i in range(2):
             deal_w2(i)
+        nc.scalar.mul(wg[:, :S], wg[:, :S], -1.0)
         score(1)
+        subtract_turned(1)
         scatter_sink(0)
-        rate(2)
         subtract(1)
+        rate(2)
         form_sink(1)
         form_source(1)
-        quantize_w1("c", third)
+        quantize_w1("b", second)
         exponentiate(0)
         score(2)
         load_eq(2)
+        subtract_turned(2)
+        third = group_w1("c", 512, 1024)
         load_wall(0)
         load_wall(1)
-        load_eq(3)
         raw_w3 = load_w3()
         load_weights(4)
 
         first_pass = []
         grouped = {}
         for s in range(1, SLICES):
+            if s == 2:
+                quantize_w1("c", third)
             if s == 4:
                 w3q = stationary(*quantize("w3", grouped["w3"], N, ("raw_w3",), ("scales_w3",)))
             for i in range(2 if s == LAST else 0):
@@ -419,21 +447,22 @@ def tile_list_cave_wall_growth_kernel(
             if s < LAST:
                 weigh_rate(s + 1)
             scatter_sink(s)
-            if s + 2 <= LAST:
-                rate(s + 2)
             product = grow(s - 1)
             if s < LAST:
-                form_z(s - 1, product)
                 subtract(s + 1)
+                form_z(s - 1, product)
+            if s + 2 <= LAST:
+                rate(s + 2)
+            if s < LAST:
                 form_sink(s + 1)
             exponentiate(s)
             if s < LAST:
                 form_source(s + 1)
             nc.vector.tensor_copy(page_a[:].indirect(idx2[:]), source[s % 2][:])
             if s <= LAST - 2:
+                load_eq(s + 2)
                 score(s + 2)
-            if s + 3 <= LAST:
-                load_eq(s + 3)
+                subtract_turned(s + 2)
             if s + 1 <= LAST:
                 load_wall(s + 1)
             if s == 2:
@@ -441,9 +470,8 @@ def tile_list_cave_wall_growth_kernel(
                 grouped["w3"] = group_w3(raw_w3)
             if s == 4:
                 load_weights(7)
-                grouped[0] = regroup(0)
-            if s == 5:
-                grouped[1] = regroup(1)
+            if s in (4, 5):
+                grouped[s - 4] = regroup(s - 4)
             if s == LAST - 1:
                 turn_first_lanes()
             if s == LAST:

@@ -28,6 +28,7 @@ OUT_TILES = N // P
 PIECES = ((0, 256), (256, 512), (512, 1024), (1024, 1536), (1536, 1792), (1792, 2048))
 VECTOR_WEAVES = (3, 4, 5)
 AHEAD = 3
+SHARED = range(3, 8)
 TURNED_FROM = 1
 VECTOR_EMPTIES_FROM = 3
 
@@ -44,8 +45,8 @@ AT = lay_out(
     (
         ("words", 4 * S), ("bytes", S), ("w2w", 2 * H), ("w2s", H),
         ("ident", 4 * P), ("page_a", 4 * T2), ("page_b", 8 * T2), ("product", 4 * T2),
-        ("scores", 4 * S), ("source", 8 * S), ("gain", 4 * S), ("crossed", 4 * S), ("sink", 8 * S), ("eq", 12 * S),
-        ("wall", 8 * T2), ("wg", 16 * S), ("results", 4 * T2),
+        ("scores", 4 * S), ("source", 8 * S), ("gain", 4 * S), ("crossed", 4 * S), ("sink", 8 * S), ("eq", 8 * S), ("rate", 2 * S),
+        ("wall", 8 * T2), ("wg", 24 * S),
         ("codes_a", 4 * 256), ("scales_a", 256), ("scales_b", 256), ("scales_c", 512),
         ("scales_w3", 768),
         ("table", 4 * T),
@@ -190,26 +191,30 @@ def tile_list_cave_wall_growth_kernel(
             w2q.extend((words[:, 2 * c0 : 2 * c0 + 2 * P], scales[:, c0 : c0 + P]) for c0 in (0, P))
 
         weights = {}
+        negated = {}
+
+        def negate(s, out):
+            nc.scalar.mul(out, weights[s][:, :S], -1.0)
+            negated[s] = out
 
         def load_weights(s):
-            both = place("wg%d" % s, 2 * S, F32, "wg", 8 * S * (0, 0, 0, 0, 1, 1, 0, 1)[s])
+            both = place("wg%d" % s, 2 * S, F32, "wg", 8 * S * {4: 1, 6: 2, 7: 0}[s])
             rows = {4: slice(0, 4), 6: slice(4, 6), 7: slice(6, 8)}[s]
             span = 16 * (rows.stop - rows.start)
             for i, matrix in enumerate((wg1, wg2)):
                 for p0 in range(0, P, span):
                     nc.sync.dma_start(out=both[p0 : p0 + span, S * i : S * i + S], in_=by_eights(matrix)[:, rows])
-            if s == LAST:
-                nc.gpsimd.tensor_scalar(both[:, :S], both[:, :S], -1.0, 0.0, MULT, ADD)
-            else:
-                nc.scalar.mul(both[:, :S], both[:, :S], -1.0)
             weights[s] = both
+            if s < LAST:
+                negate(s, both[:, :S])
             if s == 4:
                 weights[5] = both
+                negated[5] = negated[4]
 
         eqs = {}
 
         def load_eq(s):
-            eqs[s] = place("eq%d" % s, S, F32, "eq", 4 * S * (s % 3))
+            eqs[s] = place("eq%d" % s, S, F32, *(("raw_c", 2 * S) if s == 5 else ("eq", 4 * S * (s % 2))))
             nc.sync.dma_start(out=eqs[s][:], in_=slice_rows(eq, s))
 
         walls = {}
@@ -239,7 +244,7 @@ def tile_list_cave_wall_growth_kernel(
 
         def rate(s):
             for h in range(2):
-                rates[s, h] = bank_of("rate")
+                rates[s, h] = bank_of("score" if s in SHARED and h == 0 else "rate")
                 nc.tensor.matmul_mx(
                     out=rates[s, h][:], lhsT=w2q[s][0].bitcast(FP4X4), lhsT_scale=w2q[s][1],
                     rhs=vw[h], rhs_scale=vs[h], start=True, stop=True,
@@ -248,12 +253,12 @@ def tile_list_cave_wall_growth_kernel(
         gains = {}
 
         def weigh_rate(s):
-            at = ("first_gain", 0) if s == 0 else ("gain", 0)
-            gains[s] = place("gain%d" % s, S, F32, *at)
-            for h in range(2):
+            if s not in SHARED:
+                gains[s] = place("gain%d" % s, S, F32, "first_gain" if s == 0 else "gain")
+            for h in range(1 if s in SHARED else 0, 2):
                 nc.vector.tensor_tensor(gains[s][:, halves[h]], rates[s, h][:], weights[s][:, S + BANK * h : S + BANK * (h + 1)], MULT)
 
-        PRODUCT_AT = {1: ("grouped_c", 0), 3: ("grouped_w3", 0), 5: ("grouped_w3", 0), 6: ("table", 4 * T2)}
+        PRODUCT_AT = {1: ("grouped_c", 0), 2: ("growth", 0), 3: ("grouped_w3", 0), 5: ("grouped_c", 0), 6: ("table", 4 * T2)}
         GAP_AT = {1: ("raw_b", -S), 2: ("raw_c", 0), 4: ("raw_w3", 0), 7: ("codes_z", 2 * S)}
         gaps = {}
 
@@ -263,7 +268,7 @@ def tile_list_cave_wall_growth_kernel(
                 nc.gpsimd.tensor_tensor(gaps[s][:], scores[:], eqs[s][:], SUB)
                 return
             for half in halves:
-                bank = bank_of("rate")
+                bank = bank_of("score")
                 for c0 in range(0, BANK, P):
                     nc.tensor.transpose(bank[:, c0 : c0 + P], crossed[:, half][:, c0 : c0 + P], ident[:])
                 nc.scalar.copy(out=gaps[s][:, half], in_=bank[:])
@@ -272,10 +277,16 @@ def tile_list_cave_wall_growth_kernel(
 
         def subtract_turned(s):
             for half in halves:
-                bank = bank_of("turn")
+                bank = bank_of("sum")
                 add_transposed(bank, eqs[s][:, half], True)
                 add_transposed(bank, scores[:, half], False)
                 nc.scalar.mul(crossed[:, half], bank[:], -1.0)
+
+        first_rates = place("first_rates", BANK, F32, "rate")
+
+        def weigh_first_rates(s):
+            gains[s] = place("gain%d" % s, S, F32, "gain")
+            nc.gpsimd.tensor_tensor(gains[s][:, :BANK], first_rates[:], weights[s][:, S : S + BANK], MULT)
 
         def form_sink(s):
             if s == LAST:
@@ -283,7 +294,7 @@ def tile_list_cave_wall_growth_kernel(
             nc.gpsimd.tensor_tensor(sink[s % 2][:], gaps[s][:], gains[s][:], MULT)
 
         def form_source(s):
-            nc.gpsimd.tensor_tensor(source[s % 2][:], scores[:], weights[s][:, :S], MULT)
+            nc.gpsimd.tensor_tensor(source[s % 2][:], scores[:], negated[s], MULT)
 
         def scatter_sink(s):
             nc.vector.tensor_copy(page_b[s % 2][:].indirect(idx3[:]), sink[s % 2][:])
@@ -338,7 +349,7 @@ def tile_list_cave_wall_growth_kernel(
             for j in range(2):
                 words = turned[0, 2 * i + j][:].bitcast(F32)
                 for h in range(2):
-                    bank = bank_of("sum")
+                    bank = bank_of("turn")
                     for u in range(2):
                         for g2 in range(2):
                             w0 = P * (4 * u + 2 * h + g2)
@@ -416,7 +427,8 @@ def tile_list_cave_wall_growth_kernel(
         form_sink(0)
         for i in range(2):
             deal_w2(i)
-        nc.scalar.mul(wg[:, :S], wg[:, :S], -1.0)
+        negate(1, wg[:, :S])
+        negated[2] = negated[3] = negated[1]
         score(1)
         subtract_turned(1)
         scatter_sink(0)
@@ -430,13 +442,13 @@ def tile_list_cave_wall_growth_kernel(
         load_eq(2)
         subtract_turned(2)
         third = group_w1("c", 512, 1024)
+        grouped = {"w3": group_w3(load_w3())}
         load_wall(0)
         load_wall(1)
-        raw_w3 = load_w3()
         load_weights(4)
+        load_weights(6)
 
         first_pass = []
-        grouped = {}
         for s in range(1, SLICES):
             if s == 2:
                 quantize_w1("c", third)
@@ -453,11 +465,14 @@ def tile_list_cave_wall_growth_kernel(
                 form_z(s - 1, product)
             if s + 2 <= LAST:
                 rate(s + 2)
-            if s < LAST:
-                form_sink(s + 1)
-            exponentiate(s)
+            if s + 2 in SHARED:
+                nc.scalar.copy(out=first_rates[:], in_=rates[s + 2, 0][:])
             if s < LAST:
                 form_source(s + 1)
+                form_sink(s + 1)
+            if s + 2 in SHARED:
+                weigh_first_rates(s + 2)
+            exponentiate(s)
             nc.vector.tensor_copy(page_a[:].indirect(idx2[:]), source[s % 2][:])
             if s <= LAST - 2:
                 load_eq(s + 2)
@@ -466,10 +481,9 @@ def tile_list_cave_wall_growth_kernel(
             if s + 1 <= LAST:
                 load_wall(s + 1)
             if s == 2:
-                load_weights(6)
-                grouped["w3"] = group_w3(raw_w3)
-            if s == 4:
-                load_weights(7)
+                load_weights(LAST)
+            if s == 3:
+                negate(LAST, place("last_negated", S, F32, "raw_c", 2 * S)[:])
             if s in (4, 5):
                 grouped[s - 4] = regroup(s - 4)
             if s == LAST - 1:

@@ -28,9 +28,9 @@ OUT_TILES = N // P
 PIECES = ((0, 256), (256, 512), (512, 1024), (1024, 1536), (1536, 1792), (1792, 2048))
 VECTOR_WEAVES = (3, 4, 5)
 AHEAD = 3
-SHARED = range(3, 8)
+ON_GPSIMD = (0, 0, 512, 512, 512, 512, 512, 512)
 TURNED_FROM = 1
-VECTOR_EMPTIES_FROM = 3
+VECTOR_EMPTIES = ((4, 1), (4, 2), (5, 2))
 
 
 def lay_out(areas):
@@ -45,7 +45,7 @@ AT = lay_out(
     (
         ("words", 4 * S), ("bytes", S), ("w2w", 2 * H), ("w2s", H),
         ("ident", 4 * P), ("page_a", 4 * T2), ("page_b", 8 * T2), ("product", 4 * T2),
-        ("scores", 4 * S), ("source", 8 * S), ("gain", 4 * S), ("crossed", 4 * S), ("sink", 8 * S), ("eq", 8 * S), ("rate", 2 * S),
+        ("scores", 4 * S), ("source", 8 * S), ("gain", 4 * S), ("crossed", 4 * S), ("sink", 8 * S), ("eq", 8 * S), ("rate", 4 * S),
         ("wall", 8 * T2), ("wg", 24 * S),
         ("codes_a", 4 * 256), ("scales_a", 256), ("scales_b", 256), ("scales_c", 512),
         ("scales_w3", 768),
@@ -205,11 +205,8 @@ def tile_list_cave_wall_growth_kernel(
                 for p0 in range(0, P, span):
                     nc.sync.dma_start(out=both[p0 : p0 + span, S * i : S * i + S], in_=by_eights(matrix)[:, rows])
             weights[s] = both
-            if s < LAST:
-                negate(s, both[:, :S])
             if s == 4:
                 weights[5] = both
-                negated[5] = negated[4]
 
         eqs = {}
 
@@ -244,7 +241,7 @@ def tile_list_cave_wall_growth_kernel(
 
         def rate(s):
             for h in range(2):
-                rates[s, h] = bank_of("score" if s in SHARED and h == 0 else "rate")
+                rates[s, h] = bank_of("score" if ON_GPSIMD[s] >= BANK * (h + 1) else "rate")
                 nc.tensor.matmul_mx(
                     out=rates[s, h][:], lhsT=w2q[s][0].bitcast(FP4X4), lhsT_scale=w2q[s][1],
                     rhs=vw[h], rhs_scale=vs[h], start=True, stop=True,
@@ -253,10 +250,10 @@ def tile_list_cave_wall_growth_kernel(
         gains = {}
 
         def weigh_rate(s):
-            if s not in SHARED:
-                gains[s] = place("gain%d" % s, S, F32, "first_gain" if s == 0 else "gain")
-            for h in range(1 if s in SHARED else 0, 2):
-                nc.vector.tensor_tensor(gains[s][:, halves[h]], rates[s, h][:], weights[s][:, S + BANK * h : S + BANK * (h + 1)], MULT)
+            gains[s] = place("gain%d" % s, S, F32, "first_gain" if s == 0 else "gain")
+            for h in range(ON_GPSIMD[s] // BANK, 2):
+                lo, hi = max(ON_GPSIMD[s], BANK * h), BANK * (h + 1)
+                nc.vector.tensor_tensor(gains[s][:, lo:hi], rates[s, h][:, lo - BANK * h :], weights[s][:, S + lo : S + hi], MULT)
 
         PRODUCT_AT = {1: ("grouped_c", 0), 2: ("growth", 0), 3: ("grouped_w3", 0), 5: ("grouped_c", 0), 6: ("table", 4 * T2)}
         GAP_AT = {1: ("raw_b", -S), 2: ("raw_c", 0), 4: ("raw_w3", 0), 7: ("codes_z", 2 * S)}
@@ -282,11 +279,17 @@ def tile_list_cave_wall_growth_kernel(
                 add_transposed(bank, scores[:, half], False)
                 nc.scalar.mul(crossed[:, half], bank[:], -1.0)
 
-        first_rates = place("first_rates", BANK, F32, "rate")
+        first_rates = place("first_rates", S, F32, "rate")
+
+        def copy_first_rates(s):
+            for lo in range(0, ON_GPSIMD[s], BANK):
+                hi = min(lo + BANK, ON_GPSIMD[s])
+                nc.scalar.copy(out=first_rates[:, lo:hi], in_=rates[s, lo // BANK][:, : hi - lo])
 
         def weigh_first_rates(s):
-            gains[s] = place("gain%d" % s, S, F32, "gain")
-            nc.gpsimd.tensor_tensor(gains[s][:, :BANK], first_rates[:], weights[s][:, S : S + BANK], MULT)
+            if ON_GPSIMD[s]:
+                width = ON_GPSIMD[s]
+                nc.gpsimd.tensor_tensor(gains[s][:, :width], first_rates[:, :width], weights[s][:, S : S + width], MULT)
 
         def form_sink(s):
             if s == LAST:
@@ -434,8 +437,9 @@ def tile_list_cave_wall_growth_kernel(
         scatter_sink(0)
         subtract(1)
         rate(2)
-        form_sink(1)
+        copy_first_rates(2)
         form_source(1)
+        form_sink(1)
         quantize_w1("b", second)
         exponentiate(0)
         score(2)
@@ -461,17 +465,15 @@ def tile_list_cave_wall_growth_kernel(
             scatter_sink(s)
             product = grow(s - 1)
             if s < LAST:
+                weigh_first_rates(s + 1)
                 subtract(s + 1)
-                form_z(s - 1, product)
             if s + 2 <= LAST:
                 rate(s + 2)
-            if s + 2 in SHARED:
-                nc.scalar.copy(out=first_rates[:], in_=rates[s + 2, 0][:])
+                copy_first_rates(s + 2)
             if s < LAST:
+                form_z(s - 1, product)
                 form_source(s + 1)
                 form_sink(s + 1)
-            if s + 2 in SHARED:
-                weigh_first_rates(s + 2)
             exponentiate(s)
             nc.vector.tensor_copy(page_a[:].indirect(idx2[:]), source[s % 2][:])
             if s <= LAST - 2:
@@ -482,6 +484,11 @@ def tile_list_cave_wall_growth_kernel(
                 load_wall(s + 1)
             if s == 2:
                 load_weights(LAST)
+            if s == 1:
+                negate(4, weights[4][:, :S])
+                negated[5] = negated[4]
+            if s == 2:
+                negate(6, weights[6][:, :S])
             if s == 3:
                 negate(LAST, place("last_negated", S, F32, "raw_c", 2 * S)[:])
             if s in (4, 5):
@@ -509,7 +516,7 @@ def tile_list_cave_wall_growth_kernel(
                         rhs=codes.bitcast(FP8X4), rhs_scale=scales, start=(b == 0), stop=(b == 1),
                     )
                 result = results[:, nb * (hi - lo) : (nb + 1) * (hi - lo)]
-                copy = nc.vector.tensor_copy if nb == OUT_TILES - 1 and j >= VECTOR_EMPTIES_FROM else nc.scalar.copy
+                copy = nc.vector.tensor_copy if (j, nb) in VECTOR_EMPTIES else nc.scalar.copy
                 copy(out=result, in_=bank[:, : hi - lo])
                 if hi - lo == BANK:
                     nc.sync.dma_start(out=out[P * nb : P * nb + P, lo:hi], in_=result)

@@ -28,7 +28,7 @@ OUT_TILES = N // P
 PIECES = ((0, 256), (256, 512), (512, 1024), (1024, 1536), (1536, 1792), (1792, 2048))
 VECTOR_WEAVES = (3, 4, 5)
 AHEAD = 3
-ON_GPSIMD = (0, 0, 512, 512, 512, 512, 512, 512)
+ON_GPSIMD = (0, 0, 512, 512, 512, 512, 512, 1024)
 TURNED_FROM = 1
 VECTOR_EMPTIES = ((4, 1), (4, 2), (5, 2))
 
@@ -391,16 +391,17 @@ def tile_list_cave_wall_growth_kernel(
                     if c0 <= lo < c0 + S:
                         nc.scalar.copy(out=last_lanes(j)[:, :, 0], in_=lane[:, lo - c0 : hi - c0])
 
-        nc.vector.memset(tabs[:].bitcast(I32), 0)
+        nc.gpsimd.memset(tabs[:, : T // 2].bitcast(I32), 0)
+        nc.vector.memset(tabs[:, T // 2 :].bitcast(I32), 0)
         nc.gpsimd.memset(w2s[:].bitcast(I32), 0)
         nc.sync.dma_start(idx[:], offs)
         nc.sync.dma_start(idx2[:], offs2)
         nc.sync.dma_start(idx3[:], offs3)
-        load_scale_rows(nc.sync, w2s, w2_scales[0])
         load_scale_rows(nc.sync, tabs, tab_scales[0])
         table = tab_words[0].rearrange("p t i -> p (t i)").bitcast(I32)
         for c0 in range(0, T, T // 2):
             nc.sync.dma_start(out=tabw[:].bitcast(I32)[:, c0 : c0 + T // 2], in_=table[:, c0 : c0 + T // 2])
+        load_scale_rows(nc.sync, w2s, w2_scales[0])
         first = group_w1("a", 0, 256)
         nc.vector.memset(page_a[:], 0.0)
         make_identity(nc, ident[:])

@@ -208,10 +208,11 @@ def tile_list_cave_wall_growth_kernel(
             if s == 4:
                 weights[5] = both
 
+        EQ_AT = {2: ("wg", 20 * S), 3: ("wg", 16 * S), 4: ("raw_b", S), 5: ("raw_c", 2 * S)}
         eqs = {}
 
         def load_eq(s):
-            eqs[s] = place("eq%d" % s, S, F32, *(("raw_c", 2 * S) if s == 5 else ("eq", 4 * S * (s % 2))))
+            eqs[s] = place("eq%d" % s, S, F32, *EQ_AT.get(s, ("eq", 4 * S * (s % 2))))
             nc.sync.dma_start(out=eqs[s][:], in_=slice_rows(eq, s))
 
         walls = {}
@@ -416,6 +417,7 @@ def tile_list_cave_wall_growth_kernel(
         load_eq(0)
         second = group_w1("b", 256, 512)
         load_eq(1)
+        load_eq(2)
         nc.vector.tensor_copy(scale_bytes[:], tabs[:].indirect(idx[:]))
         for h in range(2):
             nc.vector.tensor_copy(words[:, halves[h]], tabw[:].indirect(idx[:, 32 * h : 32 * h + 32]))
@@ -444,14 +446,13 @@ def tile_list_cave_wall_growth_kernel(
         quantize_w1("b", second)
         exponentiate(0)
         score(2)
-        load_eq(2)
         subtract_turned(2)
         third = group_w1("c", 512, 1024)
-        grouped = {"w3": group_w3(load_w3())}
         load_wall(0)
+        grouped = {"w3": group_w3(load_w3())}
+        load_eq(3)
         load_wall(1)
         load_weights(4)
-        load_weights(6)
 
         first_pass = []
         for s in range(1, SLICES):
@@ -478,18 +479,20 @@ def tile_list_cave_wall_growth_kernel(
             exponentiate(s)
             nc.vector.tensor_copy(page_a[:].indirect(idx2[:]), source[s % 2][:])
             if s <= LAST - 2:
-                load_eq(s + 2)
                 score(s + 2)
                 subtract_turned(s + 2)
+            if s + 3 <= LAST:
+                load_eq(s + 3)
             if s + 1 <= LAST:
                 load_wall(s + 1)
             if s == 2:
                 load_weights(LAST)
             if s == 1:
+                load_weights(6)
                 negate(4, weights[4][:, :S])
                 negated[5] = negated[4]
             if s == 2:
-                negate(6, weights[6][:, :S])
+                negate(6, place("sixth_negated", S, F32, "raw_b", S)[:])
             if s == 3:
                 negate(LAST, place("last_negated", S, F32, "raw_c", 2 * S)[:])
             if s in (4, 5):

@@ -28,7 +28,7 @@ OUT_TILES = N // P
 PIECES = ((0, 256), (256, 512), (512, 1024), (1024, 1536), (1536, 1792), (1792, 2048))
 VECTOR_WEAVES = (3, 4, 5)
 AHEAD = 3
-ON_GPSIMD = (0, 0, 512, 512, 512, 512, 512, 1024)
+ON_GPSIMD = (0, 0, 512, 512, 1024, 512, 1024, 1024)
 TURNED_FROM = 1
 VECTOR_EMPTIES = ((4, 1), (4, 2), (5, 2))
 

@@ -28,7 +28,9 @@ OUT_TILES = N // P
 PIECES = ((0, 256), (256, 512), (512, 1024), (1024, 1536), (1536, 1792), (1792, 2048))
 VECTOR_WEAVES = (3, 4, 5)
 AHEAD = 3
-ON_GPSIMD = (0, 0, 512, 512, 1024, 512, 1024, 1024)
+RINGS = {"score": 3, "sum": 2, "turn": 2, "rate": 1}
+OUT_RINGS = ("rate", "sum", "sum", "score", "score", "score", "turn", "turn")
+ON_GPSIMD = (0, 0, 1024, 512, 1024, 1024, 1024, 1024)
 TURNED_FROM = 1
 VECTOR_EMPTIES = ((4, 1), (4, 2), (5, 2))
 
@@ -48,11 +50,11 @@ AT = lay_out(
         ("scores", 4 * S), ("source", 8 * S), ("gain", 4 * S), ("crossed", 4 * S), ("sink", 8 * S), ("eq", 8 * S), ("rate", 4 * S),
         ("wall", 8 * T2), ("wg", 24 * S),
         ("codes_a", 4 * 256), ("scales_a", 256), ("scales_b", 256), ("scales_c", 512),
-        ("scales_w3", 768),
+
         ("table", 4 * T),
         ("table_bytes", T), ("raw_a", 16 * 256), ("grouped_a", 8 * 256), ("dealt", 2048), ("first_gain", 4 * S),
-        ("raw_w3", 16 * 768), ("growth", 4 * T2), ("raw_b", 16 * 256), ("grouped_b", 8 * 256), ("raw_c", 16 * 512), ("grouped_c", 4 * T2), ("grouped_w3", 4 * T2),
-        ("turned", 8 * T2), ("codes_z", 4 * T2), ("scales_z", T2),
+        ("raw_w3", 16 * 768), ("growth", 4 * T2), ("raw_b", 16 * 256), ("grouped_b", 8 * 256), ("raw_c", 16 * 512), ("grouped_c", 4 * T2), ("grouped_w3", 8 * 768), ("third", 4 * T2),
+        ("turned", 8 * T2), ("codes_z", 4 * T2 + S), ("scales_z", T2),
     )
 )
 
@@ -70,7 +72,7 @@ def tile_list_cave_wall_growth_kernel(
             return sbuf.tile([P, columns], dtype, name=name, align_bytes=64, offset=AT[area] + skip)
 
         def bank_of(ring):
-            return psum.tile([P, BANK], F32, name=ring)
+            return psum.tile([P, BANK], F32, name=ring, bufs=RINGS[ring])
 
         def by_eights(rows):
             return rows.rearrange("(b e) n -> b e n", e=8)
@@ -242,7 +244,7 @@ def tile_list_cave_wall_growth_kernel(
 
         def rate(s):
             for h in range(2):
-                rates[s, h] = bank_of("score" if ON_GPSIMD[s] >= BANK * (h + 1) else "rate")
+                rates[s, h] = bank_of("score" if ON_GPSIMD[s] >= BANK * (h + 1) else ("turn", "rate")[h])
                 nc.tensor.matmul_mx(
                     out=rates[s, h][:], lhsT=w2q[s][0].bitcast(FP4X4), lhsT_scale=w2q[s][1],
                     rhs=vw[h], rhs_scale=vs[h], start=True, stop=True,
@@ -251,13 +253,13 @@ def tile_list_cave_wall_growth_kernel(
         gains = {}
 
         def weigh_rate(s):
-            gains[s] = place("gain%d" % s, S, F32, "first_gain" if s == 0 else "gain")
+            gains[s] = place("gain%d" % s, S, F32, "first_gain" if s in (0, 2, 3, 5, 7) else "gain")
             for h in range(ON_GPSIMD[s] // BANK, 2):
                 lo, hi = max(ON_GPSIMD[s], BANK * h), BANK * (h + 1)
                 nc.vector.tensor_tensor(gains[s][:, lo:hi], rates[s, h][:, lo - BANK * h :], weights[s][:, S + lo : S + hi], MULT)
 
-        PRODUCT_AT = {1: ("grouped_c", 0), 2: ("growth", 0), 3: ("grouped_w3", 0), 5: ("grouped_c", 0), 6: ("table", 4 * T2)}
-        GAP_AT = {1: ("raw_b", -S), 2: ("raw_c", 0), 4: ("raw_w3", 0), 7: ("codes_z", 2 * S)}
+        PRODUCT_AT = {1: ("grouped_c", 0), 2: ("growth", 0), 3: ("third", 0), 5: ("grouped_c", 0), 6: ("table", 4 * T2)}
+        GAP_AT = {1: ("raw_b", -S), 2: ("raw_c", 0), 7: ("codes_z", 2 * S)}
         gaps = {}
 
         def subtract(s):
@@ -449,19 +451,20 @@ def tile_list_cave_wall_growth_kernel(
         subtract_turned(2)
         third = group_w1("c", 512, 1024)
         load_wall(0)
-        grouped = {"w3": group_w3(load_w3())}
         load_eq(3)
         load_wall(1)
         load_weights(4)
+        raw_w3 = load_w3()
 
+        grouped = {}
         first_pass = []
         for s in range(1, SLICES):
             if s == 2:
                 quantize_w1("c", third)
-            if s == 4:
-                w3q = stationary(*quantize("w3", grouped["w3"], N, ("raw_w3",), ("scales_w3",)))
+            if s == LAST:
+                w3q = stationary(*quantize("w3", grouped["w3"], N, ("raw_w3",), ("codes_z", 4 * S)))
             for i in range(2 if s == LAST else 0):
-                first_pass.append(quantize("z%d" % i, grouped[i], S, ("codes_z", 4 * S * i), ("scales_z", S * i)))
+                first_pass.append(quantize("z%d" % i, grouped[i], S, ("codes_z", 5 * S * i), ("scales_z", S * i)))
             if s < LAST:
                 weigh_rate(s + 1)
             scatter_sink(s)
@@ -486,6 +489,7 @@ def tile_list_cave_wall_growth_kernel(
             if s + 1 <= LAST:
                 load_wall(s + 1)
             if s == 2:
+                grouped["w3"] = group_w3(raw_w3)
                 load_weights(LAST)
             if s == 1:
                 load_weights(6)
@@ -513,7 +517,7 @@ def tile_list_cave_wall_growth_kernel(
             at = 4 * OUT_TILES * lo
             results = place("results%d" % j, OUT_TILES * (hi - lo), F32, "wg", at)
             for nb in range(OUT_TILES):
-                bank = bank_of(("rate", "sum", "score", "turn")[(OUT_TILES * j + nb) // 2 % 4])
+                bank = bank_of(OUT_RINGS[(OUT_TILES * j + nb) % len(OUT_RINGS)])
                 for b, (codes, scales) in enumerate((first, (last_codes[:, lo:hi], last_scales[:, lo:hi]))):
                     nc.tensor.matmul_mx(
                         out=bank[:, : hi - lo], lhsT=w3q[OUT_TILES * b + nb][0], lhsT_scale=w3q[OUT_TILES * b + nb][1],

@@ -28,6 +28,7 @@ OUT_TILES = N // P
 PIECES = ((0, 256), (256, 512), (512, 1024), (1024, 1536), (1536, 1792), (1792, 2048))
 VECTOR_WEAVES = (3, 4, 5)
 AHEAD = 3
+DEFERRED = (7,)
 RINGS = {"score": 3, "sum": 2, "turn": 2, "rate": 1}
 OUT_RINGS = ("rate", "sum", "sum", "score", "score", "score", "turn", "turn")
 ON_GPSIMD = (0, 0, 1024, 512, 1024, 1024, 1024, 1024)
@@ -242,8 +243,8 @@ def tile_list_cave_wall_growth_kernel(
 
         rates = {}
 
-        def rate(s):
-            for h in range(2):
+        def rate(s, which=(0, 1)):
+            for h in which:
                 rates[s, h] = bank_of("score" if ON_GPSIMD[s] >= BANK * (h + 1) else ("turn", "rate")[h])
                 nc.tensor.matmul_mx(
                     out=rates[s, h][:], lhsT=w2q[s][0].bitcast(FP4X4), lhsT_scale=w2q[s][1],
@@ -284,15 +285,13 @@ def tile_list_cave_wall_growth_kernel(
 
         first_rates = place("first_rates", S, F32, "rate")
 
-        def copy_first_rates(s):
-            for lo in range(0, ON_GPSIMD[s], BANK):
-                hi = min(lo + BANK, ON_GPSIMD[s])
-                nc.scalar.copy(out=first_rates[:, lo:hi], in_=rates[s, lo // BANK][:, : hi - lo])
+        def copy_first_rates(s, which=(0, 1)):
+            for h in which:
+                if ON_GPSIMD[s] > BANK * h:
+                    nc.scalar.copy(out=first_rates[:, halves[h]], in_=rates[s, h][:])
 
-        def weigh_first_rates(s):
-            if ON_GPSIMD[s]:
-                width = ON_GPSIMD[s]
-                nc.gpsimd.tensor_tensor(gains[s][:, :width], first_rates[:, :width], weights[s][:, S : S + width], MULT)
+        def weigh_first_rates(s, lo, hi):
+            nc.gpsimd.tensor_tensor(gains[s][:, lo:hi], first_rates[:, lo:hi], weights[s][:, S + lo : S + hi], MULT)
 
         def form_sink(s):
             if s == LAST:
@@ -470,11 +469,16 @@ def tile_list_cave_wall_growth_kernel(
             scatter_sink(s)
             product = grow(s - 1)
             if s < LAST:
-                weigh_first_rates(s + 1)
+                weigh_first_rates(s + 1, 0, BANK if s + 1 in DEFERRED else ON_GPSIMD[s + 1])
                 subtract(s + 1)
+            if s + 1 in DEFERRED:
+                rate(s + 1, (1,))
+                copy_first_rates(s + 1, (1,))
+                weigh_first_rates(s + 1, BANK, S)
             if s + 2 <= LAST:
-                rate(s + 2)
-                copy_first_rates(s + 2)
+                which = (0,) if s + 2 in DEFERRED else (0, 1)
+                rate(s + 2, which)
+                copy_first_rates(s + 2, which)
             if s < LAST:
                 form_z(s - 1, product)
                 form_source(s + 1)
@@ -526,9 +530,9 @@ def tile_list_cave_wall_growth_kernel(
                 result = results[:, nb * (hi - lo) : (nb + 1) * (hi - lo)]
                 copy = nc.vector.tensor_copy if (j, nb) in VECTOR_EMPTIES else nc.scalar.copy
                 copy(out=result, in_=bank[:, : hi - lo])
-                if hi - lo == BANK:
+                if lo < T2 - BANK:
                     nc.sync.dma_start(out=out[P * nb : P * nb + P, lo:hi], in_=result)
-            if hi - lo < BANK:
+            if lo >= T2 - BANK:
                 nc.sync.dma_start(
                     out=out[:, lo:hi].rearrange("(b p) m -> p b m", p=P), in_=results[:].rearrange("p (b m) -> p b m", b=OUT_TILES)
                 )

@@ -398,13 +398,13 @@ def tile_list_cave_wall_growth_kernel(
         nc.gpsimd.memset(w2s[:].bitcast(I32), 0)
         nc.sync.dma_start(idx[:], offs)
         nc.sync.dma_start(idx2[:], offs2)
-        nc.sync.dma_start(idx3[:], offs3)
+        nc.sync.dma_start(out=w2w[:].bitcast(I32), in_=w2_words[0].bitcast(I32))
         load_scale_rows(nc.sync, tabs, tab_scales[0])
         table = tab_words[0].rearrange("p t i -> p (t i)").bitcast(I32)
         for c0 in range(0, T, T // 2):
             nc.sync.dma_start(out=tabw[:].bitcast(I32)[:, c0 : c0 + T // 2], in_=table[:, c0 : c0 + T // 2])
-        load_scale_rows(nc.sync, w2s, w2_scales[0])
         first = group_w1("a", 0, 256)
+        load_scale_rows(nc.sync, w2s, w2_scales[0])
         nc.vector.memset(page_a[:], 0.0)
         make_identity(nc, ident[:])
         for page in page_b:
@@ -412,9 +412,9 @@ def tile_list_cave_wall_growth_kernel(
         wg = place("wg0", 2 * S, F32, "wg")
         for s in range(4):
             weights[s] = wg
-        nc.sync.dma_start(out=w2w[:].bitcast(I32), in_=w2_words[0].bitcast(I32))
         nc.sync.dma_start(out=wg[:, S:], in_=wg2)
         nc.sync.dma_start(out=wg[:, :S], in_=wg1)
+        nc.sync.dma_start(idx3[:], offs3)
         load_eq(0)
         second = group_w1("b", 256, 512)
         load_eq(1)

@@ -25,15 +25,12 @@ SLICES = H // P
 LAST = SLICES - 1
 CHUNKS = T2 // BANK
 OUT_TILES = N // P
-PIECES = ((0, 256), (256, 512), (512, 1024), (1024, 1536), (1536, 1792), (1792, 2048))
-VECTOR_WEAVES = (3, 4, 5)
+PIECES = tuple((lo, lo + 256) for lo in range(0, T2, 256))
+VECTOR_WEAVES = (7,)
 AHEAD = 3
-DEFERRED = (7,)
-RINGS = {"score": 3, "sum": 2, "turn": 2, "rate": 1}
-OUT_RINGS = ("rate", "sum", "sum", "score", "score", "score", "turn", "turn")
-ON_GPSIMD = (0, 0, 1024, 512, 1024, 1024, 1024, 1024)
-TURNED_FROM = 1
-VECTOR_EMPTIES = ((4, 1), (4, 2), (5, 2))
+VECTOR_EMPTIES = ((6, 2), (7, 1), (7, 2))
+ROW = 4 * S
+PAGE = 4 * T2
 
 
 def lay_out(areas):
@@ -46,18 +43,25 @@ def lay_out(areas):
 
 AT = lay_out(
     (
-        ("words", 4 * S), ("bytes", S), ("w2w", 2 * H), ("w2s", H),
-        ("ident", 4 * P), ("page_a", 4 * T2), ("page_b", 8 * T2), ("product", 4 * T2),
-        ("scores", 4 * S), ("source", 8 * S), ("gain", 4 * S), ("crossed", 4 * S), ("sink", 8 * S), ("eq", 8 * S), ("rate", 4 * S),
-        ("wall", 8 * T2), ("wg", 24 * S),
-        ("codes_a", 4 * 256), ("scales_a", 256), ("scales_b", 256), ("scales_c", 512),
-
-        ("table", 4 * T),
-        ("table_bytes", T), ("raw_a", 16 * 256), ("grouped_a", 8 * 256), ("dealt", 2048), ("first_gain", 4 * S),
-        ("raw_w3", 16 * 768), ("growth", 4 * T2), ("raw_b", 16 * 256), ("grouped_b", 8 * 256), ("raw_c", 16 * 512), ("grouped_c", 4 * T2), ("grouped_w3", 8 * 768), ("third", 4 * T2),
-        ("turned", 8 * T2), ("codes_z", 4 * T2 + S), ("scales_z", T2),
+        ("words", ROW), ("bytes", S), ("w2w", 2 * H), ("w2s", H), ("ident", 4 * P),
+        ("codes_first", 4 * 256), ("scales_first", 256), ("codes_rest", ROW),
+        ("page_a", 2 * PAGE), ("page_b", 2 * PAGE),
+        ("r0", PAGE), ("r1", PAGE), ("r2", PAGE), ("s0", PAGE), ("s1", PAGE),
+        ("gap", 2 * ROW), ("rates", ROW), ("sink", 2 * ROW), ("crossed", ROW), ("eq", 3 * ROW), ("dealt", 768), ("wall", 2 * PAGE), ("wg", 3 * PAGE),
+        ("turned", 2 * PAGE), ("before", ROW), ("grouped", 2 * PAGE + 8 * 2 * N),
+        ("codes", 4 * (T2 + 2 * N)), ("scales", T2 + 2 * N), ("dealt_late", 768), ("pairs", 2 * PAGE),
     )
 )
+SCORES_AT = {0: ("s0", ROW), 1: ("r1", ROW), 2: ("s0",), 3: ("s1",), 4: ("dealt_late", 768 - ROW), 5: ("r2",), 6: ("pairs",), 7: ("s0",)}
+PRODUCT_AT = {0: ("s0",), 1: ("s1",), 2: ("dealt_late", -PAGE), 3: ("r0",), 4: ("r2",), 5: ("pairs",), 6: ("s0",)}
+RATES_AT = {0: ("s1", ROW), 1: ("r0", ROW), 2: ("r0",)}
+GAIN_AT = {1: ("r2", -ROW // 2), 2: ("r1", ROW), 3: ("r0", ROW), 4: ("r1", ROW), 5: ("s1", ROW), 6: ("r1", ROW), 7: ("s1", ROW)}
+GROWTH_AT = {0: ("r0",), 1: ("r1",), 2: ("r0",), 3: ("s1",), 4: ("r1",), 5: ("s1",), 6: ("r1",), 7: ("r2",)}
+GAP_AT = {0: ("r1", ROW), 1: ("wg", 2 * PAGE + ROW), 2: ("gap",), 3: ("gap", ROW), 4: ("codes",), 5: ("gap",), 6: ("codes",), 7: ("gap", ROW)}
+CROSSED_AT = {1: ("crossed",), 2: ("crossed",)}
+EQ_AT = {3: ("wg", 2 * PAGE), 4: ("eq", ROW), 5: ("wg", 2 * PAGE + ROW), 6: ("eq", 2 * ROW), 7: ("eq",)}
+SOURCE_AT = {0: ("gap",), 1: ("codes_rest",)}
+SINK_AT = {0: ("pairs",)}
 
 
 def tile_list_cave_wall_growth_kernel(
@@ -67,13 +71,13 @@ def tile_list_cave_wall_growth_kernel(
     with ExitStack() as ctx:
         lists = ctx.enter_context(tc.tile_pool(name="lists", bufs=1))
         sbuf = ctx.enter_context(tc.tile_pool(name="sbuf", bufs=1))
-        psum = ctx.enter_context(tc.psum_pool(name="psum", bufs=2))
+        psum = ctx.enter_context(tc.psum_pool(name="psum", bufs=1))
 
         def place(name, columns, dtype, area, skip=0):
             return sbuf.tile([P, columns], dtype, name=name, align_bytes=64, offset=AT[area] + skip)
 
-        def bank_of(ring):
-            return psum.tile([P, BANK], F32, name=ring, bufs=RINGS[ring])
+        def bank_at(name, b):
+            return psum.tile([P, BANK], F32, name=name, offset=4 * BANK * b)
 
         def by_eights(rows):
             return rows.rearrange("(b e) n -> b e n", e=8)
@@ -89,27 +93,22 @@ def tile_list_cave_wall_growth_kernel(
         idx = lists.tile([P, S // 16], U16, name="idx")
         idx2 = lists.tile([P, S // 16], U16, name="idx2")
         idx3 = lists.tile([P, S // 16], U16, name="idx3")
-        tabw = place("tabw", T, U32, "table")
-        tabs = place("tabs", T, U8, "table_bytes")
+        tabw = place("tabw", T, U32, "grouped")
+        tabs = place("tabs", T, U8, "before")
         w2w = place("w2w", 2 * H, U8, "w2w")
         w2s = place("w2s", H, U8, "w2s")
         ident = place("ident", P, F32, "ident")
-        page_a = place("page_a", T2, F32, "page_a")
-        page_b = [place("page_b%d" % i, T2, F32, "page_b", 4 * T2 * i) for i in range(2)]
-        scores = place("scores", S, F32, "scores")
-        source = [place("source%d" % i, S, F32, "source", 4 * S * i) for i in range(2)]
-        sink = [place("sink%d" % i, S, F32, "sink", 4 * S * i) for i in range(2)]
+        page_a = [place("page_a%d" % i, T2, F32, "page_a", PAGE * i) for i in range(2)]
+        page_b = [place("page_b%d" % i, T2, F32, "page_b", PAGE * i) for i in range(2)]
         halves = [slice(BANK * h, BANK * h + BANK) for h in range(2)]
         words = place("words", S, U32, "words")
         scale_bytes = place("scale_bytes", S, U8, "bytes")
         vw = [words[:, half].bitcast(FP8X4) for half in halves]
         vs = [scale_bytes[:, half] for half in halves]
 
-        def load_scale_rows(queue, plane, rows):
-            for q in range(4):
-                queue.dma_start(
-                    out=plane[32 * q : 32 * q + 4, :].bitcast(I32), in_=rows[4 * q : 4 * q + 4, :].bitcast(I32)
-                )
+        def load_scale_rows(plane, rows):
+            for r in range(4):
+                nc.sync.dma_start(out=plane[r:P:32, :].bitcast(I32), in_=rows[r:16:4, :].bitcast(I32))
 
         def by_fours(rows):
             return rows.rearrange("(p t) c -> p t c", t=4)
@@ -117,27 +116,22 @@ def tile_list_cave_wall_growth_kernel(
         def interleave(grouped, raw, run):
             nc.scalar.copy(out=grouped.rearrange("p (b c t) -> p b t c", c=run, t=4), in_=raw)
 
-        def plain_runs(raw):
-            return raw.rearrange("p (t b c) -> p b t c", t=4, c=4)
-
-        def group_w1(part, lo, hi):
-            raw = place("raw_" + part, 4 * (hi - lo), F32, "raw_" + part)
+        def load_w1(name, lo, hi, *at):
+            raw = place(name, 4 * (hi - lo), F32, *at)
             nc.sync.dma_start(out=raw[:].rearrange("p (t c) -> p t c", t=4), in_=by_fours(w1[:, lo:hi]))
-            grouped = place("grouped_" + part, 4 * (hi - lo), BF16, "grouped_" + part)
-            plain = min(hi, 512) - lo
-            planes = raw[:].rearrange("p (t c) -> p t c", t=4)
-            if plain > 0:
-                interleave(grouped[:], planes.rearrange("p t (b c) -> p b t c", c=4), 4)
-            else:
-                dealt = planes[:, :, plain:].rearrange("p t (b e) -> p b t e", e=8)
-                c0 = 4 * plain
-                interleave(grouped[:, c0 : c0 + 1024], dealt[:, :, :, 0:4], 4)
-                interleave(grouped[:, c0 + 1024 : c0 + 1536], dealt[:, :, :, 4:6], 2)
-                interleave(grouped[:, c0 + 1536 :], dealt[:, :, :, 6:8], 2)
-            return grouped
+            return raw
+
+        def group_plain(grouped, raw):
+            interleave(grouped, raw.rearrange("p (t b c) -> p b t c", t=4, c=4), 4)
+
+        def group_dealt(grouped, raw):
+            dealt = raw.rearrange("p (t b e) -> p b t e", t=4, e=8)
+            interleave(grouped[:, :1024], dealt[:, :, :, 0:4], 4)
+            interleave(grouped[:, 1024:1536], dealt[:, :, :, 4:6], 2)
+            interleave(grouped[:, 1536:], dealt[:, :, :, 6:8], 2)
 
         def load_w3():
-            raw = place("raw_w3", 8 * N, F32, "raw_w3")
+            raw = place("raw_w3", 8 * N, F32, "wg", 2 * PAGE - ROW)
             nc.sync.dma_start(out=raw[:, : 4 * N].rearrange("p (t c) -> p t c", t=4), in_=by_fours(w3[:512, :]))
             dealt = by_eights(w3[512:, :])
             nc.sync.dma_start(out=raw[:, 4 * N : 6 * N], in_=dealt[:, 0:4].rearrange("b (i t) n -> b i (t n)", i=2))
@@ -145,179 +139,106 @@ def tile_list_cave_wall_growth_kernel(
                 nc.sync.dma_start(out=raw[:, (4 + t) * N : (5 + t) * N], in_=dealt[:, 2 * t : 2 * t + 2])
             return raw
 
-        def group_w3(raw):
-            grouped = place("grouped_w3", 8 * N, BF16, "grouped_w3")
-            for b in range(2):
-                cols = slice(4 * N * b, 4 * N * (b + 1))
-                interleave(grouped[:, cols], plain_runs(raw[:, cols]), 4)
-            return grouped
-
-        def quantize(name, grouped, cut, codes_at, scales_at):
-            width = grouped.shape[1] // 4
-            codes = place(name + "_codes", width, U32, *codes_at)
-            scales = place(name + "_scales", width, U8, *scales_at)
-            for c0 in range(0, width, cut):
-                cols = slice(c0, min(c0 + cut, width))
-                nc.vector.quantize_mx(
-                    out=codes[:, cols].bitcast(FP8X4), scales=scales[:, cols], in_=grouped[:, 4 * cols.start : 4 * cols.stop]
-                )
-            return codes, scales
+        def quantize(codes, scales, grouped, cuts):
+            for lo, hi in zip(cuts, cuts[1:]):
+                nc.vector.quantize_mx(out=codes[:, lo:hi].bitcast(FP8X4), scales=scales[:, lo:hi], in_=grouped[:, 4 * lo : 4 * hi])
 
         def stationary(codes, scales):
             return [(codes[:, c0 : c0 + P].bitcast(FP8X4), scales[:, c0 : c0 + P]) for c0 in range(0, codes.shape[1], P)]
 
         w1q = []
 
-        def quantize_w1(part, grouped):
-            w1q.extend(stationary(*quantize("w1" + part, grouped, 512, ("codes_a" if part == "a" else "raw_" + part,), ("scales_" + part,))))
+        def first_w1(s, raw):
+            grouped = place("grouped_w1_%d" % s, 4 * P, BF16, "grouped", 2 * PAGE + ROW + 8 * P * s)
+            group_plain(grouped[:], raw[:])
+            return grouped
+
+        def quantize_first(s, grouped):
+            codes = place("w1_codes%d" % s, P, U32, "codes_first", 4 * P * s)
+            scales = place("w1_scales%d" % s, P, U8, "scales_first", P * s)
+            quantize(codes, scales, grouped, (0, P))
+            w1q.extend(stationary(codes[:], scales[:]))
 
         w2q = [(w2w[:, 2 * c0 : 2 * c0 + 2 * P], w2s[:, c0 : c0 + P]) for c0 in range(0, H // 2, P)]
 
         def deal_w2(i):
-            words = place("w2w_dealt%d" % i, H // 2, U8, "grouped_a", S + 768 * i)
-            scales = place("w2s_dealt%d" % i, H // 4, U8, "grouped_a", S + 768 * i + H // 2)
-            pairs = w2w[:, H:].bitcast(I32).rearrange("p (b e) -> p b e", e=4)
+            dealt_words = place("w2w_dealt%d" % i, H // 2, U8, ("dealt", "dealt_late")[i])
+            scales = place("w2s_dealt%d" % i, H // 4, U8, ("dealt", "dealt_late")[i], H // 2)
+            column_pairs = w2w[:, H:].bitcast(I32).rearrange("p (b e) -> p b e", e=4)
             if i == 0:
-                nc.gpsimd.tensor_copy(words[:].bitcast(I32).rearrange("p (b e) -> p b e", e=2), pairs[:, :, 0:2])
+                nc.gpsimd.tensor_copy(dealt_words[:].bitcast(I32).rearrange("p (b e) -> p b e", e=2), column_pairs[:, :, 0:2])
                 nc.gpsimd.tensor_copy(
                     scales[:].bitcast(I32), w2s[:, H // 2 :].bitcast(I32).rearrange("p (b e) -> p b e", e=2)[:, :, 0]
                 )
             else:
                 nc.gpsimd.tensor_copy(
-                    words[:].bitcast(I32).rearrange("p (e b) -> p e b", e=2),
-                    pairs[:, :, 2:4].rearrange("p b e -> p e b"),
+                    dealt_words[:].bitcast(I32).rearrange("p (e b) -> p e b", e=2),
+                    column_pairs[:, :, 2:4].rearrange("p b e -> p e b"),
                 )
                 nc.gpsimd.tensor_copy(
                     scales[:].rearrange("p (t b i) -> p t b i", t=2, i=2),
                     w2s[:, H // 2 :].rearrange("p (b t i) -> p t b i", t=4, i=2)[:, 2:4],
                 )
-            w2q.extend((words[:, 2 * c0 : 2 * c0 + 2 * P], scales[:, c0 : c0 + P]) for c0 in (0, P))
+            w2q.extend((dealt_words[:, 2 * c0 : 2 * c0 + 2 * P], scales[:, c0 : c0 + P]) for c0 in (0, P))
 
-        weights = {}
-        negated = {}
+        source_weights = {}
+        rate_weights = {}
 
-        def negate(s, out):
-            nc.scalar.mul(out, weights[s][:, :S], -1.0)
-            negated[s] = out
+        def negate(ap):
+            nc.scalar.mul(ap, ap, -1.0)
+
+        def negate_aside(s, *at):
+            aside = place("negated%d" % s, S, F32, *at)
+            nc.scalar.mul(aside[:], source_weights[s][:], -1.0)
+            source_weights[s] = aside
 
         def load_weights(s):
-            both = place("wg%d" % s, 2 * S, F32, "wg", 8 * S * {4: 1, 6: 2, 7: 0}[s])
+            at = PAGE * {4: 1, 6: 2, 7: 0}[s]
             rows = {4: slice(0, 4), 6: slice(4, 6), 7: slice(6, 8)}[s]
             span = 16 * (rows.stop - rows.start)
-            for i, matrix in enumerate((wg1, wg2)):
+            for i, (matrix, held) in enumerate(((wg2, rate_weights), (wg1, source_weights))):
+                held[s] = place("wg%d_%d" % (2 - i, s), S, F32, "wg", at + ROW * i)
                 for p0 in range(0, P, span):
-                    nc.sync.dma_start(out=both[p0 : p0 + span, S * i : S * i + S], in_=by_eights(matrix)[:, rows])
-            weights[s] = both
-            if s == 4:
-                weights[5] = both
+                    nc.sync.dma_start(out=held[s][p0 : p0 + span, :], in_=by_eights(matrix)[:, rows])
+                if s == 4:
+                    held[5] = held[4]
 
-        EQ_AT = {2: ("wg", 20 * S), 3: ("wg", 16 * S), 4: ("raw_b", S), 5: ("raw_c", 2 * S)}
         eqs = {}
 
         def load_eq(s):
-            eqs[s] = place("eq%d" % s, S, F32, *EQ_AT.get(s, ("eq", 4 * S * (s % 2))))
+            eqs[s] = place("eq%d" % s, S, F32, *EQ_AT.get(s, ("eq", ROW * s)))
             nc.sync.dma_start(out=eqs[s][:], in_=slice_rows(eq, s))
 
         walls = {}
 
         def load_wall(s):
-            walls[s] = place("wall%d" % s, T2, F32, "wall", 4 * T2 * (s % 2))
+            walls[s] = place("wall%d" % s, T2, F32, "wall", PAGE * (s % 2))
             nc.sync.dma_start(out=walls[s][:], in_=slice_rows(wall, s))
 
-        def score_half(s, h, weighted=None):
-            bank = bank_of("score")
-            nc.tensor.matmul_mx(
-                out=bank[:], lhsT=w1q[s][0], lhsT_scale=w1q[s][1],
-                rhs=vw[h], rhs_scale=vs[h], start=True, stop=True,
-            )
-            if weighted is not None:
-                nc.vector.tensor_tensor(weighted, bank[:], weights[s][:, halves[h]], MULT)
-            if s < TURNED_FROM:
-                nc.scalar.copy(out=scores[:, halves[h]], in_=bank[:])
-            else:
-                nc.scalar.mul(scores[:, halves[h]], bank[:], -1.0)
+        scores = {}
+        sources = {}
 
-        def score(s):
+        def score(s, first_bank=0):
+            scores[s] = place("scores%d" % s, S, F32, *SCORES_AT[s])
             for h in range(2):
-                score_half(s, h)
+                bank = bank_at("score%d%d" % (s, h), first_bank + h)
+                nc.tensor.matmul_mx(
+                    out=bank[:], lhsT=w1q[s][0], lhsT_scale=w1q[s][1], rhs=vw[h], rhs_scale=vs[h], start=True, stop=True
+                )
+                if (s, h) == (0, 0):
+                    nc.vector.tensor_tensor(sources[0][:, halves[0]], bank[:], source_weights[0][:, halves[0]], MULT)
+                nc.scalar.mul(scores[s][:, halves[h]], bank[:], -1.0)
 
         rates = {}
 
-        def rate(s, which=(0, 1)):
-            for h in which:
-                rates[s, h] = bank_of("score" if ON_GPSIMD[s] >= BANK * (h + 1) else ("turn", "rate")[h])
+        def rate(s, first_bank=0):
+            rates[s] = place("rates%d" % s, S, F32, *RATES_AT.get(s, ("rates",)))
+            for h in range(2):
+                bank = bank_at("rate%d%d" % (s, h), first_bank + h)
                 nc.tensor.matmul_mx(
-                    out=rates[s, h][:], lhsT=w2q[s][0].bitcast(FP4X4), lhsT_scale=w2q[s][1],
-                    rhs=vw[h], rhs_scale=vs[h], start=True, stop=True,
+                    out=bank[:], lhsT=w2q[s][0].bitcast(FP4X4), lhsT_scale=w2q[s][1], rhs=vw[h], rhs_scale=vs[h], start=True, stop=True
                 )
-
-        gains = {}
-
-        def weigh_rate(s):
-            gains[s] = place("gain%d" % s, S, F32, "first_gain" if s in (0, 2, 3, 5, 7) else "gain")
-            for h in range(ON_GPSIMD[s] // BANK, 2):
-                lo, hi = max(ON_GPSIMD[s], BANK * h), BANK * (h + 1)
-                nc.vector.tensor_tensor(gains[s][:, lo:hi], rates[s, h][:, lo - BANK * h :], weights[s][:, S + lo : S + hi], MULT)
-
-        PRODUCT_AT = {1: ("grouped_c", 0), 2: ("growth", 0), 3: ("third", 0), 5: ("grouped_c", 0), 6: ("table", 4 * T2)}
-        GAP_AT = {1: ("raw_b", -S), 2: ("raw_c", 0), 7: ("codes_z", 2 * S)}
-        gaps = {}
-
-        def subtract(s):
-            gaps[s] = place("gap%d" % s, S, F32, *GAP_AT.get(s, PRODUCT_AT.get(s - 1, ("product", 0))))
-            if s < TURNED_FROM:
-                nc.gpsimd.tensor_tensor(gaps[s][:], scores[:], eqs[s][:], SUB)
-                return
-            for half in halves:
-                bank = bank_of("score")
-                for c0 in range(0, BANK, P):
-                    nc.tensor.transpose(bank[:, c0 : c0 + P], crossed[:, half][:, c0 : c0 + P], ident[:])
-                nc.scalar.copy(out=gaps[s][:, half], in_=bank[:])
-
-        crossed = place("crossed", S, F32, "crossed")
-
-        def subtract_turned(s):
-            for half in halves:
-                bank = bank_of("sum")
-                add_transposed(bank, eqs[s][:, half], True)
-                add_transposed(bank, scores[:, half], False)
-                nc.scalar.mul(crossed[:, half], bank[:], -1.0)
-
-        first_rates = place("first_rates", S, F32, "rate")
-
-        def copy_first_rates(s, which=(0, 1)):
-            for h in which:
-                if ON_GPSIMD[s] > BANK * h:
-                    nc.scalar.copy(out=first_rates[:, halves[h]], in_=rates[s, h][:])
-
-        def weigh_first_rates(s, lo, hi):
-            nc.gpsimd.tensor_tensor(gains[s][:, lo:hi], first_rates[:, lo:hi], weights[s][:, S + lo : S + hi], MULT)
-
-        def form_sink(s):
-            if s == LAST:
-                sink[s % 2] = place("last_sink", S, F32, "turned", 12 * S)
-            nc.gpsimd.tensor_tensor(sink[s % 2][:], gaps[s][:], gains[s][:], MULT)
-
-        def form_source(s):
-            nc.gpsimd.tensor_tensor(source[s % 2][:], scores[:], negated[s], MULT)
-
-        def scatter_sink(s):
-            nc.vector.tensor_copy(page_b[s % 2][:].indirect(idx3[:]), sink[s % 2][:])
-
-        growths = {}
-
-        def exponentiate(s):
-            at = {0: ("growth", 0), LAST: ("raw_w3", 4 * S)}.get(s, PRODUCT_AT.get(s - 1, ("product", 0)))
-            growths[s] = place("growth%d" % s, T2, F32, *at)
-            for c0 in range(0, T2, S):
-                nc.scalar.activation(out=growths[s][:, c0 : c0 + S], in_=page_b[s % 2][:, c0 : c0 + S], func=EXP)
-
-        def grow(s):
-            product = place("product%d" % s, T2, F32, *PRODUCT_AT.get(s, ("product", 0)))
-            for c0 in range(0, T2, S):
-                cols = slice(c0, c0 + S)
-                nc.gpsimd.tensor_tensor(product[:, cols], growths[s][:, cols], page_a[:, cols], MULT)
-            return product
+                nc.scalar.mul(rates[s][:, halves[h]], bank[:], -1.0)
 
         def add_transposed(bank, rows, opens):
             for g in range(4):
@@ -326,18 +247,67 @@ def tile_list_cave_wall_growth_kernel(
                     start=(opens and g == 0), stop=(not opens and g == 3), is_transpose=True,
                 )
 
+        gaps = {}
+
+        def subtract(s):
+            gaps[s] = place("gap%d" % s, S, F32, *GAP_AT[s])
+            if s == 0:
+                nc.gpsimd.tensor_tensor(gaps[s][:], scores[s][:], eqs[s][:], ADD)
+                return
+            crossed = place("crossed%d" % s, S, F32, *CROSSED_AT.get(s, GAIN_AT[max(s - 1, 1)]))
+            for h, half in enumerate(halves):
+                bank = bank_at("sum%d%d" % (s, h), 2 + h)
+                add_transposed(bank, eqs[s][:, half], True)
+                add_transposed(bank, scores[s][:, half], False)
+                nc.scalar.copy(out=crossed[:, half], in_=bank[:])
+            for h, half in enumerate(halves):
+                bank = bank_at("back%d%d" % (s, h), h if s == 1 else 2 + h)
+                for c0 in range(0, BANK, P):
+                    nc.tensor.transpose(bank[:, c0 : c0 + P], crossed[:, half][:, c0 : c0 + P], ident[:])
+                nc.scalar.copy(out=gaps[s][:, half], in_=bank[:])
+
+        sinks = {}
+
+        def form_sink(s):
+            gain = place("gain%d" % s, S, F32, *GAIN_AT[s]) if s in GAIN_AT else rates[s]
+            nc.gpsimd.tensor_tensor(gain[:], rates[s][:], rate_weights[s][:], MULT)
+            sinks[s] = place("sink%d" % s, S, F32, *SINK_AT.get(s, ("sink", ROW * (s % 2))))
+            nc.gpsimd.tensor_tensor(sinks[s][:], gaps[s][:], gain[:], MULT)
+
+        def form_source(s):
+            sources[s] = place("source%d" % s, S, F32, *SOURCE_AT.get(s, GAP_AT[s]))
+            nc.gpsimd.tensor_tensor(sources[s][:], scores[s][:], source_weights[s][:], MULT)
+
+        def scatter_sink(s):
+            nc.vector.tensor_copy(page_b[s % 2][:].indirect(idx3[:]), sinks[s][:])
+
+        def scatter_source(s):
+            nc.vector.tensor_copy(page_a[s % 2][:].indirect(idx2[:]), sources[s][:])
+
+        growths = {}
+
+        def exponentiate(s):
+            growths[s] = place("growth%d" % s, T2, F32, *GROWTH_AT[s])
+            nc.scalar.activation(out=growths[s][:], in_=page_b[s % 2][:], func=EXP)
+
+        products = {}
+
+        def grow(s):
+            products[s] = place("product%d" % s, T2, F32, *PRODUCT_AT[s])
+            nc.gpsimd.tensor_tensor(products[s][:], growths[s][:], page_a[s % 2][:], MULT)
+
         turned = {}
 
-        def form_z(s, product):
-            for c in range(CHUNKS):
-                cols = slice(BANK * c, BANK * c + BANK)
-                bank = bank_of("sum" if c < 2 else "score")
-                add_transposed(bank, walls[s][:, cols], True)
-                add_transposed(bank, product[:, cols], False)
+        def form_z(s):
+            banks = [bank_at("z%d%d" % (s, c), 4 + c) for c in range(CHUNKS)]
+            for rows, opens in ((walls[s], True), (products[s], False)):
+                for c, bank in enumerate(banks):
+                    add_transposed(bank, rows[:, BANK * c : BANK * c + BANK], opens)
+            for c, bank in enumerate(banks):
                 if s == 0:
-                    turned[0, c] = place("turned0%d" % c, 4 * BANK, BF16, "turned", 8 * BANK * c)
+                    turned[0, c] = place("turned0%d" % c, 4 * BANK, BF16, "turned", 8 * BANK * (CHUNKS - 1 - c))
                 if s == 4:
-                    turned[1, c] = place("turned1%d" % c, 2 * BANK, BF16, "raw_w3", 4 * S + 4 * BANK * c)
+                    turned[1, c] = place("turned1%d" % c, 2 * BANK, BF16, "r2", 4 * BANK * c)
                 if s < 4:
                     nc.scalar.copy(
                         out=turned[0, c][:].rearrange("m (u g q e) -> m u g q e", u=2, g=4, e=2)[:, :, :, 32 * s : 32 * s + 32, :],
@@ -349,213 +319,258 @@ def tile_list_cave_wall_growth_kernel(
                         in_=bank[:].rearrange("m (g q) -> m g q", g=4),
                     )
 
+        grouped = place("grouped", 4 * (T2 + 2 * N), BF16, "grouped")
+
         def regroup(i):
-            grouped = place("grouped_z%d" % i, 8 * BANK, BF16, "table", 4 * T2 * i)
             for j in range(2):
-                words = turned[0, 2 * i + j][:].bitcast(F32)
+                turned_words = turned[0, 2 * i + j][:].bitcast(F32)
                 for h in range(2):
-                    bank = bank_of("turn")
+                    bank = bank_at("regroup%d%d%d" % (i, j, h), 4 + 2 * j + h)
                     for u in range(2):
                         for g2 in range(2):
                             w0 = P * (4 * u + 2 * h + g2)
                             o0 = P * (2 * u + g2)
-                            nc.tensor.transpose(bank[:, o0 : o0 + P], words[:, w0 : w0 + P], ident[:])
-                    c0 = BANK * (2 * j + h)
+                            nc.tensor.transpose(bank[:, o0 : o0 + P], turned_words[:, w0 : w0 + P], ident[:])
+                    c0 = BANK * (4 * i + 2 * j + h)
                     nc.scalar.copy(
                         out=grouped[:].bitcast(F32)[:, c0 : c0 + BANK].rearrange("p (m u) -> p m u", u=2),
                         in_=bank[:].rearrange("p (u m) -> p m u", u=2),
                     )
-            return grouped
 
         pairs = {}
 
         def turn_first_lanes():
             for c in range(CHUNKS):
-                words = turned[1, c][:].bitcast(F32)
-                bank = bank_of("turn")
+                turned_words = turned[1, c][:].bitcast(F32)
+                bank = bank_at("turn%d" % c, 4 + c)
                 for g in range(4):
-                    nc.tensor.transpose(bank[:, P * g : P * g + P], words[:, P * g : P * g + P], ident[:])
+                    nc.tensor.transpose(bank[:, P * g : P * g + P], turned_words[:, P * g : P * g + P], ident[:])
                 for j, (lo, hi) in enumerate(PIECES):
                     if lo // BANK == c:
-                        pairs[j] = place("pairs%d" % j, 2 * (hi - lo), F32, "table_bytes", 8 * lo)
+                        pairs[j] = place("pairs%d" % j, 2 * (hi - lo), F32, "pairs", 8 * lo)
                         nc.scalar.copy(out=pairs[j][:, : hi - lo], in_=bank[:, lo - BANK * c : hi - BANK * c])
 
         def last_lanes(j):
             lo, hi = PIECES[j]
             return pairs[j][:, hi - lo :].bitcast(BF16).rearrange("p (m e) -> p m e", e=2)
 
-        def form_third_lane(product):
+        def form_third_lane():
+            lane = place("lane", T2, BF16, "s1", 4 * BANK)
             for c0 in range(0, T2, S):
                 cols = slice(c0, c0 + S)
-                lane = place("lane%d" % c0, S, BF16, "grouped_c", BANK + 6 * c0)
-                nc.gpsimd.tensor_tensor(lane[:], product[:, cols], walls[LAST - 1][:, cols], ADD)
+                nc.gpsimd.tensor_tensor(lane[:, cols], products[LAST - 1][:, cols], walls[LAST - 1][:, cols], ADD)
                 for j, (lo, hi) in enumerate(PIECES):
                     if c0 <= lo < c0 + S:
-                        nc.scalar.copy(out=last_lanes(j)[:, :, 0], in_=lane[:, lo - c0 : hi - c0])
+                        nc.scalar.copy(out=last_lanes(j)[:, :, 0], in_=lane[:, lo:hi])
+
 
         nc.gpsimd.memset(tabs[:, : T // 2].bitcast(I32), 0)
         nc.vector.memset(tabs[:, T // 2 :].bitcast(I32), 0)
-        nc.gpsimd.memset(w2s[:].bitcast(I32), 0)
         nc.sync.dma_start(idx[:], offs)
+        raw_first = [load_w1("raw_w1_0", 0, P, "grouped", 2 * PAGE)]
         nc.sync.dma_start(idx2[:], offs2)
-        nc.sync.dma_start(out=w2w[:].bitcast(I32), in_=w2_words[0].bitcast(I32))
-        load_scale_rows(nc.sync, tabs, tab_scales[0])
-        table = tab_words[0].rearrange("p t i -> p (t i)").bitcast(I32)
-        for c0 in range(0, T, T // 2):
-            nc.sync.dma_start(out=tabw[:].bitcast(I32)[:, c0 : c0 + T // 2], in_=table[:, c0 : c0 + T // 2])
-        first = group_w1("a", 0, 256)
-        load_scale_rows(nc.sync, w2s, w2_scales[0])
-        nc.vector.memset(page_a[:], 0.0)
-        make_identity(nc, ident[:])
+        load_scale_rows(tabs, tab_scales[0])
+        nc.sync.dma_start(out=tabw[:].bitcast(I32), in_=tab_words[0].rearrange("p t i -> p (t i)").bitcast(I32))
+        raw_first.append(load_w1("raw_w1_1", P, 2 * P, "grouped", 2 * PAGE + 16 * P))
+        nc.gpsimd.memset(w2s[:].bitcast(I32), 0)
+        for page in page_a:
+            nc.vector.memset(page[:], 0.0)
         for page in page_b:
             nc.gpsimd.memset(page[:], 0.0)
-        wg = place("wg0", 2 * S, F32, "wg")
+        make_identity(nc, ident[:])
+        plain_weights = [place("wg%d_0" % (2 - i), S, F32, "wg", ROW * i) for i in range(2)]
         for s in range(4):
-            weights[s] = wg
-        nc.sync.dma_start(out=wg[:, S:], in_=wg2)
-        nc.sync.dma_start(out=wg[:, :S], in_=wg1)
-        nc.sync.dma_start(idx3[:], offs3)
-        load_eq(0)
-        second = group_w1("b", 256, 512)
+            rate_weights[s], source_weights[s] = plain_weights
+        for half in halves:
+            nc.sync.dma_start(out=source_weights[0][:, half], in_=wg1[:, half])
         load_eq(1)
+        nc.sync.dma_start(out=rate_weights[0][:], in_=wg2)
+        nc.sync.dma_start(out=w2w[:].bitcast(I32), in_=w2_words[0].bitcast(I32))
+        load_scale_rows(w2s, w2_scales[0])
+        load_eq(0)
+        raw_third = load_w1("raw_w1_3", 4 * P, H, "wall", PAGE)
+        raw_second = load_w1("raw_w1_2", 2 * P, 4 * P, "pairs")
+        nc.sync.dma_start(idx3[:], offs3)
         load_eq(2)
+        load_eq(3)
+        grouped_first = [first_w1(s, raw_first[s]) for s in range(2)]
         nc.vector.tensor_copy(scale_bytes[:], tabs[:].indirect(idx[:]))
+        quantize_first(0, grouped_first[0])
         for h in range(2):
             nc.vector.tensor_copy(words[:, halves[h]], tabw[:].indirect(idx[:, 32 * h : 32 * h + 32]))
-        quantize_w1("a", first)
-        rate(0)
-        weigh_rate(0)
-        for h in range(2):
-            score_half(0, h, source[0][:, halves[h]])
-        rate(1)
-        weigh_rate(1)
-        nc.vector.tensor_copy(page_a[:].indirect(idx2[:]), source[0][:])
-        subtract(0)
-        form_sink(0)
-        for i in range(2):
-            deal_w2(i)
-        negate(1, wg[:, :S])
-        negated[2] = negated[3] = negated[1]
-        score(1)
-        subtract_turned(1)
-        scatter_sink(0)
-        subtract(1)
-        rate(2)
-        copy_first_rates(2)
+        quantize_first(1, grouped_first[1])
+        sources[0] = place("source0", S, F32, *SOURCE_AT[0])
+        negate(source_weights[0][:, halves[1]])
+        score(0)
+        nc.vector.tensor_copy(page_a[0][:].indirect(idx2[:, :32]), sources[0][:, halves[0]])
+        nc.gpsimd.tensor_tensor(sources[0][:, halves[1]], scores[0][:, halves[1]], source_weights[0][:, halves[1]], MULT)
+        negate(source_weights[0][:, halves[0]])
+        score(1, 6)
+        nc.vector.tensor_copy(page_a[0][:].indirect(idx2[:, 32:]), sources[0][:, halves[1]])
         form_source(1)
+        scatter_source(1)
+        deal_w2(0)
+        subtract(1)
+        subtract(0)
+        rate(0, 4)
+        grouped_rest = place("grouped_rest", 4 * (H - 2 * P), BF16, "r2")
+        group_dealt(grouped_rest[:, 8 * P :], raw_third[:])
+        group_plain(grouped_rest[:, : 8 * P], raw_second[:])
+        form_sink(0)
+        codes_rest = place("codes_rest", H - 2 * P, U32, "codes_rest")
+        scales_rest = place("scales_rest", H - 2 * P, U8, "codes_rest", 4 * (H - 2 * P))
+        quantize(codes_rest, scales_rest, grouped_rest, (0, 2 * P, H - 2 * P))
+        w1q.extend(stationary(codes_rest[:], scales_rest[:]))
+        scatter_sink(0)
+        rate(1, 6)
         form_sink(1)
-        quantize_w1("b", second)
-        exponentiate(0)
-        score(2)
-        subtract_turned(2)
-        third = group_w1("c", 512, 1024)
+        scatter_sink(1)
         load_wall(0)
-        load_eq(3)
-        load_wall(1)
         load_weights(4)
-        raw_w3 = load_w3()
+        rate(2, 4)
+        score(2)
+        subtract(2)
+        form_sink(2)
+        form_source(2)
+        exponentiate(0)
+        load_wall(1)
+        rate(3, 6)
+        score(3)
+        subtract(3)
+        load_eq(4)
+        scatter_sink(2)
+        grow(0)
+        scatter_source(2)
+        exponentiate(1)
+        form_z(0)
+        load_wall(2)
+        form_sink(3)
+        load_eq(5)
+        form_source(3)
+        negate_aside(4, "crossed")
+        source_weights[5] = source_weights[4]
+        score(4)
+        rate(4)
+        subtract(4)
+        exponentiate(2)
+        score(5)
+        grow(1)
+        form_z(1)
+        load_wall(3)
+        load_weights(LAST)
 
-        grouped = {}
-        first_pass = []
-        for s in range(1, SLICES):
-            if s == 2:
-                quantize_w1("c", third)
-            if s == LAST:
-                w3q = stationary(*quantize("w3", grouped["w3"], N, ("raw_w3",), ("codes_z", 4 * S)))
-            for i in range(2 if s == LAST else 0):
-                first_pass.append(quantize("z%d" % i, grouped[i], S, ("codes_z", 5 * S * i), ("scales_z", S * i)))
-            if s < LAST:
-                weigh_rate(s + 1)
+        for s in range(3, SLICES):
             scatter_sink(s)
-            product = grow(s - 1)
             if s < LAST:
-                weigh_first_rates(s + 1, 0, BANK if s + 1 in DEFERRED else ON_GPSIMD[s + 1])
-                subtract(s + 1)
-            if s + 1 in DEFERRED:
-                rate(s + 1, (1,))
-                copy_first_rates(s + 1, (1,))
-                weigh_first_rates(s + 1, BANK, S)
-            if s + 2 <= LAST:
-                which = (0,) if s + 2 in DEFERRED else (0, 1)
-                rate(s + 2, which)
-                copy_first_rates(s + 2, which)
-            if s < LAST:
-                form_z(s - 1, product)
-                form_source(s + 1)
+                exponentiate(s)
+            if s == 3:
                 form_sink(s + 1)
-            exponentiate(s)
-            nc.vector.tensor_copy(page_a[:].indirect(idx2[:]), source[s % 2][:])
-            if s <= LAST - 2:
-                score(s + 2)
-                subtract_turned(s + 2)
+                form_source(s + 1)
+            grow(s - 1)
+            scatter_source(s)
+            if s < LAST:
+                form_z(s - 1)
+            if s in (5, 6):
+                regroup(s - 5)
+            if 3 < s < LAST:
+                form_sink(s + 1)
+                form_source(s + 1)
+            if s == 3:
+                deal_w2(1)
+            if s + 2 <= LAST:
+                rate(s + 2)
+            if s + 3 <= LAST:
+                score(s + 3)
+            if s + 2 <= LAST:
+                subtract(s + 2)
             if s + 3 <= LAST:
                 load_eq(s + 3)
-            if s + 1 <= LAST:
-                load_wall(s + 1)
-            if s == 2:
-                grouped["w3"] = group_w3(raw_w3)
-                load_weights(LAST)
-            if s == 1:
-                load_weights(6)
-                negate(4, weights[4][:, :S])
-                negated[5] = negated[4]
-            if s == 2:
-                negate(6, place("sixth_negated", S, F32, "raw_b", S)[:])
             if s == 3:
-                negate(LAST, place("last_negated", S, F32, "raw_c", 2 * S)[:])
+                load_weights(6)
+            if s < LAST:
+                load_wall(s + 1)
             if s in (4, 5):
-                grouped[s - 4] = regroup(s - 4)
+                negate_aside(s + 2, *EQ_AT[s + 2])
+            if s == LAST - 2:
+                raw_w3 = load_w3()
             if s == LAST - 1:
                 turn_first_lanes()
+                for b in range(2):
+                    cols = slice(4 * N * b, 4 * N * (b + 1))
+                    group_plain(grouped[:, 4 * T2 :][:, cols], raw_w3[:, cols])
             if s == LAST:
-                form_third_lane(product)
+                exponentiate(s)
+            if s == LAST:
+                form_third_lane()
 
         last_codes = place("last_codes", T2, U32, "sink")
-        last_scales = place("last_scales", T2, U8, "gain")
+        last_scales = place("last_scales", T2, U8, "crossed")
+        scales = place("scales", T2 + 2 * N, U8, "eq", ROW)
+        w3_codes = place("w3_codes", 2 * N, U32, "s1", 4 * BANK - 8 * N)
+        w3q = stationary(w3_codes[:], scales[:, T2:])
+        first_codes = {}
         woven = {}
 
         def project(j):
             lo, hi = PIECES[j]
-            i, c0 = divmod(lo, S)
-            first = [x[:, c0 : c0 + hi - lo] for x in first_pass[i]]
+            first = (first_codes[j][:], scales[:, lo:hi])
             at = 4 * OUT_TILES * lo
             results = place("results%d" % j, OUT_TILES * (hi - lo), F32, "wg", at)
             for nb in range(OUT_TILES):
-                bank = bank_of(OUT_RINGS[(OUT_TILES * j + nb) % len(OUT_RINGS)])
-                for b, (codes, scales) in enumerate((first, (last_codes[:, lo:hi], last_scales[:, lo:hi]))):
+                bank = bank_at("out%d%d" % (j, nb), (OUT_TILES * j + nb + 4) % 8)
+                for b, (z_codes, z_scales) in enumerate((first, (last_codes[:, lo:hi], last_scales[:, lo:hi]))):
                     nc.tensor.matmul_mx(
                         out=bank[:, : hi - lo], lhsT=w3q[OUT_TILES * b + nb][0], lhsT_scale=w3q[OUT_TILES * b + nb][1],
-                        rhs=codes.bitcast(FP8X4), rhs_scale=scales, start=(b == 0), stop=(b == 1),
+                        rhs=z_codes.bitcast(FP8X4), rhs_scale=z_scales, start=(b == 0), stop=(b == 1),
                     )
                 result = results[:, nb * (hi - lo) : (nb + 1) * (hi - lo)]
                 copy = nc.vector.tensor_copy if (j, nb) in VECTOR_EMPTIES else nc.scalar.copy
                 copy(out=result, in_=bank[:, : hi - lo])
-                if lo < T2 - BANK:
-                    nc.sync.dma_start(out=out[P * nb : P * nb + P, lo:hi], in_=result)
-            if lo >= T2 - BANK:
-                nc.sync.dma_start(
-                    out=out[:, lo:hi].rearrange("(b p) m -> p b m", p=P), in_=results[:].rearrange("p (b m) -> p b m", b=OUT_TILES)
-                )
+            nc.sync.dma_start(
+                out=out[:, lo:hi].rearrange("(b p) m -> p b m", p=P), in_=results[:].rearrange("p (b m) -> p b m", b=OUT_TILES)
+            )
+
+        def part_at(j):
+            return ("s1", 4 * BANK + 4 * PIECES[j][0]) if j < AHEAD else ("turned", 8 * PIECES[j - AHEAD][0])
 
         parts = {}
-        for step in range(len(PIECES) + 2):
-            j = step - 2
-            if j >= 0:
-                done = slice(*PIECES[j])
-                nc.vector.quantize_mx(out=last_codes[:, done].bitcast(FP8X4), scales=last_scales[:, done], in_=woven[j][:])
-                project(j)
-            if step < len(PIECES):
-                lo, hi = PIECES[step]
-                at = ("grouped_c", 4 * lo) if step < AHEAD else ("table", 8 * PIECES[step - AHEAD][0])
-                parts[step] = place("part%d" % step, hi - lo, F32, *at)
-                nc.vector.tensor_tensor(parts[step][:], growths[LAST][:, lo:hi], page_a[:, lo:hi], MULT)
-            j = step - 1
-            if 0 <= j < len(PIECES):
-                lo, hi = PIECES[j]
-                nc.vector.tensor_tensor(last_lanes(j)[:, :, 1], parts[j][:], walls[LAST][:, lo:hi], ADD)
-                woven[j] = place("woven%d" % j, 4 * (hi - lo), BF16, "table", 8 * lo)
-                weave = nc.vector.tensor_copy if j in VECTOR_WEAVES else nc.scalar.copy
-                weave(
-                    out=woven[j][:].bitcast(F32).rearrange("p (m u) -> p m u", u=2),
-                    in_=pairs[j][:].rearrange("p (u m) -> p m u", u=2),
-                )
+
+        def multiply(j):
+            lo, hi = PIECES[j]
+            area, at = part_at(j)
+            spare = 16 if j == 0 else 0
+            parts[j] = place("part%d" % j, spare + hi - lo, F32, area, at - 4 * spare)[:, spare:]
+            nc.vector.tensor_tensor(parts[j], growths[LAST][:, lo:hi], page_a[LAST % 2][:, lo:hi], MULT)
+
+        def finish_lanes(j):
+            lo, hi = PIECES[j]
+            nc.vector.tensor_tensor(last_lanes(j)[:, :, 1], parts[j], walls[LAST][:, lo:hi], ADD)
+            woven[j] = place("woven%d" % j, 4 * (hi - lo), BF16, "turned", 8 * lo)
+            weave = nc.vector.tensor_copy if j in VECTOR_WEAVES else nc.scalar.copy
+            weave(
+                out=woven[j][:].bitcast(F32).rearrange("p (m u) -> p m u", u=2),
+                in_=pairs[j][:].rearrange("p (u m) -> p m u", u=2),
+            )
+
+        def quantize_first_pass(j):
+            lo, hi = PIECES[j]
+            area, at = part_at(j)
+            first_codes[j] = place("first_codes%d" % j, hi - lo, U32, area, at)
+            quantize(first_codes[j], scales[:, lo:hi], grouped[:, 4 * lo : 4 * hi], (0, hi - lo))
+
+        multiply(0)
+        multiply(1)
+        finish_lanes(0)
+        quantize(w3_codes, scales[:, T2:], grouped[:, 4 * T2 :], (0, N))
+        quantize_first_pass(0)
+        finish_lanes(1)
+        quantize(w3_codes, scales[:, T2:], grouped[:, 4 * T2 :], (N, 2 * N))
+        for j in range(len(PIECES)):
+            done = slice(*PIECES[j])
+            nc.vector.quantize_mx(out=last_codes[:, done].bitcast(FP8X4), scales=last_scales[:, done], in_=woven[j][:])
+            if j + 2 < len(PIECES):
+                multiply(j + 2)
+                finish_lanes(j + 2)
+            if j + 1 < len(PIECES):
+                quantize_first_pass(j + 1)
+            project(j)

@@ -27,7 +27,6 @@ CHUNKS = T2 // BANK
 OUT_TILES = N // P
 PIECES = tuple((lo, lo + 256) for lo in range(0, T2, 256))
 VECTOR_WEAVES = (7,)
-AHEAD = 3
 VECTOR_EMPTIES = ((6, 2), (7, 1), (7, 2))
 ROW = 4 * S
 PAGE = 4 * T2
@@ -47,21 +46,25 @@ AT = lay_out(
         ("codes_first", 4 * 256), ("scales_first", 256), ("codes_rest", ROW),
         ("page_a", 2 * PAGE), ("page_b", 2 * PAGE),
         ("r0", PAGE), ("r1", PAGE), ("r2", PAGE), ("s0", PAGE), ("s1", PAGE),
-        ("gap", 2 * ROW), ("rates", ROW), ("sink", 2 * ROW), ("crossed", ROW), ("eq", 3 * ROW), ("dealt", 768), ("wall", 2 * PAGE), ("wg", 3 * PAGE),
+        ("gap", 2 * ROW), ("sink", 2 * ROW), ("crossed", ROW), ("eq", 3 * ROW), ("dealt", 768), ("rates", ROW), ("wall", 2 * PAGE), ("wg", 3 * PAGE),
         ("turned", 2 * PAGE), ("before", ROW), ("grouped", 2 * PAGE + 8 * 2 * N),
         ("codes", 4 * (T2 + 2 * N)), ("scales", T2 + 2 * N), ("dealt_late", 768), ("pairs", 2 * PAGE),
     )
 )
-SCORES_AT = {0: ("s0", ROW), 1: ("r1", ROW), 2: ("s0",), 3: ("s1",), 4: ("dealt_late", 768 - ROW), 5: ("r2",), 6: ("pairs",), 7: ("s0",)}
-PRODUCT_AT = {0: ("s0",), 1: ("s1",), 2: ("dealt_late", -PAGE), 3: ("r0",), 4: ("r2",), 5: ("pairs",), 6: ("s0",)}
-RATES_AT = {0: ("s1", ROW), 1: ("r0", ROW), 2: ("r0",)}
-GAIN_AT = {1: ("r2", -ROW // 2), 2: ("r1", ROW), 3: ("r0", ROW), 4: ("r1", ROW), 5: ("s1", ROW), 6: ("r1", ROW), 7: ("s1", ROW)}
-GROWTH_AT = {0: ("r0",), 1: ("r1",), 2: ("r0",), 3: ("s1",), 4: ("r1",), 5: ("s1",), 6: ("r1",), 7: ("r2",)}
-GAP_AT = {0: ("r1", ROW), 1: ("wg", 2 * PAGE + ROW), 2: ("gap",), 3: ("gap", ROW), 4: ("codes",), 5: ("gap",), 6: ("codes",), 7: ("gap", ROW)}
-CROSSED_AT = {1: ("crossed",), 2: ("crossed",)}
+SCORES_AT = {0: ("s0", ROW), 1: ("r1", ROW), 2: ("s0",), 3: ("s1",), 4: ("dealt_late", 768 - ROW), 5: ("r2",), 6: ("dealt_late", -PAGE), 7: ("s0",)}
+PRODUCT_AT = {0: ("s0",), 1: ("s1",), 2: ("dealt_late", -PAGE), 3: ("r2",), 4: ("dealt_late", -PAGE), 5: ("r1",), 6: ("s0",)}
+ON_VECTOR = (0,)
+GROWTH_AT = {0: "r0", 1: "r1", 2: "pairs", 3: "r0", 4: "r1", 5: "s1", 6: "r0", 7: "r0"}
+RATES_AT = {1: ("pairs", 3 * ROW), 2: ("r0",)}
+GAIN_AT = {0: ("s1", ROW), 1: ("r1",), 2: ("r1", ROW // 2)}
+GAP_AT = {0: ("r1", ROW), 1: ("wg", 2 * PAGE + ROW), 2: ("gap",), 3: ("gap", ROW), 4: ("codes",), 5: ("gap",), 6: ("gap", ROW), 7: ("codes",)}
 EQ_AT = {3: ("wg", 2 * PAGE), 4: ("eq", ROW), 5: ("wg", 2 * PAGE + ROW), 6: ("eq", 2 * ROW), 7: ("eq",)}
 SOURCE_AT = {0: ("gap",), 1: ("codes_rest",)}
-SINK_AT = {0: ("pairs",)}
+SINK_AT = {0: ("pairs", 5 * ROW // 2), 1: ("r2",)}
+
+
+def gain_at(s):
+    return GAIN_AT[s] if s in GAIN_AT else (GROWTH_AT[s - 3], ROW)
 
 
 def tile_list_cave_wall_growth_kernel(
@@ -116,10 +119,8 @@ def tile_list_cave_wall_growth_kernel(
         def interleave(grouped, raw, run):
             nc.scalar.copy(out=grouped.rearrange("p (b c t) -> p b t c", c=run, t=4), in_=raw)
 
-        def load_w1(name, lo, hi, *at):
-            raw = place(name, 4 * (hi - lo), F32, *at)
-            nc.sync.dma_start(out=raw[:].rearrange("p (t c) -> p t c", t=4), in_=by_fours(w1[:, lo:hi]))
-            return raw
+        def load_w1(raw, lo, hi):
+            nc.sync.dma_start(out=raw.rearrange("p (t c) -> p t c", t=4), in_=by_fours(w1[:, lo:hi]))
 
         def group_plain(grouped, raw):
             interleave(grouped, raw.rearrange("p (t b c) -> p b t c", t=4, c=4), 4)
@@ -164,20 +165,20 @@ def tile_list_cave_wall_growth_kernel(
         def deal_w2(i):
             dealt_words = place("w2w_dealt%d" % i, H // 2, U8, ("dealt", "dealt_late")[i])
             scales = place("w2s_dealt%d" % i, H // 4, U8, ("dealt", "dealt_late")[i], H // 2)
-            column_pairs = w2w[:, H:].bitcast(I32).rearrange("p (b e) -> p b e", e=4)
+            column_pairs = w2w[:, H:].bitcast(U32).rearrange("p (b e) -> p b e", e=4)
             if i == 0:
-                nc.gpsimd.tensor_copy(dealt_words[:].bitcast(I32).rearrange("p (b e) -> p b e", e=2), column_pairs[:, :, 0:2])
-                nc.gpsimd.tensor_copy(
-                    scales[:].bitcast(I32), w2s[:, H // 2 :].bitcast(I32).rearrange("p (b e) -> p b e", e=2)[:, :, 0]
+                nc.scalar.copy(out=dealt_words[:].bitcast(U32).rearrange("p (b e) -> p b e", e=2), in_=column_pairs[:, :, 0:2])
+                nc.scalar.copy(
+                    out=scales[:].bitcast(U32), in_=w2s[:, H // 2 :].bitcast(U32).rearrange("p (b e) -> p b e", e=2)[:, :, 0]
                 )
             else:
-                nc.gpsimd.tensor_copy(
-                    dealt_words[:].bitcast(I32).rearrange("p (e b) -> p e b", e=2),
-                    column_pairs[:, :, 2:4].rearrange("p b e -> p e b"),
+                nc.scalar.copy(
+                    out=dealt_words[:].bitcast(U32).rearrange("p (e b) -> p e b", e=2),
+                    in_=column_pairs[:, :, 2:4].rearrange("p b e -> p e b"),
                 )
-                nc.gpsimd.tensor_copy(
-                    scales[:].rearrange("p (t b i) -> p t b i", t=2, i=2),
-                    w2s[:, H // 2 :].rearrange("p (b t i) -> p t b i", t=4, i=2)[:, 2:4],
+                nc.scalar.copy(
+                    out=scales[:].bitcast(U16).rearrange("p (t b) -> p t b", t=2),
+                    in_=w2s[:, H // 2 :].bitcast(U16).rearrange("p (b t) -> p t b", t=4)[:, 2:4],
                 )
             w2q.extend((dealt_words[:, 2 * c0 : 2 * c0 + 2 * P], scales[:, c0 : c0 + P]) for c0 in (0, P))
 
@@ -215,6 +216,16 @@ def tile_list_cave_wall_growth_kernel(
             walls[s] = place("wall%d" % s, T2, F32, "wall", PAGE * (s % 2))
             nc.sync.dma_start(out=walls[s][:], in_=slice_rows(wall, s))
 
+        last_walls = {}
+
+        def load_last_walls():
+            for c in range(CHUNKS):
+                last_walls[c] = place("last_walls%d" % c, 2 * BANK, F32, "wall", ROW * c)
+                for e in range(2):
+                    nc.sync.dma_start(
+                        out=last_walls[c][:, BANK * e : BANK * e + BANK], in_=slice_rows(wall, LAST - 1 + e)[:, :, BANK * c : BANK * c + BANK]
+                    )
+
         scores = {}
         sources = {}
 
@@ -230,15 +241,22 @@ def tile_list_cave_wall_growth_kernel(
                 nc.scalar.mul(scores[s][:, halves[h]], bank[:], -1.0)
 
         rates = {}
+        gains = {}
 
         def rate(s, first_bank=0):
-            rates[s] = place("rates%d" % s, S, F32, *RATES_AT.get(s, ("rates",)))
+            if s in ON_VECTOR:
+                gains[s] = place("gain%d" % s, S, F32, *gain_at(s))
+            else:
+                rates[s] = place("rates%d" % s, S, F32, *RATES_AT.get(s, (GROWTH_AT[s - 1],)))
             for h in range(2):
                 bank = bank_at("rate%d%d" % (s, h), first_bank + h)
                 nc.tensor.matmul_mx(
                     out=bank[:], lhsT=w2q[s][0].bitcast(FP4X4), lhsT_scale=w2q[s][1], rhs=vw[h], rhs_scale=vs[h], start=True, stop=True
                 )
-                nc.scalar.mul(rates[s][:, halves[h]], bank[:], -1.0)
+                if s in ON_VECTOR:
+                    nc.vector.scalar_tensor_tensor(gains[s][:, halves[h]], bank[:], -1.0, rate_weights[s][:, halves[h]], MULT, MULT)
+                else:
+                    nc.scalar.mul(rates[s][:, halves[h]], bank[:], -1.0)
 
         def add_transposed(bank, rows, opens):
             for g in range(4):
@@ -254,7 +272,7 @@ def tile_list_cave_wall_growth_kernel(
             if s == 0:
                 nc.gpsimd.tensor_tensor(gaps[s][:], scores[s][:], eqs[s][:], ADD)
                 return
-            crossed = place("crossed%d" % s, S, F32, *CROSSED_AT.get(s, GAIN_AT[max(s - 1, 1)]))
+            crossed = place("crossed%d" % s, S, F32, *(("crossed",) if s < 3 else gain_at(s - 1)))
             for h, half in enumerate(halves):
                 bank = bank_at("sum%d%d" % (s, h), 2 + h)
                 add_transposed(bank, eqs[s][:, half], True)
@@ -268,11 +286,15 @@ def tile_list_cave_wall_growth_kernel(
 
         sinks = {}
 
+        def form_gain(s):
+            gains[s] = place("gain%d" % s, S, F32, *gain_at(s))
+            nc.gpsimd.tensor_tensor(gains[s][:], rates[s][:], rate_weights[s][:], MULT)
+
         def form_sink(s):
-            gain = place("gain%d" % s, S, F32, *GAIN_AT[s]) if s in GAIN_AT else rates[s]
-            nc.gpsimd.tensor_tensor(gain[:], rates[s][:], rate_weights[s][:], MULT)
+            if s not in gains:
+                form_gain(s)
             sinks[s] = place("sink%d" % s, S, F32, *SINK_AT.get(s, ("sink", ROW * (s % 2))))
-            nc.gpsimd.tensor_tensor(sinks[s][:], gaps[s][:], gain[:], MULT)
+            nc.gpsimd.tensor_tensor(sinks[s][:], gaps[s][:], gains[s][:], MULT)
 
         def form_source(s):
             sources[s] = place("source%d" % s, S, F32, *SOURCE_AT.get(s, GAP_AT[s]))
@@ -287,14 +309,14 @@ def tile_list_cave_wall_growth_kernel(
         growths = {}
 
         def exponentiate(s):
-            growths[s] = place("growth%d" % s, T2, F32, *GROWTH_AT[s])
+            growths[s] = place("growth%d" % s, T2, F32, GROWTH_AT[s])
             nc.scalar.activation(out=growths[s][:], in_=page_b[s % 2][:], func=EXP)
 
         products = {}
 
         def grow(s):
-            products[s] = place("product%d" % s, T2, F32, *PRODUCT_AT[s])
-            nc.gpsimd.tensor_tensor(products[s][:], growths[s][:], page_a[s % 2][:], MULT)
+            products[s] = place("product%d" % s, T2 if s < LAST - 1 else 2 * T2, F32, *PRODUCT_AT[s])
+            nc.gpsimd.tensor_tensor(products[s][:, :T2], growths[s][:], page_a[s % 2][:], MULT)
 
         turned = {}
 
@@ -350,28 +372,15 @@ def tile_list_cave_wall_growth_kernel(
                         pairs[j] = place("pairs%d" % j, 2 * (hi - lo), F32, "pairs", 8 * lo)
                         nc.scalar.copy(out=pairs[j][:, : hi - lo], in_=bank[:, lo - BANK * c : hi - BANK * c])
 
-        def last_lanes(j):
-            lo, hi = PIECES[j]
-            return pairs[j][:, hi - lo :].bitcast(BF16).rearrange("p (m e) -> p m e", e=2)
-
-        def form_third_lane():
-            lane = place("lane", T2, BF16, "s1", 4 * BANK)
-            for c0 in range(0, T2, S):
-                cols = slice(c0, c0 + S)
-                nc.gpsimd.tensor_tensor(lane[:, cols], products[LAST - 1][:, cols], walls[LAST - 1][:, cols], ADD)
-                for j, (lo, hi) in enumerate(PIECES):
-                    if c0 <= lo < c0 + S:
-                        nc.scalar.copy(out=last_lanes(j)[:, :, 0], in_=lane[:, lo:hi])
-
-
         nc.gpsimd.memset(tabs[:, : T // 2].bitcast(I32), 0)
         nc.vector.memset(tabs[:, T // 2 :].bitcast(I32), 0)
         nc.sync.dma_start(idx[:], offs)
-        raw_first = [load_w1("raw_w1_0", 0, P, "grouped", 2 * PAGE)]
+        raw_first = [place("raw_w1_%d" % s, 4 * P, F32, "grouped", 2 * PAGE + 16 * P * s) for s in range(2)]
+        load_w1(raw_first[0][:], 0, P)
         nc.sync.dma_start(idx2[:], offs2)
         load_scale_rows(tabs, tab_scales[0])
         nc.sync.dma_start(out=tabw[:].bitcast(I32), in_=tab_words[0].rearrange("p t i -> p (t i)").bitcast(I32))
-        raw_first.append(load_w1("raw_w1_1", P, 2 * P, "grouped", 2 * PAGE + 16 * P))
+        load_w1(raw_first[1][:], P, 2 * P)
         nc.gpsimd.memset(w2s[:].bitcast(I32), 0)
         for page in page_a:
             nc.vector.memset(page[:], 0.0)
@@ -388,8 +397,10 @@ def tile_list_cave_wall_growth_kernel(
         nc.sync.dma_start(out=w2w[:].bitcast(I32), in_=w2_words[0].bitcast(I32))
         load_scale_rows(w2s, w2_scales[0])
         load_eq(0)
-        raw_third = load_w1("raw_w1_3", 4 * P, H, "wall", PAGE)
-        raw_second = load_w1("raw_w1_2", 2 * P, 4 * P, "pairs")
+        raw_rest = place("raw_rest", 4 * (H - 2 * P), F32, "pairs")
+        raw_second, raw_third = raw_rest[:, : 8 * P], raw_rest[:, 8 * P :]
+        load_w1(raw_third, 4 * P, H)
+        load_w1(raw_second, 2 * P, 4 * P)
         nc.sync.dma_start(idx3[:], offs3)
         load_eq(2)
         load_eq(3)
@@ -409,104 +420,93 @@ def tile_list_cave_wall_growth_kernel(
         nc.vector.tensor_copy(page_a[0][:].indirect(idx2[:, 32:]), sources[0][:, halves[1]])
         form_source(1)
         scatter_source(1)
-        deal_w2(0)
         subtract(1)
         subtract(0)
         rate(0, 4)
+        rate(1, 6)
         grouped_rest = place("grouped_rest", 4 * (H - 2 * P), BF16, "r2")
-        group_dealt(grouped_rest[:, 8 * P :], raw_third[:])
-        group_plain(grouped_rest[:, : 8 * P], raw_second[:])
+        group_dealt(grouped_rest[:, 8 * P :], raw_third)
+        group_plain(grouped_rest[:, : 8 * P], raw_second)
+        form_gain(1)
         form_sink(0)
         codes_rest = place("codes_rest", H - 2 * P, U32, "codes_rest")
         scales_rest = place("scales_rest", H - 2 * P, U8, "codes_rest", 4 * (H - 2 * P))
         quantize(codes_rest, scales_rest, grouped_rest, (0, 2 * P, H - 2 * P))
         w1q.extend(stationary(codes_rest[:], scales_rest[:]))
         scatter_sink(0)
-        rate(1, 6)
         form_sink(1)
         scatter_sink(1)
         load_wall(0)
         load_weights(4)
-        rate(2, 4)
+        deal_w2(0)
+        rate(2, 6)
         score(2)
         subtract(2)
         form_sink(2)
         form_source(2)
         exponentiate(0)
         load_wall(1)
-        rate(3, 6)
         score(3)
+        rate(3)
         subtract(3)
         load_eq(4)
-        scatter_sink(2)
-        grow(0)
-        scatter_source(2)
-        exponentiate(1)
-        form_z(0)
-        load_wall(2)
-        form_sink(3)
-        load_eq(5)
-        form_source(3)
         negate_aside(4, "crossed")
         source_weights[5] = source_weights[4]
-        score(4)
-        rate(4)
-        subtract(4)
-        exponentiate(2)
-        score(5)
-        grow(1)
-        form_z(1)
-        load_wall(3)
-        load_weights(LAST)
 
-        for s in range(3, SLICES):
+        for s in range(2, SLICES):
             scatter_sink(s)
-            if s < LAST:
+            if s == 2:
+                exponentiate(s - 1)
+            grow(s - 2)
+            if s == LAST:
+                form_source(s)
+            scatter_source(s)
+            if s + 1 < LAST:
+                form_sink(s + 1)
+                exponentiate(s)
+                form_source(s + 1)
+            if s + 1 == LAST:
+                form_sink(s + 1)
+                exponentiate(s)
+            if s == LAST:
+                grow(s - 1)
                 exponentiate(s)
             if s == 3:
-                form_sink(s + 1)
-                form_source(s + 1)
-            grow(s - 1)
-            scatter_source(s)
-            if s < LAST:
-                form_z(s - 1)
-            if s in (5, 6):
-                regroup(s - 5)
-            if 3 < s < LAST:
-                form_sink(s + 1)
-                form_source(s + 1)
-            if s == 3:
                 deal_w2(1)
+            if s == 4:
+                form_z(s - 2)
             if s + 2 <= LAST:
+                score(s + 2)
                 rate(s + 2)
-            if s + 3 <= LAST:
-                score(s + 3)
-            if s + 2 <= LAST:
                 subtract(s + 2)
             if s + 3 <= LAST:
                 load_eq(s + 3)
+            if s != 4:
+                form_z(s - 2)
+            if s < LAST - 1:
+                load_wall(s)
+            if s == 2:
+                load_weights(LAST)
             if s == 3:
                 load_weights(6)
-            if s < LAST:
-                load_wall(s + 1)
             if s in (4, 5):
                 negate_aside(s + 2, *EQ_AT[s + 2])
+            if s in (5, 6):
+                regroup(s - 5)
             if s == LAST - 2:
                 raw_w3 = load_w3()
             if s == LAST - 1:
-                turn_first_lanes()
                 for b in range(2):
                     cols = slice(4 * N * b, 4 * N * (b + 1))
                     group_plain(grouped[:, 4 * T2 :][:, cols], raw_w3[:, cols])
             if s == LAST:
-                exponentiate(s)
-            if s == LAST:
-                form_third_lane()
+                load_last_walls()
+                turn_first_lanes()
 
         last_codes = place("last_codes", T2, U32, "sink")
         last_scales = place("last_scales", T2, U8, "crossed")
         scales = place("scales", T2 + 2 * N, U8, "eq", ROW)
-        w3_codes = place("w3_codes", 2 * N, U32, "s1", 4 * BANK - 8 * N)
+        w3_codes = place("w3_codes", 2 * N, U32, "wall", BANK - 8 * N)
         w3q = stationary(w3_codes[:], scales[:, T2:])
         first_codes = {}
         woven = {}
@@ -530,21 +530,19 @@ def tile_list_cave_wall_growth_kernel(
                 out=out[:, lo:hi].rearrange("(b p) m -> p b m", p=P), in_=results[:].rearrange("p (b m) -> p b m", b=OUT_TILES)
             )
 
-        def part_at(j):
-            return ("s1", 4 * BANK + 4 * PIECES[j][0]) if j < AHEAD else ("turned", 8 * PIECES[j - AHEAD][0])
-
-        parts = {}
-
         def multiply(j):
             lo, hi = PIECES[j]
-            area, at = part_at(j)
-            spare = 16 if j == 0 else 0
-            parts[j] = place("part%d" % j, spare + hi - lo, F32, area, at - 4 * spare)[:, spare:]
-            nc.vector.tensor_tensor(parts[j], growths[LAST][:, lo:hi], page_a[LAST % 2][:, lo:hi], MULT)
+            nc.vector.tensor_tensor(products[LAST - 1][:, T2 + lo : T2 + hi], growths[LAST][:, lo:hi], page_a[LAST % 2][:, lo:hi], MULT)
 
         def finish_lanes(j):
             lo, hi = PIECES[j]
-            nc.vector.tensor_tensor(last_lanes(j)[:, :, 1], parts[j], walls[LAST][:, lo:hi], ADD)
+            c, c0 = divmod(lo, BANK)
+            nc.vector.tensor_tensor(
+                pairs[j][:, hi - lo :].bitcast(BF16).rearrange("p (a i e) -> p a e i", i=4, e=2),
+                products[LAST - 1][:].rearrange("p (e a i) -> p a e i", e=2, i=4)[:, lo // 4 : hi // 4],
+                last_walls[c][:].rearrange("p (e a i) -> p a e i", e=2, i=4)[:, c0 // 4 : (c0 + hi - lo) // 4],
+                ADD,
+            )
             woven[j] = place("woven%d" % j, 4 * (hi - lo), BF16, "turned", 8 * lo)
             weave = nc.vector.tensor_copy if j in VECTOR_WEAVES else nc.scalar.copy
             weave(
@@ -554,16 +552,16 @@ def tile_list_cave_wall_growth_kernel(
 
         def quantize_first_pass(j):
             lo, hi = PIECES[j]
-            area, at = part_at(j)
-            first_codes[j] = place("first_codes%d" % j, hi - lo, U32, area, at)
+            c, c0 = divmod(lo, BANK)
+            first_codes[j] = place("first_codes%d" % j, hi - lo, U32, "wall", ROW * c + BANK + 4 * c0)
             quantize(first_codes[j], scales[:, lo:hi], grouped[:, 4 * lo : 4 * hi], (0, hi - lo))
 
         multiply(0)
         multiply(1)
         finish_lanes(0)
+        finish_lanes(1)
         quantize(w3_codes, scales[:, T2:], grouped[:, 4 * T2 :], (0, N))
         quantize_first_pass(0)
-        finish_lanes(1)
         quantize(w3_codes, scales[:, T2:], grouped[:, 4 * T2 :], (N, 2 * N))
         for j in range(len(PIECES)):
             done = slice(*PIECES[j])

@@ -42,25 +42,26 @@ def lay_out(areas):
 
 AT = lay_out(
     (
-        ("words", ROW), ("bytes", S), ("w2w", 2 * H), ("w2s", H), ("ident", 4 * P),
-        ("codes_first", 4 * 256), ("scales_first", 256), ("codes_rest", ROW),
+        ("words", ROW), ("bytes", S), ("gathered", S), ("ident", 4 * P),
+        ("codes_second", 4 * P), ("scales_first", 2 * P), ("codes_rest", ROW),
         ("page_a", 2 * PAGE), ("page_b", 2 * PAGE),
         ("r0", PAGE), ("r1", PAGE), ("r2", PAGE), ("s0", PAGE), ("s1", PAGE),
-        ("gap", 2 * ROW), ("sink", 2 * ROW), ("crossed", ROW), ("eq", 3 * ROW), ("dealt", 768), ("rates", ROW), ("wall", 2 * PAGE), ("wg", 3 * PAGE),
-        ("turned", 2 * PAGE), ("before", ROW), ("grouped", 2 * PAGE + 8 * 2 * N),
-        ("codes", 4 * (T2 + 2 * N)), ("scales", T2 + 2 * N), ("dealt_late", 768), ("pairs", 2 * PAGE),
+        ("gap", 2 * ROW), ("sink", 2 * ROW), ("crossed", ROW), ("dealt", 768),
+        ("turned", 2 * PAGE), ("grouped", 2 * PAGE + 8 * 2 * N),
+        ("codes", 4 * (T2 + 2 * N)), ("scales", T2 + 2 * N), ("dealt_late", 768),
+        ("rates", ROW), ("wall", 2 * PAGE), ("pairs", ROW), ("pairs_late", 3 * ROW), ("wg", PAGE),
+        ("codes_first", 4 * P), ("w2s", H), ("w2w", 2 * H), ("eq", 2 * ROW), ("wg_late", 2 * PAGE),
     )
 )
-SCORES_AT = {0: ("s0", ROW), 1: ("r1", ROW), 2: ("s0",), 3: ("s1",), 4: ("dealt_late", 768 - ROW), 5: ("r2",), 6: ("dealt_late", -PAGE), 7: ("s0",)}
+SCORES_AT = {0: ("wg_late", PAGE), 1: ("r1", ROW), 2: ("s0",), 3: ("s1",), 4: ("dealt_late", 768 - ROW), 5: ("r2",), 6: ("dealt_late", -PAGE), 7: ("s0",)}
 PRODUCT_AT = {0: ("s0",), 1: ("s1",), 2: ("dealt_late", -PAGE), 3: ("r2",), 4: ("dealt_late", -PAGE), 5: ("r1",), 6: ("s0",)}
-ON_VECTOR = (0,)
-GROWTH_AT = {0: "r0", 1: "r1", 2: "pairs", 3: "r0", 4: "r1", 5: "s1", 6: "r0", 7: "r0"}
-RATES_AT = {1: ("pairs", 3 * ROW), 2: ("r0",)}
-GAIN_AT = {0: ("s1", ROW), 1: ("r1",), 2: ("r1", ROW // 2)}
-GAP_AT = {0: ("r1", ROW), 1: ("wg", 2 * PAGE + ROW), 2: ("gap",), 3: ("gap", ROW), 4: ("codes",), 5: ("gap",), 6: ("gap", ROW), 7: ("codes",)}
-EQ_AT = {3: ("wg", 2 * PAGE), 4: ("eq", ROW), 5: ("wg", 2 * PAGE + ROW), 6: ("eq", 2 * ROW), 7: ("eq",)}
+GROWTH_AT = {0: "r0", 1: "r1", 2: "pairs_late", 3: "r0", 4: "r1", 5: "s1", 6: "r0", 7: "r0"}
+RATES_AT = {0: ("wg_late", PAGE + ROW), 1: ("wall", PAGE), 2: ("r0",)}
+GAIN_AT = {0: ("r1",), 1: ("r2", -ROW // 2), 2: ("r1", ROW)}
+GAP_AT = {0: ("r1", ROW), 1: ("wall",), 2: ("gap",), 3: ("gap", ROW), 4: ("codes",), 5: ("gap",), 6: ("gap", ROW), 7: ("codes",)}
+EQ_AT = {0: ("eq", ROW), 1: ("eq",), 2: ("grouped",), 3: ("wg_late", PAGE), 4: ("eq",), 5: ("wg_late", PAGE + ROW), 6: ("eq", ROW), 7: ("eq",)}
 SOURCE_AT = {0: ("gap",), 1: ("codes_rest",)}
-SINK_AT = {0: ("pairs", 5 * ROW // 2), 1: ("r2",)}
+SINK_AT = {0: ("pairs", 3 * ROW)}
 
 
 def gain_at(s):
@@ -97,7 +98,7 @@ def tile_list_cave_wall_growth_kernel(
         idx2 = lists.tile([P, S // 16], U16, name="idx2")
         idx3 = lists.tile([P, S // 16], U16, name="idx3")
         tabw = place("tabw", T, U32, "grouped")
-        tabs = place("tabs", T, U8, "before")
+        tabs = place("tabs", T, U8, "codes_first", -2 * P)
         w2w = place("w2w", 2 * H, U8, "w2w")
         w2s = place("w2s", H, U8, "w2s")
         ident = place("ident", P, F32, "ident")
@@ -106,6 +107,7 @@ def tile_list_cave_wall_growth_kernel(
         halves = [slice(BANK * h, BANK * h + BANK) for h in range(2)]
         words = place("words", S, U32, "words")
         scale_bytes = place("scale_bytes", S, U8, "bytes")
+        gathered = place("gathered", S, U8, "gathered")
         vw = [words[:, half].bitcast(FP8X4) for half in halves]
         vs = [scale_bytes[:, half] for half in halves]
 
@@ -132,7 +134,7 @@ def tile_list_cave_wall_growth_kernel(
             interleave(grouped[:, 1536:], dealt[:, :, :, 6:8], 2)
 
         def load_w3():
-            raw = place("raw_w3", 8 * N, F32, "wg", 2 * PAGE - ROW)
+            raw = place("raw_w3", 8 * N, F32, "wg_late", ROW)
             nc.sync.dma_start(out=raw[:, : 4 * N].rearrange("p (t c) -> p t c", t=4), in_=by_fours(w3[:512, :]))
             dealt = by_eights(w3[512:, :])
             nc.sync.dma_start(out=raw[:, 4 * N : 6 * N], in_=dealt[:, 0:4].rearrange("b (i t) n -> b i (t n)", i=2))
@@ -150,12 +152,12 @@ def tile_list_cave_wall_growth_kernel(
         w1q = []
 
         def first_w1(s, raw):
-            grouped = place("grouped_w1_%d" % s, 4 * P, BF16, "grouped", 2 * PAGE + ROW + 8 * P * s)
+            grouped = place("grouped_w1_%d" % s, 4 * P, BF16, *(("wg", -4 * P), ("grouped", 2 * PAGE + ROW))[s])
             group_plain(grouped[:], raw[:])
             return grouped
 
         def quantize_first(s, grouped):
-            codes = place("w1_codes%d" % s, P, U32, "codes_first", 4 * P * s)
+            codes = place("w1_codes%d" % s, P, U32, ("codes_first", "codes_second")[s])
             scales = place("w1_scales%d" % s, P, U8, "scales_first", P * s)
             quantize(codes, scales, grouped, (0, P))
             w1q.extend(stationary(codes[:], scales[:]))
@@ -194,11 +196,11 @@ def tile_list_cave_wall_growth_kernel(
             source_weights[s] = aside
 
         def load_weights(s):
-            at = PAGE * {4: 1, 6: 2, 7: 0}[s]
+            area, at = {4: ("grouped", ROW), 6: ("wg_late", PAGE), 7: ("wg", 0)}[s]
             rows = {4: slice(0, 4), 6: slice(4, 6), 7: slice(6, 8)}[s]
             span = 16 * (rows.stop - rows.start)
             for i, (matrix, held) in enumerate(((wg2, rate_weights), (wg1, source_weights))):
-                held[s] = place("wg%d_%d" % (2 - i, s), S, F32, "wg", at + ROW * i)
+                held[s] = place("wg%d_%d" % (2 - i, s), S, F32, area, at + ROW * i)
                 for p0 in range(0, P, span):
                     nc.sync.dma_start(out=held[s][p0 : p0 + span, :], in_=by_eights(matrix)[:, rows])
                 if s == 4:
@@ -207,7 +209,7 @@ def tile_list_cave_wall_growth_kernel(
         eqs = {}
 
         def load_eq(s):
-            eqs[s] = place("eq%d" % s, S, F32, *EQ_AT.get(s, ("eq", ROW * s)))
+            eqs[s] = place("eq%d" % s, S, F32, *EQ_AT[s])
             nc.sync.dma_start(out=eqs[s][:], in_=slice_rows(eq, s))
 
         walls = {}
@@ -244,19 +246,13 @@ def tile_list_cave_wall_growth_kernel(
         gains = {}
 
         def rate(s, first_bank=0):
-            if s in ON_VECTOR:
-                gains[s] = place("gain%d" % s, S, F32, *gain_at(s))
-            else:
-                rates[s] = place("rates%d" % s, S, F32, *RATES_AT.get(s, (GROWTH_AT[s - 1],)))
+            rates[s] = place("rates%d" % s, S, F32, *(RATES_AT[s] if s in RATES_AT else (GROWTH_AT[s - 1],)))
             for h in range(2):
                 bank = bank_at("rate%d%d" % (s, h), first_bank + h)
                 nc.tensor.matmul_mx(
                     out=bank[:], lhsT=w2q[s][0].bitcast(FP4X4), lhsT_scale=w2q[s][1], rhs=vw[h], rhs_scale=vs[h], start=True, stop=True
                 )
-                if s in ON_VECTOR:
-                    nc.vector.scalar_tensor_tensor(gains[s][:, halves[h]], bank[:], -1.0, rate_weights[s][:, halves[h]], MULT, MULT)
-                else:
-                    nc.scalar.mul(rates[s][:, halves[h]], bank[:], -1.0)
+                nc.scalar.mul(rates[s][:, halves[h]], bank[:], -1.0)
 
         def add_transposed(bank, rows, opens):
             for g in range(4):
@@ -286,13 +282,9 @@ def tile_list_cave_wall_growth_kernel(
 
         sinks = {}
 
-        def form_gain(s):
+        def form_sink(s):
             gains[s] = place("gain%d" % s, S, F32, *gain_at(s))
             nc.gpsimd.tensor_tensor(gains[s][:], rates[s][:], rate_weights[s][:], MULT)
-
-        def form_sink(s):
-            if s not in gains:
-                form_gain(s)
             sinks[s] = place("sink%d" % s, S, F32, *SINK_AT.get(s, ("sink", ROW * (s % 2))))
             nc.gpsimd.tensor_tensor(sinks[s][:], gaps[s][:], gains[s][:], MULT)
 
@@ -374,19 +366,29 @@ def tile_list_cave_wall_growth_kernel(
 
         nc.gpsimd.memset(tabs[:, : T // 2].bitcast(I32), 0)
         nc.vector.memset(tabs[:, T // 2 :].bitcast(I32), 0)
-        nc.sync.dma_start(idx[:], offs)
-        raw_first = [place("raw_w1_%d" % s, 4 * P, F32, "grouped", 2 * PAGE + 16 * P * s) for s in range(2)]
+        for offsets, source in ((idx, offs), (idx2, offs2), (idx3, offs3)):
+            nc.sync.dma_start(offsets[:], source)
+        raw_first = [place("raw_w1_0", 4 * P, F32, "page_b", PAGE - 8 * P), place("raw_w1_1", 4 * P, F32, "eq", ROW + ROW // 2)]
         load_w1(raw_first[0][:], 0, P)
-        nc.sync.dma_start(idx2[:], offs2)
-        load_scale_rows(tabs, tab_scales[0])
+        for i in range(2):
+            nc.sync.dma_start(out=tabs[64 * i : 64 * i + 32 : 4, :].bitcast(I32), in_=tab_scales[0][8 * i : 8 * i + 8, :].bitcast(I32))
         nc.sync.dma_start(out=tabw[:].bitcast(I32), in_=tab_words[0].rearrange("p t i -> p (t i)").bitcast(I32))
         load_w1(raw_first[1][:], P, 2 * P)
-        nc.gpsimd.memset(w2s[:].bitcast(I32), 0)
+        nc.gpsimd.memset(scale_bytes[:].bitcast(I32), 0)
         for page in page_a:
-            nc.vector.memset(page[:], 0.0)
-        for page in page_b:
-            nc.gpsimd.memset(page[:], 0.0)
+            nc.vector.memset(page[:].bitcast(I32), 0)
         make_identity(nc, ident[:])
+        nc.vector.tensor_copy(gathered[:], tabs[:].indirect(idx[:]))
+        for q in range(4):
+            first_row = 64 * (q // 2) + 16 * (q % 2)
+            nc.sync.dma_start(
+                out=scale_bytes[32 * q : 32 * q + 4, :].bitcast(I32), in_=gathered[first_row : first_row + 16 : 4, :].bitcast(I32)
+            )
+        grouped_first = [first_w1(0, raw_first[0])]
+        quantize_first(0, grouped_first[0])
+        nc.vector.memset(w2s[:].bitcast(I32), 0)
+        nc.vector.memset(page_b[0][:].bitcast(I32), 0)
+        nc.gpsimd.memset(page_b[1][:], 0.0)
         plain_weights = [place("wg%d_0" % (2 - i), S, F32, "wg", ROW * i) for i in range(2)]
         for s in range(4):
             rate_weights[s], source_weights[s] = plain_weights
@@ -396,20 +398,16 @@ def tile_list_cave_wall_growth_kernel(
         nc.sync.dma_start(out=rate_weights[0][:], in_=wg2)
         nc.sync.dma_start(out=w2w[:].bitcast(I32), in_=w2_words[0].bitcast(I32))
         load_scale_rows(w2s, w2_scales[0])
-        load_eq(0)
-        raw_rest = place("raw_rest", 4 * (H - 2 * P), F32, "pairs")
+        raw_rest = place("raw_rest", 4 * (H - 2 * P), F32, "pairs", ROW)
         raw_second, raw_third = raw_rest[:, : 8 * P], raw_rest[:, 8 * P :]
         load_w1(raw_third, 4 * P, H)
         load_w1(raw_second, 2 * P, 4 * P)
-        nc.sync.dma_start(idx3[:], offs3)
-        load_eq(2)
-        load_eq(3)
-        grouped_first = [first_w1(s, raw_first[s]) for s in range(2)]
-        nc.vector.tensor_copy(scale_bytes[:], tabs[:].indirect(idx[:]))
-        quantize_first(0, grouped_first[0])
+        grouped_first.append(first_w1(1, raw_first[1]))
+        load_eq(0)
         for h in range(2):
             nc.vector.tensor_copy(words[:, halves[h]], tabw[:].indirect(idx[:, 32 * h : 32 * h + 32]))
         quantize_first(1, grouped_first[1])
+        load_eq(2)
         sources[0] = place("source0", S, F32, *SOURCE_AT[0])
         negate(source_weights[0][:, halves[1]])
         score(0)
@@ -420,14 +418,15 @@ def tile_list_cave_wall_growth_kernel(
         nc.vector.tensor_copy(page_a[0][:].indirect(idx2[:, 32:]), sources[0][:, halves[1]])
         form_source(1)
         scatter_source(1)
-        subtract(1)
-        subtract(0)
         rate(0, 4)
-        rate(1, 6)
         grouped_rest = place("grouped_rest", 4 * (H - 2 * P), BF16, "r2")
         group_dealt(grouped_rest[:, 8 * P :], raw_third)
         group_plain(grouped_rest[:, : 8 * P], raw_second)
-        form_gain(1)
+        subtract(1)
+        subtract(0)
+        load_eq(3)
+        rate(1, 6)
+        rate(2, 4)
         form_sink(0)
         codes_rest = place("codes_rest", H - 2 * P, U32, "codes_rest")
         scales_rest = place("scales_rest", H - 2 * P, U8, "codes_rest", 4 * (H - 2 * P))
@@ -439,7 +438,6 @@ def tile_list_cave_wall_growth_kernel(
         load_wall(0)
         load_weights(4)
         deal_w2(0)
-        rate(2, 6)
         score(2)
         subtract(2)
         form_sink(2)
@@ -505,7 +503,7 @@ def tile_list_cave_wall_growth_kernel(
 
         last_codes = place("last_codes", T2, U32, "sink")
         last_scales = place("last_scales", T2, U8, "crossed")
-        scales = place("scales", T2 + 2 * N, U8, "eq", ROW)
+        scales = place("scales", T2 + 2 * N, U8, "gap")
         w3_codes = place("w3_codes", 2 * N, U32, "wall", BANK - 8 * N)
         w3q = stationary(w3_codes[:], scales[:, T2:])
         first_codes = {}
@@ -514,8 +512,8 @@ def tile_list_cave_wall_growth_kernel(
         def project(j):
             lo, hi = PIECES[j]
             first = (first_codes[j][:], scales[:, lo:hi])
-            at = 4 * OUT_TILES * lo
-            results = place("results%d" % j, OUT_TILES * (hi - lo), F32, "wg", at)
+            area, at = ("r1", 4 * OUT_TILES * lo) if j < 5 else ("wg_late", 4 * OUT_TILES * (lo - PIECES[5][0]))
+            results = place("results%d" % j, OUT_TILES * (hi - lo), F32, area, at)
             for nb in range(OUT_TILES):
                 bank = bank_at("out%d%d" % (j, nb), (OUT_TILES * j + nb + 4) % 8)
                 for b, (z_codes, z_scales) in enumerate((first, (last_codes[:, lo:hi], last_scales[:, lo:hi]))):

@@ -53,13 +53,13 @@ AT = lay_out(
         ("codes_first", 4 * P), ("w2s", H), ("w2w", 2 * H), ("eq", 2 * ROW), ("wg_late", 2 * PAGE),
     )
 )
-SCORES_AT = {0: ("wg_late", PAGE), 1: ("r1", ROW), 2: ("s0",), 3: ("s1",), 4: ("dealt_late", 768 - ROW), 5: ("r2",), 6: ("dealt_late", -PAGE), 7: ("s0",)}
+SCORES_AT = {0: ("wg_late", PAGE), 1: ("s1", ROW), 2: ("s0",), 3: ("s1",), 4: ("dealt_late", 768 - ROW), 5: ("r2",), 6: ("dealt_late", -PAGE), 7: ("s0",)}
 PRODUCT_AT = {0: ("s0",), 1: ("s1",), 2: ("dealt_late", -PAGE), 3: ("r2",), 4: ("dealt_late", -PAGE), 5: ("r1",), 6: ("s0",)}
 GROWTH_AT = {0: "r0", 1: "r1", 2: "pairs_late", 3: "r0", 4: "r1", 5: "s1", 6: "r0", 7: "r0"}
 RATES_AT = {0: ("wg_late", PAGE + ROW), 1: ("wall", PAGE), 2: ("r0",)}
 GAIN_AT = {0: ("r1",), 1: ("r2", -ROW // 2), 2: ("r1", ROW)}
 GAP_AT = {0: ("r1", ROW), 1: ("wall",), 2: ("gap",), 3: ("gap", ROW), 4: ("codes",), 5: ("gap",), 6: ("gap", ROW), 7: ("codes",)}
-EQ_AT = {0: ("eq", ROW), 1: ("eq",), 2: ("grouped",), 3: ("wg_late", PAGE), 4: ("eq",), 5: ("wg_late", PAGE + ROW), 6: ("eq", ROW), 7: ("eq",)}
+EQ_AT = {0: ("eq",), 1: ("eq", ROW), 2: ("grouped",), 3: ("wg_late", PAGE), 4: ("eq",), 5: ("wg_late", PAGE + ROW), 6: ("eq", ROW), 7: ("eq",)}
 SOURCE_AT = {0: ("gap",), 1: ("codes_rest",)}
 SINK_AT = {0: ("pairs", 3 * ROW)}
 
@@ -386,24 +386,24 @@ def tile_list_cave_wall_growth_kernel(
             )
         grouped_first = [first_w1(0, raw_first[0])]
         quantize_first(0, grouped_first[0])
-        nc.vector.memset(w2s[:].bitcast(I32), 0)
-        nc.vector.memset(page_b[0][:].bitcast(I32), 0)
-        nc.gpsimd.memset(page_b[1][:], 0.0)
+        nc.gpsimd.memset(w2s[:].bitcast(I32), 0)
+        for page in page_b:
+            nc.gpsimd.memset(page[:], 0.0)
         plain_weights = [place("wg%d_0" % (2 - i), S, F32, "wg", ROW * i) for i in range(2)]
         for s in range(4):
             rate_weights[s], source_weights[s] = plain_weights
         for half in halves:
             nc.sync.dma_start(out=source_weights[0][:, half], in_=wg1[:, half])
-        load_eq(1)
         nc.sync.dma_start(out=rate_weights[0][:], in_=wg2)
         nc.sync.dma_start(out=w2w[:].bitcast(I32), in_=w2_words[0].bitcast(I32))
         load_scale_rows(w2s, w2_scales[0])
         raw_rest = place("raw_rest", 4 * (H - 2 * P), F32, "pairs", ROW)
         raw_second, raw_third = raw_rest[:, : 8 * P], raw_rest[:, 8 * P :]
         load_w1(raw_third, 4 * P, H)
+        load_eq(0)
         load_w1(raw_second, 2 * P, 4 * P)
         grouped_first.append(first_w1(1, raw_first[1]))
-        load_eq(0)
+        load_eq(1)
         for h in range(2):
             nc.vector.tensor_copy(words[:, halves[h]], tabw[:].indirect(idx[:, 32 * h : 32 * h + 32]))
         quantize_first(1, grouped_first[1])
@@ -418,15 +418,15 @@ def tile_list_cave_wall_growth_kernel(
         nc.vector.tensor_copy(page_a[0][:].indirect(idx2[:, 32:]), sources[0][:, halves[1]])
         form_source(1)
         scatter_source(1)
-        rate(0, 4)
+        rate(0, 6)
         grouped_rest = place("grouped_rest", 4 * (H - 2 * P), BF16, "r2")
         group_dealt(grouped_rest[:, 8 * P :], raw_third)
         group_plain(grouped_rest[:, : 8 * P], raw_second)
-        subtract(1)
         subtract(0)
+        subtract(1)
         load_eq(3)
-        rate(1, 6)
-        rate(2, 4)
+        rate(1, 4)
+        rate(2, 6)
         form_sink(0)
         codes_rest = place("codes_rest", H - 2 * P, U32, "codes_rest")
         scales_rest = place("scales_rest", H - 2 * P, U8, "codes_rest", 4 * (H - 2 * P))
@@ -504,7 +504,7 @@ def tile_list_cave_wall_growth_kernel(
         last_codes = place("last_codes", T2, U32, "sink")
         last_scales = place("last_scales", T2, U8, "crossed")
         scales = place("scales", T2 + 2 * N, U8, "gap")
-        w3_codes = place("w3_codes", 2 * N, U32, "wall", BANK - 8 * N)
+        w3_codes = place("w3_codes", 2 * N, U32, "wall", 64 - 8 * N)
         w3q = stationary(w3_codes[:], scales[:, T2:])
         first_codes = {}
         woven = {}
@@ -550,8 +550,7 @@ def tile_list_cave_wall_growth_kernel(
 
         def quantize_first_pass(j):
             lo, hi = PIECES[j]
-            c, c0 = divmod(lo, BANK)
-            first_codes[j] = place("first_codes%d" % j, hi - lo, U32, "wall", ROW * c + BANK + 4 * c0)
+            first_codes[j] = place("first_codes%d" % j, hi - lo, U32, "wall", 64 + 4 * lo)
             quantize(first_codes[j], scales[:, lo:hi], grouped[:, 4 * lo : 4 * hi], (0, hi - lo))
 
         multiply(0)

@@ -42,15 +42,15 @@ def lay_out(areas):
 
 AT = lay_out(
     (
-        ("words", ROW), ("bytes", S), ("gathered", S), ("ident", 4 * P),
+        ("words", ROW), ("bytes", S), ("gathered", S), ("ident", 8 * P),
         ("codes_second", 4 * P), ("scales_first", 2 * P), ("codes_rest", ROW),
-        ("page_a", 2 * PAGE), ("page_b", 2 * PAGE),
+        ("page_a", 2 * PAGE), ("page_b0", PAGE),
         ("r0", PAGE), ("r1", PAGE), ("r2", PAGE), ("s0", PAGE), ("s1", PAGE),
         ("gap", 2 * ROW), ("sink", 2 * ROW), ("crossed", ROW), ("dealt", 768),
         ("turned", 2 * PAGE), ("grouped", 2 * PAGE + 8 * 2 * N),
         ("codes", 4 * (T2 + 2 * N)), ("scales", T2 + 2 * N), ("dealt_late", 768),
         ("rates", ROW), ("wall", 2 * PAGE), ("pairs", ROW), ("pairs_late", 3 * ROW), ("wg", PAGE),
-        ("codes_first", 4 * P), ("w2s", H), ("w2w", 2 * H), ("eq", 2 * ROW), ("wg_late", 2 * PAGE),
+        ("codes_first", 4 * P), ("w2s", H), ("w2w", 2 * H), ("page_b1", PAGE), ("eq", 2 * ROW), ("wg_late", 2 * PAGE),
     )
 )
 SCORES_AT = {0: ("wg_late", PAGE), 1: ("s1", ROW), 2: ("s0",), 3: ("s1",), 4: ("dealt_late", 768 - ROW), 5: ("r2",), 6: ("dealt_late", -PAGE), 7: ("s0",)}
@@ -103,7 +103,7 @@ def tile_list_cave_wall_growth_kernel(
         w2s = place("w2s", H, U8, "w2s")
         ident = place("ident", P, F32, "ident")
         page_a = [place("page_a%d" % i, T2, F32, "page_a", PAGE * i) for i in range(2)]
-        page_b = [place("page_b%d" % i, T2, F32, "page_b", PAGE * i) for i in range(2)]
+        page_b = [place("page_b%d" % i, T2, F32, "page_b%d" % i) for i in range(2)]
         halves = [slice(BANK * h, BANK * h + BANK) for h in range(2)]
         words = place("words", S, U32, "words")
         scale_bytes = place("scale_bytes", S, U8, "bytes")
@@ -152,7 +152,7 @@ def tile_list_cave_wall_growth_kernel(
         w1q = []
 
         def first_w1(s, raw):
-            grouped = place("grouped_w1_%d" % s, 4 * P, BF16, *(("wg", -4 * P), ("grouped", 2 * PAGE + ROW))[s])
+            grouped = place("grouped_w1_%d" % s, 4 * P, BF16, *(("wg", -4 * P), ("ident",))[s])
             group_plain(grouped[:], raw[:])
             return grouped
 
@@ -368,16 +368,15 @@ def tile_list_cave_wall_growth_kernel(
         nc.vector.memset(tabs[:, T // 2 :].bitcast(I32), 0)
         for offsets, source in ((idx, offs), (idx2, offs2), (idx3, offs3)):
             nc.sync.dma_start(offsets[:], source)
-        raw_first = [place("raw_w1_0", 4 * P, F32, "page_b", PAGE - 8 * P), place("raw_w1_1", 4 * P, F32, "eq", ROW + ROW // 2)]
+        raw_first = [place("raw_w1_0", 4 * P, F32, "grouped", 2 * PAGE), place("raw_w1_1", 4 * P, F32, "eq", ROW - 8 * P)]
         load_w1(raw_first[0][:], 0, P)
         for i in range(2):
             nc.sync.dma_start(out=tabs[64 * i : 64 * i + 32 : 4, :].bitcast(I32), in_=tab_scales[0][8 * i : 8 * i + 8, :].bitcast(I32))
         nc.sync.dma_start(out=tabw[:].bitcast(I32), in_=tab_words[0].rearrange("p t i -> p (t i)").bitcast(I32))
         load_w1(raw_first[1][:], P, 2 * P)
-        nc.gpsimd.memset(scale_bytes[:].bitcast(I32), 0)
+        nc.vector.memset(scale_bytes[:].bitcast(I32), 0)
         for page in page_a:
             nc.vector.memset(page[:].bitcast(I32), 0)
-        make_identity(nc, ident[:])
         nc.vector.tensor_copy(gathered[:], tabs[:].indirect(idx[:]))
         for q in range(4):
             first_row = 64 * (q // 2) + 16 * (q % 2)
@@ -386,9 +385,9 @@ def tile_list_cave_wall_growth_kernel(
             )
         grouped_first = [first_w1(0, raw_first[0])]
         quantize_first(0, grouped_first[0])
-        nc.gpsimd.memset(w2s[:].bitcast(I32), 0)
+        nc.vector.memset(w2s[:].bitcast(I32), 0)
         for page in page_b:
-            nc.gpsimd.memset(page[:], 0.0)
+            nc.vector.memset(page[:].bitcast(I32), 0)
         plain_weights = [place("wg%d_0" % (2 - i), S, F32, "wg", ROW * i) for i in range(2)]
         for s in range(4):
             rate_weights[s], source_weights[s] = plain_weights
@@ -400,13 +399,14 @@ def tile_list_cave_wall_growth_kernel(
         raw_rest = place("raw_rest", 4 * (H - 2 * P), F32, "pairs", ROW)
         raw_second, raw_third = raw_rest[:, : 8 * P], raw_rest[:, 8 * P :]
         load_w1(raw_third, 4 * P, H)
+        grouped_first.append(first_w1(1, raw_first[1]))
         load_eq(0)
         load_w1(raw_second, 2 * P, 4 * P)
-        grouped_first.append(first_w1(1, raw_first[1]))
         load_eq(1)
         for h in range(2):
             nc.vector.tensor_copy(words[:, halves[h]], tabw[:].indirect(idx[:, 32 * h : 32 * h + 32]))
         quantize_first(1, grouped_first[1])
+        make_identity(nc, ident[:])
         load_eq(2)
         sources[0] = place("source0", S, F32, *SOURCE_AT[0])
         negate(source_weights[0][:, halves[1]])

@@ -26,8 +26,10 @@ LAST = SLICES - 1
 CHUNKS = T2 // BANK
 OUT_TILES = N // P
 PIECES = tuple((lo, lo + 256) for lo in range(0, T2, 256))
-VECTOR_WEAVES = (7,)
+VECTOR_WEAVES = (6, 7)
 VECTOR_EMPTIES = ((6, 2), (7, 1), (7, 2))
+SPLIT = 2 * BANK
+WALL_CUTS = ((0, 256), (256, 512), (512, 1024), (1024, 1536), (1536, 2048))
 ROW = 4 * S
 PAGE = 4 * T2
 
@@ -221,12 +223,15 @@ def tile_list_cave_wall_growth_kernel(
         last_walls = {}
 
         def load_last_walls():
-            for c in range(CHUNKS):
-                last_walls[c] = place("last_walls%d" % c, 2 * BANK, F32, "wall", ROW * c)
+            for lo, hi in WALL_CUTS:
+                both = place("last_walls%d" % lo, 2 * (hi - lo), F32, "wall", 8 * lo)[:].rearrange("p (e m) -> p e m", e=2)
                 for e in range(2):
-                    nc.sync.dma_start(
-                        out=last_walls[c][:, BANK * e : BANK * e + BANK], in_=slice_rows(wall, LAST - 1 + e)[:, :, BANK * c : BANK * c + BANK]
-                    )
+                    nc.sync.dma_start(out=both[:, e], in_=slice_rows(wall, LAST - 1 + e)[:, :, lo:hi])
+                last_walls[lo, hi] = both
+
+        def last_wall(lo, hi):
+            cut = [cut for cut in WALL_CUTS if cut[0] <= lo and hi <= cut[1]][0]
+            return last_walls[cut][:, :, lo - cut[0] : hi - cut[0]]
 
         scores = {}
         sources = {}
@@ -282,9 +287,13 @@ def tile_list_cave_wall_growth_kernel(
 
         sinks = {}
 
-        def form_sink(s):
+        def form_gain(s):
             gains[s] = place("gain%d" % s, S, F32, *gain_at(s))
             nc.gpsimd.tensor_tensor(gains[s][:], rates[s][:], rate_weights[s][:], MULT)
+
+        def form_sink(s):
+            if s > 0:
+                form_gain(s)
             sinks[s] = place("sink%d" % s, S, F32, *SINK_AT.get(s, ("sink", ROW * (s % 2))))
             nc.gpsimd.tensor_tensor(sinks[s][:], gaps[s][:], gains[s][:], MULT)
 
@@ -303,6 +312,12 @@ def tile_list_cave_wall_growth_kernel(
         def exponentiate(s):
             growths[s] = place("growth%d" % s, T2, F32, GROWTH_AT[s])
             nc.scalar.activation(out=growths[s][:], in_=page_b[s % 2][:], func=EXP)
+
+        last_growths = []
+
+        def exponentiate_last(i, *at):
+            last_growths.append(place("last_growth%d" % i, SPLIT, F32, *at))
+            nc.scalar.activation(out=last_growths[i][:], in_=page_b[LAST % 2][:, SPLIT * i : SPLIT * (i + 1)], func=EXP)
 
         products = {}
 
@@ -364,6 +379,19 @@ def tile_list_cave_wall_growth_kernel(
                         pairs[j] = place("pairs%d" % j, 2 * (hi - lo), F32, "pairs", 8 * lo)
                         nc.scalar.copy(out=pairs[j][:, : hi - lo], in_=bank[:, lo - BANK * c : hi - BANK * c])
 
+        def last_lanes(j):
+            lo, hi = PIECES[j]
+            return pairs[j][:, hi - lo :].bitcast(BF16).rearrange("p (m e) -> p m e", e=2)
+
+        def form_third_lane():
+            lane = place("lane", SPLIT, F32, "codes", 2 * ROW - 64)
+            for lo, hi in WALL_CUTS:
+                if hi <= SPLIT:
+                    nc.gpsimd.tensor_tensor(lane[:, lo:hi], products[LAST - 1][:, lo:hi], last_wall(lo, hi)[:, 0], ADD)
+            for j, (lo, hi) in enumerate(PIECES):
+                if hi <= SPLIT:
+                    nc.scalar.copy(out=last_lanes(j)[:, :, 0], in_=lane[:, lo:hi])
+
         nc.gpsimd.memset(tabs[:, : T // 2].bitcast(I32), 0)
         nc.vector.memset(tabs[:, T // 2 :].bitcast(I32), 0)
         for offsets, source in ((idx, offs), (idx2, offs2), (idx3, offs3)):
@@ -419,6 +447,7 @@ def tile_list_cave_wall_growth_kernel(
         form_source(1)
         scatter_source(1)
         rate(0, 6)
+        form_gain(0)
         grouped_rest = place("grouped_rest", 4 * (H - 2 * P), BF16, "r2")
         group_dealt(grouped_rest[:, 8 * P :], raw_third)
         group_plain(grouped_rest[:, : 8 * P], raw_second)
@@ -468,7 +497,6 @@ def tile_list_cave_wall_growth_kernel(
                 exponentiate(s)
             if s == LAST:
                 grow(s - 1)
-                exponentiate(s)
             if s == 3:
                 deal_w2(1)
             if s == 4:
@@ -500,6 +528,9 @@ def tile_list_cave_wall_growth_kernel(
             if s == LAST:
                 load_last_walls()
                 turn_first_lanes()
+                exponentiate_last(0, GROWTH_AT[LAST])
+                form_third_lane()
+                exponentiate_last(1, "codes", ROW)
 
         last_codes = place("last_codes", T2, U32, "sink")
         last_scales = place("last_scales", T2, U8, "crossed")
@@ -508,6 +539,7 @@ def tile_list_cave_wall_growth_kernel(
         w3q = stationary(w3_codes[:], scales[:, T2:])
         first_codes = {}
         woven = {}
+        parts = {}
 
         def project(j):
             lo, hi = PIECES[j]
@@ -524,23 +556,24 @@ def tile_list_cave_wall_growth_kernel(
                 result = results[:, nb * (hi - lo) : (nb + 1) * (hi - lo)]
                 copy = nc.vector.tensor_copy if (j, nb) in VECTOR_EMPTIES else nc.scalar.copy
                 copy(out=result, in_=bank[:, : hi - lo])
-            nc.sync.dma_start(
-                out=out[:, lo:hi].rearrange("(b p) m -> p b m", p=P), in_=results[:].rearrange("p (b m) -> p b m", b=OUT_TILES)
-            )
+                nc.sync.dma_start(out=out[P * nb : P * nb + P, lo:hi], in_=result)
 
         def multiply(j):
             lo, hi = PIECES[j]
-            nc.vector.tensor_tensor(products[LAST - 1][:, T2 + lo : T2 + hi], growths[LAST][:, lo:hi], page_a[LAST % 2][:, lo:hi], MULT)
+            parts[j] = products[LAST - 1][:, T2 + lo : T2 + hi] if lo >= SPLIT else place("part%d" % j, hi - lo, F32, "codes", 2 * ROW + 4 * lo)[:]
+            nc.vector.tensor_tensor(parts[j], last_growths[lo // SPLIT][:, lo % SPLIT : lo % SPLIT + hi - lo], page_a[LAST % 2][:, lo:hi], MULT)
 
         def finish_lanes(j):
             lo, hi = PIECES[j]
-            c, c0 = divmod(lo, BANK)
-            nc.vector.tensor_tensor(
-                pairs[j][:, hi - lo :].bitcast(BF16).rearrange("p (a i e) -> p a e i", i=4, e=2),
-                products[LAST - 1][:].rearrange("p (e a i) -> p a e i", e=2, i=4)[:, lo // 4 : hi // 4],
-                last_walls[c][:].rearrange("p (e a i) -> p a e i", e=2, i=4)[:, c0 // 4 : (c0 + hi - lo) // 4],
-                ADD,
-            )
+            if lo >= SPLIT:
+                nc.vector.tensor_tensor(
+                    pairs[j][:, hi - lo :].bitcast(BF16).rearrange("p (a i e) -> p a e i", i=4, e=2),
+                    products[LAST - 1][:].rearrange("p (e a i) -> p a e i", e=2, i=4)[:, lo // 4 : hi // 4],
+                    last_wall(lo, hi).rearrange("p e (a i) -> p a e i", i=4),
+                    ADD,
+                )
+            else:
+                nc.vector.tensor_tensor(last_lanes(j)[:, :, 1], parts[j], last_wall(lo, hi)[:, 1], ADD)
             woven[j] = place("woven%d" % j, 4 * (hi - lo), BF16, "turned", 8 * lo)
             weave = nc.vector.tensor_copy if j in VECTOR_WEAVES else nc.scalar.copy
             weave(
@@ -556,10 +589,10 @@ def tile_list_cave_wall_growth_kernel(
         multiply(0)
         multiply(1)
         finish_lanes(0)
-        finish_lanes(1)
         quantize(w3_codes, scales[:, T2:], grouped[:, 4 * T2 :], (0, N))
         quantize_first_pass(0)
         quantize(w3_codes, scales[:, T2:], grouped[:, 4 * T2 :], (N, 2 * N))
+        finish_lanes(1)
         for j in range(len(PIECES)):
             done = slice(*PIECES[j])
             nc.vector.quantize_mx(out=last_codes[:, done].bitcast(FP8X4), scales=last_scales[:, done], in_=woven[j][:])

@@ -62,7 +62,7 @@ RATES_AT = {0: ("wg_late", PAGE + ROW), 1: ("wall", PAGE), 2: ("r0",)}
 GAIN_AT = {0: ("r1",), 1: ("r2", -ROW // 2), 2: ("r1", ROW)}
 GAP_AT = {0: ("r1", ROW), 1: ("wall",), 2: ("gap",), 3: ("gap", ROW), 4: ("codes",), 5: ("gap",), 6: ("gap", ROW), 7: ("codes",)}
 EQ_AT = {0: ("eq",), 1: ("eq", ROW), 2: ("grouped",), 3: ("wg_late", PAGE), 4: ("eq",), 5: ("wg_late", PAGE + ROW), 6: ("eq", ROW), 7: ("eq",)}
-SOURCE_AT = {0: ("gap",), 1: ("codes_rest",)}
+SOURCE_AT = {0: ("gap",), 1: ("gap", ROW)}
 SINK_AT = {0: ("pairs", 3 * ROW)}
 
 
@@ -392,14 +392,13 @@ def tile_list_cave_wall_growth_kernel(
                 if hi <= SPLIT:
                     nc.scalar.copy(out=last_lanes(j)[:, :, 0], in_=lane[:, lo:hi])
 
-        nc.gpsimd.memset(tabs[:, : T // 2].bitcast(I32), 0)
-        nc.vector.memset(tabs[:, T // 2 :].bitcast(I32), 0)
+        nc.vector.memset(tabs[:].bitcast(I32), 0)
         for offsets, source in ((idx, offs), (idx2, offs2), (idx3, offs3)):
             nc.sync.dma_start(offsets[:], source)
         raw_first = [place("raw_w1_0", 4 * P, F32, "grouped", 2 * PAGE), place("raw_w1_1", 4 * P, F32, "eq", ROW - 8 * P)]
         load_w1(raw_first[0][:], 0, P)
         for i in range(2):
-            nc.sync.dma_start(out=tabs[64 * i : 64 * i + 32 : 4, :].bitcast(I32), in_=tab_scales[0][8 * i : 8 * i + 8, :].bitcast(I32))
+            nc.scalar.dma_start(out=tabs[64 * i : 64 * i + 32 : 4, :].bitcast(I32), in_=tab_scales[0][8 * i : 8 * i + 8, :].bitcast(I32))
         nc.sync.dma_start(out=tabw[:].bitcast(I32), in_=tab_words[0].rearrange("p t i -> p (t i)").bitcast(I32))
         load_w1(raw_first[1][:], P, 2 * P)
         nc.vector.memset(scale_bytes[:].bitcast(I32), 0)
@@ -535,8 +534,12 @@ def tile_list_cave_wall_growth_kernel(
         last_codes = place("last_codes", T2, U32, "sink")
         last_scales = place("last_scales", T2, U8, "crossed")
         scales = place("scales", T2 + 2 * N, U8, "gap")
-        w3_codes = place("w3_codes", 2 * N, U32, "wall", 64 - 8 * N)
-        w3q = stationary(w3_codes[:], scales[:, T2:])
+        w3_codes = [place("w3_codes0", N, U32, GROWTH_AT[LAST - 1], ROW), place("w3_codes1", N, U32, "wall", 64 - 4 * N)]
+        w3q = [pair for b in range(2) for pair in stationary(w3_codes[b][:], scales[:, T2 + N * b : T2 + N * (b + 1)])]
+
+        def quantize_w3(b):
+            quantize(w3_codes[b], scales[:, T2 + N * b :], grouped[:, 4 * (T2 + N * b) :], (0, N))
+
         first_codes = {}
         woven = {}
         parts = {}
@@ -586,12 +589,12 @@ def tile_list_cave_wall_growth_kernel(
             first_codes[j] = place("first_codes%d" % j, hi - lo, U32, "wall", 64 + 4 * lo)
             quantize(first_codes[j], scales[:, lo:hi], grouped[:, 4 * lo : 4 * hi], (0, hi - lo))
 
+        quantize_w3(0)
         multiply(0)
         multiply(1)
         finish_lanes(0)
-        quantize(w3_codes, scales[:, T2:], grouped[:, 4 * T2 :], (0, N))
         quantize_first_pass(0)
-        quantize(w3_codes, scales[:, T2:], grouped[:, 4 * T2 :], (N, 2 * N))
+        quantize_w3(1)
         finish_lanes(1)
         for j in range(len(PIECES)):
             done = slice(*PIECES[j])

@@ -392,13 +392,14 @@ def tile_list_cave_wall_growth_kernel(
                 if hi <= SPLIT:
                     nc.scalar.copy(out=last_lanes(j)[:, :, 0], in_=lane[:, lo:hi])
 
-        nc.vector.memset(tabs[:].bitcast(I32), 0)
+        nc.gpsimd.memset(tabs[:, : T // 2].bitcast(I32), 0)
+        nc.vector.memset(tabs[:, T // 2 :].bitcast(I32), 0)
         for offsets, source in ((idx, offs), (idx2, offs2), (idx3, offs3)):
             nc.sync.dma_start(offsets[:], source)
         raw_first = [place("raw_w1_0", 4 * P, F32, "grouped", 2 * PAGE), place("raw_w1_1", 4 * P, F32, "eq", ROW - 8 * P)]
         load_w1(raw_first[0][:], 0, P)
         for i in range(2):
-            nc.scalar.dma_start(out=tabs[64 * i : 64 * i + 32 : 4, :].bitcast(I32), in_=tab_scales[0][8 * i : 8 * i + 8, :].bitcast(I32))
+            nc.sync.dma_start(out=tabs[64 * i : 64 * i + 32 : 4, :].bitcast(I32), in_=tab_scales[0][8 * i : 8 * i + 8, :].bitcast(I32))
         nc.sync.dma_start(out=tabw[:].bitcast(I32), in_=tab_words[0].rearrange("p t i -> p (t i)").bitcast(I32))
         load_w1(raw_first[1][:], P, 2 * P)
         nc.vector.memset(scale_bytes[:].bitcast(I32), 0)

@@ -44,7 +44,7 @@ def lay_out(areas):
 
 AT = lay_out(
     (
-        ("words", ROW), ("bytes", S), ("gathered", S), ("ident", 8 * P),
+        ("words", ROW), ("bytes", S), ("ident", 8 * P),
         ("codes_second", 4 * P), ("scales_first", 2 * P), ("codes_rest", ROW),
         ("page_a", 2 * PAGE), ("page_b0", PAGE),
         ("r0", PAGE), ("r1", PAGE), ("r2", PAGE), ("s0", PAGE), ("s1", PAGE),
@@ -62,7 +62,7 @@ RATES_AT = {0: ("wg_late", PAGE + ROW), 1: ("wall", PAGE), 2: ("r0",)}
 GAIN_AT = {0: ("r1",), 1: ("r2", -ROW // 2), 2: ("r1", ROW)}
 GAP_AT = {0: ("r1", ROW), 1: ("wall",), 2: ("gap",), 3: ("gap", ROW), 4: ("codes",), 5: ("gap",), 6: ("gap", ROW), 7: ("codes",)}
 EQ_AT = {0: ("eq",), 1: ("eq", ROW), 2: ("grouped",), 3: ("wg_late", PAGE), 4: ("eq",), 5: ("wg_late", PAGE + ROW), 6: ("eq", ROW), 7: ("eq",)}
-SOURCE_AT = {0: ("gap",), 1: ("gap", ROW)}
+SOURCE_AT = {0: ("gap",), 1: ("codes_rest",)}
 SINK_AT = {0: ("pairs", 3 * ROW)}
 
 
@@ -109,7 +109,7 @@ def tile_list_cave_wall_growth_kernel(
         halves = [slice(BANK * h, BANK * h + BANK) for h in range(2)]
         words = place("words", S, U32, "words")
         scale_bytes = place("scale_bytes", S, U8, "bytes")
-        gathered = place("gathered", S, U8, "gathered")
+        gathered = place("gathered", S, U8, "eq", ROW - S // 2)
         vw = [words[:, half].bitcast(FP8X4) for half in halves]
         vs = [scale_bytes[:, half] for half in halves]
 
@@ -396,7 +396,7 @@ def tile_list_cave_wall_growth_kernel(
         nc.vector.memset(tabs[:, T // 2 :].bitcast(I32), 0)
         for offsets, source in ((idx, offs), (idx2, offs2), (idx3, offs3)):
             nc.sync.dma_start(offsets[:], source)
-        raw_first = [place("raw_w1_0", 4 * P, F32, "grouped", 2 * PAGE), place("raw_w1_1", 4 * P, F32, "eq", ROW - 8 * P)]
+        raw_first = [place("raw_w1_0", 4 * P, F32, "grouped", 2 * PAGE), place("raw_w1_1", 4 * P, F32, "grouped", 2 * PAGE + 16 * P)]
         load_w1(raw_first[0][:], 0, P)
         for i in range(2):
             nc.sync.dma_start(out=tabs[64 * i : 64 * i + 32 : 4, :].bitcast(I32), in_=tab_scales[0][8 * i : 8 * i + 8, :].bitcast(I32))

@@ -44,26 +44,29 @@ def lay_out(areas):
 
 AT = lay_out(
     (
-        ("words", ROW), ("bytes", S), ("ident", 8 * P),
-        ("codes_second", 4 * P), ("scales_first", 2 * P), ("codes_rest", ROW),
+        ("bytes", S), ("gathered", S),
+        ("scales_first", 2 * P), ("codes_rest", ROW),
         ("page_a", 2 * PAGE), ("page_b0", PAGE),
-        ("r0", PAGE), ("r1", PAGE), ("r2", PAGE), ("s0", PAGE), ("s1", PAGE),
-        ("gap", 2 * ROW), ("sink", 2 * ROW), ("crossed", ROW), ("dealt", 768),
+        ("r0", PAGE), ("dealt", 768), ("r1", PAGE), ("r2", PAGE), ("s0", PAGE), ("s1", PAGE),
+        ("gap", 2 * ROW), ("sink", 2 * ROW), ("crossed", ROW),
         ("turned", 2 * PAGE), ("grouped", 2 * PAGE + 8 * 2 * N),
         ("codes", 4 * (T2 + 2 * N)), ("scales", T2 + 2 * N), ("dealt_late", 768),
-        ("rates", ROW), ("wall", 2 * PAGE), ("pairs", ROW), ("pairs_late", 3 * ROW), ("wg", PAGE),
-        ("codes_first", 4 * P), ("w2s", H), ("w2w", 2 * H), ("page_b1", PAGE), ("eq", 2 * ROW), ("wg_late", 2 * PAGE),
+        ("rates", ROW), ("wall", 2 * PAGE), ("pairs", 2 * PAGE), ("words", ROW), ("wg", PAGE),
+        ("codes_first", 4 * P), ("w2s", H), ("w2w", 2 * H), ("page_b1", PAGE),
+        ("eq", 2 * ROW), ("ident", 4 * P), ("wg_late", 2 * PAGE),
     )
 )
-SCORES_AT = {0: ("wg_late", PAGE), 1: ("s1", ROW), 2: ("s0",), 3: ("s1",), 4: ("dealt_late", 768 - ROW), 5: ("r2",), 6: ("dealt_late", -PAGE), 7: ("s0",)}
+SCORES_AT = {0: ("wg_late", PAGE), 1: ("wall", PAGE), 2: ("s0",), 3: ("s1",), 4: ("dealt_late", 768 - ROW), 5: ("r2",), 6: ("dealt_late", -PAGE), 7: ("s0",)}
 PRODUCT_AT = {0: ("s0",), 1: ("s1",), 2: ("dealt_late", -PAGE), 3: ("r2",), 4: ("dealt_late", -PAGE), 5: ("r1",), 6: ("s0",)}
-GROWTH_AT = {0: "r0", 1: "r1", 2: "pairs_late", 3: "r0", 4: "r1", 5: "s1", 6: "r0", 7: "r0"}
-RATES_AT = {0: ("wg_late", PAGE + ROW), 1: ("wall", PAGE), 2: ("r0",)}
-GAIN_AT = {0: ("r1",), 1: ("r2", -ROW // 2), 2: ("r1", ROW)}
-GAP_AT = {0: ("r1", ROW), 1: ("wall",), 2: ("gap",), 3: ("gap", ROW), 4: ("codes",), 5: ("gap",), 6: ("gap", ROW), 7: ("codes",)}
-EQ_AT = {0: ("eq",), 1: ("eq", ROW), 2: ("grouped",), 3: ("wg_late", PAGE), 4: ("eq",), 5: ("wg_late", PAGE + ROW), 6: ("eq", ROW), 7: ("eq",)}
+GROWTH_AT = {0: "r0", 1: "r1", 2: "grouped", 3: "r0", 4: "r1", 5: "s1", 6: "r0", 7: "r0"}
+RATES_AT = {0: ("dealt", -ROW // 2), 1: ("eq",), 2: ("r0",)}
+GAIN_AT = {0: ("r1", ROW), 1: ("r2", -ROW // 2), 2: ("r1", ROW)}
+GAP_AT = {0: ("dealt",), 1: ("wall",), 2: ("gap",), 3: ("gap", ROW), 4: ("codes",), 5: ("gap",), 6: ("gap", ROW), 7: ("codes",)}
+EQ_AT = {0: ("eq", ROW), 1: ("r0", ROW), 2: ("grouped", 3 * ROW), 3: ("wg_late", PAGE), 4: ("eq", ROW), 5: ("wg_late", PAGE + ROW), 6: ("eq",), 7: ("eq", ROW)}
+CROSSED_AT = {1: ("wg_late", PAGE + ROW), 2: ("crossed",)}
+WEIGHTS_AT = {4: (("wg_late",), ("grouped", 3 * ROW)), 6: (("wg_late", PAGE), ("wg_late", PAGE + ROW)), 7: (("wg",), ("wg", ROW))}
 SOURCE_AT = {0: ("gap",), 1: ("codes_rest",)}
-SINK_AT = {0: ("pairs", 3 * ROW)}
+SINK_AT = {0: ("grouped", 2 * ROW)}
 
 
 def gain_at(s):
@@ -109,7 +112,7 @@ def tile_list_cave_wall_growth_kernel(
         halves = [slice(BANK * h, BANK * h + BANK) for h in range(2)]
         words = place("words", S, U32, "words")
         scale_bytes = place("scale_bytes", S, U8, "bytes")
-        gathered = place("gathered", S, U8, "eq", ROW - S // 2)
+        gathered = place("gathered", S, U8, "gathered")
         vw = [words[:, half].bitcast(FP8X4) for half in halves]
         vs = [scale_bytes[:, half] for half in halves]
 
@@ -154,12 +157,12 @@ def tile_list_cave_wall_growth_kernel(
         w1q = []
 
         def first_w1(s, raw):
-            grouped = place("grouped_w1_%d" % s, 4 * P, BF16, *(("wg", -4 * P), ("ident",))[s])
+            grouped = place("grouped_w1_%d" % s, 4 * P, BF16, *(("wg", -4 * P), ("ident", -2 * P))[s])
             group_plain(grouped[:], raw[:])
             return grouped
 
         def quantize_first(s, grouped):
-            codes = place("w1_codes%d" % s, P, U32, ("codes_first", "codes_second")[s])
+            codes = place("w1_codes%d" % s, P, U32, *(("codes_first",), ("grouped", 2 * PAGE - 64))[s])
             scales = place("w1_scales%d" % s, P, U8, "scales_first", P * s)
             quantize(codes, scales, grouped, (0, P))
             w1q.extend(stationary(codes[:], scales[:]))
@@ -198,11 +201,10 @@ def tile_list_cave_wall_growth_kernel(
             source_weights[s] = aside
 
         def load_weights(s):
-            area, at = {4: ("grouped", ROW), 6: ("wg_late", PAGE), 7: ("wg", 0)}[s]
             rows = {4: slice(0, 4), 6: slice(4, 6), 7: slice(6, 8)}[s]
             span = 16 * (rows.stop - rows.start)
             for i, (matrix, held) in enumerate(((wg2, rate_weights), (wg1, source_weights))):
-                held[s] = place("wg%d_%d" % (2 - i, s), S, F32, area, at + ROW * i)
+                held[s] = place("wg%d_%d" % (2 - i, s), S, F32, *WEIGHTS_AT[s][i])
                 for p0 in range(0, P, span):
                     nc.sync.dma_start(out=held[s][p0 : p0 + span, :], in_=by_eights(matrix)[:, rows])
                 if s == 4:
@@ -273,7 +275,7 @@ def tile_list_cave_wall_growth_kernel(
             if s == 0:
                 nc.gpsimd.tensor_tensor(gaps[s][:], scores[s][:], eqs[s][:], ADD)
                 return
-            crossed = place("crossed%d" % s, S, F32, *(("crossed",) if s < 3 else gain_at(s - 1)))
+            crossed = place("crossed%d" % s, S, F32, *(CROSSED_AT[s] if s in CROSSED_AT else gain_at(s - 1)))
             for h, half in enumerate(halves):
                 bank = bank_at("sum%d%d" % (s, h), 2 + h)
                 add_transposed(bank, eqs[s][:, half], True)
@@ -424,18 +426,16 @@ def tile_list_cave_wall_growth_kernel(
         nc.sync.dma_start(out=rate_weights[0][:], in_=wg2)
         nc.sync.dma_start(out=w2w[:].bitcast(I32), in_=w2_words[0].bitcast(I32))
         load_scale_rows(w2s, w2_scales[0])
-        raw_rest = place("raw_rest", 4 * (H - 2 * P), F32, "pairs", ROW)
-        raw_second, raw_third = raw_rest[:, : 8 * P], raw_rest[:, 8 * P :]
-        load_w1(raw_third, 4 * P, H)
         grouped_first.append(first_w1(1, raw_first[1]))
-        load_eq(0)
-        load_w1(raw_second, 2 * P, 4 * P)
-        load_eq(1)
         for h in range(2):
             nc.vector.tensor_copy(words[:, halves[h]], tabw[:].indirect(idx[:, 32 * h : 32 * h + 32]))
+        raw_rest = place("raw_rest", 4 * (H - 2 * P), F32, "grouped")
+        raw_second, raw_third = raw_rest[:, : 8 * P], raw_rest[:, 8 * P :]
+        load_w1(raw_third, 4 * P, H)
+        load_w1(raw_second, 2 * P, 4 * P)
         quantize_first(1, grouped_first[1])
         make_identity(nc, ident[:])
-        load_eq(2)
+        load_eq(0)
         sources[0] = place("source0", S, F32, *SOURCE_AT[0])
         negate(source_weights[0][:, halves[1]])
         score(0)
@@ -448,13 +448,15 @@ def tile_list_cave_wall_growth_kernel(
         scatter_source(1)
         rate(0, 6)
         form_gain(0)
+        load_eq(1)
+        load_eq(2)
         grouped_rest = place("grouped_rest", 4 * (H - 2 * P), BF16, "r2")
         group_dealt(grouped_rest[:, 8 * P :], raw_third)
         group_plain(grouped_rest[:, : 8 * P], raw_second)
         subtract(0)
         subtract(1)
         load_eq(3)
-        rate(1, 4)
+        rate(1, 6)
         rate(2, 6)
         form_sink(0)
         codes_rest = place("codes_rest", H - 2 * P, U32, "codes_rest")
@@ -465,10 +467,10 @@ def tile_list_cave_wall_growth_kernel(
         form_sink(1)
         scatter_sink(1)
         load_wall(0)
-        load_weights(4)
         deal_w2(0)
         score(2)
         subtract(2)
+        load_weights(4)
         form_sink(2)
         form_source(2)
         exponentiate(0)

@@ -537,7 +537,7 @@ def tile_list_cave_wall_growth_kernel(
         last_codes = place("last_codes", T2, U32, "sink")
         last_scales = place("last_scales", T2, U8, "crossed")
         scales = place("scales", T2 + 2 * N, U8, "gap")
-        w3_codes = [place("w3_codes0", N, U32, GROWTH_AT[LAST - 1], ROW), place("w3_codes1", N, U32, "wall", 64 - 4 * N)]
+        w3_codes = [place("w3_codes0", N, U32, "codes", 2 * ROW + 4 * PIECES[3][0]), place("w3_codes1", N, U32, "wall", 64 - 4 * N)]
         w3q = [pair for b in range(2) for pair in stationary(w3_codes[b][:], scales[:, T2 + N * b : T2 + N * (b + 1)])]
 
         def quantize_w3(b):
@@ -566,7 +566,7 @@ def tile_list_cave_wall_growth_kernel(
 
         def multiply(j):
             lo, hi = PIECES[j]
-            parts[j] = products[LAST - 1][:, T2 + lo : T2 + hi] if lo >= SPLIT else place("part%d" % j, hi - lo, F32, "codes", 2 * ROW + 4 * lo)[:]
+            parts[j] = products[LAST - 1][:, T2 + lo : T2 + hi] if lo >= SPLIT else place("part%d" % j, hi - lo, F32, *(("codes", 2 * ROW + 4 * lo) if j < 3 else ("turned",)))[:]
             nc.vector.tensor_tensor(parts[j], last_growths[lo // SPLIT][:, lo % SPLIT : lo % SPLIT + hi - lo], page_a[LAST % 2][:, lo:hi], MULT)
 
         def finish_lanes(j):

from contextlib import ExitStack

import concourse.mybir as mybir
from concourse.masks import make_identity

K, H, N, T, S, T2 = 512, 1024, 384, 4096, 1024, 2048
FLOPS = 2 * K * H * S * 2 + 2 * H * N * T2

F32 = mybir.dt.float32
BF16 = mybir.dt.bfloat16
I32 = mybir.dt.int32
U32 = mybir.dt.uint32
U16 = mybir.dt.uint16
U8 = mybir.dt.uint8
FP8X4 = mybir.dt.float8_e4m3fn_x4
FP4X4 = mybir.dt.float4_e2m1fn_x4
MULT = mybir.AluOpType.mult
ADD = mybir.AluOpType.add
SUB = mybir.AluOpType.subtract
EXP = mybir.ActivationFunctionType.Exp

P = 128
BANK = 512
SLICES = H // P
LAST = SLICES - 1
CHUNKS = T2 // BANK
OUT_TILES = N // P
PIECES = tuple((lo, lo + 256) for lo in range(0, T2, 256))
VECTOR_WEAVES = (6, 7)
VECTOR_EMPTIES = ((6, 2), (7, 1), (7, 2))
SPLIT = 2 * BANK
WALL_CUTS = ((0, 256), (256, 512), (512, 1024), (1024, 1536), (1536, 2048))
ROW = 4 * S
PAGE = 4 * T2


def lay_out(areas):
    starts, at = {}, 0
    for name, size in areas:
        starts[name] = at
        at = at + size
    return starts


AT = lay_out(
    (
        ("bytes", S), ("gathered", S),
        ("scales_first", 2 * P), ("codes_rest", ROW),
        ("page_a", 2 * PAGE), ("page_b0", PAGE),
        ("r0", PAGE), ("dealt", 768), ("r1", PAGE), ("r2", PAGE), ("s0", PAGE), ("s1", PAGE),
        ("gap", 2 * ROW), ("sink", 2 * ROW), ("crossed", ROW),
        ("turned", 2 * PAGE), ("grouped", 2 * PAGE + 8 * 2 * N),
        ("codes", 4 * (T2 + 2 * N)), ("scales", T2 + 2 * N), ("dealt_late", 768),
        ("rates", ROW), ("wall", 2 * PAGE), ("pairs", 2 * PAGE), ("words", ROW), ("wg", PAGE),
        ("codes_first", 4 * P), ("w2s", H), ("w2w", 2 * H), ("page_b1", PAGE),
        ("eq", 2 * ROW), ("ident", 4 * P), ("wg_late", 2 * PAGE),
    )
)
SCORES_AT = {0: ("wg_late", PAGE), 1: ("wall", PAGE), 2: ("s0",), 3: ("s1",), 4: ("dealt_late", 768 - ROW), 5: ("r2",), 6: ("dealt_late", -PAGE), 7: ("s0",)}
PRODUCT_AT = {0: ("s0",), 1: ("s1",), 2: ("dealt_late", -PAGE), 3: ("r2",), 4: ("dealt_late", -PAGE), 5: ("r1",), 6: ("s0",)}
GROWTH_AT = {0: "r0", 1: "r1", 2: "grouped", 3: "r0", 4: "r1", 5: "s1", 6: "r0", 7: "r0"}
RATES_AT = {0: ("dealt", -ROW // 2), 1: ("eq",), 2: ("r0",)}
GAIN_AT = {0: ("r1", ROW), 1: ("r2", -ROW // 2), 2: ("r1", ROW)}
GAP_AT = {0: ("dealt",), 1: ("wall",), 2: ("gap",), 3: ("gap", ROW), 4: ("codes",), 5: ("gap",), 6: ("gap", ROW), 7: ("codes",)}
EQ_AT = {0: ("eq", ROW), 1: ("r0", ROW), 2: ("grouped", 3 * ROW), 3: ("wg_late", PAGE), 4: ("eq", ROW), 5: ("wg_late", PAGE + ROW), 6: ("eq",), 7: ("eq", ROW)}
CROSSED_AT = {1: ("wg_late", PAGE + ROW), 2: ("crossed",)}
WEIGHTS_AT = {4: (("wg_late",), ("grouped", 3 * ROW)), 6: (("wg_late", PAGE), ("wg_late", PAGE + ROW)), 7: (("wg",), ("wg", ROW))}
SOURCE_AT = {0: ("gap",), 1: ("codes_rest",)}
SINK_AT = {0: ("grouped", 2 * ROW)}


def gain_at(s):
    return GAIN_AT[s] if s in GAIN_AT else (GROWTH_AT[s - 3], ROW)


def tile_list_cave_wall_growth_kernel(
    tc, tab_words, tab_scales, offs, offs2, offs3, w1, w2_words, w2_scales, eq, wg1, wg2, wall, w3, out
):
    nc = tc.nc
    with ExitStack() as ctx:
        lists = ctx.enter_context(tc.tile_pool(name="lists", bufs=1))
        sbuf = ctx.enter_context(tc.tile_pool(name="sbuf", bufs=1))
        psum = ctx.enter_context(tc.psum_pool(name="psum", bufs=1))

        def place(name, columns, dtype, area, skip=0):
            return sbuf.tile([P, columns], dtype, name=name, align_bytes=64, offset=AT[area] + skip)

        def bank_at(name, b):
            return psum.tile([P, BANK], F32, name=name, offset=4 * BANK * b)

        def by_eights(rows):
            return rows.rearrange("(b e) n -> b e n", e=8)

        def slice_rows(matrix, s):
            if s < 4:
                return matrix[P * s : P * s + P, :]
            dealt = by_eights(matrix[512:, :])
            if s < 6:
                return dealt[32 * (s - 4) : 32 * (s - 3), 0:4]
            return dealt[:, 2 * s - 8 : 2 * s - 6]

        idx = lists.tile([P, S // 16], U16, name="idx")
        idx2 = lists.tile([P, S // 16], U16, name="idx2")
        idx3 = lists.tile([P, S // 16], U16, name="idx3")
        tabw = place("tabw", T, U32, "grouped")
        tabs = place("tabs", T, U8, "codes_first", -2 * P)
        w2w = place("w2w", 2 * H, U8, "w2w")
        w2s = place("w2s", H, U8, "w2s")
        ident = place("ident", P, F32, "ident")
        page_a = [place("page_a%d" % i, T2, F32, "page_a", PAGE * i) for i in range(2)]
        page_b = [place("page_b%d" % i, T2, F32, "page_b%d" % i) for i in range(2)]
        halves = [slice(BANK * h, BANK * h + BANK) for h in range(2)]
        words = place("words", S, U32, "words")
        scale_bytes = place("scale_bytes", S, U8, "bytes")
        gathered = place("gathered", S, U8, "gathered")
        vw = [words[:, half].bitcast(FP8X4) for half in halves]
        vs = [scale_bytes[:, half] for half in halves]

        def load_scale_rows(plane, rows):
            for r in range(4):
                nc.sync.dma_start(out=plane[r:P:32, :].bitcast(I32), in_=rows[r:16:4, :].bitcast(I32))

        def by_fours(rows):
            return rows.rearrange("(p t) c -> p t c", t=4)

        def interleave(grouped, raw, run):
            nc.scalar.copy(out=grouped.rearrange("p (b c t) -> p b t c", c=run, t=4), in_=raw)

        def load_w1(raw, lo, hi):
            nc.sync.dma_start(out=raw.rearrange("p (t c) -> p t c", t=4), in_=by_fours(w1[:, lo:hi]))

        def group_plain(grouped, raw):
            interleave(grouped, raw.rearrange("p (t b c) -> p b t c", t=4, c=4), 4)

        def group_dealt(grouped, raw):
            dealt = raw.rearrange("p (t b e) -> p b t e", t=4, e=8)
            interleave(grouped[:, :1024], dealt[:, :, :, 0:4], 4)
            interleave(grouped[:, 1024:1536], dealt[:, :, :, 4:6], 2)
            interleave(grouped[:, 1536:], dealt[:, :, :, 6:8], 2)

        def load_w3():
            raw = place("raw_w3", 8 * N, F32, "wg_late", ROW)
            nc.sync.dma_start(out=raw[:, : 4 * N].rearrange("p (t c) -> p t c", t=4), in_=by_fours(w3[:512, :]))
            dealt = by_eights(w3[512:, :])
            nc.sync.dma_start(out=raw[:, 4 * N : 6 * N], in_=dealt[:, 0:4].rearrange("b (i t) n -> b i (t n)", i=2))
            for t in (2, 3):
                nc.sync.dma_start(out=raw[:, (4 + t) * N : (5 + t) * N], in_=dealt[:, 2 * t : 2 * t + 2])
            return raw

        def quantize(codes, scales, grouped, cuts):
            for lo, hi in zip(cuts, cuts[1:]):
                nc.vector.quantize_mx(out=codes[:, lo:hi].bitcast(FP8X4), scales=scales[:, lo:hi], in_=grouped[:, 4 * lo : 4 * hi])

        def stationary(codes, scales):
            return [(codes[:, c0 : c0 + P].bitcast(FP8X4), scales[:, c0 : c0 + P]) for c0 in range(0, codes.shape[1], P)]

        w1q = []

        def first_w1(s, raw):
            grouped = place("grouped_w1_%d" % s, 4 * P, BF16, *(("wg", -4 * P), ("ident", -2 * P))[s])
            group_plain(grouped[:], raw[:])
            return grouped

        def quantize_first(s, grouped):
            codes = place("w1_codes%d" % s, P, U32, *(("codes_first",), ("grouped", 2 * PAGE - 64))[s])
            scales = place("w1_scales%d" % s, P, U8, "scales_first", P * s)
            quantize(codes, scales, grouped, (0, P))
            w1q.extend(stationary(codes[:], scales[:]))

        w2q = [(w2w[:, 2 * c0 : 2 * c0 + 2 * P], w2s[:, c0 : c0 + P]) for c0 in range(0, H // 2, P)]

        def deal_w2(i):
            dealt_words = place("w2w_dealt%d" % i, H // 2, U8, ("dealt", "dealt_late")[i])
            scales = place("w2s_dealt%d" % i, H // 4, U8, ("dealt", "dealt_late")[i], H // 2)
            column_pairs = w2w[:, H:].bitcast(U32).rearrange("p (b e) -> p b e", e=4)
            if i == 0:
                nc.scalar.copy(out=dealt_words[:].bitcast(U32).rearrange("p (b e) -> p b e", e=2), in_=column_pairs[:, :, 0:2])
                nc.scalar.copy(
                    out=scales[:].bitcast(U32), in_=w2s[:, H // 2 :].bitcast(U32).rearrange("p (b e) -> p b e", e=2)[:, :, 0]
                )
            else:
                nc.scalar.copy(
                    out=dealt_words[:].bitcast(U32).rearrange("p (e b) -> p e b", e=2),
                    in_=column_pairs[:, :, 2:4].rearrange("p b e -> p e b"),
                )
                nc.scalar.copy(
                    out=scales[:].bitcast(U16).rearrange("p (t b) -> p t b", t=2),
                    in_=w2s[:, H // 2 :].bitcast(U16).rearrange("p (b t) -> p t b", t=4)[:, 2:4],
                )
            w2q.extend((dealt_words[:, 2 * c0 : 2 * c0 + 2 * P], scales[:, c0 : c0 + P]) for c0 in (0, P))

        source_weights = {}
        rate_weights = {}

        def negate(ap):
            nc.scalar.mul(ap, ap, -1.0)

        def negate_aside(s, *at):
            aside = place("negated%d" % s, S, F32, *at)
            nc.scalar.mul(aside[:], source_weights[s][:], -1.0)
            source_weights[s] = aside

        def load_weights(s):
            rows = {4: slice(0, 4), 6: slice(4, 6), 7: slice(6, 8)}[s]
            span = 16 * (rows.stop - rows.start)
            for i, (matrix, held) in enumerate(((wg2, rate_weights), (wg1, source_weights))):
                held[s] = place("wg%d_%d" % (2 - i, s), S, F32, *WEIGHTS_AT[s][i])
                for p0 in range(0, P, span):
                    nc.sync.dma_start(out=held[s][p0 : p0 + span, :], in_=by_eights(matrix)[:, rows])
                if s == 4:
                    held[5] = held[4]

        eqs = {}

        def load_eq(s):
            eqs[s] = place("eq%d" % s, S, F32, *EQ_AT[s])
            nc.sync.dma_start(out=eqs[s][:], in_=slice_rows(eq, s))

        walls = {}

        def load_wall(s):
            walls[s] = place("wall%d" % s, T2, F32, "wall", PAGE * (s % 2))
            nc.sync.dma_start(out=walls[s][:], in_=slice_rows(wall, s))

        last_walls = {}

        def load_last_walls():
            for lo, hi in WALL_CUTS:
                both = place("last_walls%d" % lo, 2 * (hi - lo), F32, "wall", 8 * lo)[:].rearrange("p (e m) -> p e m", e=2)
                for e in range(2):
                    nc.sync.dma_start(out=both[:, e], in_=slice_rows(wall, LAST - 1 + e)[:, :, lo:hi])
                last_walls[lo, hi] = both

        def last_wall(lo, hi):
            cut = [cut for cut in WALL_CUTS if cut[0] <= lo and hi <= cut[1]][0]
            return last_walls[cut][:, :, lo - cut[0] : hi - cut[0]]

        scores = {}
        sources = {}

        def score(s, first_bank=0):
            scores[s] = place("scores%d" % s, S, F32, *SCORES_AT[s])
            for h in range(2):
                bank = bank_at("score%d%d" % (s, h), first_bank + h)
                nc.tensor.matmul_mx(
                    out=bank[:], lhsT=w1q[s][0], lhsT_scale=w1q[s][1], rhs=vw[h], rhs_scale=vs[h], start=True, stop=True
                )
                if (s, h) == (0, 0):
                    nc.vector.tensor_tensor(sources[0][:, halves[0]], bank[:], source_weights[0][:, halves[0]], MULT)
                nc.scalar.mul(scores[s][:, halves[h]], bank[:], -1.0)

        rates = {}
        gains = {}

        def rate(s, first_bank=0):
            rates[s] = place("rates%d" % s, S, F32, *(RATES_AT[s] if s in RATES_AT else (GROWTH_AT[s - 1],)))
            for h in range(2):
                bank = bank_at("rate%d%d" % (s, h), first_bank + h)
                nc.tensor.matmul_mx(
                    out=bank[:], lhsT=w2q[s][0].bitcast(FP4X4), lhsT_scale=w2q[s][1], rhs=vw[h], rhs_scale=vs[h], start=True, stop=True
                )
                nc.scalar.mul(rates[s][:, halves[h]], bank[:], -1.0)

        def add_transposed(bank, rows, opens):
            for g in range(4):
                nc.tensor.matmul(
                    bank[:, P * g : P * g + P], lhsT=rows[:, P * g : P * g + P], rhs=ident[:],
                    start=(opens and g == 0), stop=(not opens and g == 3), is_transpose=True,
                )

        gaps = {}

        def subtract(s):
            gaps[s] = place("gap%d" % s, S, F32, *GAP_AT[s])
            if s == 0:
                nc.gpsimd.tensor_tensor(gaps[s][:], scores[s][:], eqs[s][:], ADD)
                return
            crossed = place("crossed%d" % s, S, F32, *(CROSSED_AT[s] if s in CROSSED_AT else gain_at(s - 1)))
            for h, half in enumerate(halves):
                bank = bank_at("sum%d%d" % (s, h), 2 + h)
                add_transposed(bank, eqs[s][:, half], True)
                add_transposed(bank, scores[s][:, half], False)
                nc.scalar.copy(out=crossed[:, half], in_=bank[:])
            for h, half in enumerate(halves):
                bank = bank_at("back%d%d" % (s, h), h if s == 1 else 2 + h)
                for c0 in range(0, BANK, P):
                    nc.tensor.transpose(bank[:, c0 : c0 + P], crossed[:, half][:, c0 : c0 + P], ident[:])
                nc.scalar.copy(out=gaps[s][:, half], in_=bank[:])

        sinks = {}

        def form_gain(s):
            gains[s] = place("gain%d" % s, S, F32, *gain_at(s))
            nc.gpsimd.tensor_tensor(gains[s][:], rates[s][:], rate_weights[s][:], MULT)

        def form_sink(s):
            if s > 0:
                form_gain(s)
            sinks[s] = place("sink%d" % s, S, F32, *SINK_AT.get(s, ("sink", ROW * (s % 2))))
            nc.gpsimd.tensor_tensor(sinks[s][:], gaps[s][:], gains[s][:], MULT)

        def form_source(s):
            sources[s] = place("source%d" % s, S, F32, *SOURCE_AT.get(s, GAP_AT[s]))
            nc.gpsimd.tensor_tensor(sources[s][:], scores[s][:], source_weights[s][:], MULT)

        def scatter_sink(s):
            nc.vector.tensor_copy(page_b[s % 2][:].indirect(idx3[:]), sinks[s][:])

        def scatter_source(s):
            nc.vector.tensor_copy(page_a[s % 2][:].indirect(idx2[:]), sources[s][:])

        growths = {}

        def exponentiate(s):
            growths[s] = place("growth%d" % s, T2, F32, GROWTH_AT[s])
            nc.scalar.activation(out=growths[s][:], in_=page_b[s % 2][:], func=EXP)

        last_growths = []

        def exponentiate_last(i, *at):
            last_growths.append(place("last_growth%d" % i, SPLIT, F32, *at))
            nc.scalar.activation(out=last_growths[i][:], in_=page_b[LAST % 2][:, SPLIT * i : SPLIT * (i + 1)], func=EXP)

        products = {}

        def grow(s):
            products[s] = place("product%d" % s, T2 if s < LAST - 1 else 2 * T2, F32, *PRODUCT_AT[s])
            nc.gpsimd.tensor_tensor(products[s][:, :T2], growths[s][:], page_a[s % 2][:], MULT)

        turned = {}

        def form_z(s):
            banks = [bank_at("z%d%d" % (s, c), 4 + c) for c in range(CHUNKS)]
            for rows, opens in ((walls[s], True), (products[s], False)):
                for c, bank in enumerate(banks):
                    add_transposed(bank, rows[:, BANK * c : BANK * c + BANK], opens)
            for c, bank in enumerate(banks):
                if s == 0:
                    turned[0, c] = place("turned0%d" % c, 4 * BANK, BF16, "turned", 8 * BANK * (CHUNKS - 1 - c))
                if s == 4:
                    turned[1, c] = place("turned1%d" % c, 2 * BANK, BF16, "r2", 4 * BANK * c)
                if s < 4:
                    nc.scalar.copy(
                        out=turned[0, c][:].rearrange("m (u g q e) -> m u g q e", u=2, g=4, e=2)[:, :, :, 32 * s : 32 * s + 32, :],
                        in_=bank[:].rearrange("m (g q u e) -> m u g q e", g=4, u=2, e=2),
                    )
                else:
                    nc.scalar.copy(
                        out=turned[1, c][:].rearrange("m (g q) -> m g q", g=4)[:, :, P * (s - 4) : P * (s - 3)],
                        in_=bank[:].rearrange("m (g q) -> m g q", g=4),
                    )

        grouped = place("grouped", 4 * (T2 + 2 * N), BF16, "grouped")

        def regroup(i):
            for j in range(2):
                turned_words = turned[0, 2 * i + j][:].bitcast(F32)
                for h in range(2):
                    bank = bank_at("regroup%d%d%d" % (i, j, h), 4 + 2 * j + h)
                    for u in range(2):
                        for g2 in range(2):
                            w0 = P * (4 * u + 2 * h + g2)
                            o0 = P * (2 * u + g2)
                            nc.tensor.transpose(bank[:, o0 : o0 + P], turned_words[:, w0 : w0 + P], ident[:])
                    c0 = BANK * (4 * i + 2 * j + h)
                    nc.scalar.copy(
                        out=grouped[:].bitcast(F32)[:, c0 : c0 + BANK].rearrange("p (m u) -> p m u", u=2),
                        in_=bank[:].rearrange("p (u m) -> p m u", u=2),
                    )

        pairs = {}

        def turn_first_lanes():
            for c in range(CHUNKS):
                turned_words = turned[1, c][:].bitcast(F32)
                bank = bank_at("turn%d" % c, 4 + c)
                for g in range(4):
                    nc.tensor.transpose(bank[:, P * g : P * g + P], turned_words[:, P * g : P * g + P], ident[:])
                for j, (lo, hi) in enumerate(PIECES):
                    if lo // BANK == c:
                        pairs[j] = place("pairs%d" % j, 2 * (hi - lo), F32, "pairs", 8 * lo)
                        nc.scalar.copy(out=pairs[j][:, : hi - lo], in_=bank[:, lo - BANK * c : hi - BANK * c])

        def last_lanes(j):
            lo, hi = PIECES[j]
            return pairs[j][:, hi - lo :].bitcast(BF16).rearrange("p (m e) -> p m e", e=2)

        def form_third_lane():
            lane = place("lane", SPLIT, F32, "codes", 2 * ROW - 64)
            for lo, hi in WALL_CUTS:
                if hi <= SPLIT:
                    nc.gpsimd.tensor_tensor(lane[:, lo:hi], products[LAST - 1][:, lo:hi], last_wall(lo, hi)[:, 0], ADD)
            for j, (lo, hi) in enumerate(PIECES):
                if hi <= SPLIT:
                    nc.scalar.copy(out=last_lanes(j)[:, :, 0], in_=lane[:, lo:hi])

        nc.gpsimd.memset(tabs[:, : T // 2].bitcast(I32), 0)
        nc.vector.memset(tabs[:, T // 2 :].bitcast(I32), 0)
        for offsets, source in ((idx, offs), (idx2, offs2), (idx3, offs3)):
            nc.sync.dma_start(offsets[:], source)
        raw_first = [place("raw_w1_0", 4 * P, F32, "grouped", 2 * PAGE), place("raw_w1_1", 4 * P, F32, "grouped", 2 * PAGE + 16 * P)]
        load_w1(raw_first[0][:], 0, P)
        for i in range(2):
            nc.sync.dma_start(out=tabs[64 * i : 64 * i + 32 : 4, :].bitcast(I32), in_=tab_scales[0][8 * i : 8 * i + 8, :].bitcast(I32))
        nc.sync.dma_start(out=tabw[:].bitcast(I32), in_=tab_words[0].rearrange("p t i -> p (t i)").bitcast(I32))
        load_w1(raw_first[1][:], P, 2 * P)
        nc.vector.memset(scale_bytes[:].bitcast(I32), 0)
        for page in page_a:
            nc.vector.memset(page[:].bitcast(I32), 0)
        nc.vector.tensor_copy(gathered[:], tabs[:].indirect(idx[:]))
        for q in range(4):
            first_row = 64 * (q // 2) + 16 * (q % 2)
            nc.sync.dma_start(
                out=scale_bytes[32 * q : 32 * q + 4, :].bitcast(I32), in_=gathered[first_row : first_row + 16 : 4, :].bitcast(I32)
            )
        grouped_first = [first_w1(0, raw_first[0])]
        quantize_first(0, grouped_first[0])
        nc.vector.memset(w2s[:].bitcast(I32), 0)
        for page in page_b:
            nc.vector.memset(page[:].bitcast(I32), 0)
        plain_weights = [place("wg%d_0" % (2 - i), S, F32, "wg", ROW * i) for i in range(2)]
        for s in range(4):
            rate_weights[s], source_weights[s] = plain_weights
        for half in halves:
            nc.sync.dma_start(out=source_weights[0][:, half], in_=wg1[:, half])
        nc.sync.dma_start(out=rate_weights[0][:], in_=wg2)
        nc.sync.dma_start(out=w2w[:].bitcast(I32), in_=w2_words[0].bitcast(I32))
        load_scale_rows(w2s, w2_scales[0])
        grouped_first.append(first_w1(1, raw_first[1]))
        for h in range(2):
            nc.vector.tensor_copy(words[:, halves[h]], tabw[:].indirect(idx[:, 32 * h : 32 * h + 32]))
        raw_rest = place("raw_rest", 4 * (H - 2 * P), F32, "grouped")
        raw_second, raw_third = raw_rest[:, : 8 * P], raw_rest[:, 8 * P :]
        load_w1(raw_third, 4 * P, H)
        load_w1(raw_second, 2 * P, 4 * P)
        quantize_first(1, grouped_first[1])
        make_identity(nc, ident[:])
        load_eq(0)
        sources[0] = place("source0", S, F32, *SOURCE_AT[0])
        negate(source_weights[0][:, halves[1]])
        score(0)
        nc.vector.tensor_copy(page_a[0][:].indirect(idx2[:, :32]), sources[0][:, halves[0]])
        nc.gpsimd.tensor_tensor(sources[0][:, halves[1]], scores[0][:, halves[1]], source_weights[0][:, halves[1]], MULT)
        negate(source_weights[0][:, halves[0]])
        score(1, 6)
        nc.vector.tensor_copy(page_a[0][:].indirect(idx2[:, 32:]), sources[0][:, halves[1]])
        form_source(1)
        scatter_source(1)
        rate(0, 6)
        form_gain(0)
        load_eq(1)
        load_eq(2)
        grouped_rest = place("grouped_rest", 4 * (H - 2 * P), BF16, "r2")
        group_dealt(grouped_rest[:, 8 * P :], raw_third)
        group_plain(grouped_rest[:, : 8 * P], raw_second)
        subtract(0)
        subtract(1)
        load_eq(3)
        rate(1, 6)
        rate(2, 6)
        form_sink(0)
        codes_rest = place("codes_rest", H - 2 * P, U32, "codes_rest")
        scales_rest = place("scales_rest", H - 2 * P, U8, "codes_rest", 4 * (H - 2 * P))
        quantize(codes_rest, scales_rest, grouped_rest, (0, 2 * P, H - 2 * P))
        w1q.extend(stationary(codes_rest[:], scales_rest[:]))
        scatter_sink(0)
        form_sink(1)
        scatter_sink(1)
        load_wall(0)
        deal_w2(0)
        score(2)
        subtract(2)
        load_weights(4)
        form_sink(2)
        form_source(2)
        exponentiate(0)
        load_wall(1)
        score(3)
        rate(3)
        subtract(3)
        load_eq(4)
        negate_aside(4, "crossed")
        source_weights[5] = source_weights[4]

        for s in range(2, SLICES):
            scatter_sink(s)
            if s == 2:
                exponentiate(s - 1)
            grow(s - 2)
            if s == LAST:
                form_source(s)
            scatter_source(s)
            if s + 1 < LAST:
                form_sink(s + 1)
                exponentiate(s)
                form_source(s + 1)
            if s + 1 == LAST:
                form_sink(s + 1)
                exponentiate(s)
            if s == LAST:
                grow(s - 1)
            if s == 3:
                deal_w2(1)
            if s == 4:
                form_z(s - 2)
            if s + 2 <= LAST:
                score(s + 2)
                rate(s + 2)
                subtract(s + 2)
            if s + 3 <= LAST:
                load_eq(s + 3)
            if s != 4:
                form_z(s - 2)
            if s < LAST - 1:
                load_wall(s)
            if s == 2:
                load_weights(LAST)
            if s == 3:
                load_weights(6)
            if s in (4, 5):
                negate_aside(s + 2, *EQ_AT[s + 2])
            if s in (5, 6):
                regroup(s - 5)
            if s == LAST - 2:
                raw_w3 = load_w3()
            if s == LAST - 1:
                for b in range(2):
                    cols = slice(4 * N * b, 4 * N * (b + 1))
                    group_plain(grouped[:, 4 * T2 :][:, cols], raw_w3[:, cols])
            if s == LAST:
                load_last_walls()
                turn_first_lanes()
                exponentiate_last(0, GROWTH_AT[LAST])
                form_third_lane()
                exponentiate_last(1, "codes", ROW)

        last_codes = place("last_codes", T2, U32, "sink")
        last_scales = place("last_scales", T2, U8, "crossed")
        scales = place("scales", T2 + 2 * N, U8, "gap")
        w3_codes = [place("w3_codes0", N, U32, "codes", 2 * ROW + 4 * PIECES[3][0]), place("w3_codes1", N, U32, "wall", 64 - 4 * N)]
        w3q = [pair for b in range(2) for pair in stationary(w3_codes[b][:], scales[:, T2 + N * b : T2 + N * (b + 1)])]

        def quantize_w3(b):
            quantize(w3_codes[b], scales[:, T2 + N * b :], grouped[:, 4 * (T2 + N * b) :], (0, N))

        first_codes = {}
        woven = {}
        parts = {}

        def project(j):
            lo, hi = PIECES[j]
            first = (first_codes[j][:], scales[:, lo:hi])
            area, at = ("r1", 4 * OUT_TILES * lo) if j < 5 else ("wg_late", 4 * OUT_TILES * (lo - PIECES[5][0]))
            results = place("results%d" % j, OUT_TILES * (hi - lo), F32, area, at)
            for nb in range(OUT_TILES):
                bank = bank_at("out%d%d" % (j, nb), (OUT_TILES * j + nb + 4) % 8)
                for b, (z_codes, z_scales) in enumerate((first, (last_codes[:, lo:hi], last_scales[:, lo:hi]))):
                    nc.tensor.matmul_mx(
                        out=bank[:, : hi - lo], lhsT=w3q[OUT_TILES * b + nb][0], lhsT_scale=w3q[OUT_TILES * b + nb][1],
                        rhs=z_codes.bitcast(FP8X4), rhs_scale=z_scales, start=(b == 0), stop=(b == 1),
                    )
                result = results[:, nb * (hi - lo) : (nb + 1) * (hi - lo)]
                copy = nc.vector.tensor_copy if (j, nb) in VECTOR_EMPTIES else nc.scalar.copy
                copy(out=result, in_=bank[:, : hi - lo])
                nc.sync.dma_start(out=out[P * nb : P * nb + P, lo:hi], in_=result)

        def multiply(j):
            lo, hi = PIECES[j]
            parts[j] = products[LAST - 1][:, T2 + lo : T2 + hi] if lo >= SPLIT else place("part%d" % j, hi - lo, F32, *(("codes", 2 * ROW + 4 * lo) if j < 3 else ("turned",)))[:]
            nc.vector.tensor_tensor(parts[j], last_growths[lo // SPLIT][:, lo % SPLIT : lo % SPLIT + hi - lo], page_a[LAST % 2][:, lo:hi], MULT)

        def finish_lanes(j):
            lo, hi = PIECES[j]
            if lo >= SPLIT:
                nc.vector.tensor_tensor(
                    pairs[j][:, hi - lo :].bitcast(BF16).rearrange("p (a i e) -> p a e i", i=4, e=2),
                    products[LAST - 1][:].rearrange("p (e a i) -> p a e i", e=2, i=4)[:, lo // 4 : hi // 4],
                    last_wall(lo, hi).rearrange("p e (a i) -> p a e i", i=4),
                    ADD,
                )
            else:
                nc.vector.tensor_tensor(last_lanes(j)[:, :, 1], parts[j], last_wall(lo, hi)[:, 1], ADD)
            woven[j] = place("woven%d" % j, 4 * (hi - lo), BF16, "turned", 8 * lo)
            weave = nc.vector.tensor_copy if j in VECTOR_WEAVES else nc.scalar.copy
            weave(
                out=woven[j][:].bitcast(F32).rearrange("p (m u) -> p m u", u=2),
                in_=pairs[j][:].rearrange("p (u m) -> p m u", u=2),
            )

        def quantize_first_pass(j):
            lo, hi = PIECES[j]
            first_codes[j] = place("first_codes%d" % j, hi - lo, U32, "wall", 64 + 4 * lo)
            quantize(first_codes[j], scales[:, lo:hi], grouped[:, 4 * lo : 4 * hi], (0, hi - lo))

        quantize_w3(0)
        multiply(0)
        multiply(1)
        finish_lanes(0)
        quantize_first_pass(0)
        quantize_w3(1)
        finish_lanes(1)
        for j in range(len(PIECES)):
            done = slice(*PIECES[j])
            nc.vector.quantize_mx(out=last_codes[:, done].bitcast(FP8X4), scales=last_scales[:, done], in_=woven[j][:])
            if j + 2 < len(PIECES):
                multiply(j + 2)
                finish_lanes(j + 2)
            if j + 1 < len(PIECES):
                quantize_first_pass(j + 1)
            project(j)
